import numpy as np, ml_dtypes
CORES = [6,15,38,47]
N = 4
BF = ml_dtypes.bfloat16
def gentries(a):
    return np.ascontiguousarray(a.reshape(8, 16, -1).transpose(0, 2, 1)).reshape(8, -1)
def gtable(e):
    e = np.asarray(e); return np.ascontiguousarray(e.reshape(8, -1, 16).transpose(0, 2, 1)).reshape(128, -1).astype(np.int32)
V, K, B, CAP, E0, EC, RO = 1024, 8, 128, 128, 2176, 640, 3
E = E0 + RO * EC
JJ, KK = np.triu_indices(K, 1)
def turn(ends):
    f = ends.reshape(-1); o = np.argsort(f, kind="stable"); s = f[o]; r = np.empty(len(f), np.int64); r[o] = np.arange(len(f)) - np.searchsorted(s, s)
    return r.reshape(-1, 2)
def place(rng, a, b):
    a = np.concatenate(a); b = np.concatenate(b); lo = np.minimum(a, b); hi = np.maximum(a, b)
    first = np.sort(np.unique(lo * V + hi, return_index=True)[1]); first = first[lo[first] != hi[first]]
    ends = np.stack([lo[first], hi[first]], 1); ends = ends[np.all(turn(ends) < K, axis=1)][:E0]
    slot = np.argsort(rng.random((V, K)), axis=1)[ends, turn(ends)]
    name = rng.permutation(np.concatenate([np.array([0, E0 - 1]), rng.permutation(np.arange(1, E0 - 1))[:len(ends) - 2]]))
    nb = np.full((V, K), -1); en = np.full((V, K), -1); nb[ends, slot] = ends[:, ::-1]; en[ends, slot] = name[:, None]
    return nb, en
def world(rng, make):
    pl = np.argsort(rng.random((N, 8, B)), axis=-1)
    got = [[place(rng, *make(q, g, pl[q - 1, g], pl[q, g])) for g in range(8)] for q in range(N)]
    return np.array([[h[0] for h in r] for r in got]), np.array([[h[1] for h in r] for r in got])
def seam(first, last, lo, hi):
    i = np.arange(lo, hi - 1)
    return np.concatenate([first[i], last[i] + V - B]), np.concatenate([first[i + 1], last[i + 1] + V - B])
def roads(rng, share, first, last):
    n = V - 2 * B; p = B + rng.permutation(n); t = rng.permutation(n); h = 3 * B // 4; i = 4 * np.arange(8); j = i + 33
    a = [last[i] + V - B, first[i], first[j], last[j] + V - B]; b = [last[i + 2], first[i + 2], first[j + 2] + V - B, last[j + 2] + V - B]
    for w in (first, last + V - B):
        for d, c in ((1, 0.85), (3, 0.5)):
            i = np.flatnonzero(rng.random(B - d) < c); a.append(w[i]); b.append(w[i + d])
    for s, w in enumerate((first, last + V - B)):
        c = p[t[s * h:(s + 1) * h]]; i = rng.permutation(B - 1)[:h]; a += [c, c]; b += [w[i], w[i + 1]]
    m = int(share * 1.3 * (E0 - len(np.concatenate(a)))); i = (n * rng.random(m) ** 1.5).astype(np.int64)
    a.append(p[i]); b.append(p[(i + rng.integers(1, 7, m)) % n])
    return a, b
def shares(rng):
    return np.stack([rng.permutation(np.repeat(np.array([0.25, 0.5, 0.75, 1.0]), 2)) for q in range(N)])
def tri(t):
    out = []; c = K
    while t > 0:
        while c * (c - 1) // 2 > t: c -= 1
        out.append(c); t -= c * (c - 1) // 2
    return out
def hubs(rng, iso, t, first, last):
    a, b = [], []; v = B + iso; use = [0, 0]
    for i, c in enumerate(tri(t)):
        s = i % 2
        if use[s] + c > B: s = 1 - s
        w = (first, last + V - B)[s][use[s]:use[s] + c]; use[s] += c
        a.append(np.full(len(w), v)); b.append(w); v += 1
    for i in range(CAP // 4):
        m = v + np.arange(5); a.append(m); b.append(np.roll(m, 1)); v += 5
    r = rng.permutation(np.arange(v, V - B)); r = r[:len(r) // 5 * 5].reshape(-1, 5); i, j = np.triu_indices(5, 1)
    a.append(r[:, i].reshape(-1)); b.append(r[:, j].reshape(-1)); x, y = seam(first, last, B - 8, B); a.append(x); b.append(y)
    return a, b
def fives(rng, n, first, last):
    a, b = [], []
    for i, c in enumerate(np.array_split(B + rng.permutation(V - 2 * B), n)):
        m = len(c)
        if i % 3 == 0: x, y = np.triu_indices(m, 1); a.append(c[x]); b.append(c[y])
        elif i % 3 == 1: a.append(np.full(m - 1, c[0])); b.append(c[1:])
        else: a.append(np.repeat(c[:2], m - 2)); b.append(np.tile(c[2:], 2))
        w = (first, last + V - B)[i % 2][i // 2 * 2:i // 2 * 2 + 2]; a.append(np.full(len(w), c[0])); b.append(w)
    x, y = seam(first, last, 0, B); a.append(x); b.append(y)
    return a, b
def full(rng, first, last):
    n = min((E0 - 2 * B) // (K * K), (V - 2 * B) // (2 * K)); p = (B + rng.permutation(n * 2 * K)).reshape(n, 2, K); x, y = seam(first, last, 0, B)
    return [np.repeat(p[:, 0], K, axis=1).reshape(-1), x], [np.tile(p[:, 1], (1, K)).reshape(-1), y]
def knots(rng):
    n = min(E0 // (K * (K + 1) // 2), (V - 2 * B) // (K + 1)); p = (B + rng.permutation(n * (K + 1))).reshape(n, K + 1); x, y = np.triu_indices(K + 1, 1)
    return [p[:, x].reshape(-1)], [p[:, y].reshape(-1)]
def stuffed(rng, first, last):
    h = B // K; n = min((E0 - 2 * h * K) // (K * (K + 1) // 2), (V - 2 * B - 2 * h) // (K + 1)); z = n * K; i = np.arange(z)
    c = B + rng.permutation(n); v = B + n + rng.permutation(2 * h); p = B + n + 2 * h + rng.permutation(z); w = np.concatenate([first[:h * K], last[:h * K] + V - B])
    a = [np.repeat(v, K), c[i % n], p[::2]]; b = [w, p, p[(i[::2] + K - 1) % z]]
    for d in range(1, K // 2): a.append(p); b.append(p[(i + d) % z])
    return a, b
def around(w):
    d = np.arange(1, K // 2 + 1)[:, None]; i = np.arange(B)[None, :]
    return np.tile(w, K // 2), w[(i + d) % B].reshape(-1)
def rims(rng, shift, first, last):
    r = B + rng.permutation(V - 2 * B); r = r[:len(r) // 5 * 5].reshape(-1, 5)
    x, y = around((first + shift) % B); s, t = around(last + V - B)
    return [x, s, r.reshape(-1)], [y, t, np.roll(r, 1, axis=1).reshape(-1)]
def small(rng, start, first, last):
    n = V - 2 * B; p = B + rng.permutation(n); i = np.arange(1, n); far = np.maximum(i - rng.integers(1, 4, n - 1), 0); on = rng.random(n - 1) >= start
    a, b = [p[i][on]], [p[far][on]]; x, y = seam(first, last, 0, B); a.append(x); b.append(y); h = B // 4; t = rng.permutation(n)
    for s, w in enumerate((first, last + V - B)):
        c = p[t[s * h:(s + 1) * h]]; a += [c, c]; b += [w[0:2 * h:2], w[1:2 * h:2]]
    return a, b
def which(nb, en):
    bl = np.full(V + 1, 2); bl[:B] = 0; bl[V - B:V] = 1; bl[V] = 3; own = bl[:V][None, None, :, None]
    q, g, v, k = np.nonzero((bl[nb] == own) & (own < 2)); m = np.full((N, 8, E0), -1); m[q, g, en[q, g, v, k]] = bl[v]
    return m[:, :, None, :]
def usual(rng, nb, en):
    v = np.clip(np.exp2(2 + 5.5 * rng.random((N, 8, 1, E0))) * (0.5 + rng.random((N, 8, 16, E0))), 1, 255).astype(np.int64)
    near = np.where(rng.random((1, 8, 1, 1)) < 0.5, rng.integers(15, 60, v.shape), 20 + 10 * rng.integers(0, 3, v.shape))
    return np.where(which(nb, en) >= 0, near, v)
def pack(v, nb, en):
    return {"lens": np.ascontiguousarray(v.reshape(N, 128, E0)).astype(np.float32).astype(BF), "en": np.stack([gtable(a.transpose(0, 2, 1).reshape(8, -1)) for a in en]),
            "nb": np.stack([gtable(a.transpose(0, 2, 1).reshape(8, -1)) for a in nb])}
def setup_inputs(rng):
    sh = shares(rng); nb, en = world(rng, lambda q, g, first, last: roads(rng, sh[q, g], first, last))
    return pack(usual(rng, nb, en), nb, en)
def setup_inputs_spread(rng):
    sh = shares(rng); nb, en = world(rng, lambda q, g, first, last: roads(rng, sh[q, g], first, last))
    return pack(np.clip(np.exp2(8 * rng.random((N, 8, 1, E0))) * rng.random((N, 8, 16, E0)), 1, 255).astype(np.int64), nb, en)
def setup_inputs_ends(rng):
    sh = shares(rng)
    def make(q, g, first, last):
        if g % 2:
            a, b = hubs(rng, CAP * (1 + (g // 2 + q + 1) % (RO - 1)), EC - CAP // 4 + 3 * len(JJ), first, last); far = [[0, V - 1]]
        else:
            a, b = roads(rng, sh[q, g], first, last); far = [[0, V - 1], [B, V - B - 1], [0, B], [V - 1, V - B - 1], [0, V - B - 1], [V - 1, B]]
        far = np.array(far); return [far[:, 0]] + a, [far[:, 1]] + b
    nb, en = world(rng, make); pr = rng.choice(np.array([0.0, 0.25, 0.75, 0.75, 0.9, 1.0]), (N, 8, 1, E0))
    return pack(np.where(rng.random((N, 8, 16, E0)) < pr, 1, 255), nb, en)
def setup_inputs_corners(rng):
    c4 = CAP // 4
    def make(q, g, first, last):
        c = (q + g) % 8
        if c < 4: return hubs(rng, 0, EC - c4 + (0, -1, 1, 3 * len(JJ))[c], first, last)
        if c == 4: return hubs(rng, CAP * (RO - 1), EC - c4, first, last)
        return fives(rng, CAP + (0, -1, 1)[c - 5], first, last)
    nb, en = world(rng, make)
    return pack(usual(rng, nb, en), nb, en)
def setup_inputs_crowd(rng):
    def make(q, g, first, last):
        if g >= 6: return rims(rng, g - 6, first, last)
        if g == 3: return stuffed(rng, first, last)
        if g == 4: return knots(rng)
        if g % 3 == 0: return full(rng, first, last)
        if g % 3 == 1: return fives(rng, CAP, first, last)
        return hubs(rng, 0, EC - CAP // 4 + 3 * len(JJ), first, last)
    nb, en = world(rng, make); w = which(nb, en); r = np.argsort(rng.random((1, 8, 16, 1)), axis=2)
    c = rng.choice(np.array([0, 1, 7, 8, 9, 10, 15, 16]), (N, 8, 1, E0))
    for q in range(0, N, 2):
        for s, k in ((q, 1), ((q + 1) % N, 0)):
            c[s, 6] = np.where(w[s, 6] == k, rng.integers(0, 2, (1, E0)) + 7 * int(k == 1 - q // 2 % 2), c[s, 6])
    side = 20 + (r < c)
    return pack(np.where((rng.random((N, 8, 1, E0)) < 0.5) & (w < 0), 10, side), nb, en)
def setup_inputs_calm(rng):
    st = np.stack([rng.permutation(np.array([0.05, 0.1, 0.15, 0.2, 0.25, 0.35, 0.5, 0.7])) for q in range(N)])
    nb, en = world(rng, lambda q, g, first, last: small(rng, st[q, g], first, last))
    return pack(rng.integers(1, 5, (N, 8, 16, E0)), nb, en)
def check_inputs(d):
    bad = []
    for k, lo, hi in (("lens", 1, 255), ("en", -1, E0 - 1), ("nb", -1, V - 1)):
        a = np.asarray(d[k]).astype(np.float64)
        if not (np.all(a >= lo) and np.all(a <= hi)): bad.append("range of " + k)
        elif not np.all(a == np.floor(a)): bad.append("whole numbers of " + k)
    if bad: return bad
    for q in range(N):
        nl = gentries(np.asarray(d["nb"][q])).astype(np.int64); el = gentries(np.asarray(d["en"][q])).astype(np.int64)
        for g in range(8):
            n, e = nl[g], el[g]; f = np.flatnonzero(e >= 0)
            if np.any((n >= 0) != (e >= 0)): bad.append("empty slots alike in en and nb"); continue
            v = f % V; u = n[f]; o = np.argsort(e[f], kind="stable"); s = e[f][o]
            if len(s) % 2 or np.any(s[0::2] != s[1::2]) or np.any(s[2::2] == s[1:-1:2]): bad.append("every edge in two slots"); continue
            a, b = o[0::2], o[1::2]
            if np.any(v[a] != u[b]) or np.any(v[b] != u[a]): bad.append("ends of an edge name each other")
            if np.any(v[a] == v[b]): bad.append("two different ends")
            if len(np.unique(np.minimum(v[a], v[b]) * V + np.maximum(v[a], v[b]))) != len(a): bad.append("no two edges between the same vertices")
    return sorted(set(bad))
def contract(nb, en, x, mid, live, t):
    me = np.arange(V); big = (K + 1) * V; deg = np.add.reduce((nb >= 0).astype(np.int64), axis=1)
    key = np.where(live & (me >= B) & (me < V - B), deg * V + me, big); m = key
    for hop in range(2): m = np.minimum(m, np.min(np.append(m, big)[nb], axis=1))
    go = np.flatnonzero((m == key) & (key < big))[:CAP]
    un, ue = nb[go], en[go]; u, w = un[:, JJ], un[:, KK]; ok = (u >= 0) & (w >= 0)
    z = np.minimum(x[:, ue[:, JJ]] + x[:, ue[:, KK]], 255)
    same = (nb[u] == w[..., None]) & ok[..., None]; has = np.any(same, axis=2); side = np.max(np.where(same, en[u], -1), axis=2)
    a, p = np.nonzero(has); zz = z[:, a, p]; e = side[a, p]; old = x[:, e]
    win = np.add.reduce((zz < old).astype(np.int64), axis=0) >= 9
    x[:, e] = np.minimum(zz, old); mid[e[win]] = go[a[win]]
    live[go] = False; dead = np.zeros(V + 1, bool); dead[go] = True; hit = dead[nb]
    nb[hit] = -1; en[hit] = -1; nb[go] = -1; en[go] = -1
    new = ok & ~has; s = np.zeros((len(go), K, K), np.int64); s[:, JJ, KK] = new; s[:, KK, JJ] = new
    before = np.add.accumulate(s, axis=2) - s; free = nb[un] < 0
    fits = before < np.add.reduce(free.astype(np.int64), axis=2)[..., None]
    given = np.take_along_axis(np.argsort(~free, axis=2, kind="stable"), before, 2)
    a, p = np.nonzero(new & fits[:, JJ, KK] & fits[:, KK, JJ]); a, p = a[:EC], p[:EC]; j, k = JJ[p], KK[p]; e = E0 + EC * t + np.arange(len(a))
    x[:, e] = z[:, a, p]; mid[e] = go[a]
    u, w = un[a, j], un[a, k]; nb[u, given[a, j, k]] = w; en[u, given[a, j, k]] = e; nb[w, given[a, k, j]] = u; en[w, given[a, k, j]] = e
def meet(nr, er, xr, ns, es, xs):
    far = nr[V - B:] - (V - B); same = (far[:, :, None] == ns[:B][:, None, :]) & (far >= 0)[:, :, None]
    a, l, m = np.nonzero(same); e = er[V - B + a, l]; f = es[a, m]; p = xr[:, e]; o = xs[:, f]
    xr[:, e] = np.minimum(p, o); xs[:, f] = np.minimum(p, o)
    c = np.add.reduce((p > o).astype(np.int64), axis=0) >= 9; nr[V - B + a[c], l[c]] = -1; er[V - B + a[c], l[c]] = -1
    c = np.add.reduce((o > p).astype(np.int64), axis=0) >= 9; ns[a[c], m[c]] = -1; es[a[c], m[c]] = -1
def reference(lens, en, nb):
    fn = np.ascontiguousarray(np.stack([gentries(a) for a in nb]).astype(np.int64).reshape(N, 8, K, V).transpose(0, 1, 3, 2))
    fe = np.ascontiguousarray(np.stack([gentries(a) for a in en]).astype(np.int64).reshape(N, 8, K, V).transpose(0, 1, 3, 2))
    x = np.zeros((N, 8, 16, E), np.int64); x[..., :E0] = lens.astype(np.float32).astype(np.int64).reshape(N, 8, 16, E0)
    mid = np.full((N, 8, E), -1, np.int64); live = np.ones((N, 8, V), bool)
    for t in range(RO):
        for q in range(N):
            for g in range(8): contract(fn[q, g], fe[q, g], x[q, g], mid[q, g], live[q, g], t)
        for q in range(N):
            s = (q + 1) % N
            for g in range(8): meet(fn[q, g], fe[q, g], x[q, g], fn[s, g], fe[s, g], x[s, g])
    return {"ylen": x.reshape(N, 128, E).astype(np.float32).astype(BF), "ymid": mid.astype(np.float32),
            "yen": fe.transpose(0, 1, 3, 2).reshape(N, 8, K * V).astype(np.float32), "ynb": fn.transpose(0, 1, 3, 2).reshape(N, 8, K * V).astype(np.float32)}

@@ -1,0 +1,722 @@
+from concourse.bass import DstId, RemoteDMATransfer
+from concourse.mybir import AluOpType as AL, ActivationFunctionType as AF
+
+F, H, B, I, U = "float32", "float16", "bfloat16", "int32", "uint16"
+SB = {
+    "RAW": (2048, I), "X": (5136, B), "RT": (1040, F), "RTH": (1024, H), "TA": (1024, F), "TB": (1024, F), "FL": (1024, B), "FLS": (256, B),
+    "G1": (8192, B), "LN": (512, U), "KT": (1040, B), "HT": (1040, B), "CT": (1040, B), "UT": (1040, F), "IT": (1040, F), "GU": (1024, B),
+    "P": (1040, F), "M": (1040, F), "MT": (3088, F), "OV": (9472, B), "EQ": (1024, B), "D2": (1024, H), "T1": (1024, H), "GB": (1024, B),
+    "GC": (1024, B), "XS": (1024, B), "IDB": (1024, B), "U1J": (1024, F), "LO": (1024, B), "HI": (1024, B), "IO": (1024, F),
+    "IOB": (128, B), "ALL": (2048, B), "Y": (2304, B), "Z": (144 * 14, B), "CM": (128 * 64, B), "ONE": (512, B), "RST": (512, B),
+    "RS1": (512, B), "LUT": (2048, B), "EA": (256, U), "EB": (256, U), "MO": (256, F), "MU": (256, U), "WN": (3456, B), "GA": (1024, F), "ZZ": (1024, F),
+    "SF": (2560, F), "SI": (1024, I), "SH": (640, B), "SU": (640, U), "S16": (64, H), "W5": (512, F), "W6": (512, F), "WI": (512, I), "WJ": (512, I),
+    "WB": (512, B), "R": (512, B), "PR": (512, B), "SV": (512, B), "INW": (528, H), "NT": (512, F), "WW": (1168, F), "TG2": (128, H), "CW": (640, H), "YY": (640, F),
+    "YC": (640, H), "GI": (1280, H), "GL": (1280, B), "SRC": (1280, B), "GW": (1168, B), "G0": (128, H), "XA": (640, B), "XB": (640, B),
+    "TP": (384, B), "TR": (384, B), "EQS": (1024, B), "PRS": (1024, H), "FLG": (128, B), "NUS": (128, F), "INC": (128, H), "TG": (128, H),
+    "SW": (1152, B), "SC": (1024, B), "OH": (1024, B), "NE": (1024, H), "SND": (3072, B), "RX": (3072, B), "COL": (16, F), "COI": (16, I), "ZER": (1024, B),
+    "CF": (1024, F),
+}
+LISTS = {"a": 64, "gt": 64, "sp": 64, "go": 8, "u": 64, "cs": 32, "cw": 40, "i2": 80, "ex": 80, "lu": 80, "ov": 80, "st": 8, "sc": 64, "sx": 64, "sr": 128}
+for _k, _n in LISTS.items():
+    SB["L" + _k] = (_n, U)
+SB.update({"LM": (64, B), "SRG": (2048, B), "KP": (256, B), "SM": (3072, B), "SND": (1024, B), "O0": (128, I), "NAM": (640, B), "ZB": (1024, B)})
+ALIAS = {"WI": ("RAW", 1024), "WJ": ("RAW", 1536), "SI": ("RAW", 0), "TA": ("GA", 0), "TB": ("ZZ", 0), "GC": ("GB", 0), "EQS": ("SM", 0), "OH": ("SM", 1024),
+         "SC": ("SM", 2048), "SRG": ("SM", 0), "NE": ("PRS", 0), "CF": ("GA", 0), "YY": ("WW", 0), "NT": ("W5", 0), "GL": ("G1", 0), "SRC": ("G1", 1280),
+         "GU": ("G1", 2560), "GW": ("G1", 3584), "WB": ("G1", 4752), "R": ("G1", 5264), "PR": ("G1", 5776), "SV": ("G1", 6288)}
+SCRATCH = {k: ("sbuf", [128, n], d) for k, (n, d) in SB.items() if k not in ALIAS}
+for _b in range(8):
+    SCRATCH["pb%d" % _b] = ("psum", [128, 512], F)
+ND = 24
+SEMAPHORES = ["cv", "cs", "cp", "cg"] + ["o%d" % i for i in range(6)] + ["d%d" % i for i in range(ND)] + ["a%d" % i for i in range(12)]
+SIZE = {F: 4, H: 2, B: 2, I: 4, U: 2}
+CYC, PEC, LAT = 1.04, 0.6, 120.0
+PEN = [0.6, 50.0]
+HQ_ = [["ssssssss", "ssssssss"], [["vs"] * 8] * 2, [["vs"] * 8] * 2]
+EDGE = [2, 2, 2]
+PAIRS = [(j, k) for j in range(8) for k in range(j + 1, 8)]
+PASSES, PLAN = [12], {}
+GAT, SCA = 1.56, 3.8
+
+
+def S(n, a=0, b=None, st=1):
+    b = SB[n][0] if b is None else b
+    n, o = ALIAS.get(n, (n, 0))
+    return (n, a + o, b + o, st)
+
+
+def IND(w, o):
+    return ("ind", w, o)
+
+
+def cols(x):
+    return 16 * cols(x[2]) if x[0] == "ind" else len(range(x[1], x[2], x[3]))
+
+
+def masks(x):
+    n, a, b, st = x
+    per = 4 if n.startswith("pb") else 16 // SIZE[SB[n][1]]
+    if st == 1:
+        m = ((1 << (b - a)) - 1) << a
+    else:
+        m = 0
+        for c in range(a, b, st):
+            m |= 1 << c
+    lo, hi = a // per, (b - 1) // per
+    return n, m, ((1 << (hi - lo + 1)) - 1) << lo
+
+
+def program(ops, T, nxt, prv):
+    def ap(x):
+        if x[0] == "ind":
+            return ap(x[1]).indirect(ap(x[2]))
+        return T[x[0]][:, x[1]:x[2]] if x[3] == 1 else T[x[0]][:, x[1]:x[2]:x[3]]
+
+    def flat(xs):
+        out = []
+        for x in xs:
+            if isinstance(x, tuple):
+                out += [x[1], x[2]] if x[0] == "ind" else [x]
+        return out
+
+    def add(q, fn, rd, wr, cost, **kw):
+        r, w = flat(rd), []
+        for x in wr:
+            if x[0] == "ind":
+                w.append(x[1]); r.append(x[2])
+            else:
+                w.append(x)
+        o = dict(q=q, fn=fn, rd=[masks(x) for x in r], wr=[masks(x) for x in w], cost=cost)
+        o.update(kw); ops.append(o)
+        return o
+
+    def two(*xs):
+        return all(not x[0].startswith("pb") and SIZE[SB[x[0]][1]] == 2 for x in xs)
+
+    def fl(*xs):
+        return all(x[0] != "ind" and (x[0].startswith("pb") or SB[x[0]][1] in (F, B)) for x in xs)
+
+    def aff_ok(out, a, s1, op0, op1):
+        return fl(out, a) and not (isinstance(s1, tuple) and s1[0].startswith("pb")) and ((op0 == AL.mult and op1 in (None, AL.add)) or (op0 == AL.add and op1 is None))
+
+    def vcost(out, a, f):
+        if out[0] == "ind": return 50 + cols(out) * SCA * CYC
+        if a[0] == "ind": return 50 + cols(a) * GAT * CYC
+        return max(64, cols(out) * f) * CYC
+
+    def sc(x):
+        return ap(x) if isinstance(x, tuple) else x
+
+    def tt(out, a, b, op):
+        f = 1 if (a[0].startswith("pb") or b[0].startswith("pb")) else 2
+        add("v", lambda e: [e["v"].tensor_tensor(ap(out), ap(a), ap(b), op)], [a, b], [out], vcost(out, a, f))
+
+    def ts(out, a, s1, op0, s2=None, op1=None, flex=True):
+        flex = flex and aff_ok(out, a, s1, op0, op1)
+        if flex:
+            def fa(e):
+                if e["pick"] == "v": return fn(e)
+                if op0 == AL.add: return [e["s"].activation(ap(out), ap(a), AF.Identity, bias=sc(s1))]
+                if op1 is None: return [e["s"].activation(ap(out), ap(a), AF.Identity, scale=sc(s1))]
+                return [e["s"].activation(ap(out), ap(a), AF.Identity, bias=sc(s2), scale=sc(s1))]
+            add("vs", fa, [a, s1, s2], [out], vcost(out, a, 0.5 if two(out, a) else 1), cs=vcost(out, a, 1) + 15)
+
+        def fn(e):
+            if op1 is None: return [e["v"].tensor_scalar(ap(out), ap(a), sc(s1), None, op0)]
+            return [e["v"].tensor_scalar(ap(out), ap(a), sc(s1), sc(s2), op0, op1)]
+        if not flex:
+            add("v", fn, [a, s1, s2], [out], vcost(out, a, 0.5 if a[0] != "ind" and two(out, a) else 1))
+
+    def cp(out, a):
+        if out[0] != "ind" and fl(out, a[1] if a[0] == "ind" else a): return mv(out, a)
+        add("v", lambda e: [e["v"].tensor_copy(ap(out), ap(a))], [a], [out], vcost(out, a, 0.5 if a[0] != "ind" and out[0] != "ind" and two(out, a) else 1))
+
+    def ms(out, c):
+        add("v", lambda e: [e["v"].memset(ap(out), c)], [], [out], max(64, cols(out) * (0.5 if two(out) else 1)) * CYC)
+
+    def scan(out, d0, d1, init, op0, op1):
+        add("v", lambda e: [e["v"].tensor_tensor_scan(ap(out), ap(d0), ap(d1), init, op0, op1)], [d0, d1], [out], max(64, cols(out) * (0.5 if two(out, d0, d1) else 1)) * CYC)
+
+    def act(out, a, func, bias=0.0, scale=1.0):
+        add("s", lambda e: [e["s"].activation(ap(out), ap(a), func, bias=sc(bias), scale=sc(scale))], [a, bias, scale], [out], vcost(out, a, 1) + 15)
+
+    def mv(out, a, bias=None, q="vs"):
+        def fn(e):
+            if e["pick"] == "s":
+                if bias is None: return [e["s"].activation(ap(out), ap(a), AF.Copy)]
+                return [e["s"].activation(ap(out), ap(a), AF.Identity, bias=sc(bias))]
+            if bias is None: return [e["v"].tensor_copy(ap(out), ap(a))]
+            return [e["v"].tensor_scalar(ap(out), ap(a), sc(bias), None, AL.add)]
+        add(q, fn, [a, bias], [out], vcost(out, a, 0.5 if a[0] != "ind" and two(out, a) else 1), cs=vcost(out, a, 1) + 15)
+
+    def put(out, a):
+        add("s", lambda e: [e["s"].activation(ap(out), ap(a), AF.Silu)], [a], [out], vcost(out, a, 1) + 15)
+
+    def pe(mm, first=True, last=True, grp=None):
+        n = len(mm)
+        st = [(first if i == 0 else len(m) > 3) for i, m in enumerate(mm)]
+        sp = [(last if i == n - 1 else len(mm[i + 1]) > 3) for i in range(n)]
+        add("p", lambda e: [e["p"].matmul(ap(m[0]), ap(m[1]), ap(m[2]), st[i], sp[i]) for i, m in enumerate(mm)],
+            [m[1] for m in mm] + [m[2] for m in mm], [m[0] for m in mm], sum(max(64, cols(m[0])) for m in mm) * PEC + 60, grp=grp)
+
+    def iota(out, pat, base, cm=0):
+        kw = {} if SB[out[0]][1] == I else {"allow_small_or_imprecise_dtypes": True}
+        add("g", lambda e: [e["g"].iota(ap(out), pat, base, cm, **kw)], [], [out], 160 + 2 * cols(out) * CYC)
+
+    def asel(out, a, pat, op, fill, base, cm=1):
+        add("g", lambda e: [e["g"].affine_select(ap(out), ap(a), pat, op, float(fill), base, cm)], [a], [out], 210 + 2 * cols(out) * CYC)
+
+    def dma(q, pairs, rd, wr, lat):
+        add(q, lambda e: [e[q].dma_start(o, i) for o, i in pairs], rd, wr, 60.0 * len(pairs), dma=lat)
+
+    def pb(b, a=0, e=512, st=1):
+        return ("pb%d" % b, a, e, st)
+
+    def pool(name):
+        pos = [0]
+        def take(n):
+            a = pos[0]; pos[0] += n + (-n) % 8
+            assert pos[0] <= SB[name][0], name
+            return S(name, a, a + n)
+        return take
+    sf, si, sh, su = pool("SF"), pool("SI"), pool("SH"), pool("SU")
+
+    def sub(x, a, b, st=1):
+        return (x[0], x[1] + a, x[1] + b, st)
+    cmn, zn = {}, {}
+
+    def C(n):
+        i = cmn.setdefault(n, len(cmn)); return S("CM", 128 * i, 128 * i + 128)
+
+    def Zs(n, c=None, off=15):
+        i = zn.setdefault(n, len(zn))
+        if c is None: return S("Z", 144 * i + off, 144 * i + off + 128, 16)
+        return S("Z", 144 * i + 15 - c, 144 * i + 143 - c)
+
+    def Yc(r, c):
+        return S("Y", 144 * r + 15 - c, 144 * r + 143 - c)
+
+    def Al(r):
+        return S("ALL", 128 * r, 128 * r + 128)
+
+    def lh(z, r):
+        return Yc(0, r) if z == "c0" else Zs(z, r)
+
+    def ext(out, parts, n):
+        pe([(out, lh(z, r), sub(src, r, n, 16)) for z, src in parts for r in range(16)])
+
+    def extc(out, z, src, more=()):
+        pe([(out, lh(z, r), sub(src, 64 * r, 64 * r + 64)) for r in range(16)] + list(more))
+
+    def blk(b0, r):
+        return pb(b0 + r // 8, 64 * (r % 8), 64 * (r % 8) + 64)
+
+    def w2r(b0, parts):
+        for half in range(4):
+            mm = []
+            for r in range(4 * half, 4 * half + 4):
+                for i, (lf, rf) in enumerate(parts):
+                    mm.append((blk(b0, r), lf(r), rf(r)) + ((1,) if i == 0 else ()))
+            pe(mm)
+
+    def halves(fn):
+        for h in range(2): fn(h, 512 * h, 512 * h + 512)
+
+    nb, en = T["nb"], T["en"]
+    RAW = T["RAW"]
+    dma("y", [(RAW[:, 0:512], nb[:, :]), (RAW[:, 512:1024], en[:, :])] +
+        [(RAW[16 * g:16 * g + 16, 1024:1536], nb[16 * (g ^ 1):16 * (g ^ 1) + 16, :]) for g in range(8)], [], [S("RAW", 0, 1536)], 2500)
+    dma("s", [(RAW[16 * g:16 * g + 16, 1536:2048], en[16 * (g ^ 1):16 * (g ^ 1) + 16, :]) for g in range(8)], [], [S("RAW", 1536, 2048)], 2500)
+    dma("y", [(T["X"][:, 16:2192], T["lens"][:, :])], [], [S("X", 16, 2192)], 4000)
+    RC, HQ, M3, NTB, A64 = [S("COL", i, i + 1) for i in range(5)]
+    M8 = [S("COL", 8 + t, 9 + t) for t in range(3)]
+    ONE = S("ONE", 0, 128)
+    ms(S("ONE"), 1.0); ms(S("ZER"), 0.0)
+    o0 = S("O0", 0, 64); iota(o0, [[2, 32], [1024, 2]], 0, 64)
+    iota(S("COI", 0, 1), [[0, 1]], 0, 1)
+    iota(S("TB"), [[0, 64], [-2048, 2], [0, 8]], 1)
+    ts(S("COI", 1, 2), S("COI", 0, 1), 15, AL.bitwise_and); cp(RC, S("COI", 1, 2))
+    ts(S("COI", 2, 3), S("COI", 0, 1), 4, AL.arith_shift_right, 1, AL.bitwise_and); cp(HQ, S("COI", 2, 3))
+    ts(S("COI", 3, 4), S("COI", 0, 1), 8, AL.bitwise_and); ts(A64, S("COI", 3, 4), 8.0, AL.mult)
+    ts(M3, RC, 3.0, AL.is_equal); ts(NTB, RC, 64.0, AL.mult, float(1015 - 2 ** 23 - 2048), AL.add)
+    for t in range(3): ts(M8[t], RC, 8.0, AL.is_equal, float(4 + 20 * t), AL.mult)
+    o1 = S("O0", 64, 128); ts(o1, o0, 2047, AL.bitwise_and); o2 = su(64); ts(o2, o1, HQ, AL.add)
+
+    def aff(name, c0, al, be, src=ONE):
+        asel(C(name), src, [[-16, 8], [-al, 2], [-be, 8]], AL.is_equal, 0, -c0)
+
+    def poke(x, ch, w):
+        asel(x, x, [[-16, 8]], AL.not_equal, w, -ch)
+
+    def zmake(name, ws, off=15):
+        for ch, w in ws: poke(Zs(name, None, off), ch, w)
+    ms(S("Z"), 0.0); ms(S("Y"), 0.0)
+    aff("DUP", 0, 0, 1); aff("ID", 0, 8, 1); aff("FN0", 0, 1000, 1); aff("FN1", 1000, -1000, 1)
+    iota(S("LO"), [[0, 32], [1, 32]], 1); iota(S("HI"), [[1, 32], [0, 32]], 0)
+    asel(S("Y", 15, 2304, 16), S("ONE", 0, 144), [[-1, 16], [-16, 9]], AL.is_equal, 0, 0)
+    asel(C("BLK"), ONE, [[-16, 8], [0, 16]], AL.is_ge, 0, 0); asel(C("BLK"), C("BLK"), [[16, 8], [0, 16]], AL.is_ge, 0, 15, -1)
+    B8c = sub(C("BLK"), 0, 128, 16)
+    asel(Zs("lo8"), B8c, [[16, 8]], AL.is_ge, 0, 7, -1)
+    zmake("key", [(0, 2048), (1, 1), (2, 32)])
+    V1, VW, DGO, A1C = sf(64), S("W5"), sf(64), sf(64)
+    iota(V1, [[1, 64]], 1); ts(V1, V1, NTB, AL.add, float(-(1015 - 2 ** 23 - 2048)), AL.add)
+    INEL = sh(64)
+    t0 = sf(64); ts(t0, V1, 128.5, AL.is_lt, 16.0, AL.mult); t1 = sf(64); ts(t1, V1, 896.5, AL.is_gt, 16.0, AL.mult); tt(INEL, t0, t1, AL.add)
+    ms(S("RST"), 0.0); ms(S("RST", 0, 512, 8), 1.0e6); ms(S("RS1"), 1.0); ms(S("RS1", 0, 512, 8), 0.0)
+    for n, c in (("KT", 16.0), ("HT", 200.0), ("CT", 0.0), ("UT", 255.0), ("IT", 0.0), ("P", 204800.0), ("M", 204800.0), ("MT", -1.0), ("RT", 0.0), ("X", 0.0), ("INW", 0.0)):
+        ms(S(n, 0, 16), c)
+    tt(S("TA"), IND(S("RAW"), o2), S("TB"), AL.add)
+    add("v", lambda e: [e["v"].transpose(ap(S("TB")), ap(S("TA")))], [S("TA")], [S("TB")], 1024 * CYC)
+    act(S("FL"), S("TB"), AF.Sign)
+
+    def f0(h, a, b):
+        pe([(pb(1 + h), C("DUP"), S("FL", a, b))])
+        tt(S("RTH", a, b), pb(1 + h), S("TB", a, b), AL.mult); tt(S("RT", 16 + a, 16 + b), pb(1 + h), S("TB", a, b), AL.mult)
+        pe([(pb(4 + h), Yc(0, 1), S("LO", a, b)), (pb(4 + h), Yc(0, 2), S("HI", a, b))])
+        mv(S("IDB", a, b), pb(4 + h), M3)
+    halves(f0)
+    cp(S("FLS", 0, 128), S("FL", 896, 1024)); cp(S("FLS", 128, 256), S("FL", 0, 128))
+    iota(S("U1J"), [[1, 64], [64, 16]], 1)
+    for k in range(4):
+        asel(S("ALL", 512 * k, 512 * k + 512), S("ONE"), [[-1, 4], [-16, 8], [0, 16]], AL.is_equal, 0, -4 * k)
+    zmake("pow", [(k, 2 ** k) for k in range(8)])
+    zmake("lab", [(0, 1), (1, 8192), (2, 262144), (3, 256)]); zmake("id", [(1, 1), (2, 32)])
+    ts(C("N8K"), C("ID"), -8192.0, AL.mult); ts(C("NID"), C("ID"), -1.0, AL.mult)
+    iota(VW, [[0, 8], [16, 64]], 0); ts(VW, VW, RC, AL.add)
+    ts(S("W6"), VW, -1.0, AL.mult, 1039.0, AL.add)
+    tt(S("OH", 0, 512), S("RAW", 0, 512), VW, AL.is_gt); ts(S("SC", 0, 512), S("RAW", 512, 1024), 0.0, AL.is_lt); tt(S("INW", 16, 528), S("SC", 0, 512), S("W6"), AL.mult)
+    ts(C("I2176"), C("ID"), 2176.0, AL.mult)
+    pe([(pb(6), C("I2176"), S("OH", 0, 512)), (pb(6), C("NID"), S("INW", 16, 528))])
+    tt(S("W6"), pb(6), S("RAW", 512, 1024), AL.add)
+    EO = S("SU", 128, 640); ts(EO, S("W6"), 1040.0, AL.add)
+    EW = S("OV", 0, 5392)
+    dma("y", [(T["OV"][:, 1024 * k:1024 * k + 1024], T["ZER"][:, :]) for k in range(1, 6)], [S("ZER")], [S("OV", 1024, 6144)], 6000)
+    dma("y", [(T["X"][:, a:b], T["ZER"][:, 0:b - a]) for a, b in ((2192, 3216), (3216, 4240), (4240, 5136))], [S("ZER")], [S("X", 2192, 5136)], 5000)
+    ms(S("MO"), 15.0)
+
+    def zero_ov():
+        dma("y", [(T["OV"][:, 1024 * k:1024 * k + 1024], T["ZER"][:, :]) for k in range(8)], [S("ZER")], [S("OV", 0, 8192)], 9000)
+
+    def ends():
+        for k in range(16): cp(IND(EW, sub(EO, 32 * k, 32 * k + 32)), S("IDB", 512 * (k % 2), 512 * (k % 2) + 512))
+        for s_, L in enumerate(("EA", "EB")):
+            ext(pb(6 + s_, 0, 136), [("id", S("OV", 1040 + 2176 * s_, 3216 + 2176 * s_))], 2176)
+            ts(S(L, 0, 136), pb(6 + s_, 0, 136), 15.0, AL.add)
+        zero_ov()
+    asel(Zs("en"), B8c, [[-16, 8]], AL.is_ge, 0, -8); ts(Zs("pown"), Zs("pow"), -1.0, AL.mult)
+    asel(C("LT"), C("BLK"), [[16, 8], [1, 16]], AL.is_gt, 0, 0, -1)
+    iota(DGO, [[16, 64]], 129); ts(DGO, DGO, RC, AL.add)
+    for k in range(8): ms(sub(C("P2"), k, 128, 8), float(2 ** (11 - k)))
+    aff("SB0", 0, 1000, 0, C("P2")); aff("SB1", 1000, -1000, 0, C("P2")); aff("FB0", 4, 1000, 0); aff("FB1", 1004, -1000, 0)
+    asel(C("B8"), ONE, [[-8, 16], [0, 8]], AL.is_ge, 0, 0); asel(C("B8"), C("B8"), [[8, 16], [0, 8]], AL.is_ge, 0, 7, -1)
+    asel(C("L8"), C("B8"), [[16, 8], [1, 16]], AL.is_gt, 0, 0, -1); asel(C("L8"), C("L8"), [[-1, 128]], AL.not_equal, -16, 0)
+    made = set()
+    for i, (j, k) in enumerate(PAIRS):
+        b, d = i // 16, i % 16
+        for x, (n, src, w) in enumerate((("R%d%d" % (b, j // 2), 8 * (j % 2) + k, 8.0), ("T%d%d" % (b, k // 2), 8 * (k % 2) + j, 1.0), ("D%d" % b, d, (8 * j + k) / 128.0))):
+            if n not in made: ms(C(n), 0.0); made.add(n)
+            if x == 1: poke(sub(C(n), d, 128, 16), src, w)
+            else: ts(sub(C(n), d, 128, 16), sub(C("ID"), src, 128, 16), w, AL.mult)
+    tt(C("LW"), C("LT"), C("BLK"), AL.subtract)
+    asel(C("LS"), C("LW"), [[-1, 128]], AL.not_equal, 512, 0); asel(C("LW"), C("LW"), [[-1, 128]], AL.not_equal, 1024, 0)
+    ts(C("EN2K"), C("FN1"), 2048.0, AL.mult)
+    iota(S("IO"), [[1, 1024]], 0); cp(S("IOB"), S("IO", 0, 128))
+    cp(Zs("all"), B8c); ts(Zs("8k"), B8c, 8192.0, AL.mult)
+    zmake("es", [(6, 1), (3, 2048)]); zmake("om", [(5, 1)]); cp(Zs("l17"), Zs("lo8")); zmake("l17", [(0, 0)])
+    ms(C("D12"), 0.0); poke(sub(C("D12"), 1, 128, 16), 1, 1); poke(sub(C("D12"), 2, 128, 16), 2, 1)
+    ms(C("CV"), 0.0); ms(C("CV2"), 0.0); ms(C("KD"), 0.0); ms(C("KD2"), 0.0)
+    CV, KD = C("CV"), C("KD")
+    for ch, w, off in ((1, 1, 15), (2, 32, 15), (7, 1, 23), (8, 32, 23)): poke(sub(CV, off, off + 128, 16), ch, w)
+    for off in (15, 23): poke(sub(KD, off, off + 128, 16), 0, 1)
+    DW, DOV, DX = sf(32), sf(80), sf(64)
+    ts(DW, sub(DGO, 0, 32), 511.0, AL.add); ts(DX, DGO, -1.0, AL.mult, 2176.0, AL.add)
+    ts(sub(DOV, 0, 64), DGO, 8063.0, AL.add); ts(sub(DOV, 64, 80), sub(DGO, 0, 16), 9087.0, AL.add)
+    DS = sf(128); ts(DS, S("IO", 0, 128), 1024.0, AL.add); ts(A1C, S("IO", 0, 64), A64, AL.add, 1.0, AL.add)
+    asel(C("GE8"), C("B8"), [[-16, 8], [-1, 16]], AL.is_ge, 0, 0)
+    pe([(pb(7, 0, 1), C("P2"), S("Y", 15, 16))]); P2C = S("COL", 5, 6); cp(P2C, pb(7, 0, 1))
+    ts(S("WI", 0, 256), S("IO", 0, 256), P2C, AL.mult); ts(S("WJ", 0, 256), S("WI", 0, 256), 2048, AL.bitwise_and)
+    ts(S("KP"), S("WJ", 0, 256), 0.0, AL.is_equal); pe([(pb(7, 0, 256), C("GE8"), S("KP"))])
+    for n in range(8): ts(S("LUT", 256 * n, 256 * n + 256), pb(7, 0, 256), float(n), AL.is_gt)
+    aff("FE0", 8, 1000, 1); aff("FE1", 1008, -1000, 1); aff("DUPE", 8, 0, 1)
+    zmake("k4", [(0, 4096)]); ts(C("INT"), C("ID"), 4096.0, AL.mult)
+    for r in (0, 1, 14, 15): poke(sub(C("INT"), r, 128, 16), r, 0)
+    for h in range(2):
+        m = 320 * h; pe([(pb(6 + h, 0, 320), Yc(0, 7), S("LO", m, m + 320)), (pb(6 + h, 0, 320), Yc(0, 8), S("HI", m, m + 320))]); mv(S("NAM", m, m + 320), pb(6 + h, 0, 320))
+    ms(C("NEG"), -1.0); aff("NDUPE", 8, 0, 1, C("NEG"))
+    for s_ in range(4):
+        for ha in range(2): aff("NP%d%d" % (s_, ha), 8 * ha + 2 * s_, 1, 0, C("NEG"))
+    for ha in range(2): tt(C("SH%d" % ha), C("FN%d" % ha), C("FE%d" % ha), AL.add); ts(C("SH%d" % ha), C("SH%d" % ha), 8192.0, AL.mult)
+    ts(C("NDUPE"), C("NDUPE"), 1.0 / 8192, AL.mult)
+    for s_ in range(4): ts(C("NQ%d" % s_), C("NP%d1" % s_), 1.0 / 8192, AL.mult)
+
+    OK_, DG, M1, A1F, BF_, CH, R1, CON, TG1, TG2, RK, LB1, LB2, GG = [sf(64) for _ in range(14)]
+    MI, AI, LI, HI_, XI, NI, KI = [si(64) for _ in range(7)]
+    BB, LOB, HIB, SELF, SS, INB, RK1, CB, LP, LM = [sh(64) for _ in range(9)] + [S("LM")]
+    E = {"nxt": nxt, "prv": prv, "zero_ov": zero_ov}
+    for k, w in (("ci", 40), ("c4", 40), ("yi", 40), ("hk", 80), ("vl", 40), ("rr", 80), ("w0", 64), ("w1", 64)): E[k] = si(w)
+    for k in ("c2", "i2", "r2", "u2", "t2", "t3"): E[k] = sf(80)
+    for k in ("q0", "q1", "q2", "q3"): E[k] = sf(128)
+    A1H = S("S16")
+    AL_, GTL, SPL, GOL, UL, CSL, CWL, I2, EXL, LUL, OVL, STL, SCL, SXL, SRL = [S("L" + k) for k in LISTS]
+    RTW, XW = S("RT"), S("X")
+
+    def hop(tab, z, order, extra, t):
+        for i in range(0, 16, 2):
+            r = order[i]
+            mv(S("G1", 512 * r, 512 * r + 1024), IND(tab, S("LN", 32 * r, 32 * r + 64)), None, HQ_[t][z == "lab"][i // 2])
+            pe([(pb(0), Zs(z, x), S("G1", 512 * x, 512 * x + 512)) for x in (r, r + 1)] + (extra if i == 0 else []), i == 0, i == 14, "hop")
+
+    def fold(out, f, src, a, n):
+        pe([(out, C(f + "0"), S(src, a, a + n, 2)), (out, C(f + "1"), S(src, a + 1, a + n, 2))])
+
+    def part_a(t):
+        fold(pb(3), "FN", "RTH", 0, 1024); ts(S("LN"), pb(3), 15.0, AL.add)
+        for h in range(2):
+            a, b = 512 * h, 512 * h + 512
+            pe([(pb(1 + h), Zs("lo8", 0), S("FL", a, b)), (pb(1 + h), C("ID"), S("IDB", a, b))] + [(blk(1, r), Yc(r, 0), INEL) for r in range(8 * h, 8 * h + 8)])
+            mv(S("KT", 16 + a, 16 + b), pb(1 + h))
+        extc(pb(3, 0, 64), "lo8", S("FL"), [(pb(3, 0, 64), C("ID"), INEL)])
+        ts(DG, pb(3, 0, 64), 256.0, AL.mult); ts(TG1, DG, 8.0, AL.mult); tt(OK_, TG1, V1, AL.add)
+        hop(S("KT"), "key", list(range(16)), [], t)
+        scan(S("W5"), S("RST"), pb(0), 0.0, AL.add, AL.min)
+        tt(M1, S("W5", 7, 512, 8), OK_, AL.min); ts(MI, M1, 32768.0, AL.min); ts(AI, MI, 2047, AL.bitwise_and)
+        ts(AL_, AI, 15.0, AL.add)
+        tt(S("GB"), IND(RTW, AL_), S("U1J"), AL.is_equal)
+        ts(LI, MI, 31, AL.bitwise_and); cp(LOB, LI); ts(HI_, MI, 5, AL.arith_shift_right, 63, AL.bitwise_and); cp(HIB, HI_)
+        cp(A1H, AI); tt(SELF, AI, V1, AL.is_equal)
+        ext(pb(3, 0, 64), [("pow", S("GB"))], 1024); cp(BB, pb(3, 0, 64))
+        w2r(1, [(lambda r: Yc(r, 1), lambda r: LOB), (lambda r: Yc(r, 2), lambda r: HIB), (lambda r: Yc(r, 0), lambda r: BB)])
+        halves(lambda h, a, b: mv(S("HT", 16 + a, 16 + b), pb(1 + h), M3))
+        w2r(1, [(Al, lambda r: A1H)])
+
+        def f(h, a, b):
+            tt(S("EQ", a, b), pb(1 + h), S("RT", 16 + a, 16 + b), AL.is_equal)
+            mv(S("MT", 16 + 1024 * t + a, 16 + 1024 * t + b), pb(1 + h), -1.0)
+            pe([(pb(1 + h), C("DUP"), S("EQ", a, b))] + [(blk(1, r), Al(r), SELF) for r in range(8 * h, 8 * h + 8)])
+            tt(S("D2", a, b), pb(1 + h), S("RT", 16 + a, 16 + b), AL.mult)
+        halves(f)
+
+        hop(S("HT"), "lab", list(range(16)), [(pb(0, k, 512, 8), C("N8K"), A1H) for k in range(8)], t)
+        extc(pb(4, 0, 64), "en", S("D2")); ts(SPL, pb(4, 0, 64), 2063.0, AL.add, 4111.0, AL.min)
+        mv(S("XS"), IND(XW, SPL))
+        ts(S("W5"), pb(0), 0.0, AL.max, 4096.0, AL.min); scan(S("W6"), S("RS1"), S("W5"), 0.0, AL.mult, AL.add)
+        cp(XI, S("W6", 7, 512, 8)); ts(NI, XI, 3840, AL.bitwise_and)
+        tt(TG1, NI, DG, AL.is_equal); tt(CH, TG1, SELF, AL.mult)
+        scan(INB, S("ONE", 0, 64), CH, 0.0, AL.mult, AL.add)
+        pe([(pb(3, 0, 1), C("LT"), sub(INB, 63, 64))])
+        ts(R1, INB, pb(3, 0, 1), AL.add); ts(TG1, R1, 128.5, AL.is_lt); tt(CON, TG1, CH, AL.mult); tt(RK1, R1, CON, AL.mult)
+        ts(TG1, CON, 0.0, AL.is_equal); tt(TG2, TG1, DGO, AL.mult); tt(TG1, TG2, RK1, AL.max); cp(GTL, TG1)
+        ms(S("WW", 0, 144), 0.0); put(IND(S("WW"), GTL), S("U1J")); cp(S("TG2"), S("WW", 1, 129))
+        ext(pb(3, 0, 8), [("c0", S("TG2"))], 128); ts(GOL, pb(3, 0, 8), 15.0, AL.add)
+        cp(S("G0"), IND(RTW, GOL))
+        fold(pb(3, 0, 64), "FN", "G0", 0, 128); pe([(pb(3, 128, 256), C("DUP"), S("G0"))])
+        ts(UL, pb(3, 0, 64), 15.0, AL.add)
+        ts(TG2, CON, 16.0, AL.mult); tt(INEL, INEL, TG2, AL.add)
+        w2r(4, [(lambda r: Yc(r, 0), lambda r: RK1)])
+        halves(lambda h, a, b: mv(S("CT", 16 + a, 16 + b), pb(4 + h)))
+        mv(S("GC"), IND(S("CT"), AL_)); ext(pb(4, 0, 64), [("c0", S("GC"))], 1024)
+        cp(RK, pb(4, 0, 64)); ts(CB, RK, 0.0, AL.is_gt); tt(GG, CB, SELF, AL.is_gt)
+        ts(LB1, RK, -200.0, AL.add); tt(LB2, LB1, GG, AL.mult); ts(LP, LB2, 200.0, AL.add, 1024.0, AL.mult)
+        ts(LB1, RK, -1.0, AL.mult, -200.0, AL.add); tt(LB2, LB1, GG, AL.mult); ts(LM, LB2, 200.0, AL.add, 1024.0, AL.mult)
+        for b0, tab, lab in ((4, "P", LP), (4, "M", LM)):
+            w2r(b0, [(lambda r: C("ID"), lambda r: S("XS", r, 1024, 16)), (Al, lambda r, lab=lab: lab)])
+            halves(lambda h, a, b, b0=b0, tab=tab: mv(S(tab, 16 + a, 16 + b), pb(b0 + h)))
+        w2r(4, [(Al, lambda r: CB)])
+        halves(lambda h, a, b: tt(S("T1", a, b), pb(4 + h), S("D2", a, b), AL.mult))
+
+    def part_b(t):
+        for h in range(2):
+            a, b = 512 * h, 512 * h + 512
+            pe([(pb(1 + h), C("ID"), S("IDB", a, b)), (pb(1 + h), Zs("pown", 5), S("EQ", a, b)), (pb(1 + h), Zs("en", 6), S("D2", a, b))] +
+               [(pb(1 + h, x, x + 384), Zs(z, c), S("FL", a + x, a + x + 384)) for x in (128 - 128 * h,) for z, c in (("lo8", 4), ("pow", 5))], True, False, "ut%d" % h)
+        if t:
+            pe([(pb(7), C("INT"), S("ONE"))] + [(pb(7), Zs("k4", r), S("SRG", 512 * i, 512 * i + 512)) for i, r in enumerate((14, 15, 0, 1))])
+            tt(S("W6"), pb(7), S("W5"), AL.min); scan(S("WW", 0, 512), S("RS1"), S("W6"), 0.0, AL.mult, AL.add); cp(XI, S("WW", 7, 512, 8))
+        ts(KI, XI, 255, AL.bitwise_and); tt(SS, KI, BB, AL.add)
+        for h in range(2):
+            pe([(pb(1 + h, 384 * h, 384 * h + 128), Zs(z, c), S("FLS", 128 - 128 * h, 256 - 128 * h)) for z, c in (("lo8", 4), ("pow", 5))] +
+               [(blk(1, r), Yc(r, 0), SS) for r in range(8 * h, 8 * h + 8)], False, True, "ut%d" % h)
+            mv(S("UT", 16 + 512 * h, 528 + 512 * h), pb(1 + h))
+        n = 2176 + 640 * t; nch = -(-n // 512); w = -(-n // (32 * nch)) * 32
+        for i, a in enumerate(range(0, n, w)):
+            b = min(n, a + w); k = i % 2; ga, zz = S("GA", 512 * k, 512 * k + b - a), S("ZZ", 512 * k, 512 * k + b - a)
+            act(ga, IND(S("P"), S("EA", a // 16, b // 16)), AF.Copy)
+            tt(zz, IND(S("M"), S("EB", a // 16, b // 16)), ga, AL.add)
+            z, x = pb(4 + k, 0, b - a), S("X", 16 + a, 16 + b)
+            if i % EDGE[t] == 0:
+                act(z, zz, AF.Abs); tt(S("WN", a, b), z, x, AL.is_lt); tt(x, z, x, AL.min)
+            else:
+                zb = S("ZB", 512 * k, 512 * k + b - a); act(zb, zz, AF.Abs)
+                pe([(z, C("ID"), x), (z, C("NID"), zb)]); act(zb, z, AF.Relu)
+                ts(S("WN", a, b), zb, 0.0, AL.is_gt); pe([(z, C("ID"), x), (z, C("NID"), zb)]); mv(x, z)
+        q = n // 16; cnt = pb(4, 0, q); ext(cnt, [("all", S("WN"))], n)
+        f, d = S("CF", 0, q), S("CF", 256, 256 + q)
+        ts(f, cnt, 8.5, AL.is_gt); ts(d, S("EA", 0, q), float(1024 * t), AL.add); tt(S("CF", 512, 512 + q), d, S("MO", 0, q), AL.subtract)
+        tt(d, S("CF", 512, 512 + q), f, AL.mult); tt(S("MO", 0, q), S("MO", 0, q), d, AL.add)
+        cp(S("GU"), IND(S("UT"), UL)); act(S("IT", 16, 1040), IND(S("UT"), UL), AF.Copy)
+        J = lambda x, jj: sub(x, 128 * jj, 128 * jj + 128)
+        gu = lambda jj, h: S("GU", 2 * jj + h, 1024, 8)
+        pe([(J(pb(0), jj), C("SB%d" % h), gu(jj, h)) + ((1,) if h == 0 else ()) for jj in range(4) for h in range(2)])
+        cp(S("WI"), pb(0)); ts(S("WJ"), S("WI"), 2048, AL.bitwise_and)
+        for jj in range(4): tt(J(S("WB"), jj), pb(3, 128, 256), J(S("WJ"), jj), AL.is_gt)
+        pe([m for jj in range(4) for m in [(J(pb(0), jj), C("FB0"), gu(jj, 0), 1), (J(pb(0), jj), C("FB1"), gu(jj, 1)), (J(pb(0), jj), C("L8"), J(S("WB"), jj))]])
+        act(S("R"), pb(0), AF.Relu, -7.0 / 8192, -1.0 / 8192)
+        tr = lambda n, p, b: [(J(p, b), C("%s%d%d" % (n, b, x)), J(S("R"), x)) for x in sorted(set(PAIRS[i][n == "T"] // 2 for i in range(16 * b, min(28, 16 * b + 16))))]
+        grp = lambda l: [m + ((1,) if i == 0 else ()) for i, m in enumerate(l)]
+        pe(grp(tr("R", pb(0), 0)) + grp(tr("R", pb(0), 1))); pe(grp(tr("T", pb(3), 0)) + grp(tr("T", pb(3), 1)))
+        mv(S("WB", 0, 256), pb(0, 0, 256)); tt(S("PR", 0, 256), pb(3, 0, 256), S("WB", 0, 256), AL.mult)
+        for b in range(2): ts(S("SV", b, 256, 2), J(S("PR"), b), 0.0, AL.is_gt)
+        pe([(pb(3, 0, 256), C("BLK"), S("SV", 0, 256))]); scan(S("INW", 16, 272), S("ONE", 0, 256), pb(3, 0, 256), 0.0, AL.mult, AL.add)
+        ext(pb(3, 0, 16), [("c0", S("INW", 15, 271))], 256); ext(pb(3, 16, 32), [("c0", S("INW", 16, 272))], 256)
+        for b in range(2):
+            p = J(pb(0), b)
+            pe([(p, C("ID"), J(S("WB"), b)), (p, C("D%d" % b), ONE)] + tr("T", pb(0), b) + [(p, C("LW"), S("SV", b, 256, 2)), (p, C("ID"), S("INW", 16 + b, 272, 2))])
+        for b in range(2): act(S("NT", b, 256, 2), J(pb(0), b), AF.Identity, -1025.0 - 2057.0 / 8192)
+        ts(sub(TG1, 0, 32), pb(3, 0, 32), 640.0, AL.min); s0, e0, z0, z1 = sub(TG1, 0, 16), sub(TG1, 16, 32), sub(TG2, 0, 16), sub(TG2, 16, 32)
+        tt(z0, s0, e0, AL.is_equal); tt(z1, z0, sub(DW, 0, 16), AL.mult); tt(z0, z1, s0, AL.max); cp(sub(CSL, 0, 16), z0)
+        iota(S("WW", 0, 640), [[0, 640]], 0); put(IND(S("WW"), sub(CSL, 0, 16)), S("IO", 32, 288))
+        scan(S("CW"), S("WW", 0, 640), S("WW", 0, 640), 0.0, AL.max, AL.max)
+        ext(pb(3, 0, 40), [("c0", S("CW"))], 640); ts(CWL, pb(3, 0, 40), -32.0, AL.add)
+        tt(S("YC"), IND(S("NT", 0, 256), CWL), S("IO", 0, 640), AL.subtract); ts(S("YC"), S("YC"), -0.5, AL.max, 0.5, AL.min)
+        ci, c4, yi, hk, vl, rr = E["ci"], E["c4"], E["yi"], E["hk"], E["vl"], E["rr"]
+        c2, i2, r2, u2, t2, t3 = E["c2"], E["i2"], E["r2"], E["u2"], E["t2"], E["t3"]
+        lo, hi = (lambda x: sub(x, 0, 40)), (lambda x: sub(x, 40, 80))
+        ts(ci, pb(3, 0, 40), -32.0, AL.add); ts(c4, ci, 254, AL.bitwise_and); ts(lo(c2), c4, 4.0, AL.mult, -3.0, AL.add); ts(hi(c2), c4, 4.0, AL.mult, 1.0, AL.add)
+        ext(pb(3, 64, 104), [("8k", S("YC"))], 640); ts(yi, pb(3, 64, 104), 65536.0, AL.add)
+        ts(lo(hk), yi, 9, AL.arith_shift_right, 15, AL.bitwise_and); ts(hi(hk), yi, 6, AL.arith_shift_right, 7, AL.bitwise_and)
+        ts(vl, lo(hk), 0.0, AL.is_gt)
+        tt(t2, hk, c2, AL.add); tt(lo(i2), lo(t2), vl, AL.mult); tt(hi(i2), hi(t2), vl, AL.mult); ts(I2, i2, 15.0, AL.add)
+        ts(lo(rr), yi, 3, AL.arith_shift_right, 7, AL.bitwise_and); ts(hi(rr), yi, 7, AL.bitwise_and); ts(r2, rr, 256.0, AL.mult)
+        hs = ((lo, 0, 3), (hi, 640, 0))
+        for f_, a, b in hs:
+            cp(S("GI", a, a + 640), IND(S("IT"), f_(I2)))
+            ext(pb(b, 0, 40), [("om", S("GI", a, a + 640))], 640); tt(f_(t3), pb(b, 0, 40), f_(r2), AL.add); cp(f_(LUL), f_(t3))
+            mv(S("GL", a, a + 640), IND(S("LUT"), f_(LUL)))
+            ext(pb(b, 64, 104), [("id", S("GI", a, a + 640))], 640); cp(f_(u2), pb(b, 64, 104))
+            ts(f_(t2), f_(u2), 0.0, AL.is_equal); tt(f_(t3), f_(t2), f_(DOV), AL.mult)
+        for i in range(4):
+            a, m = 320 * i, 320 * (i % 2); o = (a + 640) % 1280; p = pb(1 + i % 2, 0, 320)
+            pe([(p, C("ID"), S("NAM", m, m + 320)), (p, C("D12"), S("GI", o, o + 320))])
+            mv(S("SRC", a, a + 320), p, M8[t])
+        for f_, a, b in hs:
+            ext(pb(b, 0, 40), [("l17", S("GL", a, a + 640))], 640); ts(f_(t2), pb(b, 0, 40), 1024.0, AL.mult, -1.0, AL.add, False)
+            tt(f_(i2), f_(t2), f_(u2), AL.add); tt(f_(t2), f_(i2), f_(t3), AL.max); cp(f_(OVL), f_(t2))
+            cp(IND(S("OV"), f_(OVL)), S("SRC", a, a + 640))
+        ext(pb(0, 128, 208), [("es", S("GI"))], 1280); ts(EXL, pb(0, 128, 208), 15.0, AL.add)
+        c0 = 136 + 40 * t
+        ts(S("EA", c0, c0 + 40), lo(u2), 15.0, AL.add); ts(S("EB", c0, c0 + 40), hi(u2), 15.0, AL.add)
+        ts(lo(r2), vl, float(1024 * t), AL.mult, 15.0, AL.add); tt(S("MO", c0, c0 + 40), lo(r2), lo(u2), AL.add)
+        mv(S("XA"), IND(XW, lo(EXL))); tt(S("XB"), IND(XW, hi(EXL)), S("XA"), AL.add); ts(S("X", 16 + n, 656 + n), S("XB"), 255.0, AL.min)
+        for bk, a, b in ((6, 896, 1024), (7, 0, 128), (1, 128, 512), (2, 512, 896)):
+            p = pb(bk, 0, b - a)
+            pe([(p, C("ID"), S("RTH", a, b)), (p, C("NID"), S("T1", a, b))], True, False)
+            pe([(p, sub(C("CV"), 15 - l, 143 - l), S("OV", 1024 * l + a, 1024 * l + b)) for l in range(8)], False, True)
+            cp(S("RTH", a, b), p); act(S("FL", a, b), p, AF.Sign); mv(S("RT", 16 + a, 16 + b), p)
+        if t < 2: E["zero_ov"]()
+
+    def swap(src, dst, w, k):
+        def fn(e):
+            trs = [RemoteDMATransfer(dst_ids=[DstId(rid=to[0], pnc=to[1])], dma_engine_mask=to[2], remote_sem=T.sem["a%d" % (k + i)],
+                                     src=T[src[0]][:, src[1] + w * i:src[1] + w * i + w], dst=T[dst[0]][:, dst[1] + w * (1 - i):dst[1] + w * (2 - i)])
+                   for i, to in enumerate((E["nxt"], E["prv"]))]
+            return [e["g"].remote_dma_fused(trs, local_sem=T.sem["o%d" % (k // 2)])]
+        o = add("g", fn, [src], [], 300.0, send=("o%d" % (k // 2), E["nxt"][3] + E["prv"][3]))
+        add("x", None, [], [sub(dst, w, 2 * w)], 3000.0 + 6 * w, after=o, sem=("a%d" % k, E["prv"][4]))
+        add("x", None, [], [sub(dst, 0, w)], 3000.0 + 6 * w, after=o, sem=("a%d" % (k + 1), E["nxt"][4]))
+
+    def part_c(t):
+        TP, TR = S("TP", 128 * t, 128 * t + 128), S("TR", 128 * t, 128 * t + 128)
+        SND, RX = S("SND"), S("RX", 1024 * t, 1024 * t + 1024)
+        q0, q1, q2, q3 = E["q0"], E["q1"], E["q2"], E["q3"]
+        h0, h1 = (lambda x: sub(x, 0, 64)), (lambda x: sub(x, 64, 128))
+        base = (896, 0)
+        for s_ in range(2):
+            pe([(pb(6, 64 * s_, 64 * s_ + 64), C("FN%d" % ha), S("RTH", base[s_] + 64 * ha, base[s_] + 64 * ha + 64)) for ha in range(2)])
+        ts(h0(q0), pb(6, 0, 64), -896.0, AL.add, 0.0, AL.max); tt(h0(q1), h0(q0), A1C, AL.is_gt); tt(h0(TP), h0(q0), h0(q1), AL.mult)
+        ts(h1(q0), pb(6, 64, 128), 0.0, AL.is_equal, 200.0, AL.mult); ts(h1(q1), pb(6, 64, 128), 200.0, AL.min); tt(h1(TP), h1(q0), h1(q1), AL.max)
+        swap(TP, TR, 64, 4 * t)
+        for s_ in range(2):
+            fold(pb(6 + s_, 0, 64), "FE", "RTH", base[s_], 128); ts(sub(SRL, 64 * s_, 64 * s_ + 64), pb(6 + s_, 0, 64), 2063.0, AL.add)
+        for s_ in range(2):
+            rr_, rs_ = (h0(TP), h0(TR)) if s_ == 0 else (h1(TR), h1(TP))
+            bl = lambda s, ha: pb(6 + s_, 128 * s + 64 * ha, 128 * s + 64 * ha + 64)
+            two_ = [[(bl(s, ha), C(("DUP", "DUPE")[ha]), rr_) for s in range(4) for ha in range(2)], [(bl(s, ha), C("NP%d%d" % (s, ha)), rs_) for s in range(4) for ha in range(2)]]
+            pe([(pb(6 + s_), C("ID"), S("ZER", 0, 512))] + two_[s_] +
+               [(bl(s, ha), C("NDUPE" if s_ == 0 else "NQ%d" % s), S("RTH", base[s_] + 64 * ha, base[s_] + 64 * ha + 64)) for s in range(4) for ha in range(2)], True, False)
+            pe(two_[1 - s_], False, True)
+            ts(S("PRS", 512 * s_, 512 * s_ + 512), pb(6 + s_), -0.5, AL.max, 0.5, AL.min)
+        for s_ in range(2):
+            pe([(pb(6, 64 * s_, 64 * s_ + 64), C("SH%d" % ha), S("PRS", 512 * s_ + 128 * s + 64 * ha, 512 * s_ + 128 * s + 64 * ha + 64)) for s in range(4) for ha in range(2)])
+        ts(S("WI", 0, 128), pb(6, 0, 128), 32768.0, AL.add); ts(S("WJ", 0, 128), S("WI", 0, 128), 8191, AL.bitwise_and)
+        ts(S("FLG"), S("WJ", 0, 128), 0.0, AL.is_gt); ts(q3, S("WJ", 0, 128), 1.0 / 8192, AL.mult, -513.5, AL.add)
+        pc = pb(6, 0, 128); pe([(pc, C("BLK"), S("FLG"))])
+        for s_ in range(2): scan(S("INC", 64 * s_, 64 * s_ + 64), S("ONE", 0, 64), sub(pc, 64 * s_, 64 * s_ + 64), 512.0 * s_, AL.mult, AL.add)
+        tt(q0, S("INC"), pc, AL.subtract); ts(q1, pc, 0.0, AL.is_equal); tt(q2, q1, DS, AL.mult); tt(S("TG"), q0, q2, AL.max)
+        pe([(pb(7, 0, 128), C("LS"), S("FLG")), (pb(7, 0, 128), C("ID"), S("INC"))]); tt(S("NUS"), pb(7, 0, 128), q3, AL.add)
+        ext(pb(6, 0, 8), [("c0", S("TG"))], 128); cp(STL, pb(6, 0, 8))
+        iota(S("SW", 0, 1024), [[0, 1024]], 0); cp(IND(S("SW"), STL), S("IOB"))
+        scan(S("SC"), S("SW", 0, 1024), S("SW", 0, 1024), 0.0, AL.max, AL.max)
+        ext(pb(6, 0, 64), [("c0", S("SC"))], 1024); cp(SCL, pb(6, 0, 64))
+        tt(S("NE"), IND(S("NUS"), SCL), S("IO"), AL.subtract); ts(S("NE"), S("NE"), -0.5, AL.max, 0.5, AL.min)
+        ext(pb(7, 0, 64), [("8k", S("NE"))], 1024)
+        w0, w1 = E["w0"], E["w1"]; ts(w0, pb(7, 0, 64), 65536.0, AL.add); ts(w1, w0, 8191, AL.bitwise_and)
+        ts(h0(q0), w1, 0.0, AL.is_equal); tt(h0(q1), h0(q0), DX, AL.mult); tt(h0(q2), w1, h0(q1), AL.add); ts(SXL, h0(q2), -1.0, AL.mult, 6159.0, AL.add)
+        mv(SND, IND(XW, SXL))
+        swap(SND, RX, 512, 4 * t + 2)
+        GT, SG, MN, GX = S("EQS"), S("OH"), S("SC"), S("SRG")
+
+        def f(h, a, b):
+            pe([(pb(6 + h), C("ID"), sub(RX, a, b))])
+            tt(sub(GT, a, b), pb(6 + h), sub(SND, a, b), AL.is_lt); tt(sub(MN, a, b), pb(6 + h), sub(SND, a, b), AL.min)
+            pe([(pb(6 + h), C("BLK"), sub(GT, a, b))]); act(sub(SG, a, b), pb(6 + h), AF.Sign, 8.5, -1.0)
+            tt(IND(XW, sub(SXL, 32 * h, 32 * h + 32)), sub(MN, a, b), sub(SG, a, b), AL.mult)
+        halves(f)
+        for h in range(2): mv(sub(GX, 1024 * h, 1024 * h + 1024), IND(XW, sub(SRL, 64 * h, 64 * h + 64)))
+        pe([(pb(6, 0, 256), sub(C("KD"), 15 - l, 143 - l), sub(GX, l, 2048, 8)) for l in range(8)])
+        KP = S("KP"); ts(KP, pb(6, 0, 256), 0.0, AL.is_gt)
+        for s_ in range(2):
+            k_, a = sub(KP, 128 * s_, 128 * s_ + 128), base[s_]
+            tt(S("RTH", a, a + 128), S("RTH", a, a + 128), k_, AL.mult)
+            if t < 2: tt(S("RT", 16 + a, 144 + a), S("RT", 16 + a, 144 + a), k_, AL.mult)
+            tt(S("FLS", 128 * s_, 128 * s_ + 128), S("FL", a, a + 128), k_, AL.mult)
+
+    part_a(0)
+    ends()
+    for t in range(3):
+        part_b(t)
+        if t < 2: part_a(t + 1)
+        if t == 2:
+            cp(S("MU"), S("MO"))
+            for k, n in enumerate(("P", "M", "UT", "IT")):
+                mv(S(n, 16, 1040), IND(S("MT"), S("MU", 64 * k, 64 * k + 64)))
+                dma("y", [(T["ymid"][:, 1024 * k:1024 * k + 1024], T[n][0:128:16, 16:1040])], [S(n, 16, 1040)], [], 2500)
+        part_c(t)
+    for k in range(4):
+        a, b = 1024 * k, 1024 * k + 1024
+        act(S("G1", a, b), S("X", 16 + a, 16 + b), AF.Abs)
+        dma("y", [(T["ylen"][:, a:b], T["G1"][:, a:b])], [S("G1", a, b)], [], 3500)
+    for h in range(2):
+        a, b = 512 * h, 512 * h + 512
+        pcs = [(0, 128, S("FLS", 128, 256)), (128, 512, S("FL", 128, 512))] if h == 0 else [(0, 384, S("FL", 512, 896)), (384, 512, S("FLS", 0, 128))]
+        pe([(pb(1 + h), C("ID"), S("RTH", a, b))] + [(pb(1 + h, x, y), C("EN2K"), s_) for x, y, s_ in pcs])
+        ts(S("TA", a, b), pb(1 + h), -1.0, AL.add)
+    dma("y", [(T["ynb"][g, :], T["GA"][16 * g:16 * g + 8, :]) for g in range(8)], [S("TA")], [], 2500)
+    dma("s", [(T["yen"][g, :], T["GA"][16 * g + 8:16 * g + 16, :]) for g in range(8)], [S("TA")], [], 2500)
+
+
+def emit(ops, g, T):
+    n = len(ops); last = {}; grp = {}
+    for i, o in enumerate(ops):
+        deps, order = set(), set()
+        dm = "dma" in o or o["q"] == "x" or "send" in o
+        for kind, accs in (("r", o["rd"]), ("w", o["wr"])):
+            for name, m, bm in accs:
+                ps = name.startswith("pb")
+                for j, k2, m2, bm2 in last.get(name, []):
+                    if j == i: continue
+                    p = ops[j]
+                    if ps and (p["q"] != o["q"] or o["q"] == "vs"): hit = True
+                    elif kind == "r" and k2 == "r": hit = False
+                    elif ps and o["q"] == "p": hit = True
+                    elif dm or "dma" in p or p["q"] == "x": hit = bool(bm & bm2)
+                    else: hit = bool(m & m2)
+                    if hit:
+                        (order if (o["q"] == "p" and p["q"] == "p") else deps).add(j)
+        for kind, accs in (("r", o["rd"]), ("w", o["wr"])):
+            for name, m, bm in accs:
+                l = last.setdefault(name, [])
+                if kind == "w" and not name.startswith("pb"): l[:] = [x for x in l if x[2] & ~m or x[0] == i]
+                if name.startswith("pb"): l[:] = [x for x in l if x[0] == i or (o["q"] != "p" and ops[x[0]]["q"] in ("p", o["q"]))]
+                l.append((i, kind, m, bm))
+        if "after" in o: order.add([k for k in range(i) if ops[k] is o["after"]][0])
+        o["deps"], o["order"] = deps, order
+    succ = [[] for _ in ops]
+    for i, o in enumerate(ops):
+        for j in o["deps"] | o["order"]: succ[j].append(i)
+    pri = [0.0] * n
+    for i in range(n - 1, -1, -1):
+        pri[i] = ops[i]["cost"] + ops[i].get("dma", 0) + LAT + max([pri[k] for k in succ[i]] or [0.0])
+    fw = [[(j, LAT + ops[j].get("dma", 0)) for j in o["deps"]] + [(j, ops[j].get("dma", 0)) for j in o["order"]] for o in ops]
+    bw = [[] for _ in ops]
+    for i in range(n):
+        for j, lag in fw[i]: bw[j].append((i, lag))
+
+    def place(order, pre, back):
+        busy = {q: [] for q in "vspgyx"}; res = [None] * n
+        for i in order:
+            o = ops[i]; best = None
+            rdy = max([res[j][1] + lag for j, lag in pre[i]] + [o.get("dma", 0.0) if back else 0.0])
+            for q in o["q"]:
+                c = o.get("cs", o["cost"]) if q == "s" else o["cost"]
+                st, l = rdy, busy[q]
+                lo, hi = 0, len(l)
+                while lo < hi:
+                    mid = (lo + hi) // 2
+                    if l[mid][1] <= st: lo = mid + 1
+                    else: hi = mid
+                while q != "x" and lo < len(l) and l[lo][0] < st + c:
+                    st = max(st, l[lo][1]); lo += 1
+                key = st + c + (PEN[0] * c + PEN[1] if q == "v" else 0.0)
+                if best is None or key < best[0]: best = (key, q, st, c, lo)
+            _, q, st, c, lo = best
+            if q != "x": busy[q].insert(lo, (st, st + c))
+            res[i] = (st, st + c, q)
+        return res
+    if n not in PLAN:
+        res = place(sorted(range(n), key=lambda i: (-pri[i], i)), fw, False); top = None
+        for _ in range(PASSES[0]):
+            span = max(res[i][1] + ops[i].get("dma", 0) for i in range(n))
+            if top is None or span < top[0]: top = (span, res)
+            rb = place(sorted(range(n), key=lambda i: (-res[i][1], -i)), bw, True)
+            res = place(sorted(range(n), key=lambda i: (-rb[i][1], i)), fw, False)
+        PLAN[n] = top[1]
+    end = [0.0] * n
+    for i, o in enumerate(ops):
+        o["st"], o["pick"] = PLAN[n][i][0], PLAN[n][i][2]; o["cost"] = PLAN[n][i][1] - o["st"]; end[i] = PLAN[n][i][1] + o.get("dma", 0)
+    seq = sorted(range(n), key=lambda i: (ops[i]["st"], i))
+    e = {"v": g.vector, "s": g.scalar, "p": g.tensor, "g": g, "y": g.sync}
+    cnt = {}; know = {q: {} for q in e}; nd = [0]
+    for i in seq:
+        o = ops[i]; q = o["pick"]
+        if q == "x":
+            o["sig"], o["know"] = o["sem"], {}; cnt[o["sem"][0]] = o["sem"][1]
+            continue
+        kn = know[q]; need = {}
+        for j in o["deps"]:
+            s_, v = ops[j]["sig"]; need[s_] = max(need.get(s_, (0, j)), (v, j))
+        for s_, (v, j) in sorted(need.items(), key=lambda x: -end[x[1][1]]):
+            if kn.get(s_, 0) < v:
+                e[q].wait_ge(T.sem[s_], v); kn[s_] = v
+                for a, b in ops[j]["know"].items(): kn[a] = max(kn.get(a, 0), b)
+        o["know"] = dict(kn); e["pick"] = q
+        ins = o["fn"](e)
+        if "send" in o:
+            cnt[o["send"][0]] = o["send"][1]; o["sig"] = o["send"]
+            continue
+        if "dma" in o:
+            s_, inc = "d%d" % nd[0], 16; nd[0] += 1
+        else:
+            s_, inc = "c" + q, 1; ins = ins[-1:]
+        for x in ins:
+            x.then_inc(T.sem[s_], inc); cnt[s_] = cnt.get(s_, 0) + inc
+        o["sig"] = (s_, cnt[s_])
+    for s_, v in cnt.items(): g.wait_ge(T.sem[s_], v)
+    return max(end), {q: sum(o["cost"] for o in ops if o["pick"] == q) for q in "vspg"}
+
+
+INFO = []
+
+
+def rank_program(g, core, T, topo):
+    rank = T.rank_of(core)
+    if rank is None:
+        return
+    n = len(T.cores)
+
+    def peer(to, half):
+        eng = topo.engines(core, to); back = topo.engines(to, core)
+        eng = eng[:len(eng) // 2] if half == 0 else eng[len(eng) // 2:]
+        rid, pid, _ = topo.addr(to)
+        return (rid, pid, sum(1 << x for x in eng), len(eng), len(back) // 2)
+    ops = []
+    program(ops, T, peer(T.cores[(rank + 1) % n], 0), peer(T.cores[(rank - 1) % n], 1))
+    INFO.append((emit(ops, g, T), ops))

@@ -1,3 +1,4 @@
+import numpy as np
 from concourse.bass import DstId, RemoteDMATransfer
 from concourse.mybir import AluOpType as AL, ActivationFunctionType as AF
 
@@ -10,8 +11,8 @@ SB = {
     "IOB": (128, B), "ALL": (2048, B), "Y": (2304, B), "Z": (144 * 14, B), "CM": (128 * 64, B), "ONE": (512, B), "RST": (512, B),
     "RS1": (512, B), "LUT": (2048, B), "EA": (256, U), "EB": (256, U), "MO": (256, F), "MU": (256, U), "WN": (3456, B), "GA": (1024, F), "ZZ": (1024, F),
     "SF": (2560, F), "SI": (1024, I), "SH": (640, B), "SU": (640, U), "S16": (64, H), "W5": (512, F), "W6": (512, F), "WI": (512, I), "WJ": (512, I),
-    "WB": (512, B), "R": (512, B), "PR": (512, B), "SV": (512, B), "INW": (528, H), "NT": (512, F), "WW": (1168, F), "TG2": (128, H), "CW": (640, H), "YY": (640, F),
-    "YC": (640, H), "GI": (1280, H), "GL": (1280, B), "SRC": (1280, B), "GW": (1168, B), "G0": (128, H), "XA": (640, B), "XB": (640, B),
+    "WB": (512, B), "R": (512, B), "PR": (512, B), "SV": (512, B), "INW": (528, H), "NT": (512, F), "WW": (2568, F), "TG2": (128, H), "CW": (640, H), "YY": (640, F),
+    "YC": (640, H), "GI": (1280, H), "GL": (1280, B), "SRC": (1280, B), "GW": (1168, B), "G0": (128, H), "XB": (640, B),
     "TP": (384, B), "TR": (384, B), "EQS": (1024, B), "PRS": (1024, H), "FLG": (128, B), "NUS": (128, F), "INC": (128, H), "TG": (128, H),
     "SW": (1152, B), "SC": (1024, B), "OH": (1024, B), "NE": (1024, H), "SND": (3072, B), "RX": (3072, B), "COL": (16, F), "COI": (16, I), "ZER": (1024, B),
     "CF": (1024, F),
@@ -19,7 +20,7 @@ SB = {
 LISTS = {"a": 64, "gt": 64, "sp": 64, "go": 8, "u": 64, "cs": 32, "cw": 40, "i2": 80, "ex": 80, "lu": 80, "ov": 80, "st": 8, "sc": 64, "sx": 64, "sr": 128}
 for _k, _n in LISTS.items():
     SB["L" + _k] = (_n, U)
-SB.update({"LM": (64, B), "SRG": (2048, B), "KP": (256, B), "SM": (3072, B), "SND": (1024, B), "O0": (128, I), "NAM": (640, B), "ZB": (1024, B)})
+SB.update({"LM": (64, B), "SRG": (2048, B), "KP": (256, B), "SM": (3072, B), "SND": (1024, B), "O0": (128, I), "NAM": (640, B), "ZB": (1024, B), "V7": (64, F), "R2": (80, B), "UM": (160, F)})
 ALIAS = {"WI": ("RAW", 1024), "WJ": ("RAW", 1536), "SI": ("RAW", 0), "TA": ("GA", 0), "TB": ("ZZ", 0), "GC": ("GB", 0), "EQS": ("SM", 0), "OH": ("SM", 1024),
          "SC": ("SM", 2048), "SRG": ("SM", 0), "NE": ("PRS", 0), "CF": ("GA", 0), "YY": ("WW", 0), "NT": ("W5", 0), "GL": ("G1", 0), "SRC": ("G1", 1280),
          "GU": ("G1", 2560), "GW": ("G1", 3584), "WB": ("G1", 4752), "R": ("G1", 5264), "PR": ("G1", 5776), "SV": ("G1", 6288)}
@@ -29,13 +30,16 @@ for _b in range(8):
 ND = 24
 SEMAPHORES = ["cv", "cs", "cp", "cg"] + ["o%d" % i for i in range(6)] + ["d%d" % i for i in range(ND)] + ["a%d" % i for i in range(12)]
 SIZE = {F: 4, H: 2, B: 2, I: 4, U: 2}
-CYC, PEC, LAT = 1.04, 0.6, 120.0
+CYC, PEC, LAT = 0.95, 0.48, 120.0
 PEN = [0.6, 50.0]
 HQ_ = [["ssssssss", "ssssssss"], [["vs"] * 8] * 2, [["vs"] * 8] * 2]
 EDGE = [2, 2, 2]
 PAIRS = [(j, k) for j in range(8) for k in range(j + 1, 8)]
-PASSES, PLAN = [12], {}
-GAT, SCA = 1.56, 3.8
+PASSES, PLAN, SEED, TEMP = [2000], {}, [1], [1000.0]
+GUESS = [({"o": 1, "g": 1, "s": 1, "p": 1, "x": 1.2}, 130.0, 2.0), ({"o": 1, "g": 0.75, "s": 0.55, "p": 1, "x": 1.2}, 130.0, 1.0),
+         ({"o": 1, "g": 1.3, "s": 1.55, "p": 1, "x": 1}, 100.0, 1.0), ({"o": 1, "g": 1.25, "s": 0.7, "p": 1.3, "x": 1.6}, 200.0, 1.0)]
+BIAS = {"ends": 0.0, "pm": 0.0, "edge": 0.0, "seam": 0.0}
+GAT, SCA = 1.5, 3.5
 
 
 def S(n, a=0, b=None, st=1):
@@ -71,6 +75,8 @@ def program(ops, T, nxt, prv):
             return ap(x[1]).indirect(ap(x[2]))
         return T[x[0]][:, x[1]:x[2]] if x[3] == 1 else T[x[0]][:, x[1]:x[2]:x[3]]
 
+    tag = [""]
+
     def flat(xs):
         out = []
         for x in xs:
@@ -85,7 +91,8 @@ def program(ops, T, nxt, prv):
                 w.append(x[1]); r.append(x[2])
             else:
                 w.append(x)
-        o = dict(q=q, fn=fn, rd=[masks(x) for x in r], wr=[masks(x) for x in w], cost=cost)
+        kind = q if q in ("p", "x") else "s" if any(x[0] == "ind" for x in wr) else "g" if any(isinstance(x, tuple) and x[0] == "ind" for x in rd) else "o"
+        o = dict(q=q, fn=fn, tag=tag[0], kind=kind, rd=[masks(x) for x in r], wr=[masks(x) for x in w], cost=cost)
         o.update(kw); ops.append(o)
         return o
 
@@ -233,7 +240,8 @@ def program(ops, T, nxt, prv):
     ms(S("ONE"), 1.0); ms(S("ZER"), 0.0)
     o0 = S("O0", 0, 64); iota(o0, [[2, 32], [1024, 2]], 0, 64)
     iota(S("COI", 0, 1), [[0, 1]], 0, 1)
-    iota(S("TB"), [[0, 64], [-2048, 2], [0, 8]], 1)
+    ms(S("TB"), 1.0)
+    for c in range(8, 16): ms(S("TB", c, 1024, 16), -2047.0)
     ts(S("COI", 1, 2), S("COI", 0, 1), 15, AL.bitwise_and); cp(RC, S("COI", 1, 2))
     ts(S("COI", 2, 3), S("COI", 0, 1), 4, AL.arith_shift_right, 1, AL.bitwise_and); cp(HQ, S("COI", 2, 3))
     ts(S("COI", 3, 4), S("COI", 0, 1), 8, AL.bitwise_and); ts(A64, S("COI", 3, 4), 8.0, AL.mult)
@@ -251,7 +259,10 @@ def program(ops, T, nxt, prv):
         for ch, w in ws: poke(Zs(name, None, off), ch, w)
     ms(S("Z"), 0.0); ms(S("Y"), 0.0)
     aff("DUP", 0, 0, 1); aff("ID", 0, 8, 1); aff("FN0", 0, 1000, 1); aff("FN1", 1000, -1000, 1)
-    iota(S("LO"), [[0, 32], [1, 32]], 1); iota(S("HI"), [[1, 32], [0, 32]], 0)
+    iota(S("HI"), [[1, 32], [0, 32]], 0)
+    ms(S("XB", 0, 512), 1.0); ms(S("XB", 0, 512, 32), 0.0)
+    for h in range(2): scan(S("LO", 512 * h, 512 * h + 512), S("XB", 0, 512), S("ONE"), 0.0, AL.mult, AL.add)
+    M0 = S("COL", 6, 7); ts(M0, RC, 0.0, AL.is_equal)
     asel(S("Y", 15, 2304, 16), S("ONE", 0, 144), [[-1, 16], [-16, 9]], AL.is_equal, 0, 0)
     asel(C("BLK"), ONE, [[-16, 8], [0, 16]], AL.is_ge, 0, 0); asel(C("BLK"), C("BLK"), [[16, 8], [0, 16]], AL.is_ge, 0, 15, -1)
     B8c = sub(C("BLK"), 0, 128, 16)
@@ -259,10 +270,10 @@ def program(ops, T, nxt, prv):
     zmake("key", [(0, 2048), (1, 1), (2, 32)])
     V1, VW, DGO, A1C = sf(64), S("W5"), sf(64), sf(64)
     iota(V1, [[1, 64]], 1); ts(V1, V1, NTB, AL.add, float(-(1015 - 2 ** 23 - 2048)), AL.add)
-    INEL = sh(64)
+    INEL = sh(64); V769 = S("V7"); ts(V769, V1, 769.0, AL.add)
     t0 = sf(64); ts(t0, V1, 128.5, AL.is_lt, 16.0, AL.mult); t1 = sf(64); ts(t1, V1, 896.5, AL.is_gt, 16.0, AL.mult); tt(INEL, t0, t1, AL.add)
     ms(S("RST"), 0.0); ms(S("RST", 0, 512, 8), 1.0e6); ms(S("RS1"), 1.0); ms(S("RS1", 0, 512, 8), 0.0)
-    for n, c in (("KT", 16.0), ("HT", 200.0), ("CT", 0.0), ("UT", 255.0), ("IT", 0.0), ("P", 204800.0), ("M", 204800.0), ("MT", -1.0), ("RT", 0.0), ("X", 0.0), ("INW", 0.0)):
+    for n, c in (("KT", 16.0), ("HT", 200.0), ("CT", 0.0), ("UT", 0.0), ("IT", 0.0), ("MT", -1.0), ("RT", 0.0), ("X", 0.0), ("INW", 0.0)):
         ms(S(n, 0, 16), c)
     tt(S("TA"), IND(S("RAW"), o2), S("TB"), AL.add)
     add("v", lambda e: [e["v"].transpose(ap(S("TB")), ap(S("TA")))], [S("TA")], [S("TB")], 1024 * CYC)
@@ -302,6 +313,8 @@ def program(ops, T, nxt, prv):
             ext(pb(6 + s_, 0, 136), [("id", S("OV", 1040 + 2176 * s_, 3216 + 2176 * s_))], 2176)
             ts(S(L, 0, 136), pb(6 + s_, 0, 136), 15.0, AL.add)
         zero_ov()
+    for n in ("P", "M"): ms(S(n, 0, 15), 0.0); ms(S(n, 15, 16), 204800.0)
+    ts(S("UT", 15, 16), M0, 255.0, AL.mult)
     asel(Zs("en"), B8c, [[-16, 8]], AL.is_ge, 0, -8); ts(Zs("pown"), Zs("pow"), -1.0, AL.mult)
     asel(C("LT"), C("BLK"), [[16, 8], [1, 16]], AL.is_gt, 0, 0, -1)
     iota(DGO, [[16, 64]], 129); ts(DGO, DGO, RC, AL.add)
@@ -321,7 +334,7 @@ def program(ops, T, nxt, prv):
     ts(C("EN2K"), C("FN1"), 2048.0, AL.mult)
     iota(S("IO"), [[1, 1024]], 0); cp(S("IOB"), S("IO", 0, 128))
     cp(Zs("all"), B8c); ts(Zs("8k"), B8c, 8192.0, AL.mult)
-    zmake("es", [(6, 1), (3, 2048)]); zmake("om", [(5, 1)]); cp(Zs("l17"), Zs("lo8")); zmake("l17", [(0, 0)])
+    zmake("om", [(5, 1)]); ts(Zs("l17"), Zs("lo8"), 1024.0, AL.mult); zmake("l17", [(0, 0)])
     ms(C("D12"), 0.0); poke(sub(C("D12"), 1, 128, 16), 1, 1); poke(sub(C("D12"), 2, 128, 16), 2, 1)
     ms(C("CV"), 0.0); ms(C("CV2"), 0.0); ms(C("KD"), 0.0); ms(C("KD2"), 0.0)
     CV, KD = C("CV"), C("KD")
@@ -329,7 +342,7 @@ def program(ops, T, nxt, prv):
     for off in (15, 23): poke(sub(KD, off, off + 128, 16), 0, 1)
     DW, DOV, DX = sf(32), sf(80), sf(64)
     ts(DW, sub(DGO, 0, 32), 511.0, AL.add); ts(DX, DGO, -1.0, AL.mult, 2176.0, AL.add)
-    ts(sub(DOV, 0, 64), DGO, 8063.0, AL.add); ts(sub(DOV, 64, 80), sub(DGO, 0, 16), 9087.0, AL.add)
+    ts(sub(DOV, 0, 64), DGO, 8064.0, AL.add); ts(sub(DOV, 64, 80), sub(DGO, 0, 16), 9088.0, AL.add)
     DS = sf(128); ts(DS, S("IO", 0, 128), 1024.0, AL.add); ts(A1C, S("IO", 0, 64), A64, AL.add, 1.0, AL.add)
     asel(C("GE8"), C("B8"), [[-16, 8], [-1, 16]], AL.is_ge, 0, 0)
     pe([(pb(7, 0, 1), C("P2"), S("Y", 15, 16))]); P2C = S("COL", 5, 6); cp(P2C, pb(7, 0, 1))
@@ -369,11 +382,12 @@ def program(ops, T, nxt, prv):
         pe([(out, C(f + "0"), S(src, a, a + n, 2)), (out, C(f + "1"), S(src, a + 1, a + n, 2))])
 
     def part_a(t):
-        fold(pb(3), "FN", "RTH", 0, 1024); ts(S("LN"), pb(3), 15.0, AL.add)
         for h in range(2):
-            a, b = 512 * h, 512 * h + 512
-            pe([(pb(1 + h), Zs("lo8", 0), S("FL", a, b)), (pb(1 + h), C("ID"), S("IDB", a, b))] + [(blk(1, r), Yc(r, 0), INEL) for r in range(8 * h, 8 * h + 8)])
-            mv(S("KT", 16 + a, 16 + b), pb(1 + h))
+            a, b, k = 512 * h, 512 * h + 512, 3 * h
+            pe([(pb(k), C("ID"), S("IDB", a, b))] + [(pb(k, 64 * r, 64 * r + 64), Yc(8 * h + r, 0), INEL) for r in range(8)], True, False)
+            pe([(pb(k), Zs("lo8", 0), S("FL", a, b))], False, True)
+            mv(S("KT", 16 + a, 16 + b), pb(k))
+            fold(pb(1 + h, 0, 256), "FN", "RTH", a, 512); ts(S("LN", 256 * h, 256 * h + 256), pb(1 + h, 0, 256), 15.0, AL.add)
         extc(pb(3, 0, 64), "lo8", S("FL"), [(pb(3, 0, 64), C("ID"), INEL)])
         ts(DG, pb(3, 0, 64), 256.0, AL.mult); ts(TG1, DG, 8.0, AL.mult); tt(OK_, TG1, V1, AL.add)
         hop(S("KT"), "key", list(range(16)), [], t)
@@ -384,8 +398,11 @@ def program(ops, T, nxt, prv):
         ts(LI, MI, 31, AL.bitwise_and); cp(LOB, LI); ts(HI_, MI, 5, AL.arith_shift_right, 63, AL.bitwise_and); cp(HIB, HI_)
         cp(A1H, AI); tt(SELF, AI, V1, AL.is_equal)
         ext(pb(3, 0, 64), [("pow", S("GB"))], 1024); cp(BB, pb(3, 0, 64))
-        w2r(1, [(lambda r: Yc(r, 1), lambda r: LOB), (lambda r: Yc(r, 2), lambda r: HIB), (lambda r: Yc(r, 0), lambda r: BB)])
-        halves(lambda h, a, b: mv(S("HT", 16 + a, 16 + b), pb(1 + h), M3))
+        for h in range(2):
+            pe([(pb(1 + h), C("ID"), S("ZER", 0, 512))] + [(blk(1, r), Yc(r, c), x) for r in range(8 * h, 8 * h + 8) for c, x in ((1, LOB), (2, HIB))], True, False)
+        for h in range(2):
+            pe([(blk(1, r), Yc(r, 0), BB) for r in range(8 * h, 8 * h + 8)], False, True)
+            mv(S("HT", 16 + 512 * h, 528 + 512 * h), pb(1 + h), M3)
         w2r(1, [(Al, lambda r: A1H)])
 
         def f(h, a, b):
@@ -403,9 +420,9 @@ def program(ops, T, nxt, prv):
         tt(TG1, NI, DG, AL.is_equal); tt(CH, TG1, SELF, AL.mult)
         scan(INB, S("ONE", 0, 64), CH, 0.0, AL.mult, AL.add)
         pe([(pb(3, 0, 1), C("LT"), sub(INB, 63, 64))])
-        ts(R1, INB, pb(3, 0, 1), AL.add); ts(TG1, R1, 128.5, AL.is_lt); tt(CON, TG1, CH, AL.mult); tt(RK1, R1, CON, AL.mult)
-        ts(TG1, CON, 0.0, AL.is_equal); tt(TG2, TG1, DGO, AL.mult); tt(TG1, TG2, RK1, AL.max); cp(GTL, TG1)
+        ts(TG1, CH, 0.0, AL.is_equal); tt(TG2, TG1, V769, AL.mult); tt(TG1, TG2, INB, AL.add); ts(GTL, TG1, pb(3, 0, 1), AL.add)
         ms(S("WW", 0, 144), 0.0); put(IND(S("WW"), GTL), S("U1J")); cp(S("TG2"), S("WW", 1, 129))
+        ts(R1, INB, pb(3, 0, 1), AL.add); ts(TG1, R1, 128.5, AL.is_lt); tt(CON, TG1, CH, AL.mult); tt(RK1, R1, CON, AL.mult)
         ext(pb(3, 0, 8), [("c0", S("TG2"))], 128); ts(GOL, pb(3, 0, 8), 15.0, AL.add)
         cp(S("G0"), IND(RTW, GOL))
         fold(pb(3, 0, 64), "FN", "G0", 0, 128); pe([(pb(3, 128, 256), C("DUP"), S("G0"))])
@@ -417,25 +434,31 @@ def program(ops, T, nxt, prv):
         cp(RK, pb(4, 0, 64)); ts(CB, RK, 0.0, AL.is_gt); tt(GG, CB, SELF, AL.is_gt)
         ts(LB1, RK, -200.0, AL.add); tt(LB2, LB1, GG, AL.mult); ts(LP, LB2, 200.0, AL.add, 1024.0, AL.mult)
         ts(LB1, RK, -1.0, AL.mult, -200.0, AL.add); tt(LB2, LB1, GG, AL.mult); ts(LM, LB2, 200.0, AL.add, 1024.0, AL.mult)
+        w2r(4, [(Al, lambda r: CB)])
+        halves(lambda h, a, b: tt(S("T1", a, b), pb(4 + h), S("D2", a, b), AL.mult))
+        tag[0] = "ends"
+        if t == 0: ends()
+        tag[0] = "pm"
         for b0, tab, lab in ((4, "P", LP), (4, "M", LM)):
             w2r(b0, [(lambda r: C("ID"), lambda r: S("XS", r, 1024, 16)), (Al, lambda r, lab=lab: lab)])
             halves(lambda h, a, b, b0=b0, tab=tab: mv(S(tab, 16 + a, 16 + b), pb(b0 + h)))
-        w2r(4, [(Al, lambda r: CB)])
-        halves(lambda h, a, b: tt(S("T1", a, b), pb(4 + h), S("D2", a, b), AL.mult))
 
     def part_b(t):
+        tag[0] = ""
         for h in range(2):
             a, b = 512 * h, 512 * h + 512
-            pe([(pb(1 + h), C("ID"), S("IDB", a, b)), (pb(1 + h), Zs("pown", 5), S("EQ", a, b)), (pb(1 + h), Zs("en", 6), S("D2", a, b))] +
+            pe([(pb(1 + h), C("ID"), S("IDB", a, b)), (pb(1 + h), Zs("pown", 5), S("EQ", a, b))] +
                [(pb(1 + h, x, x + 384), Zs(z, c), S("FL", a + x, a + x + 384)) for x in (128 - 128 * h,) for z, c in (("lo8", 4), ("pow", 5))], True, False, "ut%d" % h)
         if t:
-            pe([(pb(7), C("INT"), S("ONE"))] + [(pb(7), Zs("k4", r), S("SRG", 512 * i, 512 * i + 512)) for i, r in enumerate((14, 15, 0, 1))])
+            pe([(pb(7), C("INT"), S("ONE"))], True, False)
+            for h in range(2): pe([(pb(7), Zs("k4", r), S("SRG", 512 * i, 512 * i + 512)) for i, r in list(enumerate((14, 15, 0, 1)))[2 * h:2 * h + 2]], False, h == 1)
             tt(S("W6"), pb(7), S("W5"), AL.min); scan(S("WW", 0, 512), S("RS1"), S("W6"), 0.0, AL.mult, AL.add); cp(XI, S("WW", 7, 512, 8))
         ts(KI, XI, 255, AL.bitwise_and); tt(SS, KI, BB, AL.add)
         for h in range(2):
             pe([(pb(1 + h, 384 * h, 384 * h + 128), Zs(z, c), S("FLS", 128 - 128 * h, 256 - 128 * h)) for z, c in (("lo8", 4), ("pow", 5))] +
                [(blk(1, r), Yc(r, 0), SS) for r in range(8 * h, 8 * h + 8)], False, True, "ut%d" % h)
             mv(S("UT", 16 + 512 * h, 528 + 512 * h), pb(1 + h))
+        tag[0] = "edge"
         n = 2176 + 640 * t; nch = -(-n // 512); w = -(-n // (32 * nch)) * 32
         for i, a in enumerate(range(0, n, w)):
             b = min(n, a + w); k = i % 2; ga, zz = S("GA", 512 * k, 512 * k + b - a), S("ZZ", 512 * k, 512 * k + b - a)
@@ -452,7 +475,9 @@ def program(ops, T, nxt, prv):
         f, d = S("CF", 0, q), S("CF", 256, 256 + q)
         ts(f, cnt, 8.5, AL.is_gt); ts(d, S("EA", 0, q), float(1024 * t), AL.add); tt(S("CF", 512, 512 + q), d, S("MO", 0, q), AL.subtract)
         tt(d, S("CF", 512, 512 + q), f, AL.mult); tt(S("MO", 0, q), S("MO", 0, q), d, AL.add)
-        cp(S("GU"), IND(S("UT"), UL)); act(S("IT", 16, 1040), IND(S("UT"), UL), AF.Copy)
+        tag[0] = ""
+        for h in range(2): mv(S("GU", 512 * h, 512 * h + 512), IND(S("UT"), sub(UL, 32 * h, 32 * h + 32)), None, "vs"[h])
+        act(S("IT", 16, 1040), IND(S("UT"), UL), AF.Copy)
         J = lambda x, jj: sub(x, 128 * jj, 128 * jj + 128)
         gu = lambda jj, h: S("GU", 2 * jj + h, 1024, 8)
         pe([(J(pb(0), jj), C("SB%d" % h), gu(jj, h)) + ((1,) if h == 0 else ()) for jj in range(4) for h in range(2)])
@@ -483,34 +508,38 @@ def program(ops, T, nxt, prv):
         ts(ci, pb(3, 0, 40), -32.0, AL.add); ts(c4, ci, 254, AL.bitwise_and); ts(lo(c2), c4, 4.0, AL.mult, -3.0, AL.add); ts(hi(c2), c4, 4.0, AL.mult, 1.0, AL.add)
         ext(pb(3, 64, 104), [("8k", S("YC"))], 640); ts(yi, pb(3, 64, 104), 65536.0, AL.add)
         ts(lo(hk), yi, 9, AL.arith_shift_right, 15, AL.bitwise_and); ts(hi(hk), yi, 6, AL.arith_shift_right, 7, AL.bitwise_and)
-        ts(vl, lo(hk), 0.0, AL.is_gt)
-        tt(t2, hk, c2, AL.add); tt(lo(i2), lo(t2), vl, AL.mult); tt(hi(i2), hi(t2), vl, AL.mult); ts(I2, i2, 15.0, AL.add)
-        ts(lo(rr), yi, 3, AL.arith_shift_right, 7, AL.bitwise_and); ts(hi(rr), yi, 7, AL.bitwise_and); ts(r2, rr, 256.0, AL.mult)
+        tt(t2, hk, c2, AL.add); ts(I2, t2, 15.0, AL.add)
+        ts(vl, lo(hk), 0.0, AL.is_gt); ts(lo(i2), lo(hk), 0.0, AL.is_equal)
+        ts(lo(rr), yi, 3, AL.arith_shift_right, 7, AL.bitwise_and); ts(hi(rr), yi, 7, AL.bitwise_and); ts(S("R2"), rr, 256.0, AL.mult)
         hs = ((lo, 0, 3), (hi, 640, 0))
         for f_, a, b in hs:
+            tt(f_(t3), lo(i2), f_(DOV), AL.mult)
             cp(S("GI", a, a + 640), IND(S("IT"), f_(I2)))
-            ext(pb(b, 0, 40), [("om", S("GI", a, a + 640))], 640); tt(f_(t3), pb(b, 0, 40), f_(r2), AL.add); cp(f_(LUL), f_(t3))
+            pe([(pb(b, 0, 40), C("ID"), f_(S("R2")))] + [(pb(b, 0, 40), Zs("om", r), S("GI", a + r, a + 640, 16)) for r in range(16)]); cp(f_(LUL), pb(b, 0, 40))
             mv(S("GL", a, a + 640), IND(S("LUT"), f_(LUL)))
-            ext(pb(b, 64, 104), [("id", S("GI", a, a + 640))], 640); cp(f_(u2), pb(b, 64, 104))
-            ts(f_(t2), f_(u2), 0.0, AL.is_equal); tt(f_(t3), f_(t2), f_(DOV), AL.mult)
+            pe([(pb(b, 64, 104), Zs("id", r), S("GI", a + r, a + 640, 16)) for r in range(16)], True, False)
         for i in range(4):
             a, m = 320 * i, 320 * (i % 2); o = (a + 640) % 1280; p = pb(1 + i % 2, 0, 320)
             pe([(p, C("ID"), S("NAM", m, m + 320)), (p, C("D12"), S("GI", o, o + 320))])
             mv(S("SRC", a, a + 320), p, M8[t])
         for f_, a, b in hs:
-            ext(pb(b, 0, 40), [("l17", S("GL", a, a + 640))], 640); ts(f_(t2), pb(b, 0, 40), 1024.0, AL.mult, -1.0, AL.add, False)
-            tt(f_(i2), f_(t2), f_(u2), AL.add); tt(f_(t2), f_(i2), f_(t3), AL.max); cp(f_(OVL), f_(t2))
+            pe([(pb(b, 64, 104), Zs("l17", r), S("GL", a + r, a + 640, 16)) for r in range(16)], False, True)
+            tt(f_(t2), pb(b, 64, 104), f_(t3), AL.max); ts(f_(OVL), f_(t2), -1.0, AL.add)
             cp(IND(S("OV"), f_(OVL)), S("SRC", a, a + 640))
-        ext(pb(0, 128, 208), [("es", S("GI"))], 1280); ts(EXL, pb(0, 128, 208), 15.0, AL.add)
-        c0 = 136 + 40 * t
+        ext(pb(0, 128, 208), [("id", S("GI"))], 1280)
+        c0 = 136 + 40 * t; um = S("UM", 0, 80)
+        for f_, a, b in hs:
+            tt(f_(u2), f_(pb(0, 128, 208)), vl, AL.mult); tt(f_(um), f_(u2), vl, AL.add)
+        ts(EXL, um, 14.0, AL.add)
         ts(S("EA", c0, c0 + 40), lo(u2), 15.0, AL.add); ts(S("EB", c0, c0 + 40), hi(u2), 15.0, AL.add)
         ts(lo(r2), vl, float(1024 * t), AL.mult, 15.0, AL.add); tt(S("MO", c0, c0 + 40), lo(r2), lo(u2), AL.add)
-        mv(S("XA"), IND(XW, lo(EXL))); tt(S("XB"), IND(XW, hi(EXL)), S("XA"), AL.add); ts(S("X", 16 + n, 656 + n), S("XB"), 255.0, AL.min)
+        mv(S("YY"), IND(S("P"), lo(EXL))); tt(S("XB"), IND(S("M"), hi(EXL)), S("YY"), AL.add); ts(S("X", 16 + n, 656 + n), S("XB"), 255.0, AL.min)
         for bk, a, b in ((6, 896, 1024), (7, 0, 128), (1, 128, 512), (2, 512, 896)):
             p = pb(bk, 0, b - a)
             pe([(p, C("ID"), S("RTH", a, b)), (p, C("NID"), S("T1", a, b))], True, False)
             pe([(p, sub(C("CV"), 15 - l, 143 - l), S("OV", 1024 * l + a, 1024 * l + b)) for l in range(8)], False, True)
-            cp(S("RTH", a, b), p); act(S("FL", a, b), p, AF.Sign); mv(S("RT", 16 + a, 16 + b), p)
+            cp(S("RTH", a, b), p); act(S("FL", a, b), p, AF.Sign)
+            if t < 2: mv(S("RT", 16 + a, 16 + b), p)
         if t < 2: E["zero_ov"]()
 
     def swap(src, dst, w, k):
@@ -524,6 +553,7 @@ def program(ops, T, nxt, prv):
         add("x", None, [], [sub(dst, 0, w)], 3000.0 + 6 * w, after=o, sem=("a%d" % (k + 1), E["nxt"][4]))
 
     def part_c(t):
+        tag[0] = "seam"
         TP, TR = S("TP", 128 * t, 128 * t + 128), S("TR", 128 * t, 128 * t + 128)
         SND, RX = S("SND"), S("RX", 1024 * t, 1024 * t + 1024)
         q0, q1, q2, q3 = E["q0"], E["q1"], E["q2"], E["q3"]
@@ -560,7 +590,7 @@ def program(ops, T, nxt, prv):
         ext(pb(7, 0, 64), [("8k", S("NE"))], 1024)
         w0, w1 = E["w0"], E["w1"]; ts(w0, pb(7, 0, 64), 65536.0, AL.add); ts(w1, w0, 8191, AL.bitwise_and)
         ts(h0(q0), w1, 0.0, AL.is_equal); tt(h0(q1), h0(q0), DX, AL.mult); tt(h0(q2), w1, h0(q1), AL.add); ts(SXL, h0(q2), -1.0, AL.mult, 6159.0, AL.add)
-        mv(SND, IND(XW, SXL))
+        mv(sub(SND, 0, 512), IND(XW, sub(SXL, 0, 32)), None, "s"); mv(sub(SND, 512, 1024), IND(XW, sub(SXL, 32, 64)))
         swap(SND, RX, 512, 4 * t + 2)
         GT, SG, MN, GX = S("EQS"), S("OH"), S("SC"), S("SRG")
 
@@ -580,13 +610,12 @@ def program(ops, T, nxt, prv):
             tt(S("FLS", 128 * s_, 128 * s_ + 128), S("FL", a, a + 128), k_, AL.mult)
 
     part_a(0)
-    ends()
     for t in range(3):
         part_b(t)
         if t < 2: part_a(t + 1)
         if t == 2:
             cp(S("MU"), S("MO"))
-            for k, n in enumerate(("P", "M", "UT", "IT")):
+            for k, n in enumerate(("WW", "RT", "UT", "IT")):
                 mv(S(n, 16, 1040), IND(S("MT"), S("MU", 64 * k, 64 * k + 64)))
                 dma("y", [(T["ymid"][:, 1024 * k:1024 * k + 1024], T[n][0:128:16, 16:1040])], [S(n, 16, 1040)], [], 2500)
         part_c(t)
@@ -636,7 +665,7 @@ def emit(ops, g, T):
     for i in range(n - 1, -1, -1):
         pri[i] = ops[i]["cost"] + ops[i].get("dma", 0) + LAT + max([pri[k] for k in succ[i]] or [0.0])
     fw = [[(j, LAT + ops[j].get("dma", 0)) for j in o["deps"]] + [(j, ops[j].get("dma", 0)) for j in o["order"]] for o in ops]
-    bw = [[] for _ in ops]
+    bw = [[] for _ in ops]; pen = [PEN[0]] * n
     for i in range(n):
         for j, lag in fw[i]: bw[j].append((i, lag))
 
@@ -655,19 +684,53 @@ def emit(ops, g, T):
                     else: hi = mid
                 while q != "x" and lo < len(l) and l[lo][0] < st + c:
                     st = max(st, l[lo][1]); lo += 1
-                key = st + c + (PEN[0] * c + PEN[1] if q == "v" else 0.0)
+                key = st + c + (pen[i] * c + PEN[1] if q == "v" else 0.0)
                 if best is None or key < best[0]: best = (key, q, st, c, lo)
             _, q, st, c, lo = best
             if q != "x": busy[q].insert(lo, (st, st + c))
             res[i] = (st, st + c, q)
         return res
     if n not in PLAN:
-        res = place(sorted(range(n), key=lambda i: (-pri[i], i)), fw, False); top = None
-        for _ in range(PASSES[0]):
-            span = max(res[i][1] + ops[i].get("dma", 0) for i in range(n))
-            if top is None or span < top[0]: top = (span, res)
-            rb = place(sorted(range(n), key=lambda i: (-res[i][1], -i)), bw, True)
-            res = place(sorted(range(n), key=lambda i: (-rb[i][1], i)), fw, False)
+        left = [len(x) for x in fw]; ready = [i for i in range(n) if not left[i]]; first = []
+        while ready:
+            i = max(ready, key=lambda i: (pri[i] - BIAS.get(ops[i]["tag"], 0.0), -i)); ready.remove(i); first.append(i)
+            for k, _ in bw[i]:
+                left[k] -= 1
+                if not left[k]: ready.append(k)
+        res = place(first, fw, False); top = None
+        hard = [list(o["deps"]) for o in ops]; soft = [list(o["order"]) for o in ops]; late = [o.get("dma", 0.0) for o in ops]
+
+        def score(res):
+            sq = sorted(range(n), key=lambda i: (res[i][0], i)); tot = 0.0
+            for fac, lat, wt in GUESS:
+                free = {}; en_ = [0.0] * n
+                for i in sq:
+                    q = res[i][2]; st = 0.0 if q == "x" else free.get(q, 0.0)
+                    for j in hard[i]:
+                        if en_[j] + lat > st: st = en_[j] + lat
+                    for j in soft[i]:
+                        if en_[j] > st: st = en_[j]
+                    st += (res[i][1] - res[i][0]) * fac[ops[i]["kind"]]; free[q] = st; en_[i] = st + late[i] * fac["x"]
+                tot += wt * max(en_)
+            return tot
+        rng = np.random.RandomState(SEED[0]); cur = None
+        for it in range(PASSES[0]):
+            sc_ = score(res)
+            if top is None or sc_ < top[0]: top = (sc_, res, list(pen))
+            if cur is None or sc_ < cur[0] + TEMP[0] * (1.0 - it / PASSES[0]): cur = (sc_, res, list(pen))
+            key = [cur[1][i][0] for i in range(n)]; pen[:] = cur[2]
+            c0 = rng.uniform(0, max(key)); wd = rng.choice([5000.0, 15000.0, 30000.0]); nz = rng.normal(0, rng.choice([300.0, 1000.0, 2500.0]), n)
+            flip = rng.uniform(0, 1, n) < rng.choice([0.0, 0.1])
+            for i in range(n):
+                if it and abs(key[i] - c0) < wd:
+                    key[i] += nz[i]
+                    if flip[i]: pen[i] = 3.0 if cur[1][i][2] == "v" else -1.0
+                for j, _ in fw[i]:
+                    if key[j] >= key[i]: key[i] = key[j] + 0.001
+            res = place(sorted(range(n), key=lambda i: (key[i], i)), fw, False)
+            if it % 2 == 0:
+                rb = place(sorted(range(n), key=lambda i: (-res[i][1], -i)), bw, True)
+                res = place(sorted(range(n), key=lambda i: (-rb[i][1], i)), fw, False)
         PLAN[n] = top[1]
     end = [0.0] * n
     for i, o in enumerate(ops):

@@ -5,25 +5,24 @@ from concourse.mybir import AluOpType as AL, ActivationFunctionType as AF
 F, H, B, I, U = "float32", "float16", "bfloat16", "int32", "uint16"
 SB = {
     "RAW": (2048, I), "X": (5136, B), "RT": (1040, F), "RTH": (1024, H), "TA": (1024, F), "TB": (1024, F), "FL": (1024, B), "FLS": (256, B),
-    "G1": (8192, B), "LN": (512, U), "KT": (1040, B), "HT": (1040, B), "CT": (1040, B), "UT": (1040, F), "IT": (1040, F), "GU": (1024, B),
-    "P": (1040, F), "M": (1040, F), "MT": (3088, F), "OV": (9472, B), "EQ": (1024, B), "D2": (1024, H), "T1": (1024, H), "GB": (1024, B),
-    "GC": (1024, B), "XS": (1024, B), "IDB": (1024, B), "U1J": (1024, F), "LO": (1024, B), "HI": (1024, B), "IO": (1024, F),
-    "IOB": (128, B), "ALL": (2048, B), "Y": (2304, B), "Z": (144 * 14, B), "CM": (128 * 64, B), "ONE": (512, B), "RST": (512, B),
-    "RS1": (512, B), "LUT": (2048, B), "EA": (256, U), "EB": (256, U), "MO": (256, F), "MU": (256, U), "WN": (3456, B), "GA": (1024, F), "ZZ": (1024, F),
-    "SF": (2560, F), "SI": (1024, I), "SH": (640, B), "SU": (640, U), "S16": (64, H), "W5": (512, F), "W6": (512, F), "WI": (512, I), "WJ": (512, I),
-    "WB": (512, B), "R": (512, B), "PR": (512, B), "SV": (512, B), "INW": (528, H), "NT": (512, F), "WW": (2568, F), "TG2": (128, H), "CW": (640, H), "YY": (640, F),
-    "YC": (640, H), "GI": (1280, H), "GL": (1280, B), "SRC": (1280, B), "GW": (1168, B), "G0": (128, H), "XB": (640, B),
+    "G1": (9216, B), "LN": (512, U), "KT": (1040, B), "CT": (1040, B), "IT": (1040, B), "GR": (1024, H), "HE": (2048, B),
+    "P": (1040, F), "M": (1040, F), "GA": (5392, F), "OV": (9472, B), "EQ": (1024, B), "D2": (1024, H), "GB": (1024, B),
+    "GC": (1024, B), "XS": (1024, B), "IDB": (1024, B), "U1J": (1024, F), "LO": (1024, B), "HI": (1024, B), "IO": (1056, F),
+    "IOB": (128, B), "ALL": (2048, B), "Y": (2304, B), "Z": (144 * 14, B), "CM": (128 * 68, B), "ONE": (512, B), "RST": (512, B),
+    "LUT": (2048, B), "EA": (256, U), "EB": (256, U), "ENC": (256, F), "GAW": (256, F), "WN": (3456, B), "ZZ": (1024, F), "ZF": (273, F), "TH": (512, B),
+    "SF": (2560, F), "SI": (1024, I), "SH": (640, B), "SU": (640, U), "S16": (512, H), "W5": (512, F), "W6": (512, F), "WI": (512, I), "WJ": (512, I),
+    "WB": (512, B), "R": (512, B), "PR": (512, B), "SV": (512, B), "INW": (528, H), "NT": (512, F), "WW": (896, F), "CW": (640, H),
+    "YC": (640, H), "GI": (1280, B), "GL": (1280, B), "SRC": (1280, B), "G0": (128, H), "XB": (640, B), "RKW": (64, B), "QS": (64, B), "QR": (256, B),
     "TP": (384, B), "TR": (384, B), "EQS": (1024, B), "PRS": (1024, H), "FLG": (128, B), "NUS": (128, F), "INC": (128, H), "TG": (128, H),
     "SW": (1152, B), "SC": (1024, B), "OH": (1024, B), "NE": (1024, H), "SND": (3072, B), "RX": (3072, B), "COL": (16, F), "COI": (16, I), "ZER": (1024, B),
-    "CF": (1024, F),
 }
-LISTS = {"a": 64, "gt": 64, "sp": 64, "go": 8, "u": 64, "cs": 32, "cw": 40, "i2": 80, "ex": 80, "lu": 80, "ov": 80, "st": 8, "sc": 64, "sx": 64, "sr": 128}
+LISTS = {"a": 64, "mk": 64, "sp": 64, "go": 8, "u": 64, "cs": 32, "cw": 40, "i2": 80, "ex": 80, "lu": 80, "ov": 80, "st": 8, "sc": 64, "sx": 64, "sr": 128, "gq": 4, "q": 8}
 for _k, _n in LISTS.items():
     SB["L" + _k] = (_n, U)
-SB.update({"LM": (64, B), "SRG": (2048, B), "KP": (256, B), "SM": (3072, B), "SND": (1024, B), "O0": (128, I), "NAM": (640, B), "ZB": (1024, B), "V7": (64, F), "R2": (80, B), "UM": (160, F)})
+SB.update({"SRG": (2048, B), "KP": (256, B), "SM": (3072, B), "SND": (1024, B), "O0": (128, I), "NAM": (640, B), "ZB": (1024, B), "R2": (80, B), "UM": (160, F)})
 ALIAS = {"WI": ("RAW", 1024), "WJ": ("RAW", 1536), "SI": ("RAW", 0), "TA": ("GA", 0), "TB": ("ZZ", 0), "GC": ("GB", 0), "EQS": ("SM", 0), "OH": ("SM", 1024),
-         "SC": ("SM", 2048), "SRG": ("SM", 0), "NE": ("PRS", 0), "CF": ("GA", 0), "YY": ("WW", 0), "NT": ("W5", 0), "GL": ("G1", 0), "SRC": ("G1", 1280),
-         "GU": ("G1", 2560), "GW": ("G1", 3584), "WB": ("G1", 4752), "R": ("G1", 5264), "PR": ("G1", 5776), "SV": ("G1", 6288)}
+         "SC": ("SM", 2048), "NE": ("PRS", 0), "NT": ("W5", 0), "GL": ("G1", 0), "SRC": ("G1", 1280),
+         "HE": ("G1", 2560), "WB": ("G1", 4752), "R": ("G1", 5264), "PR": ("G1", 5776), "SV": ("G1", 6288)}
 SCRATCH = {k: ("sbuf", [128, n], d) for k, (n, d) in SB.items() if k not in ALIAS}
 for _b in range(8):
     SCRATCH["pb%d" % _b] = ("psum", [128, 512], F)
@@ -32,13 +31,16 @@ SEMAPHORES = ["cv", "cs", "cp", "cg"] + ["o%d" % i for i in range(6)] + ["d%d" %
 SIZE = {F: 4, H: 2, B: 2, I: 4, U: 2}
 CYC, PEC, LAT = 0.95, 0.48, 120.0
 PEN = [0.6, 50.0]
-HQ_ = [["ssssssss", "ssssssss"], [["vs"] * 8] * 2, [["vs"] * 8] * 2]
 EDGE = [2, 2, 2]
+MBK, STEPS, NEAR, JIT = [4], [30000], [3], [10.0]
+MARK, CUT, HOPW, EDW = [1], [1024], [512], [512]
+HAS = ["vmvm"]
+BLOCKS = [(j, s) for s in range(4) for j in range(2 * s, 8) if j != 2 * s + 1]
 PAIRS = [(j, k) for j in range(8) for k in range(j + 1, 8)]
-PASSES, PLAN, SEED, TEMP = [2000], {}, [1], [1000.0]
+PASSES, PLAN, SEED, TEMP = [100], {}, [1], [1000.0]
 GUESS = [({"o": 1, "g": 1, "s": 1, "p": 1, "x": 1.2}, 130.0, 2.0), ({"o": 1, "g": 0.75, "s": 0.55, "p": 1, "x": 1.2}, 130.0, 1.0),
          ({"o": 1, "g": 1.3, "s": 1.55, "p": 1, "x": 1}, 100.0, 1.0), ({"o": 1, "g": 1.25, "s": 0.7, "p": 1.3, "x": 1.6}, 200.0, 1.0)]
-BIAS = {"ends": 0.0, "pm": 0.0, "edge": 0.0, "seam": 0.0}
+BIAS, TRIES = {"ends0": 20000.0}, [1]
 GAT, SCA = 1.5, 3.5
 
 
@@ -75,7 +77,7 @@ def program(ops, T, nxt, prv):
             return ap(x[1]).indirect(ap(x[2]))
         return T[x[0]][:, x[1]:x[2]] if x[3] == 1 else T[x[0]][:, x[1]:x[2]:x[3]]
 
-    tag = [""]
+    tag = ["", 0]
 
     def flat(xs):
         out = []
@@ -92,7 +94,7 @@ def program(ops, T, nxt, prv):
             else:
                 w.append(x)
         kind = q if q in ("p", "x") else "s" if any(x[0] == "ind" for x in wr) else "g" if any(isinstance(x, tuple) and x[0] == "ind" for x in rd) else "o"
-        o = dict(q=q, fn=fn, tag=tag[0], kind=kind, rd=[masks(x) for x in r], wr=[masks(x) for x in w], cost=cost)
+        o = dict(q=q, fn=fn, tag=tag[0] + str(tag[1]), kind=kind, rd=[masks(x) for x in r], wr=[masks(x) for x in w], cost=cost)
         o.update(kw); ops.append(o)
         return o
 
@@ -162,8 +164,13 @@ def program(ops, T, nxt, prv):
         n = len(mm)
         st = [(first if i == 0 else len(m) > 3) for i, m in enumerate(mm)]
         sp = [(last if i == n - 1 else len(mm[i + 1]) > 3) for i in range(n)]
-        add("p", lambda e: [e["p"].matmul(ap(m[0]), ap(m[1]), ap(m[2]), st[i], sp[i]) for i, m in enumerate(mm)],
-            [m[1] for m in mm] + [m[2] for m in mm], [m[0] for m in mm], sum(max(64, cols(m[0])) for m in mm) * PEC + 60, grp=grp)
+        part, c = [], 0
+        for i, m in enumerate(mm):
+            part.append(i); c += max(64, cols(m[0])) * (4 if SB[m[2][0]][1] == F else 1)
+            if c >= CUT[0] or i == n - 1:
+                add("p", lambda e, part=part: [e["p"].matmul(ap(mm[i][0]), ap(mm[i][1]), ap(mm[i][2]), st[i], sp[i]) for i in part],
+                    [mm[i][1] for i in part] + [mm[i][2] for i in part], [mm[i][0] for i in part], c * PEC + (60 if i == n - 1 else 10))
+                part, c = [], 0
 
     def iota(out, pat, base, cm=0):
         kw = {} if SB[out[0]][1] == I else {"allow_small_or_imprecise_dtypes": True}
@@ -206,7 +213,7 @@ def program(ops, T, nxt, prv):
         return S("ALL", 128 * r, 128 * r + 128)
 
     def lh(z, r):
-        return Yc(0, r) if z == "c0" else Zs(z, r)
+        return Yc(0, r) if z == "c0" else S("YF", 15 - r, 143 - r) if z == "f0" else Zs(z, r)
 
     def ext(out, parts, n):
         pe([(out, lh(z, r), sub(src, r, n, 16)) for z, src in parts for r in range(16)])
@@ -267,59 +274,71 @@ def program(ops, T, nxt, prv):
     asel(C("BLK"), ONE, [[-16, 8], [0, 16]], AL.is_ge, 0, 0); asel(C("BLK"), C("BLK"), [[16, 8], [0, 16]], AL.is_ge, 0, 15, -1)
     B8c = sub(C("BLK"), 0, 128, 16)
     asel(Zs("lo8"), B8c, [[16, 8]], AL.is_ge, 0, 7, -1)
-    zmake("key", [(0, 2048), (1, 1), (2, 32)])
-    V1, VW, DGO, A1C = sf(64), S("W5"), sf(64), sf(64)
+    zmake("key", [(0, 2048 * 256), (1, 256), (2, 32 * 256)])
+    V1, VW, DGO, A1C, JK, JG, V256 = sf(64), S("W5"), sf(64), sf(64), sf(64), sf(8), sf(64)
     iota(V1, [[1, 64]], 1); ts(V1, V1, NTB, AL.add, float(-(1015 - 2 ** 23 - 2048)), AL.add)
-    INEL = sh(64); V769 = S("V7"); ts(V769, V1, 769.0, AL.add)
+    INEL = sh(64); ts(JK, V1, -8185.0, AL.add); ts(V256, V1, 256.0, AL.mult, -128.0, AL.add)
     t0 = sf(64); ts(t0, V1, 128.5, AL.is_lt, 16.0, AL.mult); t1 = sf(64); ts(t1, V1, 896.5, AL.is_gt, 16.0, AL.mult); tt(INEL, t0, t1, AL.add)
-    ms(S("RST"), 0.0); ms(S("RST", 0, 512, 8), 1.0e6); ms(S("RS1"), 1.0); ms(S("RS1", 0, 512, 8), 0.0)
-    for n, c in (("KT", 16.0), ("HT", 200.0), ("CT", 0.0), ("UT", 0.0), ("IT", 0.0), ("MT", -1.0), ("RT", 0.0), ("X", 0.0), ("INW", 0.0)):
+    for k in range(8): ms(S("RST", k, 512, 8), -float(2 ** (k - 1)) if k else 1.0e8)
+    for n, c in (("KT", 16.0), ("CT", 0.0), ("IT", 0.0), ("RT", 0.0), ("X", 0.0), ("INW", 0.0)):
         ms(S(n, 0, 16), c)
+    ts(S("KT", 15, 16), M3, -16.0, AL.mult, 16.0, AL.add)
     tt(S("TA"), IND(S("RAW"), o2), S("TB"), AL.add)
     add("v", lambda e: [e["v"].transpose(ap(S("TB")), ap(S("TA")))], [S("TA")], [S("TB")], 1024 * CYC)
     act(S("FL"), S("TB"), AF.Sign)
 
     def f0(h, a, b):
         pe([(pb(1 + h), C("DUP"), S("FL", a, b))])
-        tt(S("RTH", a, b), pb(1 + h), S("TB", a, b), AL.mult); tt(S("RT", 16 + a, 16 + b), pb(1 + h), S("TB", a, b), AL.mult)
+        tt(S("RTH", a, b), pb(1 + h), S("TB", a, b), AL.mult)
         pe([(pb(4 + h), Yc(0, 1), S("LO", a, b)), (pb(4 + h), Yc(0, 2), S("HI", a, b))])
         mv(S("IDB", a, b), pb(4 + h), M3)
     halves(f0)
-    cp(S("FLS", 0, 128), S("FL", 896, 1024)); cp(S("FLS", 128, 256), S("FL", 0, 128))
     iota(S("U1J"), [[1, 64], [64, 16]], 1)
+    iota(S("IO"), [[1, 1056]], 0); cp(S("IOB"), S("IO", 0, 128))
     for k in range(4):
         asel(S("ALL", 512 * k, 512 * k + 512), S("ONE"), [[-1, 4], [-16, 8], [0, 16]], AL.is_equal, 0, -4 * k)
-    zmake("pow", [(k, 2 ** k) for k in range(8)])
-    zmake("lab", [(0, 1), (1, 8192), (2, 262144), (3, 256)]); zmake("id", [(1, 1), (2, 32)])
-    ts(C("N8K"), C("ID"), -8192.0, AL.mult); ts(C("NID"), C("ID"), -1.0, AL.mult)
-    iota(VW, [[0, 8], [16, 64]], 0); ts(VW, VW, RC, AL.add)
+    for k in range(8): ts(sub(C("PW"), k, 128, 8), sub(C("ID"), k, 128, 8), float(2 ** k), AL.mult)
+    pe([(pb(7, 0, 8), C("PW"), Zs("lo8"))]); cp(Zs("pow"), pb(7, 0, 8)); zmake("id", [(1, 1), (2, 32)])
+    ts(C("I8"), C("ID"), 8.0, AL.mult); ts(C("NID"), C("ID"), -1.0, AL.mult); ts(C("IDK"), C("ID"), 1.0 / 1024, AL.mult)
+    RC1, WX = S("COL", 7, 8), S("COL", 11, 12)
+    ts(RC1, RC, 1.0, AL.add); ts(sub(t0, 0, 1), RC, 7.5, AL.is_gt, -16384.0, AL.mult); ts(sub(t1, 0, 1), RC, 7.5, AL.is_lt, RC, AL.mult)
+    tt(WX, sub(t0, 0, 1), sub(t1, 0, 1), AL.add); ts(Zs("idx"), B8c, WX, AL.mult, flex=False)
+    iota(S("QS"), [[1, 4], [4, 16]], 0); ts(sub(t0, 0, 1), RC, 4.0, AL.mult, 1024.0, AL.add); ts(sub(JG, 0, 4), S("IO", 0, 4), sub(t0, 0, 1), AL.add)
+    ms(S("ENC"), 2048.0); ms(C("FK"), 0.0)
+    for c, z in ((0, "lo8"), (4, "lo8"), (5, "pow")): cp(sub(C("FK"), c, 128, 16), Zs(z))
+    ts(sub(t0, 0, 1), RC, 0.5, AL.is_gt); ts(C("KS"), C("ID"), sub(t0, 0, 1), AL.mult); ts(S("CT", 15, 16), M0, 1000.0, AL.mult)
+    tag[0] = "ends"
+    ms(S("ZF"), 0.0); iota(VW, [[0, 8], [16, 64]], 0); ts(VW, VW, RC, AL.add)
     ts(S("W6"), VW, -1.0, AL.mult, 1039.0, AL.add)
     tt(S("OH", 0, 512), S("RAW", 0, 512), VW, AL.is_gt); ts(S("SC", 0, 512), S("RAW", 512, 1024), 0.0, AL.is_lt); tt(S("INW", 16, 528), S("SC", 0, 512), S("W6"), AL.mult)
-    ts(C("I2176"), C("ID"), 2176.0, AL.mult)
-    pe([(pb(6), C("I2176"), S("OH", 0, 512)), (pb(6), C("NID"), S("INW", 16, 528))])
-    tt(S("W6"), pb(6), S("RAW", 512, 1024), AL.add)
-    EO = S("SU", 128, 640); ts(EO, S("W6"), 1040.0, AL.add)
-    EW = S("OV", 0, 5392)
-    dma("y", [(T["OV"][:, 1024 * k:1024 * k + 1024], T["ZER"][:, :]) for k in range(1, 6)], [S("ZER")], [S("OV", 1024, 6144)], 6000)
+    ts(C("I136"), C("ID"), 136.0, AL.mult); ts(C("N4080"), C("ID"), -4080.0, AL.mult)
+    pe([(pb(6), C("I136"), S("OH", 0, 512)), (pb(6), C("NID"), S("INW", 16, 528)), (pb(6), C("N4080"), S("SC", 0, 512))])
+    ts(S("WI"), S("RAW", 512, 1024), 4, AL.arith_shift_right); ts(S("W6"), S("WI"), -4351.0, AL.mult, 1040.0, AL.add)
+    ts(pb(7), S("RAW", 512, 1024), 272.0, AL.mult, flex=False); tt(S("W6"), pb(7), S("W6"), AL.add); tt(pb(6), pb(6), S("W6"), AL.add)
+    EO = S("SU", 128, 640); ts(EO, pb(6), 0.0, AL.add)
+    dma("y", [(T["GA"][0:128:16, 1024:5392], T["ZF"][:, :])], [S("ZF")], [S("GA", 1024, 5392)], 2500)
+    tag[0] = ""
     dma("y", [(T["X"][:, a:b], T["ZER"][:, 0:b - a]) for a, b in ((2192, 3216), (3216, 4240), (4240, 5136))], [S("ZER")], [S("X", 2192, 5136)], 5000)
-    ms(S("MO"), 15.0)
+    dma("y", [(T["OV"][:, 1024 * k:1024 * k + 1024], T["ZER"][:, :]) for k in range(8)], [S("ZER")], [S("OV", 0, 8192)], 9000)
 
     def zero_ov():
-        dma("y", [(T["OV"][:, 1024 * k:1024 * k + 1024], T["ZER"][:, :]) for k in range(8)], [S("ZER")], [S("OV", 0, 8192)], 9000)
+        dma("y", [(T["OV"][c:128:16, 0:8192], T["ZER"][:, 0:512]) for c in (1, 2, 7, 8)], [S("ZER")], [S("OV", 0, 8192)], 4000)
 
     def ends():
-        for k in range(16): cp(IND(EW, sub(EO, 32 * k, 32 * k + 32)), S("IDB", 512 * (k % 2), 512 * (k % 2) + 512))
-        for s_, L in enumerate(("EA", "EB")):
-            ext(pb(6 + s_, 0, 136), [("id", S("OV", 1040 + 2176 * s_, 3216 + 2176 * s_))], 2176)
-            ts(S(L, 0, 136), pb(6 + s_, 0, 136), 15.0, AL.add)
-        zero_ov()
-    for n in ("P", "M"): ms(S(n, 0, 15), 0.0); ms(S(n, 15, 16), 204800.0)
-    ts(S("UT", 15, 16), M0, 255.0, AL.mult)
-    asel(Zs("en"), B8c, [[-16, 8]], AL.is_ge, 0, -8); ts(Zs("pown"), Zs("pow"), -1.0, AL.mult)
+        tag[0] = "ends"
+        for k in range(16): put(IND(S("GA"), sub(EO, 32 * k, 32 * k + 32)), S("IO", 32 + 512 * (k % 2), 544 + 512 * (k % 2)))
+        dma("y", [(T["W6"][:, 0:272], T["GA"][0:128:16, 1040:5392])], [S("GA", 1040, 5392)], [S("W6", 0, 272)], 2500)
+        for s_, L in enumerate(("EA", "EB")): ts(S(L, 0, 136), S("W6", 136 * s_, 136 * s_ + 136), -15.8, AL.add, 15.0, AL.max)
+    for n in ("P", "M"): ms(S(n, 0, 15), 0.0); ms(S(n, 15, 16), 1000.0)
+    asel(Zs("en"), B8c, [[-16, 8]], AL.is_ge, 0, -8)
     asel(C("LT"), C("BLK"), [[16, 8], [1, 16]], AL.is_gt, 0, 0, -1)
     iota(DGO, [[16, 64]], 129); ts(DGO, DGO, RC, AL.add)
     for k in range(8): ms(sub(C("P2"), k, 128, 8), float(2 ** (11 - k)))
-    aff("SB0", 0, 1000, 0, C("P2")); aff("SB1", 1000, -1000, 0, C("P2")); aff("FB0", 4, 1000, 0); aff("FB1", 1004, -1000, 0)
+    aff("FB0", 4, 1000, 0); aff("FB1", 1004, -1000, 0)
+    for n, off in (("ha", 16), ("hb", 23)): ts(Zs(n), Zs("lo8"), -2.0, AL.mult); ts(Zs(n, None, off), Zs("en"), -2.0, AL.mult)
+    x4 = S("IO", 0, 8, 2); ts(sub(t0, 0, 4), x4, RC, AL.is_equal); ts(sub(t1, 0, 4), x4, 9.0, AL.add, RC, AL.is_equal)
+    tt(sub(t0, 8, 12), sub(t0, 0, 4), sub(t1, 0, 4), AL.add); ts(sub(t1, 8, 12), sub(t0, 8, 12), -8.0, AL.mult, -1.5, AL.add)
+    for jj in range(4): ts(S("TH", 128 * jj, 128 * jj + 128), ONE, sub(t1, 8 + jj, 9 + jj), AL.mult, flex=False)
     asel(C("B8"), ONE, [[-8, 16], [0, 8]], AL.is_ge, 0, 0); asel(C("B8"), C("B8"), [[8, 16], [0, 8]], AL.is_ge, 0, 7, -1)
     asel(C("L8"), C("B8"), [[16, 8], [1, 16]], AL.is_gt, 0, 0, -1); asel(C("L8"), C("L8"), [[-1, 128]], AL.not_equal, -16, 0)
     made = set()
@@ -327,12 +346,10 @@ def program(ops, T, nxt, prv):
         b, d = i // 16, i % 16
         for x, (n, src, w) in enumerate((("R%d%d" % (b, j // 2), 8 * (j % 2) + k, 8.0), ("T%d%d" % (b, k // 2), 8 * (k % 2) + j, 1.0), ("D%d" % b, d, (8 * j + k) / 128.0))):
             if n not in made: ms(C(n), 0.0); made.add(n)
-            if x == 1: poke(sub(C(n), d, 128, 16), src, w)
-            else: ts(sub(C(n), d, 128, 16), sub(C("ID"), src, 128, 16), w, AL.mult)
+            ts(sub(C(n), d, 128, 16), sub(C("ID"), src, 128, 16), w, AL.mult)
     tt(C("LW"), C("LT"), C("BLK"), AL.subtract)
     asel(C("LS"), C("LW"), [[-1, 128]], AL.not_equal, 512, 0); asel(C("LW"), C("LW"), [[-1, 128]], AL.not_equal, 1024, 0)
     ts(C("EN2K"), C("FN1"), 2048.0, AL.mult)
-    iota(S("IO"), [[1, 1024]], 0); cp(S("IOB"), S("IO", 0, 128))
     cp(Zs("all"), B8c); ts(Zs("8k"), B8c, 8192.0, AL.mult)
     zmake("om", [(5, 1)]); ts(Zs("l17"), Zs("lo8"), 1024.0, AL.mult); zmake("l17", [(0, 0)])
     ms(C("D12"), 0.0); poke(sub(C("D12"), 1, 128, 16), 1, 1); poke(sub(C("D12"), 2, 128, 16), 2, 1)
@@ -350,160 +367,169 @@ def program(ops, T, nxt, prv):
     ts(S("KP"), S("WJ", 0, 256), 0.0, AL.is_equal); pe([(pb(7, 0, 256), C("GE8"), S("KP"))])
     for n in range(8): ts(S("LUT", 256 * n, 256 * n + 256), pb(7, 0, 256), float(n), AL.is_gt)
     aff("FE0", 8, 1000, 1); aff("FE1", 1008, -1000, 1); aff("DUPE", 8, 0, 1)
-    zmake("k4", [(0, 4096)]); ts(C("INT"), C("ID"), 4096.0, AL.mult)
-    for r in (0, 1, 14, 15): poke(sub(C("INT"), r, 128, 16), r, 0)
     for h in range(2):
         m = 320 * h; pe([(pb(6 + h, 0, 320), Yc(0, 7), S("LO", m, m + 320)), (pb(6 + h, 0, 320), Yc(0, 8), S("HI", m, m + 320))]); mv(S("NAM", m, m + 320), pb(6 + h, 0, 320))
     ms(C("NEG"), -1.0); aff("NDUPE", 8, 0, 1, C("NEG"))
     for s_ in range(4):
         for ha in range(2): aff("NP%d%d" % (s_, ha), 8 * ha + 2 * s_, 1, 0, C("NEG"))
+        tt(C("VB%d" % s_), C("DUP"), C("NP%d0" % s_), AL.subtract)
     for ha in range(2): tt(C("SH%d" % ha), C("FN%d" % ha), C("FE%d" % ha), AL.add); ts(C("SH%d" % ha), C("SH%d" % ha), 8192.0, AL.mult)
     ts(C("NDUPE"), C("NDUPE"), 1.0 / 8192, AL.mult)
     for s_ in range(4): ts(C("NQ%d" % s_), C("NP%d1" % s_), 1.0 / 8192, AL.mult)
 
-    OK_, DG, M1, A1F, BF_, CH, R1, CON, TG1, TG2, RK, LB1, LB2, GG = [sf(64) for _ in range(14)]
-    MI, AI, LI, HI_, XI, NI, KI = [si(64) for _ in range(7)]
-    BB, LOB, HIB, SELF, SS, INB, RK1, CB, LP, LM = [sh(64) for _ in range(9)] + [S("LM")]
+    OK_, M1, CH, NCH, TG1, TG2, TG3, TG4, LB1, LB2, GG, G4 = [sf(64) for _ in range(12)]
+    MI, AI, BI = [si(64) for _ in range(3)]
+    SELF, INB, RK1, CB, CON, BB = [sh(64) for _ in range(6)]
     E = {"nxt": nxt, "prv": prv, "zero_ov": zero_ov}
     for k, w in (("ci", 40), ("c4", 40), ("yi", 40), ("hk", 80), ("vl", 40), ("rr", 80), ("w0", 64), ("w1", 64)): E[k] = si(w)
-    for k in ("c2", "i2", "r2", "u2", "t2", "t3"): E[k] = sf(80)
+    for k in ("c2", "i2", "u2", "t2", "t3"): E[k] = sf(80)
     for k in ("q0", "q1", "q2", "q3"): E[k] = sf(128)
-    A1H = S("S16")
-    AL_, GTL, SPL, GOL, UL, CSL, CWL, I2, EXL, LUL, OVL, STL, SCL, SXL, SRL = [S("L" + k) for k in LISTS]
+    A1H, A1G, LP, LM = [S("S16", 64 * i, 64 * i + 64) for i in range(4)]
+    IDR, E2 = S("S16", 256, 384), S("S16", 384, 512)
+    AL_, MKL, SPL, GOL, UL, CSL, CWL, I2, EXL, LUL, OVL, STL, SCL, SXL, SRL, GQL, QL = [S("L" + k) for k in LISTS]
     RTW, XW = S("RT"), S("X")
 
-    def hop(tab, z, order, extra, t):
-        for i in range(0, 16, 2):
-            r = order[i]
-            mv(S("G1", 512 * r, 512 * r + 1024), IND(tab, S("LN", 32 * r, 32 * r + 64)), None, HQ_[t][z == "lab"][i // 2])
-            pe([(pb(0), Zs(z, x), S("G1", 512 * x, 512 * x + 512)) for x in (r, r + 1)] + (extra if i == 0 else []), i == 0, i == 14, "hop")
+    def hop():
+        w = HOPW[0]
+        for r in range(16):
+            for a in range(512 * r, 512 * r + 512, w): mv(S("G1", a, a + w), IND(S("KT"), S("LN", a // 16, (a + w) // 16)))
+            pe([(pb(0), Zs("key", r), S("G1", 512 * r, 512 * r + 512))], r == 0, r == 15)
 
     def fold(out, f, src, a, n):
         pe([(out, C(f + "0"), S(src, a, a + n, 2)), (out, C(f + "1"), S(src, a + 1, a + n, 2))])
 
     def part_a(t):
+        tag[:] = ["a", t]
         for h in range(2):
             a, b, k = 512 * h, 512 * h + 512, 3 * h
             pe([(pb(k), C("ID"), S("IDB", a, b))] + [(pb(k, 64 * r, 64 * r + 64), Yc(8 * h + r, 0), INEL) for r in range(8)], True, False)
-            pe([(pb(k), Zs("lo8", 0), S("FL", a, b))], False, True)
+            pe([(pb(k), C("FK"), S("FL", a, b))], False, True)
             mv(S("KT", 16 + a, 16 + b), pb(k))
             fold(pb(1 + h, 0, 256), "FN", "RTH", a, 512); ts(S("LN", 256 * h, 256 * h + 256), pb(1 + h, 0, 256), 15.0, AL.add)
         extc(pb(3, 0, 64), "lo8", S("FL"), [(pb(3, 0, 64), C("ID"), INEL)])
-        ts(DG, pb(3, 0, 64), 256.0, AL.mult); ts(TG1, DG, 8.0, AL.mult); tt(OK_, TG1, V1, AL.add)
-        hop(S("KT"), "key", list(range(16)), [], t)
+        ts(TG1, pb(3, 0, 64), 2048.0 * 256, AL.mult); tt(OK_, TG1, V256, AL.add)
+        for h in range(2): pe([(pb(1 + h), C("DUP"), S("RTH", 512 * h, 512 * h + 512))]); mv(S("RT", 16 + 512 * h, 528 + 512 * h), pb(1 + h))
+        hop()
         scan(S("W5"), S("RST"), pb(0), 0.0, AL.add, AL.min)
-        tt(M1, S("W5", 7, 512, 8), OK_, AL.min); ts(MI, M1, 32768.0, AL.min); ts(AI, MI, 2047, AL.bitwise_and)
+        tt(M1, S("W5", 7, 512, 8), OK_, AL.min); ts(MI, M1, 128.0, AL.add, float(2 ** 23), AL.min); ts(AI, MI, 8, AL.arith_shift_right, 2047, AL.bitwise_and)
         ts(AL_, AI, 15.0, AL.add)
         tt(S("GB"), IND(RTW, AL_), S("U1J"), AL.is_equal)
-        ts(LI, MI, 31, AL.bitwise_and); cp(LOB, LI); ts(HI_, MI, 5, AL.arith_shift_right, 63, AL.bitwise_and); cp(HIB, HI_)
-        cp(A1H, AI); tt(SELF, AI, V1, AL.is_equal)
-        ext(pb(3, 0, 64), [("pow", S("GB"))], 1024); cp(BB, pb(3, 0, 64))
+        cp(A1H, AI); tt(SELF, AI, V1, AL.is_equal); ts(BI, MI, 255, AL.bitwise_and); ts(BB, BI, -1.0, AL.mult)
         for h in range(2):
-            pe([(pb(1 + h), C("ID"), S("ZER", 0, 512))] + [(blk(1, r), Yc(r, c), x) for r in range(8 * h, 8 * h + 8) for c, x in ((1, LOB), (2, HIB))], True, False)
-        for h in range(2):
-            pe([(blk(1, r), Yc(r, 0), BB) for r in range(8 * h, 8 * h + 8)], False, True)
-            mv(S("HT", 16 + 512 * h, 528 + 512 * h), pb(1 + h), M3)
+            pe([(pb(4 + h), C("KS"), S("KT", 16 + 512 * h, 528 + 512 * h))] + [(blk(4, r), Yc(r, 5), BB) for r in range(8 * h, 8 * h + 8)], True, False)
+        ts(LB1, AI, -1000.0, AL.add, flex=False); ts(LB2, AI, -1.0, AL.mult, -1000.0, AL.add, flex=False)
+        tag[0] = "spk"
         w2r(1, [(Al, lambda r: A1H)])
 
         def f(h, a, b):
             tt(S("EQ", a, b), pb(1 + h), S("RT", 16 + a, 16 + b), AL.is_equal)
-            mv(S("MT", 16 + 1024 * t + a, 16 + 1024 * t + b), pb(1 + h), -1.0)
-            pe([(pb(1 + h), C("DUP"), S("EQ", a, b))] + [(blk(1, r), Al(r), SELF) for r in range(8 * h, 8 * h + 8)])
-            tt(S("D2", a, b), pb(1 + h), S("RT", 16 + a, 16 + b), AL.mult)
+            pe([(pb(1 + h), C("ID"), S("EQ", a, b))] + [(blk(1, r), Al(r), SELF) for r in range(8 * h, 8 * h + 8)])
+            tt(S("D2", a, b), pb(1 + h), S("RTH", a, b), AL.mult)
         halves(f)
-
-        hop(S("HT"), "lab", list(range(16)), [(pb(0, k, 512, 8), C("N8K"), A1H) for k in range(8)], t)
-        extc(pb(4, 0, 64), "en", S("D2")); ts(SPL, pb(4, 0, 64), 2063.0, AL.add, 4111.0, AL.min)
-        mv(S("XS"), IND(XW, SPL))
-        ts(S("W5"), pb(0), 0.0, AL.max, 4096.0, AL.min); scan(S("W6"), S("RS1"), S("W5"), 0.0, AL.mult, AL.add)
-        cp(XI, S("W6", 7, 512, 8)); ts(NI, XI, 3840, AL.bitwise_and)
-        tt(TG1, NI, DG, AL.is_equal); tt(CH, TG1, SELF, AL.mult)
+        extc(pb(1, 0, 64), "en", S("D2")); ts(SPL, pb(1, 0, 64), 2063.0, AL.add, 4111.0, AL.min)
+        for h in range(2): mv(S("XS", 512 * h, 512 * h + 512), IND(XW, sub(SPL, 32 * h, 32 * h + 32)))
+        tag[0] = "a"
+        pe([(pb(3, 0, 64), C("I8"), A1H)] + [(pb(3, 0, 64), Zs("idx", r), S("GB", r, 1024, 16)) for r in range(16)])
+        tt(TG1, pb(3, 0, 64), JK, AL.min); ts(MKL, TG1, 16376.0, AL.add)
+        cp(IND(S("G1"), MKL), S("ZER"))
+        if MARK[0]:
+            dma("y", [(T["IT"][:, 16:528], T["G1"][3:128:16, 0:8192])], [S("G1", 0, 8192)], [S("IT", 16, 528)], 2300)
+            pe([(pb(3, 0, 64), C("NID"), SELF)] + [(pb(3, 0, 64), C("ID"), S("IT", 16 + k, 528, 8)) for k in range(8)])
+        else:
+            for r0 in range(0, 16, 4):
+                pe(([(pb(3, 0, 64), C("NID"), SELF)] if r0 == 0 else []) +
+                   [(pb(3, 0, 64), Yc(3, r), S("G1", 512 * r + k, 512 * r + 512, 8)) for r in range(r0, r0 + 4) for k in range(8)], r0 == 0, r0 == 12)
+        ts(CH, pb(3, 0, 64), -1.0, AL.is_equal); ts(NCH, pb(3, 0, 64), -1.0, AL.not_equal, 1000.0, AL.mult)
         scan(INB, S("ONE", 0, 64), CH, 0.0, AL.mult, AL.add)
-        pe([(pb(3, 0, 1), C("LT"), sub(INB, 63, 64))])
-        ts(TG1, CH, 0.0, AL.is_equal); tt(TG2, TG1, V769, AL.mult); tt(TG1, TG2, INB, AL.add); ts(GTL, TG1, pb(3, 0, 1), AL.add)
-        ms(S("WW", 0, 144), 0.0); put(IND(S("WW"), GTL), S("U1J")); cp(S("TG2"), S("WW", 1, 129))
-        ts(R1, INB, pb(3, 0, 1), AL.add); ts(TG1, R1, 128.5, AL.is_lt); tt(CON, TG1, CH, AL.mult); tt(RK1, R1, CON, AL.mult)
-        ext(pb(3, 0, 8), [("c0", S("TG2"))], 128); ts(GOL, pb(3, 0, 8), 15.0, AL.add)
+        off = pb(3, 0, 1); pe([(off, C("LT"), sub(INB, 63, 64))])
+        tt(TG2, INB, NCH, AL.add); ts(RK1, TG2, off, AL.add); ts(CON, RK1, 128.5, AL.is_lt)
+        for h in range(2):
+            pe([(blk(4, r), Yc(r, 0), RK1) for r in range(8 * h, 8 * h + 8)], False, True)
+            mv(S("CT", 16 + 512 * h, 528 + 512 * h), pb(4 + h))
+        x0, x1, x2, x3 = [sub(G4, 8 * i, 8 * i + 4) for i in range(4)]
+        tt(x0, sub(INB, 0, 64, 16), sub(CH, 0, 64, 16), AL.subtract); tt(x1, x0, sub(INB, 15, 64, 16), AL.is_equal)
+        tt(x2, x1, sub(JG, 0, 4), AL.mult); tt(x3, x2, x0, AL.add); ts(GQL, x3, off, AL.add)
+        QR, E1 = S("QR", 0, 128), S("QR", 128, 256)
+        ms(S("G1", 0, 128), 0.0); cp(IND(S("G1", 0, 1920), GQL), S("QS")); scan(QR, S("G1", 0, 128), S("G1", 0, 128), 0.0, AL.max, AL.max)
+        ext(pb(3, 0, 8), [("c0", QR)], 128); cp(QL, pb(3, 0, 8)); ts(IDR, QR, 16.0, AL.mult, RC1, AL.add)
+        ext(pb(4, 0, 64), [("c0", S("CT", 16, 1040))], 1024); cp(S("RKW"), pb(4, 0, 64))
+        tt(E1, IND(S("RKW"), QL), S("IO", 1, 129), AL.is_equal); tt(E2, E1, IDR, AL.mult)
+        ext(pb(3, 0, 8), [("all", E2)], 128); ts(GOL, pb(3, 0, 8), 15.0, AL.add)
         cp(S("G0"), IND(RTW, GOL))
-        fold(pb(3, 0, 64), "FN", "G0", 0, 128); pe([(pb(3, 128, 256), C("DUP"), S("G0"))])
-        ts(UL, pb(3, 0, 64), 15.0, AL.add)
+        fold(pb(3, 0, 64), "FN", "G0", 0, 128); ts(UL, pb(3, 0, 64), 15.0, AL.add)
         ts(TG2, CON, 16.0, AL.mult); tt(INEL, INEL, TG2, AL.add)
-        w2r(4, [(lambda r: Yc(r, 0), lambda r: RK1)])
-        halves(lambda h, a, b: mv(S("CT", 16 + a, 16 + b), pb(4 + h)))
-        mv(S("GC"), IND(S("CT"), AL_)); ext(pb(4, 0, 64), [("c0", S("GC"))], 1024)
-        cp(RK, pb(4, 0, 64)); ts(CB, RK, 0.0, AL.is_gt); tt(GG, CB, SELF, AL.is_gt)
-        ts(LB1, RK, -200.0, AL.add); tt(LB2, LB1, GG, AL.mult); ts(LP, LB2, 200.0, AL.add, 1024.0, AL.mult)
-        ts(LB1, RK, -1.0, AL.mult, -200.0, AL.add); tt(LB2, LB1, GG, AL.mult); ts(LM, LB2, 200.0, AL.add, 1024.0, AL.mult)
-        w2r(4, [(Al, lambda r: CB)])
-        halves(lambda h, a, b: tt(S("T1", a, b), pb(4 + h), S("D2", a, b), AL.mult))
-        tag[0] = "ends"
-        if t == 0: ends()
+        tag[0] = "lab"
+        for h in range(2): mv(S("GC", 512 * h, 512 * h + 512), IND(S("CT"), sub(AL_, 32 * h, 32 * h + 32)))
+        ext(pb(5, 0, 64), [("c0", S("GC"))], 1024)
+        ts(CB, pb(5, 0, 64), 128.5, AL.is_lt); tt(GG, CB, SELF, AL.is_gt)
+        tt(LP, LB1, GG, AL.mult); tt(LM, LB2, GG, AL.mult)
+        w2r(1, [(Al, lambda r: CB)])
+        halves(lambda h, a, b: tt(S("D2", a, b), pb(1 + h), S("D2", a, b), AL.mult))
+        spokes()
+
+    def spokes():
         tag[0] = "pm"
-        for b0, tab, lab in ((4, "P", LP), (4, "M", LM)):
-            w2r(b0, [(lambda r: C("ID"), lambda r: S("XS", r, 1024, 16)), (Al, lambda r, lab=lab: lab)])
-            halves(lambda h, a, b, b0=b0, tab=tab: mv(S(tab, 16 + a, 16 + b), pb(b0 + h)))
+        for b0, tab, lab in ((4, "P", LP), (MBK[0], "M", LM)):
+            w2r(b0, [(Al, lambda r, lab=lab: lab), (lambda r: C("IDK"), lambda r: S("XS", r, 1024, 16))])
+            halves(lambda h, a, b, b0=b0, tab=tab: mv(S(tab, 16 + a, 16 + b), pb(b0 + h), 1000.0))
 
     def part_b(t):
-        tag[0] = ""
-        for h in range(2):
-            a, b = 512 * h, 512 * h + 512
-            pe([(pb(1 + h), C("ID"), S("IDB", a, b)), (pb(1 + h), Zs("pown", 5), S("EQ", a, b))] +
-               [(pb(1 + h, x, x + 384), Zs(z, c), S("FL", a + x, a + x + 384)) for x in (128 - 128 * h,) for z, c in (("lo8", 4), ("pow", 5))], True, False, "ut%d" % h)
-        if t:
-            pe([(pb(7), C("INT"), S("ONE"))], True, False)
-            for h in range(2): pe([(pb(7), Zs("k4", r), S("SRG", 512 * i, 512 * i + 512)) for i, r in list(enumerate((14, 15, 0, 1)))[2 * h:2 * h + 2]], False, h == 1)
-            tt(S("W6"), pb(7), S("W5"), AL.min); scan(S("WW", 0, 512), S("RS1"), S("W6"), 0.0, AL.mult, AL.add); cp(XI, S("WW", 7, 512, 8))
-        ts(KI, XI, 255, AL.bitwise_and); tt(SS, KI, BB, AL.add)
-        for h in range(2):
-            pe([(pb(1 + h, 384 * h, 384 * h + 128), Zs(z, c), S("FLS", 128 - 128 * h, 256 - 128 * h)) for z, c in (("lo8", 4), ("pow", 5))] +
-               [(blk(1, r), Yc(r, 0), SS) for r in range(8 * h, 8 * h + 8)], False, True, "ut%d" % h)
-            mv(S("UT", 16 + 512 * h, 528 + 512 * h), pb(1 + h))
+        tag[:] = ["b", t]
+        for h, a in enumerate((896, 0) if t else ()):
+            p = pb(6 + h, 0, 128)
+            pe([(p, C("ID"), S("IDB", a, a + 128))] + [(sub(p, 64 * i, 64 * i + 64), Yc(a // 64 + i, 5), BB) for i in range(2)], True, False)
+            pe([(p, C("FK"), S("FLS", 128 * h, 128 * h + 128))], False, True); mv(S("CT", 16 + a, 144 + a), p)
         tag[0] = "edge"
-        n = 2176 + 640 * t; nch = -(-n // 512); w = -(-n // (32 * nch)) * 32
+        n = 2176 + 640 * t; nch = -(-n // EDW[0]); w = -(-n // (32 * nch)) * 32
         for i, a in enumerate(range(0, n, w)):
-            b = min(n, a + w); k = i % 2; ga, zz = S("GA", 512 * k, 512 * k + b - a), S("ZZ", 512 * k, 512 * k + b - a)
+            b = min(n, a + w); k = i % 2; ga, zz = S("GA", 16 + a, 16 + b), S("ZZ", 512 * k, 512 * k + b - a)
             act(ga, IND(S("P"), S("EA", a // 16, b // 16)), AF.Copy)
             tt(zz, IND(S("M"), S("EB", a // 16, b // 16)), ga, AL.add)
             z, x = pb(4 + k, 0, b - a), S("X", 16 + a, 16 + b)
             if i % EDGE[t] == 0:
-                act(z, zz, AF.Abs); tt(S("WN", a, b), z, x, AL.is_lt); tt(x, z, x, AL.min)
+                act(z, zz, AF.Abs, 0.0, 1024.0); tt(S("WN", a, b), z, x, AL.is_lt); tt(x, z, x, AL.min)
             else:
-                zb = S("ZB", 512 * k, 512 * k + b - a); act(zb, zz, AF.Abs)
+                zb = S("ZB", 512 * k, 512 * k + b - a); act(zb, zz, AF.Abs, 0.0, 1024.0)
                 pe([(z, C("ID"), x), (z, C("NID"), zb)]); act(zb, z, AF.Relu)
                 ts(S("WN", a, b), zb, 0.0, AL.is_gt); pe([(z, C("ID"), x), (z, C("NID"), zb)]); mv(x, z)
-        q = n // 16; cnt = pb(4, 0, q); ext(cnt, [("all", S("WN"))], n)
-        f, d = S("CF", 0, q), S("CF", 256, 256 + q)
-        ts(f, cnt, 8.5, AL.is_gt); ts(d, S("EA", 0, q), float(1024 * t), AL.add); tt(S("CF", 512, 512 + q), d, S("MO", 0, q), AL.subtract)
-        tt(d, S("CF", 512, 512 + q), f, AL.mult); tt(S("MO", 0, q), S("MO", 0, q), d, AL.add)
-        tag[0] = ""
-        for h in range(2): mv(S("GU", 512 * h, 512 * h + 512), IND(S("UT"), sub(UL, 32 * h, 32 * h + 32)), None, "vs"[h])
-        act(S("IT", 16, 1040), IND(S("UT"), UL), AF.Copy)
+        tag[0] = "b"
+        cp(S("GR"), IND(RTW, UL))
+        for h in range(2): mv(S("IT", 16 + 512 * h, 528 + 512 * h), IND(S("CT"), sub(UL, 32 * h, 32 * h + 32)))
         J = lambda x, jj: sub(x, 128 * jj, 128 * jj + 128)
-        gu = lambda jj, h: S("GU", 2 * jj + h, 1024, 8)
-        pe([(J(pb(0), jj), C("SB%d" % h), gu(jj, h)) + ((1,) if h == 0 else ()) for jj in range(4) for h in range(2)])
-        cp(S("WI"), pb(0)); ts(S("WJ"), S("WI"), 2048, AL.bitwise_and)
-        for jj in range(4): tt(J(S("WB"), jj), pb(3, 128, 256), J(S("WJ"), jj), AL.is_gt)
+        gu = lambda jj, h: S("IT", 16 + 2 * jj + h, 1040, 8)
+        FG = S("QR", 0, 128); ts(FG, S("G0"), 0.0, AL.is_gt)
+        pe([(pb(0), C("ID"), S("TH"))] + [(J(pb(0), jj), C("VB%d" % jj), FG) for jj in range(4)], True, False)
+        for i in range(4):
+            p, he = pb((3, 1, 2, 6)[i]), S("HE", 512 * i, 512 * i + 512)
+            pe([(J(p, x), C("NP%d0" % s), S("G0")) for x, (j, s) in enumerate(BLOCKS[4 * i:4 * i + 4])], True, False)
+            pe([(J(p, x), C("ID"), S("GR", j, 1024, 8)) for x, (j, s) in enumerate(BLOCKS[4 * i:4 * i + 4])], False, True)
+            if HAS[0][i] == "v": ts(he, p, 0.0, AL.is_equal)
+            elif HAS[0][i] == "s": act(he, p, AF.Abs); act(he, he, AF.Relu, 1.0, -1.0)
+            else: act(he, p, AF.Abs); ts(he, he, 0.0, AL.is_equal)
+            pe([m for x, (j, s) in enumerate(BLOCKS[4 * i:4 * i + 4])
+                for m in [(J(pb(0), j // 2), Zs("ha", 8 * (j % 2) + 2 * s), J(he, x)), (J(pb(0), s), Zs("hb", j), J(he, x))]], False, i == 3)
+        ts(S("WB"), pb(0), 0.0, AL.is_gt)
         pe([m for jj in range(4) for m in [(J(pb(0), jj), C("FB0"), gu(jj, 0), 1), (J(pb(0), jj), C("FB1"), gu(jj, 1)), (J(pb(0), jj), C("L8"), J(S("WB"), jj))]])
-        act(S("R"), pb(0), AF.Relu, -7.0 / 8192, -1.0 / 8192)
-        tr = lambda n, p, b: [(J(p, b), C("%s%d%d" % (n, b, x)), J(S("R"), x)) for x in sorted(set(PAIRS[i][n == "T"] // 2 for i in range(16 * b, min(28, 16 * b + 16))))]
+        ts(S("PR"), pb(0), -7.5, AL.is_lt); act(S("R"), pb(0), AF.Relu, -7.0 / 8192, -1.0 / 8192)
+        tr = lambda n, p, b, src: [(p, C("%s%d%d" % (n, b, x)), J(S(src), x)) for x in sorted(set(PAIRS[i][n == "T"] // 2 for i in range(16 * b, min(28, 16 * b + 16))))]
         grp = lambda l: [m + ((1,) if i == 0 else ()) for i, m in enumerate(l)]
-        pe(grp(tr("R", pb(0), 0)) + grp(tr("R", pb(0), 1))); pe(grp(tr("T", pb(3), 0)) + grp(tr("T", pb(3), 1)))
-        mv(S("WB", 0, 256), pb(0, 0, 256)); tt(S("PR", 0, 256), pb(3, 0, 256), S("WB", 0, 256), AL.mult)
-        for b in range(2): ts(S("SV", b, 256, 2), J(S("PR"), b), 0.0, AL.is_gt)
+        pe([m for b in range(2) for m in grp(tr("R", pb(3, b, 256, 2), b, "PR") + tr("T", pb(3, b, 256, 2), b, "PR"))])
+        ts(S("SV", 0, 256), pb(3, 0, 256), 8.5, AL.is_gt)
         pe([(pb(3, 0, 256), C("BLK"), S("SV", 0, 256))]); scan(S("INW", 16, 272), S("ONE", 0, 256), pb(3, 0, 256), 0.0, AL.mult, AL.add)
-        ext(pb(3, 0, 16), [("c0", S("INW", 15, 271))], 256); ext(pb(3, 16, 32), [("c0", S("INW", 16, 272))], 256)
+        z0, z1, z2 = sub(TG3, 0, 16), sub(TG3, 16, 32), sub(TG4, 0, 16)
+        ext(pb(2, 0, 16), [("all", S("SV", 0, 256))], 256); ts(S("SV", 256, 272), pb(2, 0, 16), 0.0, AL.is_equal, 4096.0, AL.mult)
+        pe([(pb(3, 0, 16), Yc(0, r), S("INW", 15 + r, 271, 16)) for r in range(16)] + [(pb(3, 0, 16), C("ID"), S("SV", 256, 272))])
         for b in range(2):
-            p = J(pb(0), b)
-            pe([(p, C("ID"), J(S("WB"), b)), (p, C("D%d" % b), ONE)] + tr("T", pb(0), b) + [(p, C("LW"), S("SV", b, 256, 2)), (p, C("ID"), S("INW", 16 + b, 272, 2))])
-        for b in range(2): act(S("NT", b, 256, 2), J(pb(0), b), AF.Identity, -1025.0 - 2057.0 / 8192)
-        ts(sub(TG1, 0, 32), pb(3, 0, 32), 640.0, AL.min); s0, e0, z0, z1 = sub(TG1, 0, 16), sub(TG1, 16, 32), sub(TG2, 0, 16), sub(TG2, 16, 32)
-        tt(z0, s0, e0, AL.is_equal); tt(z1, z0, sub(DW, 0, 16), AL.mult); tt(z0, z1, s0, AL.max); cp(sub(CSL, 0, 16), z0)
+            p = pb(0, b, 256, 2)
+            pe([(p, C("D%d" % b), ONE)] + tr("R", p, b, "R") + tr("T", p, b, "R") + [(p, C("LW"), S("SV", b, 256, 2)), (p, C("ID"), S("INW", 16 + b, 272, 2))])
+        act(S("NT", 0, 256), pb(0, 0, 256), AF.Identity, -1025.0 - 2057.0 / 8192)
+        ts(z0, pb(3, 0, 16), 639.5, AL.is_gt, 1024.0, AL.mult); tt(z1, pb(3, 0, 16), z0, AL.add); tt(z2, z1, sub(DW, 0, 16), AL.min); cp(sub(CSL, 0, 16), z2)
         iota(S("WW", 0, 640), [[0, 640]], 0); put(IND(S("WW"), sub(CSL, 0, 16)), S("IO", 32, 288))
         scan(S("CW"), S("WW", 0, 640), S("WW", 0, 640), 0.0, AL.max, AL.max)
         ext(pb(3, 0, 40), [("c0", S("CW"))], 640); ts(CWL, pb(3, 0, 40), -32.0, AL.add)
         tt(S("YC"), IND(S("NT", 0, 256), CWL), S("IO", 0, 640), AL.subtract); ts(S("YC"), S("YC"), -0.5, AL.max, 0.5, AL.min)
         ci, c4, yi, hk, vl, rr = E["ci"], E["c4"], E["yi"], E["hk"], E["vl"], E["rr"]
-        c2, i2, r2, u2, t2, t3 = E["c2"], E["i2"], E["r2"], E["u2"], E["t2"], E["t3"]
+        c2, i2, u2, t2, t3 = E["c2"], E["i2"], E["u2"], E["t2"], E["t3"]
         lo, hi = (lambda x: sub(x, 0, 40)), (lambda x: sub(x, 40, 80))
         ts(ci, pb(3, 0, 40), -32.0, AL.add); ts(c4, ci, 254, AL.bitwise_and); ts(lo(c2), c4, 4.0, AL.mult, -3.0, AL.add); ts(hi(c2), c4, 4.0, AL.mult, 1.0, AL.add)
         ext(pb(3, 64, 104), [("8k", S("YC"))], 640); ts(yi, pb(3, 64, 104), 65536.0, AL.add)
@@ -526,21 +552,31 @@ def program(ops, T, nxt, prv):
             pe([(pb(b, 64, 104), Zs("l17", r), S("GL", a + r, a + 640, 16)) for r in range(16)], False, True)
             tt(f_(t2), pb(b, 64, 104), f_(t3), AL.max); ts(f_(OVL), f_(t2), -1.0, AL.add)
             cp(IND(S("OV"), f_(OVL)), S("SRC", a, a + 640))
+        tag[0] = "new"
         ext(pb(0, 128, 208), [("id", S("GI"))], 1280)
         c0 = 136 + 40 * t; um = S("UM", 0, 80)
         for f_, a, b in hs:
             tt(f_(u2), f_(pb(0, 128, 208)), vl, AL.mult); tt(f_(um), f_(u2), vl, AL.add)
         ts(EXL, um, 14.0, AL.add)
         ts(S("EA", c0, c0 + 40), lo(u2), 15.0, AL.add); ts(S("EB", c0, c0 + 40), hi(u2), 15.0, AL.add)
-        ts(lo(r2), vl, float(1024 * t), AL.mult, 15.0, AL.add); tt(S("MO", c0, c0 + 40), lo(r2), lo(u2), AL.add)
-        mv(S("YY"), IND(S("P"), lo(EXL))); tt(S("XB"), IND(S("M"), hi(EXL)), S("YY"), AL.add); ts(S("X", 16 + n, 656 + n), S("XB"), 255.0, AL.min)
+        YY = S("GA", 16 + n, 656 + n)
+        mv(YY, IND(S("P"), lo(EXL))); tt(S("XB"), IND(S("M"), hi(EXL)), YY, AL.add); ts(S("X", 16 + n, 656 + n), S("XB"), 1024.0, AL.mult, 255.0, AL.min)
+        tag[0] = "rows"
         for bk, a, b in ((6, 896, 1024), (7, 0, 128), (1, 128, 512), (2, 512, 896)):
             p = pb(bk, 0, b - a)
-            pe([(p, C("ID"), S("RTH", a, b)), (p, C("NID"), S("T1", a, b))], True, False)
+            pe([(p, C("ID"), S("RTH", a, b)), (p, C("NID"), S("D2", a, b))], True, False)
             pe([(p, sub(C("CV"), 15 - l, 143 - l), S("OV", 1024 * l + a, 1024 * l + b)) for l in range(8)], False, True)
             cp(S("RTH", a, b), p); act(S("FL", a, b), p, AF.Sign)
-            if t < 2: mv(S("RT", 16 + a, 16 + b), p)
         if t < 2: E["zero_ov"]()
+        tag[0] = "mid"
+        dma("y", [(T["GAW"][:, :], T["GA"][0:128:16, 16:4112])], [S("GA", 16, 4112)], [S("GAW")], 2500)
+        y = pb(4, 0, 256); mm = []
+        for r in range(16):
+            a, b, c = 256 * r, min(max(n, 256 * r), 256 * r + 256), min(max(n + 640, 256 * r), 256 * r + 256)
+            if b > a: mm.append((pb(4, 0, b - a), Zs("all", r), S("WN", a, b)))
+            if c > b: mm.append((pb(4, b - a, c - a), Zs("all", r), S("ONE", 0, c - b)))
+        for i in range(0, len(mm), 4): pe(mm[i:i + 4], i == 0, i + 4 >= len(mm))
+        ts(y, y, 8.5, AL.is_gt, 2048.0 * (t + 1), AL.mult); tt(y, y, S("GAW"), AL.add); tt(S("ENC"), y, S("ENC"), AL.max)
 
     def swap(src, dst, w, k):
         def fn(e):
@@ -586,38 +622,41 @@ def program(ops, T, nxt, prv):
         iota(S("SW", 0, 1024), [[0, 1024]], 0); cp(IND(S("SW"), STL), S("IOB"))
         scan(S("SC"), S("SW", 0, 1024), S("SW", 0, 1024), 0.0, AL.max, AL.max)
         ext(pb(6, 0, 64), [("c0", S("SC"))], 1024); cp(SCL, pb(6, 0, 64))
-        tt(S("NE"), IND(S("NUS"), SCL), S("IO"), AL.subtract); ts(S("NE"), S("NE"), -0.5, AL.max, 0.5, AL.min)
+        tt(S("NE"), IND(S("NUS"), SCL), S("IO", 0, 1024), AL.subtract); ts(S("NE"), S("NE"), -0.5, AL.max, 0.5, AL.min)
         ext(pb(7, 0, 64), [("8k", S("NE"))], 1024)
         w0, w1 = E["w0"], E["w1"]; ts(w0, pb(7, 0, 64), 65536.0, AL.add); ts(w1, w0, 8191, AL.bitwise_and)
-        ts(h0(q0), w1, 0.0, AL.is_equal); tt(h0(q1), h0(q0), DX, AL.mult); tt(h0(q2), w1, h0(q1), AL.add); ts(SXL, h0(q2), -1.0, AL.mult, 6159.0, AL.add)
+        tt(h0(q2), w1, DX, AL.max); ts(SXL, h0(q2), -1.0, AL.mult, 6159.0, AL.add)
         mv(sub(SND, 0, 512), IND(XW, sub(SXL, 0, 32)), None, "s"); mv(sub(SND, 512, 1024), IND(XW, sub(SXL, 32, 64)))
-        swap(SND, RX, 512, 4 * t + 2)
+        swap(SND, RX, 512, 4 * t + 2); tag[0] = "cmp"
         GT, SG, MN, GX = S("EQS"), S("OH"), S("SC"), S("SRG")
 
         def f(h, a, b):
             pe([(pb(6 + h), C("ID"), sub(RX, a, b))])
             tt(sub(GT, a, b), pb(6 + h), sub(SND, a, b), AL.is_lt); tt(sub(MN, a, b), pb(6 + h), sub(SND, a, b), AL.min)
-            pe([(pb(6 + h), C("BLK"), sub(GT, a, b))]); act(sub(SG, a, b), pb(6 + h), AF.Sign, 8.5, -1.0)
+            pe([(pb(6 + h), C("BLK"), sub(GT, a, b))])
+            if h:
+                act(S("W6"), pb(6 + h), AF.Identity, 8.5, -1.0); put(IND(S("GA"), sub(SXL, 32, 64)), S("W6"))
+                mv(sub(GX, 1024, 2048), IND(S("GA", 0, 2832 + 640 * t), sub(SRL, 64, 128)))
+            act(sub(SG, a, b), pb(6 + h), AF.Sign, 8.5, -1.0)
             tt(IND(XW, sub(SXL, 32 * h, 32 * h + 32)), sub(MN, a, b), sub(SG, a, b), AL.mult)
+            if not h: mv(sub(GX, 0, 1024), IND(XW, sub(SRL, 0, 64)))
         halves(f)
-        for h in range(2): mv(sub(GX, 1024 * h, 1024 * h + 1024), IND(XW, sub(SRL, 64 * h, 64 * h + 64)))
-        pe([(pb(6, 0, 256), sub(C("KD"), 15 - l, 143 - l), sub(GX, l, 2048, 8)) for l in range(8)])
-        KP = S("KP"); ts(KP, pb(6, 0, 256), 0.0, AL.is_gt)
         for s_ in range(2):
-            k_, a = sub(KP, 128 * s_, 128 * s_ + 128), base[s_]
-            tt(S("RTH", a, a + 128), S("RTH", a, a + 128), k_, AL.mult)
+            k_, a, p = S("KP", 128 * s_, 128 * s_ + 128), base[s_], pb(6 + s_, 0, 128)
+            pe([(p, sub(C("KD"), 15 - l, 143 - l), sub(GX, 1024 * s_ + l, 1024 * s_ + 1024, 8)) for l in range(8)])
+            ts(k_, p, 0.0, AL.is_gt)
             if t < 2: tt(S("RT", 16 + a, 144 + a), S("RT", 16 + a, 144 + a), k_, AL.mult)
+            tt(S("RTH", a, a + 128), S("RTH", a, a + 128), k_, AL.mult)
             tt(S("FLS", 128 * s_, 128 * s_ + 128), S("FL", a, a + 128), k_, AL.mult)
 
     part_a(0)
     for t in range(3):
+        if t == 0: ends()
         part_b(t)
         if t < 2: part_a(t + 1)
         if t == 2:
-            cp(S("MU"), S("MO"))
-            for k, n in enumerate(("WW", "RT", "UT", "IT")):
-                mv(S(n, 16, 1040), IND(S("MT"), S("MU", 64 * k, 64 * k + 64)))
-                dma("y", [(T["ymid"][:, 1024 * k:1024 * k + 1024], T[n][0:128:16, 16:1040])], [S(n, 16, 1040)], [], 2500)
+            cp(S("WI", 256, 512), S("ENC")); ts(S("WJ", 256, 512), S("WI", 256, 512), 2047, AL.bitwise_and); ts(S("GAW"), S("WJ", 256, 512), -1.0, AL.add)
+            dma("y", [(T["ymid"][:, :], T["GAW"][:, :])], [S("GAW")], [], 2500)
         part_c(t)
     for k in range(4):
         a, b = 1024 * k, 1024 * k + 1024
@@ -628,8 +667,114 @@ def program(ops, T, nxt, prv):
         pcs = [(0, 128, S("FLS", 128, 256)), (128, 512, S("FL", 128, 512))] if h == 0 else [(0, 384, S("FL", 512, 896)), (384, 512, S("FLS", 0, 128))]
         pe([(pb(1 + h), C("ID"), S("RTH", a, b))] + [(pb(1 + h, x, y), C("EN2K"), s_) for x, y, s_ in pcs])
         ts(S("TA", a, b), pb(1 + h), -1.0, AL.add)
-    dma("y", [(T["ynb"][g, :], T["GA"][16 * g:16 * g + 8, :]) for g in range(8)], [S("TA")], [], 2500)
-    dma("s", [(T["yen"][g, :], T["GA"][16 * g + 8:16 * g + 16, :]) for g in range(8)], [S("TA")], [], 2500)
+    dma("y", [(T["ynb"][g, :], T["GA"][16 * g:16 * g + 8, 0:1024]) for g in range(8)], [S("TA")], [], 2500)
+    dma("s", [(T["yen"][g, :], T["GA"][16 * g + 8:16 * g + 16, 0:1024]) for g in range(8)], [S("TA")], [], 2500)
+
+
+def polish(ops, fw, res, rng):
+    n = len(ops); anc = [0] * n; jp = []; js = [[] for _ in ops]
+    for i in range(n):
+        cover = 0
+        for j, _ in fw[i]: cover |= anc[j]
+        jp.append([(j, lag) for j, lag in fw[i] if not cover >> j & 1])
+        for j, lag in fw[i]: anc[i] |= anc[j] | 1 << j
+        for j, lag in jp[i]: js[j].append((i, lag))
+    late = [o.get("dma", 0.0) for o in ops]
+    cost = lambda i, q: ops[i].get("cs", ops[i]["cost"]) if q == "s" else ops[i]["cost"]
+    pick = [r[2] for r in res]; dur = [cost(i, pick[i]) for i in range(n)] + [0.0]
+    topo = sorted(range(n), key=lambda i: (res[i][0], i)); pos = [0] * n
+    mp, mn = [n] * (n + 1), [n] * (n + 1); last = {}
+    for k, i in enumerate(topo):
+        pos[i] = k
+        if pick[i] != "x":
+            if pick[i] in last: mp[i] = last[pick[i]]; mn[last[pick[i]]] = i
+            last[pick[i]] = i
+    fin, tail = [0.0] * (n + 1), [0.0] * (n + 1)
+
+    def times(a, b):
+        for i in topo[a:]:
+            s = fin[mp[i]]
+            for j, lag in jp[i]:
+                if fin[j] + lag > s: s = fin[j] + lag
+            fin[i] = s + dur[i]
+        for i in topo[b::-1]:
+            s = tail[mn[i]]
+            if late[i] > s: s = late[i]
+            for k, lag in js[i]:
+                if tail[k] + lag > s: s = tail[k] + lag
+            tail[i] = s + dur[i]
+    head = lambda i: max([fin[j] + lag for j, lag in jp[i]] + [0.0])
+    rest = lambda i: max([tail[k] + lag for k, lag in js[i]] + [late[i]])
+
+    def guess(seq, before, after):
+        s, st = fin[before], []
+        for i, d in seq:
+            s = max(s, head(i)); st.append(s); s += d
+        t, worst = tail[after], 0.0
+        for (i, d), s in zip(seq[::-1], st[::-1]):
+            t = max(t, rest(i)) + d; worst = max(worst, s + t)
+        return worst
+
+    def move(u, q, before, after):
+        mn[mp[u]], mp[mn[u]] = mn[u], mp[u]
+        mp[u], mn[u] = before, after; mn[before] = u; mp[after] = u; mp[n] = mn[n] = n
+        pick[u] = q; dur[u] = cost(u, q)
+        a = min([pos[u]] + ([pos[after]] if after < n else [])); b = max([pos[u]] + ([pos[before]] if before < n else []))
+        seg = topo[a:b + 1]; inside = set(seg); left = {}
+        for i in seg: left[i] = sum(1 for j, _ in jp[i] if j in inside) + (mp[i] in inside)
+        ready = [i for i in seg if not left[i]][::-1]; out = []
+        while ready:
+            i = ready.pop(); out.append(i)
+            for k in [k for k, _ in js[i]] + [mn[i]]:
+                if k in inside:
+                    left[k] -= 1
+                    if not left[k]: ready.append(k)
+        assert len(out) == len(seg)
+        topo[a:b + 1] = out
+        for k, i in enumerate(out): pos[i] = a + k
+        times(max(a - 1, 0), min(b + 1, n - 1))
+    times(0, n - 1); best = None; tabu = {}
+    for it in range(STEPS[0]):
+        span = max(tail)
+        if best is None or span < best[0] - 1e-6: best = (span, [(fin[i] - dur[i], fin[i], pick[i]) for i in range(n)])
+        i = max(range(n), key=lambda i: (tail[i] > span - 1e-6 and fin[i] - dur[i] < 1e-6, rng.rand())) if it == 0 or tail[path[0]] < span - 1e-6 else path[0]
+        path = [i]
+        while True:
+            nx = [k for k, lag in js[i] if abs(tail[i] - dur[i] - lag - tail[k]) < 1e-6]
+            if mn[i] < n and abs(tail[i] - dur[i] - tail[mn[i]]) < 1e-6: nx.append(mn[i])
+            if not nx: break
+            i = nx[rng.randint(len(nx))] if len(nx) > 1 else nx[0]; path.append(i)
+        blocks = [[path[0]]]
+        for a, b in zip(path, path[1:]):
+            if mn[a] == b: blocks[-1].append(b)
+            else: blocks.append([b])
+        blocks = [b for b in blocks if len(b) > 1]; cand = []
+        for bi in rng.permutation(len(blocks))[:NEAR[0]]:
+            b = blocks[bi]; D = lambda l: [(x, dur[x]) for x in l]
+            for x in range(len(b) - 1):
+                for y in sorted(set((x + 1, len(b) - 1))):
+                    if y - x < 12 and all(tail[k] <= tail[b[y]] and k != b[y] for k, _ in js[b[x]]) and not any(anc[z] >> b[x] & 1 for z in b[x + 1:y + 1]):
+                        cand.append((guess(D(b[x + 1:y + 1] + [b[x]]), mp[b[x]], mn[b[y]]), b[x], pick[b[x]], b[y], mn[b[y]]))
+            for y in range(2, min(len(b), 12)):
+                if all(fin[j] <= fin[b[0]] and j != b[0] for j, _ in jp[b[y]]) and not any(anc[b[y]] >> z & 1 for z in b[:y]):
+                    cand.append((guess(D([b[y]] + b[:y]), mp[b[0]], mn[b[y]]), b[y], pick[b[y]], mp[b[0]], b[0]))
+            for u in b:
+                if len(ops[u]["q"]) == 2:
+                    q = "s" if pick[u] == "v" else "v"; k = pos[u] - 1
+                    while k >= 0 and pick[topo[k]] != q: k -= 1
+                    if k < 0: continue
+                    w = topo[k]; h = head(u); r = rest(u); d = cost(u, q)
+                    for _ in range(4):
+                        cand.append((max(max(h, fin[w]) + d + max(r, tail[mn[w]]), fin[mp[u]] + tail[mn[u]]), u, q, w, mn[w]))
+                        if mp[w] == n or anc[u] >> w & 1 or any(fin[j] > fin[w] - dur[w] for j, _ in jp[u]): break
+                        w = mp[w]
+        free = [c for c in cand if tabu.get((c[1], c[3]), -1) < it or c[0] < best[0] - 1.0]
+        if not free: continue
+        c = min(free, key=lambda c: c[0] + rng.rand() * JIT[0])
+        tabu[(c[1], mp[c[1]])] = it + 8 + rng.randint(12)
+        if c[2] == pick[c[1]] and c[3] < n: tabu[(c[3], mp[c[3]])] = it + 8 + rng.randint(12)
+        move(c[1], c[2], c[3], c[4])
+    return best[1] if best else res
 
 
 def emit(ops, g, T):
@@ -691,13 +836,15 @@ def emit(ops, g, T):
             res[i] = (st, st + c, q)
         return res
     if n not in PLAN:
-        left = [len(x) for x in fw]; ready = [i for i in range(n) if not left[i]]; first = []
-        while ready:
-            i = max(ready, key=lambda i: (pri[i] - BIAS.get(ops[i]["tag"], 0.0), -i)); ready.remove(i); first.append(i)
-            for k, _ in bw[i]:
-                left[k] -= 1
-                if not left[k]: ready.append(k)
-        res = place(first, fw, False); top = None
+        def start(bias):
+            key = [-pri[i] - bias.get(ops[i]["tag"], 0.0) for i in range(n)]
+            for i in range(n - 1, -1, -1):
+                for j, _ in fw[i]:
+                    if key[j] >= key[i]: key[j] = key[i] - 0.001
+            res = place(sorted(range(n), key=lambda i: (key[i], i)), fw, False)
+            rb = place(sorted(range(n), key=lambda i: (-res[i][1], -i)), bw, True)
+            return res, place(sorted(range(n), key=lambda i: (-rb[i][1], i)), fw, False)
+        top = None
         hard = [list(o["deps"]) for o in ops]; soft = [list(o["order"]) for o in ops]; late = [o.get("dma", 0.0) for o in ops]
 
         def score(res):
@@ -713,7 +860,15 @@ def emit(ops, g, T):
                     st += (res[i][1] - res[i][0]) * fac[ops[i]["kind"]]; free[q] = st; en_[i] = st + late[i] * fac["x"]
                 tot += wt * max(en_)
             return tot
-        rng = np.random.RandomState(SEED[0]); cur = None
+        rng = np.random.RandomState(SEED[0]); cur = None; tags = sorted(set(o["tag"] for o in ops)); good = None
+        for it in range(TRIES[0]):
+            bias = dict(good[1]) if good else dict(BIAS)
+            for _ in range(rng.randint(1, 4) if it else 0):
+                k = tags[rng.randint(len(tags))]; bias[k] = bias.get(k, 0.0) + rng.normal(0, rng.choice([1500.0, 6000.0]))
+            for r_ in start(bias):
+                sc_ = score(r_)
+                if good is None or sc_ < good[0]: good = (sc_, bias, r_)
+        res = good[2]
         for it in range(PASSES[0]):
             sc_ = score(res)
             if top is None or sc_ < top[0]: top = (sc_, res, list(pen))
@@ -731,7 +886,8 @@ def emit(ops, g, T):
             if it % 2 == 0:
                 rb = place(sorted(range(n), key=lambda i: (-res[i][1], -i)), bw, True)
                 res = place(sorted(range(n), key=lambda i: (-rb[i][1], i)), fw, False)
-        PLAN[n] = top[1]
+        PLAN[n] = polish(ops, fw, top[1], rng)
+        INFO.append((score(top[1]), score(PLAN[n])))
     end = [0.0] * n
     for i, o in enumerate(ops):
         o["st"], o["pick"] = PLAN[n][i][0], PLAN[n][i][2]; o["cost"] = PLAN[n][i][1] - o["st"]; end[i] = PLAN[n][i][1] + o.get("dma", 0)

@@ -4,44 +4,50 @@ from concourse.mybir import AluOpType as AL, ActivationFunctionType as AF
 
 F, H, B, I, U = "float32", "float16", "bfloat16", "int32", "uint16"
 SB = {
-    "RAW": (2048, I), "X": (5136, B), "RT": (1040, F), "RTH": (1024, H), "TA": (1024, F), "TB": (1024, F), "FL": (1024, B), "FLS": (256, B),
+    "RAW": (2048, I), "X": (5152, B), "RT": (1040, F), "RTH": (1024, H), "TA": (1024, F), "TB": (1024, F), "FL": (1024, B), "FLS": (256, B),
     "G1": (9216, B), "LN": (512, U), "KT": (1040, B), "CT": (1040, B), "IT": (1040, B), "GR": (1024, H), "HE": (2048, B),
     "P": (1040, F), "M": (1040, F), "GA": (5392, F), "OV": (9472, B), "EQ": (1024, B), "D2": (1024, H), "GB": (1024, B),
     "GC": (1024, B), "XS": (1024, B), "IDB": (1024, B), "U1J": (1024, F), "LO": (1024, B), "HI": (1024, B), "IO": (1056, F),
-    "IOB": (128, B), "ALL": (2048, B), "Y": (2304, B), "Z": (144 * 14, B), "CM": (128 * 68, B), "ONE": (512, B), "RST": (512, B),
+    "IOB": (128, B), "ALL": (2048, B), "Y": (2304, B), "Z": (144 * 14, B), "CM": (128 * 72, B), "ONE": (512, B), "RST": (512, B),
     "LUT": (2048, B), "EA": (256, U), "EB": (256, U), "ENC": (256, F), "GAW": (256, F), "WN": (3456, B), "ZZ": (1024, F), "ZF": (273, F), "TH": (512, B),
-    "SF": (2560, F), "SI": (1024, I), "SH": (640, B), "SU": (640, U), "S16": (512, H), "W5": (512, F), "W6": (512, F), "WI": (512, I), "WJ": (512, I),
+    "SF": (2624, F), "SI": (1024, I), "SH": (832, B), "SU": (640, U), "S16": (512, H), "W5": (512, F), "W6": (512, F), "WI": (512, I), "WJ": (512, I),
     "WB": (512, B), "R": (512, B), "PR": (512, B), "SV": (512, B), "INW": (528, H), "NT": (512, F), "WW": (896, F), "CW": (640, H),
     "YC": (640, H), "GI": (1280, B), "GL": (1280, B), "SRC": (1280, B), "G0": (128, H), "XB": (640, B), "RKW": (64, B), "QS": (64, B), "QR": (256, B),
     "TP": (384, B), "TR": (384, B), "EQS": (1024, B), "PRS": (1024, H), "FLG": (128, B), "NUS": (128, F), "INC": (128, H), "TG": (128, H),
-    "SW": (1152, B), "SC": (1024, B), "OH": (1024, B), "NE": (1024, H), "SND": (3072, B), "RX": (3072, B), "COL": (16, F), "COI": (16, I), "ZER": (1024, B),
+    "SW": (1152, B), "SC": (1024, B), "OH": (1024, B), "NE": (1024, H), "SND": (3072, B), "RX": (2048, B), "ONF": (8, F), "EI": (512, I), "OVT": (2048, B), "COL": (16, F), "COI": (16, I), "ZER": (1024, B),
 }
 LISTS = {"a": 64, "mk": 64, "sp": 64, "go": 8, "u": 64, "cs": 32, "cw": 40, "i2": 80, "ex": 80, "lu": 80, "ov": 80, "st": 8, "sc": 64, "sx": 64, "sr": 128, "gq": 4, "q": 8}
+SB["Lsh"] = (32, U)
 for _k, _n in LISTS.items():
     SB["L" + _k] = (_n, U)
 SB.update({"SRG": (2048, B), "KP": (256, B), "SM": (3072, B), "SND": (1024, B), "O0": (128, I), "NAM": (640, B), "ZB": (1024, B), "R2": (80, B), "UM": (160, F)})
-ALIAS = {"WI": ("RAW", 1024), "WJ": ("RAW", 1536), "SI": ("RAW", 0), "TA": ("GA", 0), "TB": ("ZZ", 0), "GC": ("GB", 0), "EQS": ("SM", 0), "OH": ("SM", 1024),
+ALIAS = {"WI": ("RAW", 1024), "WJ": ("RAW", 1536), "SI": ("RAW", 0), "TA": ("P", 16), "TB": ("ZZ", 0), "GC": ("GB", 0), "EQS": ("SM", 0), "OH": ("SM", 1024),
          "SC": ("SM", 2048), "NE": ("PRS", 0), "NT": ("W5", 0), "GL": ("G1", 0), "SRC": ("G1", 1280),
-         "HE": ("G1", 2560), "WB": ("G1", 4752), "R": ("G1", 5264), "PR": ("G1", 5776), "SV": ("G1", 6288)}
+         "LO": ("EQ", 0), "HI": ("XS", 0), "ZB": ("SRG", 0), "HE": ("G1", 2560), "WB": ("G1", 4752), "R": ("G1", 5264), "PR": ("G1", 5776), "SV": ("G1", 6288)}
 SCRATCH = {k: ("sbuf", [128, n], d) for k, (n, d) in SB.items() if k not in ALIAS}
 for _b in range(8):
     SCRATCH["pb%d" % _b] = ("psum", [128, 512], F)
-ND = 24
-SEMAPHORES = ["cv", "cs", "cp", "cg"] + ["o%d" % i for i in range(6)] + ["d%d" % i for i in range(ND)] + ["a%d" % i for i in range(12)]
+ND = 30
+SEMAPHORES = ["cv", "cs", "cp", "cg"] + ["o%d" % i for i in range(9)] + ["d%d" % i for i in range(ND)] + ["a%d" % i for i in range(9)]
 SIZE = {F: 4, H: 2, B: 2, I: 4, U: 2}
-CYC, PEC, LAT = 0.95, 0.48, 120.0
-PEN = [0.6, 50.0]
-EDGE = [2, 2, 2]
-MBK, STEPS, NEAR, JIT = [4], [30000], [3], [10.0]
-MARK, CUT, HOPW, EDW = [1], [1024], [512], [512]
-HAS = ["vmvm"]
+CYC, PEC, LAT = 0.9, 0.45, 120.0
+PEN = [1.0, 50.0]
+EDGE = [2, 3, 99]
+EQS, CMP, ABS = ["vv"], [["vs", "vs", "vv"]], [""]
+XF, XSE = [1.25, 1.2], [1]
+POP, OVD = [1], [2, 0]
+MBK, STEPS, NEAR, JIT = [4], [10, 16000], [3], [10.0]
+MARK, CUT, HOPW, EDW = [3], [1024], [512], [512]
+HAS = ["mmvv"]
 BLOCKS = [(j, s) for s in range(4) for j in range(2 * s, 8) if j != 2 * s + 1]
-PAIRS = [(j, k) for j in range(8) for k in range(j + 1, 8)]
-PASSES, PLAN, SEED, TEMP = [100], {}, [1], [1000.0]
+PAIRS = [(0, 8 * j + k, j, k) for j in range(2) for k in range(j + 1, 8)]
+PAIRS += [(1, d, j, k) for d, (j, k) in enumerate((j, k) for j in range(2, 8) for k in range(j + 1, 8))]
+PASSES, PLAN, SEED, TEMP = [400], {}, [5], [1000.0]
 GUESS = [({"o": 1, "g": 1, "s": 1, "p": 1, "x": 1.2}, 130.0, 2.0), ({"o": 1, "g": 0.75, "s": 0.55, "p": 1, "x": 1.2}, 130.0, 1.0),
          ({"o": 1, "g": 1.3, "s": 1.55, "p": 1, "x": 1}, 100.0, 1.0), ({"o": 1, "g": 1.25, "s": 0.7, "p": 1.3, "x": 1.6}, 200.0, 1.0)]
-BIAS, TRIES = {"ends0": 20000.0}, [1]
-GAT, SCA = 1.5, 3.5
+BIAS = dict([("ends0", 20000.0)] + [(k + str(t), 5000.0) for k in ("pm", "lab", "spk", "edge", "new") for t in range(3)] +
+                   [(k + str(t), 3000.0) for k in ("seam", "own", "cmp", "rows") for t in range(3)] + [("edge1", 10000.0), ("edge2", 10000.0)])
+GAT, SCA = 1.56, 3.8
 
 
 def S(n, a=0, b=None, st=1):
@@ -180,7 +186,7 @@ def program(ops, T, nxt, prv):
         add("g", lambda e: [e["g"].affine_select(ap(out), ap(a), pat, op, float(fill), base, cm)], [a], [out], 210 + 2 * cols(out) * CYC)
 
     def dma(q, pairs, rd, wr, lat):
-        add(q, lambda e: [e[q].dma_start(o, i) for o, i in pairs], rd, wr, 60.0 * len(pairs), dma=lat)
+        add(q, lambda e: [e[q].dma_start(o, i) for o, i in pairs], rd, wr, 60.0 * len(pairs), dma=lat * XF[1])
 
     def pb(b, a=0, e=512, st=1):
         return ("pb%d" % b, a, e, st)
@@ -247,13 +253,15 @@ def program(ops, T, nxt, prv):
     ms(S("ONE"), 1.0); ms(S("ZER"), 0.0)
     o0 = S("O0", 0, 64); iota(o0, [[2, 32], [1024, 2]], 0, 64)
     iota(S("COI", 0, 1), [[0, 1]], 0, 1)
-    ms(S("TB"), 1.0)
-    for c in range(8, 16): ms(S("TB", c, 1024, 16), -2047.0)
+    blank = ["R1%d" % x for x in (1, 2, 3)] + ["T%d%d" % (b, x) for b in range(2) for x in range(b, 4)] + ["CV", "CV2", "KD", "KD2", "FK"]
+    for n in blank: C(n)
+    ms(S("Z"), 0.0); ms(S("Y"), 0.0); ms(C("FK"), 0.0); w = 128 * len(blank) - 128
+    dma("y", [(T["CM"][:, a:min(w, a + 1024)], T["ZER"][:, 0:min(w, a + 1024) - a]) for a in range(0, w, 1024)], [S("ZER"), S("RAW"), S("X", 16, 2192)], [S("CM", 0, w)], 4000)
     ts(S("COI", 1, 2), S("COI", 0, 1), 15, AL.bitwise_and); cp(RC, S("COI", 1, 2))
     ts(S("COI", 2, 3), S("COI", 0, 1), 4, AL.arith_shift_right, 1, AL.bitwise_and); cp(HQ, S("COI", 2, 3))
     ts(S("COI", 3, 4), S("COI", 0, 1), 8, AL.bitwise_and); ts(A64, S("COI", 3, 4), 8.0, AL.mult)
     ts(M3, RC, 3.0, AL.is_equal); ts(NTB, RC, 64.0, AL.mult, float(1015 - 2 ** 23 - 2048), AL.add)
-    for t in range(3): ts(M8[t], RC, 8.0, AL.is_equal, float(4 + 20 * t), AL.mult)
+    for t in range(2): ts(M8[t], RC, 10.0, AL.is_equal, (4.0, 20.0)[t], AL.mult)
     o1 = S("O0", 64, 128); ts(o1, o0, 2047, AL.bitwise_and); o2 = su(64); ts(o2, o1, HQ, AL.add)
 
     def aff(name, c0, al, be, src=ONE):
@@ -264,32 +272,32 @@ def program(ops, T, nxt, prv):
 
     def zmake(name, ws, off=15):
         for ch, w in ws: poke(Zs(name, None, off), ch, w)
-    ms(S("Z"), 0.0); ms(S("Y"), 0.0)
     aff("DUP", 0, 0, 1); aff("ID", 0, 8, 1); aff("FN0", 0, 1000, 1); aff("FN1", 1000, -1000, 1)
-    iota(S("HI"), [[1, 32], [0, 32]], 0)
-    ms(S("XB", 0, 512), 1.0); ms(S("XB", 0, 512, 32), 0.0)
-    for h in range(2): scan(S("LO", 512 * h, 512 * h + 512), S("XB", 0, 512), S("ONE"), 0.0, AL.mult, AL.add)
+    ms(S("XB", 0, 512), 1.0); ms(S("XB", 0, 512, 32), 0.0); ms(S("GB", 0, 512), 0.0); ms(S("GB", 0, 512, 32), 1.0)
+    for h in range(2):
+        scan(S("LO", 512 * h, 512 * h + 512), S("XB", 0, 512), S("ONE"), 0.0, AL.mult, AL.add)
+        scan(S("HI", 512 * h, 512 * h + 512), S("ONE"), S("GB", 0, 512), 16.0 * h - 1.0, AL.mult, AL.add)
     M0 = S("COL", 6, 7); ts(M0, RC, 0.0, AL.is_equal)
     asel(S("Y", 15, 2304, 16), S("ONE", 0, 144), [[-1, 16], [-16, 9]], AL.is_equal, 0, 0)
     asel(C("BLK"), ONE, [[-16, 8], [0, 16]], AL.is_ge, 0, 0); asel(C("BLK"), C("BLK"), [[16, 8], [0, 16]], AL.is_ge, 0, 15, -1)
     B8c = sub(C("BLK"), 0, 128, 16)
     asel(Zs("lo8"), B8c, [[16, 8]], AL.is_ge, 0, 7, -1)
     zmake("key", [(0, 2048 * 256), (1, 256), (2, 32 * 256)])
-    V1, VW, DGO, A1C, JK, JG, V256 = sf(64), S("W5"), sf(64), sf(64), sf(64), sf(8), sf(64)
+    V1, VW, DGO, A1C, JK, JG, V256 = sf(64), S("W5"), sf(64), sf(128), sf(64), sf(8), sf(64)
     iota(V1, [[1, 64]], 1); ts(V1, V1, NTB, AL.add, float(-(1015 - 2 ** 23 - 2048)), AL.add)
     INEL = sh(64); ts(JK, V1, -8185.0, AL.add); ts(V256, V1, 256.0, AL.mult, -128.0, AL.add)
     t0 = sf(64); ts(t0, V1, 128.5, AL.is_lt, 16.0, AL.mult); t1 = sf(64); ts(t1, V1, 896.5, AL.is_gt, 16.0, AL.mult); tt(INEL, t0, t1, AL.add)
     for k in range(8): ms(S("RST", k, 512, 8), -float(2 ** (k - 1)) if k else 1.0e8)
-    for n, c in (("KT", 16.0), ("CT", 0.0), ("IT", 0.0), ("RT", 0.0), ("X", 0.0), ("INW", 0.0)):
+    for n, c in (("KT", 16.0), ("CT", 0.0), ("IT", 0.0), ("RT", 0.0), ("X", 0.0), ("INW", 0.0), ("GA", 0.0)):
         ms(S(n, 0, 16), c)
     ts(S("KT", 15, 16), M3, -16.0, AL.mult, 16.0, AL.add)
-    tt(S("TA"), IND(S("RAW"), o2), S("TB"), AL.add)
+    ts(S("TA"), IND(S("RAW"), o2), 1.0, AL.add); ts(C("NE2K"), C("FN1"), -2048.0, AL.mult)
     add("v", lambda e: [e["v"].transpose(ap(S("TB")), ap(S("TA")))], [S("TA")], [S("TB")], 1024 * CYC)
     act(S("FL"), S("TB"), AF.Sign)
 
     def f0(h, a, b):
-        pe([(pb(1 + h), C("DUP"), S("FL", a, b))])
-        tt(S("RTH", a, b), pb(1 + h), S("TB", a, b), AL.mult)
+        pe([(pb(1 + h), C("NE2K"), S("FL", a, b))])
+        tt(S("RTH", a, b), pb(1 + h), S("TB", a, b), AL.add)
         pe([(pb(4 + h), Yc(0, 1), S("LO", a, b)), (pb(4 + h), Yc(0, 2), S("HI", a, b))])
         mv(S("IDB", a, b), pb(4 + h), M3)
     halves(f0)
@@ -299,30 +307,36 @@ def program(ops, T, nxt, prv):
         asel(S("ALL", 512 * k, 512 * k + 512), S("ONE"), [[-1, 4], [-16, 8], [0, 16]], AL.is_equal, 0, -4 * k)
     for k in range(8): ts(sub(C("PW"), k, 128, 8), sub(C("ID"), k, 128, 8), float(2 ** k), AL.mult)
     pe([(pb(7, 0, 8), C("PW"), Zs("lo8"))]); cp(Zs("pow"), pb(7, 0, 8)); zmake("id", [(1, 1), (2, 32)])
+    PWC, PWN, JK2 = S("COL", 14, 15), S("COL", 15, 16), sf(64)
+    pe([(pb(7, 0, 1), C("PW"), S("ONE", 0, 1))]); cp(PWC, pb(7, 0, 1)); ts(PWN, pb(7, 0, 1), -1.0, AL.mult); ts(JK2, V1, -9209.0, AL.add)
+    ts(sub(t0, 16, 17), RC, 1.5, AL.is_gt); ts(sub(t1, 16, 17), RC, 13.5, AL.is_lt, sub(t0, 16, 17), AL.mult); ts(C("INT"), C("ID"), sub(t1, 16, 17), AL.mult)
+
     ts(C("I8"), C("ID"), 8.0, AL.mult); ts(C("NID"), C("ID"), -1.0, AL.mult); ts(C("IDK"), C("ID"), 1.0 / 1024, AL.mult)
     RC1, WX = S("COL", 7, 8), S("COL", 11, 12)
     ts(RC1, RC, 1.0, AL.add); ts(sub(t0, 0, 1), RC, 7.5, AL.is_gt, -16384.0, AL.mult); ts(sub(t1, 0, 1), RC, 7.5, AL.is_lt, RC, AL.mult)
     tt(WX, sub(t0, 0, 1), sub(t1, 0, 1), AL.add); ts(Zs("idx"), B8c, WX, AL.mult, flex=False)
     iota(S("QS"), [[1, 4], [4, 16]], 0); ts(sub(t0, 0, 1), RC, 4.0, AL.mult, 1024.0, AL.add); ts(sub(JG, 0, 4), S("IO", 0, 4), sub(t0, 0, 1), AL.add)
-    ms(S("ENC"), 2048.0); ms(C("FK"), 0.0)
+    iota(S("ENC"), [[0, 256]], 2048)
     for c, z in ((0, "lo8"), (4, "lo8"), (5, "pow")): cp(sub(C("FK"), c, 128, 16), Zs(z))
     ts(sub(t0, 0, 1), RC, 0.5, AL.is_gt); ts(C("KS"), C("ID"), sub(t0, 0, 1), AL.mult); ts(S("CT", 15, 16), M0, 1000.0, AL.mult)
     tag[0] = "ends"
-    ms(S("ZF"), 0.0); iota(VW, [[0, 8], [16, 64]], 0); ts(VW, VW, RC, AL.add)
-    ts(S("W6"), VW, -1.0, AL.mult, 1039.0, AL.add)
-    tt(S("OH", 0, 512), S("RAW", 0, 512), VW, AL.is_gt); ts(S("SC", 0, 512), S("RAW", 512, 1024), 0.0, AL.is_lt); tt(S("INW", 16, 528), S("SC", 0, 512), S("W6"), AL.mult)
-    ts(C("I136"), C("ID"), 136.0, AL.mult); ts(C("N4080"), C("ID"), -4080.0, AL.mult)
-    pe([(pb(6), C("I136"), S("OH", 0, 512)), (pb(6), C("NID"), S("INW", 16, 528)), (pb(6), C("N4080"), S("SC", 0, 512))])
-    ts(S("WI"), S("RAW", 512, 1024), 4, AL.arith_shift_right); ts(S("W6"), S("WI"), -4351.0, AL.mult, 1040.0, AL.add)
-    ts(pb(7), S("RAW", 512, 1024), 272.0, AL.mult, flex=False); tt(S("W6"), pb(7), S("W6"), AL.add); tt(pb(6), pb(6), S("W6"), AL.add)
-    EO = S("SU", 128, 640); ts(EO, pb(6), 0.0, AL.add)
+    ms(S("ZF"), 0.0); VW = pb(5, 0, 256)
+    for h in range(4): ts(sub(VW, 64 * h, 64 * h + 64), S("IO", 0, 1024, 16), RC, AL.add)
+    EO = S("SU", 128, 640)
+    ts(C("I136"), C("ID"), 136.0, AL.mult)
+    for a in range(0, 512, 256):
+        en_, w, x, y, p, q = S("RAW", 512 + a, 768 + a), S("W6", a, a + 256), S("OH", a, a + 256), S("EI", a, a + 256), pb(7, 0, 256), pb(6, 0, 256)
+        tt(x, VW, S("RAW", a, a + 256), AL.is_lt); pe([(q, C("I136"), x)])
+        ts(y, en_, 4, AL.logical_shift_right); ts(w, y, -4351.0, AL.mult, 1040.0, AL.add)
+        ts(p, en_, 272.0, AL.mult, flex=False); tt(w, p, w, AL.add); tt(w, q, w, AL.add); tt(w, VW, w, AL.max); cp(sub(EO, a, a + 256), w)
     dma("y", [(T["GA"][0:128:16, 1024:5392], T["ZF"][:, :])], [S("ZF")], [S("GA", 1024, 5392)], 2500)
     tag[0] = ""
-    dma("y", [(T["X"][:, a:b], T["ZER"][:, 0:b - a]) for a, b in ((2192, 3216), (3216, 4240), (4240, 5136))], [S("ZER")], [S("X", 2192, 5136)], 5000)
-    dma("y", [(T["OV"][:, 1024 * k:1024 * k + 1024], T["ZER"][:, :]) for k in range(8)], [S("ZER")], [S("OV", 0, 8192)], 9000)
+    dma("y", [(T["X"][:, a:b], T["ZER"][:, 0:b - a]) for a, b in ((2192, 3216), (3216, 4240), (4240, 5152))], [S("ZER"), S("RAW"), S("X", 16, 2192)], [S("X", 2192, 5152)], 5000)
+    ms(S("X", 4112, 4113), 300.0)
+    dma("y", [(T["OV"][:, 1024 * k:1024 * k + 1024], T["ZER"][:, :]) for k in range(8)], [S("ZER"), S("X", 2192, 2200)], [S("OV", 0, 8192)], 12000)
 
     def zero_ov():
-        dma("y", [(T["OV"][c:128:16, 0:8192], T["ZER"][:, 0:512]) for c in (1, 2, 7, 8)], [S("ZER")], [S("OV", 0, 8192)], 4000)
+        dma("y", [(T["OV"][c:128:8, 0:8192], T["ZER"][:, :]) for c in (1, 2)], [S("ZER")], [S("OV", 0, 8192)], 4000)
 
     def ends():
         tag[0] = "ends"
@@ -341,26 +355,32 @@ def program(ops, T, nxt, prv):
     for jj in range(4): ts(S("TH", 128 * jj, 128 * jj + 128), ONE, sub(t1, 8 + jj, 9 + jj), AL.mult, flex=False)
     asel(C("B8"), ONE, [[-8, 16], [0, 8]], AL.is_ge, 0, 0); asel(C("B8"), C("B8"), [[8, 16], [0, 8]], AL.is_ge, 0, 7, -1)
     asel(C("L8"), C("B8"), [[16, 8], [1, 16]], AL.is_gt, 0, 0, -1); asel(C("L8"), C("L8"), [[-1, 128]], AL.not_equal, -16, 0)
-    made = set()
-    for i, (j, k) in enumerate(PAIRS):
-        b, d = i // 16, i % 16
-        for x, (n, src, w) in enumerate((("R%d%d" % (b, j // 2), 8 * (j % 2) + k, 8.0), ("T%d%d" % (b, k // 2), 8 * (k % 2) + j, 1.0), ("D%d" % b, d, (8 * j + k) / 128.0))):
-            if n not in made: ms(C(n), 0.0); made.add(n)
-            ts(sub(C(n), d, 128, 16), sub(C("ID"), src, 128, 16), w, AL.mult)
+    cmn["R00"] = cmn["I8"]
+    for b, d, j, k in PAIRS:
+        poke(sub(C("T%d%d" % (b, k // 2)), d, 128, 16), 8 * (k % 2) + j, 1.0)
+        if b: poke(sub(C("R1%d" % (j // 2)), d, 128, 16), 8 * (j % 2) + k, 8.0)
+    DB = [S("COL", 12, 13), S("COL", 13, 14)]; x3 = sh(8)
+    ts(DB[0], RC, 1.0 / 128, AL.mult, -1025.0 - 2057.0 / 8192, AL.add); ts(sub(x3, 0, 4), S("IO", 0, 64, 16), RC, AL.add)
+    pe([(pb(7, 0, 1), C("R1%d" % x), sub(x3, x, x + 1)) for x in (1, 2, 3)]); ts(DB[1], pb(7, 0, 1), 1.0 / 1024, AL.mult, -1025.0 - 2057.0 / 8192, AL.add)
     tt(C("LW"), C("LT"), C("BLK"), AL.subtract)
     asel(C("LS"), C("LW"), [[-1, 128]], AL.not_equal, 512, 0); asel(C("LW"), C("LW"), [[-1, 128]], AL.not_equal, 1024, 0)
     ts(C("EN2K"), C("FN1"), 2048.0, AL.mult)
     cp(Zs("all"), B8c); ts(Zs("8k"), B8c, 8192.0, AL.mult)
     zmake("om", [(5, 1)]); ts(Zs("l17"), Zs("lo8"), 1024.0, AL.mult); zmake("l17", [(0, 0)])
-    ms(C("D12"), 0.0); poke(sub(C("D12"), 1, 128, 16), 1, 1); poke(sub(C("D12"), 2, 128, 16), 2, 1)
-    ms(C("CV"), 0.0); ms(C("CV2"), 0.0); ms(C("KD"), 0.0); ms(C("KD2"), 0.0)
     CV, KD = C("CV"), C("KD")
-    for ch, w, off in ((1, 1, 15), (2, 32, 15), (7, 1, 23), (8, 32, 23)): poke(sub(CV, off, off + 128, 16), ch, w)
-    for off in (15, 23): poke(sub(KD, off, off + 128, 16), 0, 1)
+    for ch, w, off in ((1, 1, 15), (2, 32, 15), (9, 1, 23), (10, 32, 23)): poke(sub(CV, off, off + 128, 16), ch, w)
+    for x in range(2 - OVD[0], 2):
+        m = C("MV%d" % x); ms(m, 0.0)
+        for l in range(4 * x, 4 * x + 4): ms(sub(m, l, 128, 8), 1.0)
+        m2 = S("KP", 128 * x, 128 * x + 128); ts(m2, m, 32.0, AL.mult)
+        for c, y in enumerate((m, m2)): asel(y, y, [[-8, 8], [-4, 2], [-1, 8]], AL.is_equal, 0, 4 * x - 64 * c)
+        tt(m, m, m2, AL.add)
+    for off in (15, 23): poke(sub(KD, off, off + 128, 16), 0, 4096)
     DW, DOV, DX = sf(32), sf(80), sf(64)
-    ts(DW, sub(DGO, 0, 32), 511.0, AL.add); ts(DX, DGO, -1.0, AL.mult, 2176.0, AL.add)
+    ts(DW, sub(DGO, 0, 32), 511.0, AL.add); ts(DX, DGO, -1.0, AL.mult, 2175.0, AL.add)
     ts(sub(DOV, 0, 64), DGO, 8064.0, AL.add); ts(sub(DOV, 64, 80), sub(DGO, 0, 16), 9088.0, AL.add)
-    DS = sf(128); ts(DS, S("IO", 0, 128), 1024.0, AL.add); ts(A1C, S("IO", 0, 64), A64, AL.add, 1.0, AL.add)
+    DS = sf(64); ts(DS, S("IO", 0, 64), 512.0, AL.add); ts(sub(A1C, 0, 64), S("IO", 0, 64), A64, AL.add, 1.0, AL.add)
+    N896 = sh(64); ms(N896, -896.0); ms(sub(A1C, 64, 128), 0.0)
     asel(C("GE8"), C("B8"), [[-16, 8], [-1, 16]], AL.is_ge, 0, 0)
     pe([(pb(7, 0, 1), C("P2"), S("Y", 15, 16))]); P2C = S("COL", 5, 6); cp(P2C, pb(7, 0, 1))
     ts(S("WI", 0, 256), S("IO", 0, 256), P2C, AL.mult); ts(S("WJ", 0, 256), S("WI", 0, 256), 2048, AL.bitwise_and)
@@ -368,18 +388,21 @@ def program(ops, T, nxt, prv):
     for n in range(8): ts(S("LUT", 256 * n, 256 * n + 256), pb(7, 0, 256), float(n), AL.is_gt)
     aff("FE0", 8, 1000, 1); aff("FE1", 1008, -1000, 1); aff("DUPE", 8, 0, 1)
     for h in range(2):
-        m = 320 * h; pe([(pb(6 + h, 0, 320), Yc(0, 7), S("LO", m, m + 320)), (pb(6 + h, 0, 320), Yc(0, 8), S("HI", m, m + 320))]); mv(S("NAM", m, m + 320), pb(6 + h, 0, 320))
-    ms(C("NEG"), -1.0); aff("NDUPE", 8, 0, 1, C("NEG"))
+        m = 320 * h; pe([(pb(6 + h, 0, 320), Yc(0, 9), S("LO", m, m + 320)), (pb(6 + h, 0, 320), Yc(0, 10), S("HI", m, m + 320))]); mv(S("NAM", m, m + 320), pb(6 + h, 0, 320), M8[0])
+    ms(C("NEG"), -1.0); ms(C("K8"), 8192.0)
     for s_ in range(4):
         for ha in range(2): aff("NP%d%d" % (s_, ha), 8 * ha + 2 * s_, 1, 0, C("NEG"))
         tt(C("VB%d" % s_), C("DUP"), C("NP%d0" % s_), AL.subtract)
-    for ha in range(2): tt(C("SH%d" % ha), C("FN%d" % ha), C("FE%d" % ha), AL.add); ts(C("SH%d" % ha), C("SH%d" % ha), 8192.0, AL.mult)
-    ts(C("NDUPE"), C("NDUPE"), 1.0 / 8192, AL.mult)
-    for s_ in range(4): ts(C("NQ%d" % s_), C("NP%d1" % s_), 1.0 / 8192, AL.mult)
+    ms(C("N13"), -1.0 / 8192)
+    for ha, (c0, al) in enumerate(((0, 1000), (1000, -1000))):
+        aff("SH%d" % ha, c0, al, 1, C("K8")); asel(C("SH%d" % ha), C("SH%d" % ha), [[-16, 8], [-al, 2], [-1, 8]], AL.not_equal, 8192, -c0 - 8)
+        aff("NFE%d" % ha, c0 + 8, al, 1, C("N13"))
+    for s_ in range(4): aff("NQ%d" % s_, 8 + 2 * s_, 1, 0, C("N13"))
 
     OK_, M1, CH, NCH, TG1, TG2, TG3, TG4, LB1, LB2, GG, G4 = [sf(64) for _ in range(12)]
     MI, AI, BI = [si(64) for _ in range(3)]
-    SELF, INB, RK1, CB, CON, BB = [sh(64) for _ in range(6)]
+    SELF, INB, RK1, CB, CON, BB, DGB, BG, SD, DEAD = [sh(64) for _ in range(10)]
+    ms(DEAD, 0.0)
     E = {"nxt": nxt, "prv": prv, "zero_ov": zero_ov}
     for k, w in (("ci", 40), ("c4", 40), ("yi", 40), ("hk", 80), ("vl", 40), ("rr", 80), ("w0", 64), ("w1", 64)): E[k] = si(w)
     for k in ("c2", "i2", "u2", "t2", "t3"): E[k] = sf(80)
@@ -401,16 +424,17 @@ def program(ops, T, nxt, prv):
     def part_a(t):
         tag[:] = ["a", t]
         for h in range(2):
-            a, b, k = 512 * h, 512 * h + 512, 3 * h
+            a, b, k = 512 * h, 512 * h + 512, 2 * h
             pe([(pb(k), C("ID"), S("IDB", a, b))] + [(pb(k, 64 * r, 64 * r + 64), Yc(8 * h + r, 0), INEL) for r in range(8)], True, False)
             pe([(pb(k), C("FK"), S("FL", a, b))], False, True)
             mv(S("KT", 16 + a, 16 + b), pb(k))
-            fold(pb(1 + h, 0, 256), "FN", "RTH", a, 512); ts(S("LN", 256 * h, 256 * h + 256), pb(1 + h, 0, 256), 15.0, AL.add)
-        extc(pb(3, 0, 64), "lo8", S("FL"), [(pb(3, 0, 64), C("ID"), INEL)])
-        ts(TG1, pb(3, 0, 64), 2048.0 * 256, AL.mult); tt(OK_, TG1, V256, AL.add)
+            fold(pb(1, 0, 256), "FN", "RTH", a, 512); ts(S("LN", 256 * h, 256 * h + 256), pb(1, 0, 256), 15.0, AL.add)
+        extc(pb(2, 0, 64), "lo8", S("FL"), [(pb(2, 0, 64), C("ID"), INEL)])
+        ts(TG1, pb(2, 0, 64), 2048.0 * 256, AL.mult); tt(OK_, TG1, V256, AL.add)
+        if t >= MARK[0]: cp(DGB, pb(2, 0, 64))
         for h in range(2): pe([(pb(1 + h), C("DUP"), S("RTH", 512 * h, 512 * h + 512))]); mv(S("RT", 16 + 512 * h, 528 + 512 * h), pb(1 + h))
         hop()
-        scan(S("W5"), S("RST"), pb(0), 0.0, AL.add, AL.min)
+        scan(S("W5"), S("RST"), pb(0), 0.0, AL.add, AL.min); ops[-1]["meet"] = True
         tt(M1, S("W5", 7, 512, 8), OK_, AL.min); ts(MI, M1, 128.0, AL.add, float(2 ** 23), AL.min); ts(AI, MI, 8, AL.arith_shift_right, 2047, AL.bitwise_and)
         ts(AL_, AI, 15.0, AL.add)
         tt(S("GB"), IND(RTW, AL_), S("U1J"), AL.is_equal)
@@ -418,28 +442,20 @@ def program(ops, T, nxt, prv):
         for h in range(2):
             pe([(pb(4 + h), C("KS"), S("KT", 16 + 512 * h, 528 + 512 * h))] + [(blk(4, r), Yc(r, 5), BB) for r in range(8 * h, 8 * h + 8)], True, False)
         ts(LB1, AI, -1000.0, AL.add, flex=False); ts(LB2, AI, -1.0, AL.mult, -1000.0, AL.add, flex=False)
-        tag[0] = "spk"
-        w2r(1, [(Al, lambda r: A1H)])
-
-        def f(h, a, b):
-            tt(S("EQ", a, b), pb(1 + h), S("RT", 16 + a, 16 + b), AL.is_equal)
-            pe([(pb(1 + h), C("ID"), S("EQ", a, b))] + [(blk(1, r), Al(r), SELF) for r in range(8 * h, 8 * h + 8)])
-            tt(S("D2", a, b), pb(1 + h), S("RTH", a, b), AL.mult)
-        halves(f)
-        extc(pb(1, 0, 64), "en", S("D2")); ts(SPL, pb(1, 0, 64), 2063.0, AL.add, 4111.0, AL.min)
-        for h in range(2): mv(S("XS", 512 * h, 512 * h + 512), IND(XW, sub(SPL, 32 * h, 32 * h + 32)))
-        tag[0] = "a"
+        tt(SD, SELF, DEAD, AL.add)
         pe([(pb(3, 0, 64), C("I8"), A1H)] + [(pb(3, 0, 64), Zs("idx", r), S("GB", r, 1024, 16)) for r in range(16)])
-        tt(TG1, pb(3, 0, 64), JK, AL.min); ts(MKL, TG1, 16376.0, AL.add)
-        cp(IND(S("G1"), MKL), S("ZER"))
-        if MARK[0]:
-            dma("y", [(T["IT"][:, 16:528], T["G1"][3:128:16, 0:8192])], [S("G1", 0, 8192)], [S("IT", 16, 528)], 2300)
-            pe([(pb(3, 0, 64), C("NID"), SELF)] + [(pb(3, 0, 64), C("ID"), S("IT", 16 + k, 528, 8)) for k in range(8)])
+        y, WD = pb(3, 0, 64), S("IT", 16, 528)
+        if t < MARK[0]:
+            tt(TG1, y, JK, AL.min); ts(MKL, TG1, 16376.0, AL.add); cp(IND(S("G1"), MKL), S("ZER"))
+            dma("y", [(T["IT"][:, 16:528], T["G1"][3:128:16, 0:8192])], [S("G1", 0, 8192)], [WD], 2300)
+            pe([(y, C("I8"), SELF)] + [(y, C("NID"), sub(WD, k, 512, 8)) for k in range(8)]); edge = 7.5
         else:
-            for r0 in range(0, 16, 4):
-                pe(([(pb(3, 0, 64), C("NID"), SELF)] if r0 == 0 else []) +
-                   [(pb(3, 0, 64), Yc(3, r), S("G1", 512 * r + k, 512 * r + 512, 8)) for r in range(r0, r0 + 4) for k in range(8)], r0 == 0, r0 == 12)
-        ts(CH, pb(3, 0, 64), -1.0, AL.is_equal); ts(NCH, pb(3, 0, 64), -1.0, AL.not_equal, 1000.0, AL.mult)
+            dma("y", [(T["GA"][0:128:16, 0:6144], T["ONF"][:, :])], [S("ONF")], [S("GA", 0, 6144)], 2500)
+            tt(TG1, y, JK2, AL.min); ts(MKL, TG1, 15352.0, AL.add); put(IND(S("GA"), MKL), S("IO", 32, 1056))
+            dma("y", [(T["W6"][16 * g + 2:16 * g + 14, :], T["GA"][16 * g:16 * g + 1, 0:6144]) for g in range(8)], [S("GA", 0, 6144)], [S("W6")], 2300)
+            act(WD, S("W6"), AF.Sign, -2.0)
+            pe([(y, C("I136"), SELF), (y, C("NID"), DGB), (y, C("NID"), DGB)] + [(y, C("INT"), sub(WD, k, 512, 8)) for k in range(8)]); edge = 127.5
+        ts(CH, y, edge, AL.is_gt); ts(NCH, y, edge, AL.is_lt, 1000.0, AL.mult)
         scan(INB, S("ONE", 0, 64), CH, 0.0, AL.mult, AL.add)
         off = pb(3, 0, 1); pe([(off, C("LT"), sub(INB, 63, 64))])
         tt(TG2, INB, NCH, AL.add); ts(RK1, TG2, off, AL.add); ts(CON, RK1, 128.5, AL.is_lt)
@@ -461,14 +477,19 @@ def program(ops, T, nxt, prv):
         tag[0] = "lab"
         for h in range(2): mv(S("GC", 512 * h, 512 * h + 512), IND(S("CT"), sub(AL_, 32 * h, 32 * h + 32)))
         ext(pb(5, 0, 64), [("c0", S("GC"))], 1024)
-        ts(CB, pb(5, 0, 64), 128.5, AL.is_lt); tt(GG, CB, SELF, AL.is_gt)
-        tt(LP, LB1, GG, AL.mult); tt(LM, LB2, GG, AL.mult)
-        w2r(1, [(Al, lambda r: CB)])
-        halves(lambda h, a, b: tt(S("D2", a, b), pb(1 + h), S("D2", a, b), AL.mult))
-        spokes()
+        ts(CB, pb(5, 0, 64), 128.5, AL.is_lt); tt(BG, CB, BB, AL.mult); tt(GG, CB, SD, AL.is_gt)
+        tt(LP, LB1, GG, AL.mult); tt(LM, LB2, GG, AL.mult); tt(DEAD, DEAD, CON, AL.add)
+        w2r(1, [(Al, lambda r: BG)])
+        for h in range(2):
+            p = pb(1 + h)
+            if EQS[0][h] == "v": ts(p, p, PWN, AL.is_equal)
+            else: act(p, p, AF.Abs, PWC); act(p, p, AF.Relu, 1.0, -1.0)
+            tt(S("D2", 512 * h, 512 * h + 512), p, S("RTH", 512 * h, 512 * h + 512), AL.mult)
+        extc(pb(1, 0, 64), "en", S("D2")); ts(SPL, pb(1, 0, 64), 2063.0, AL.add)
 
     def spokes():
         tag[0] = "pm"
+        for h in range(2): mv(S("XS", 512 * h, 512 * h + 512), IND(XW, sub(SPL, 32 * h, 32 * h + 32)))
         for b0, tab, lab in ((4, "P", LP), (MBK[0], "M", LM)):
             w2r(b0, [(Al, lambda r, lab=lab: lab), (lambda r: C("IDK"), lambda r: S("XS", r, 1024, 16))])
             halves(lambda h, a, b, b0=b0, tab=tab: mv(S(tab, 16 + a, 16 + b), pb(b0 + h), 1000.0))
@@ -491,9 +512,10 @@ def program(ops, T, nxt, prv):
             else:
                 zb = S("ZB", 512 * k, 512 * k + b - a); act(zb, zz, AF.Abs, 0.0, 1024.0)
                 pe([(z, C("ID"), x), (z, C("NID"), zb)]); act(zb, z, AF.Relu)
-                ts(S("WN", a, b), zb, 0.0, AL.is_gt); pe([(z, C("ID"), x), (z, C("NID"), zb)]); mv(x, z)
+                ts(S("WN", a, b), zb, 0.0, AL.is_gt)
+                pe([(z, C("ID"), x), (z, C("NID"), zb)]); mv(x, z)
         tag[0] = "b"
-        cp(S("GR"), IND(RTW, UL))
+        for h in range(2): ts(S("GR", 512 * h, 512 * h + 512), IND(RTW, sub(UL, 32 * h, 32 * h + 32)), -1.0, AL.max)
         for h in range(2): mv(S("IT", 16 + 512 * h, 528 + 512 * h), IND(S("CT"), sub(UL, 32 * h, 32 * h + 32)))
         J = lambda x, jj: sub(x, 128 * jj, 128 * jj + 128)
         gu = lambda jj, h: S("IT", 16 + 2 * jj + h, 1040, 8)
@@ -501,17 +523,18 @@ def program(ops, T, nxt, prv):
         pe([(pb(0), C("ID"), S("TH"))] + [(J(pb(0), jj), C("VB%d" % jj), FG) for jj in range(4)], True, False)
         for i in range(4):
             p, he = pb((3, 1, 2, 6)[i]), S("HE", 512 * i, 512 * i + 512)
-            pe([(J(p, x), C("NP%d0" % s), S("G0")) for x, (j, s) in enumerate(BLOCKS[4 * i:4 * i + 4])], True, False)
-            pe([(J(p, x), C("ID"), S("GR", j, 1024, 8)) for x, (j, s) in enumerate(BLOCKS[4 * i:4 * i + 4])], False, True)
+            a, part, K = 64 * (i // 2), list(enumerate(BLOCKS[8 * (i % 2):8 * (i % 2) + 8])), (lambda x, n: sub(x, 64 * n, 64 * n + 64))
+            pe([(K(p, x), C("NP%d0" % s), S("G0", a, a + 64)) for x, (j, s) in part], True, False)
+            pe([(K(p, x), C("ID"), S("GR", 8 * a + j, 8 * a + 512, 8)) for x, (j, s) in part], False, True)
             if HAS[0][i] == "v": ts(he, p, 0.0, AL.is_equal)
             elif HAS[0][i] == "s": act(he, p, AF.Abs); act(he, he, AF.Relu, 1.0, -1.0)
             else: act(he, p, AF.Abs); ts(he, he, 0.0, AL.is_equal)
-            pe([m for x, (j, s) in enumerate(BLOCKS[4 * i:4 * i + 4])
-                for m in [(J(pb(0), j // 2), Zs("ha", 8 * (j % 2) + 2 * s), J(he, x)), (J(pb(0), s), Zs("hb", j), J(he, x))]], False, i == 3)
-        ts(S("WB"), pb(0), 0.0, AL.is_gt)
-        pe([m for jj in range(4) for m in [(J(pb(0), jj), C("FB0"), gu(jj, 0), 1), (J(pb(0), jj), C("FB1"), gu(jj, 1)), (J(pb(0), jj), C("L8"), J(S("WB"), jj))]])
-        ts(S("PR"), pb(0), -7.5, AL.is_lt); act(S("R"), pb(0), AF.Relu, -7.0 / 8192, -1.0 / 8192)
-        tr = lambda n, p, b, src: [(p, C("%s%d%d" % (n, b, x)), J(S(src), x)) for x in sorted(set(PAIRS[i][n == "T"] // 2 for i in range(16 * b, min(28, 16 * b + 16))))]
+            pe([m for x, (j, s) in part for m in [(K(pb(0), 2 * (j // 2) + i // 2), Zs("ha", 8 * (j % 2) + 2 * s), K(he, x)),
+                                                  (K(pb(0), 2 * s + i // 2), Zs("hb", j), K(he, x))]], False, i == 3)
+        pe([(J(pb(7), jj), C("FB%d" % h), gu(jj, h)) for jj in range(4) for h in range(2)], True, False)
+        ts(S("WB"), pb(0), 0.0, AL.is_gt); ops[-1]["meet"] = True; pe([(pb(7), C("L8"), S("WB"))], False, True)
+        ts(S("PR"), pb(7), -7.5, AL.is_lt); act(S("R"), pb(7), AF.Relu, -7.0 / 8192, -1.0 / 8192)
+        tr = lambda n, p, b, src: [(p, C("%s%d%d" % (n, b, x)), J(S(src), x)) for x in sorted(set(q[2 + (n == "T")] // 2 for q in PAIRS if q[0] == b))]
         grp = lambda l: [m + ((1,) if i == 0 else ()) for i, m in enumerate(l)]
         pe([m for b in range(2) for m in grp(tr("R", pb(3, b, 256, 2), b, "PR") + tr("T", pb(3, b, 256, 2), b, "PR"))])
         ts(S("SV", 0, 256), pb(3, 0, 256), 8.5, AL.is_gt)
@@ -521,8 +544,8 @@ def program(ops, T, nxt, prv):
         pe([(pb(3, 0, 16), Yc(0, r), S("INW", 15 + r, 271, 16)) for r in range(16)] + [(pb(3, 0, 16), C("ID"), S("SV", 256, 272))])
         for b in range(2):
             p = pb(0, b, 256, 2)
-            pe([(p, C("D%d" % b), ONE)] + tr("R", p, b, "R") + tr("T", p, b, "R") + [(p, C("LW"), S("SV", b, 256, 2)), (p, C("ID"), S("INW", 16 + b, 272, 2))])
-        act(S("NT", 0, 256), pb(0, 0, 256), AF.Identity, -1025.0 - 2057.0 / 8192)
+            pe(tr("R", p, b, "R") + tr("T", p, b, "R") + [(p, C("LW"), S("SV", b, 256, 2)), (p, C("ID"), S("INW", 16 + b, 272, 2))])
+        for b in range(2): mv(S("NT", b, 256, 2), pb(0, b, 256, 2), DB[b])
         ts(z0, pb(3, 0, 16), 639.5, AL.is_gt, 1024.0, AL.mult); tt(z1, pb(3, 0, 16), z0, AL.add); tt(z2, z1, sub(DW, 0, 16), AL.min); cp(sub(CSL, 0, 16), z2)
         iota(S("WW", 0, 640), [[0, 640]], 0); put(IND(S("WW"), sub(CSL, 0, 16)), S("IO", 32, 288))
         scan(S("CW"), S("WW", 0, 640), S("WW", 0, 640), 0.0, AL.max, AL.max)
@@ -544,14 +567,12 @@ def program(ops, T, nxt, prv):
             pe([(pb(b, 0, 40), C("ID"), f_(S("R2")))] + [(pb(b, 0, 40), Zs("om", r), S("GI", a + r, a + 640, 16)) for r in range(16)]); cp(f_(LUL), pb(b, 0, 40))
             mv(S("GL", a, a + 640), IND(S("LUT"), f_(LUL)))
             pe([(pb(b, 64, 104), Zs("id", r), S("GI", a + r, a + 640, 16)) for r in range(16)], True, False)
-        for i in range(4):
-            a, m = 320 * i, 320 * (i % 2); o = (a + 640) % 1280; p = pb(1 + i % 2, 0, 320)
-            pe([(p, C("ID"), S("NAM", m, m + 320)), (p, C("D12"), S("GI", o, o + 320))])
-            mv(S("SRC", a, a + 320), p, M8[t])
         for f_, a, b in hs:
             pe([(pb(b, 64, 104), Zs("l17", r), S("GL", a + r, a + 640, 16)) for r in range(16)], False, True)
             tt(f_(t2), pb(b, 64, 104), f_(t3), AL.max); ts(f_(OVL), f_(t2), -1.0, AL.add)
-            cp(IND(S("OV"), f_(OVL)), S("SRC", a, a + 640))
+            tt(IND(S("OV"), f_(OVL)), S("GI", 640 - a, 1280 - a), S("NAM"), AL.add)
+        ops[-1]["meet"] = True
+        if t < 2: ts(S("NAM"), S("NAM"), M8[1], AL.add)
         tag[0] = "new"
         ext(pb(0, 128, 208), [("id", S("GI"))], 1280)
         c0 = 136 + 40 * t; um = S("UM", 0, 80)
@@ -562,116 +583,130 @@ def program(ops, T, nxt, prv):
         YY = S("GA", 16 + n, 656 + n)
         mv(YY, IND(S("P"), lo(EXL))); tt(S("XB"), IND(S("M"), hi(EXL)), YY, AL.add); ts(S("X", 16 + n, 656 + n), S("XB"), 1024.0, AL.mult, 255.0, AL.min)
         tag[0] = "rows"
-        for bk, a, b in ((6, 896, 1024), (7, 0, 128), (1, 128, 512), (2, 512, 896)):
-            p = pb(bk, 0, b - a)
-            pe([(p, C("ID"), S("RTH", a, b)), (p, C("NID"), S("D2", a, b))], True, False)
-            pe([(p, sub(C("CV"), 15 - l, 143 - l), S("OV", 1024 * l + a, 1024 * l + b)) for l in range(8)], False, True)
-            cp(S("RTH", a, b), p); act(S("FL", a, b), p, AF.Sign)
+        for x in range(2 - OVD[0], 2):
+            dma("ys"[x], [(T["OVT"][64 * c:64 * c + 64, 1024 * x:1024 * x + 1024], T["OV"][c + 1:128:8, 4096 * x:4096 * x + 4096]) for c in range(2)],
+                [S("OV", 4096 * x, 4096 * x + 4096)], [S("OVT", 1024 * x, 1024 * x + 1024)], 2800)
+        for part in (((pb(6, 0, 128), 896, 1024), (pb(6, 128, 256), 0, 128)), ((pb(1, 0, 384), 128, 512),), ((pb(2, 0, 384), 512, 896),)):
+            pe([m for p, a, b in part for m in [(p, C("ID"), S("RTH", a, b)), (p, C("NID"), S("D2", a, b))]], True, False)
+            far = OVD[0] if len(part) == 1 or OVD[1] else 0
+            pe([(p, sub(C("CV"), 15 - l, 143 - l), S("OV", 1024 * l + a, 1024 * l + b)) for p, a, b in part for l in range(8 - 4 * far)] +
+               [(p, C("MV%d" % x), S("OVT", 1024 * x + a, 1024 * x + b)) for p, a, b in part for x in range(2 - far, 2)], False, True)
+            for p, a, b in part: cp(S("RTH", a, b), p)
+            for p, a, b in part: act(S("FL", a, b), p, AF.Sign)
         if t < 2: E["zero_ov"]()
         tag[0] = "mid"
         dma("y", [(T["GAW"][:, :], T["GA"][0:128:16, 16:4112])], [S("GA", 16, 4112)], [S("GAW")], 2500)
-        y = pb(4, 0, 256); mm = []
+
+    def middles(t):
+        tag[0] = "mid"
+        n = 2176 + 640 * t; y = pb(0, 0, 256); mm = []
         for r in range(16):
             a, b, c = 256 * r, min(max(n, 256 * r), 256 * r + 256), min(max(n + 640, 256 * r), 256 * r + 256)
-            if b > a: mm.append((pb(4, 0, b - a), Zs("all", r), S("WN", a, b)))
-            if c > b: mm.append((pb(4, b - a, c - a), Zs("all", r), S("ONE", 0, c - b)))
+            if b > a: mm.append((pb(0, 0, b - a), Zs("all", r), S("WN", a, b)))
+            if c > b: mm.append((pb(0, b - a, c - a), Zs("all", r), S("ONE", 0, c - b)))
         for i in range(0, len(mm), 4): pe(mm[i:i + 4], i == 0, i + 4 >= len(mm))
         ts(y, y, 8.5, AL.is_gt, 2048.0 * (t + 1), AL.mult); tt(y, y, S("GAW"), AL.add); tt(S("ENC"), y, S("ENC"), AL.max)
 
-    def swap(src, dst, w, k):
-        def fn(e):
-            trs = [RemoteDMATransfer(dst_ids=[DstId(rid=to[0], pnc=to[1])], dma_engine_mask=to[2], remote_sem=T.sem["a%d" % (k + i)],
-                                     src=T[src[0]][:, src[1] + w * i:src[1] + w * i + w], dst=T[dst[0]][:, dst[1] + w * (1 - i):dst[1] + w * (2 - i)])
-                   for i, to in enumerate((E["nxt"], E["prv"]))]
-            return [e["g"].remote_dma_fused(trs, local_sem=T.sem["o%d" % (k // 2)])]
-        o = add("g", fn, [src], [], 300.0, send=("o%d" % (k // 2), E["nxt"][3] + E["prv"][3]))
-        add("x", None, [], [sub(dst, w, 2 * w)], 3000.0 + 6 * w, after=o, sem=("a%d" % k, E["prv"][4]))
-        add("x", None, [], [sub(dst, 0, w)], 3000.0 + 6 * w, after=o, sem=("a%d" % (k + 1), E["nxt"][4]))
+    def send(src, dst, k, to, by):
+        o = add("g", lambda e: [e["g"].remote_dma(ap(dst), ap(src), T.sem["a%d" % k], T.sem["o%d" % k], E[to][1], E[to][0], E[to][2])], [src], [], 300.0, send=("o%d" % k, E[to][3]))
+        add("x", None, [], [dst], (3000.0 + 3.5 * cols(src)) * XF[0], after=o, sem=("a%d" % k, E[by][4]))
+    base = (896, 0)
+    SND = S("SND")
 
     def part_c(t):
         tag[0] = "seam"
-        TP, TR = S("TP", 128 * t, 128 * t + 128), S("TR", 128 * t, 128 * t + 128)
-        SND, RX = S("SND"), S("RX", 1024 * t, 1024 * t + 1024)
-        q0, q1, q2, q3 = E["q0"], E["q1"], E["q2"], E["q3"]
-        h0, h1 = (lambda x: sub(x, 0, 64)), (lambda x: sub(x, 64, 128))
-        base = (896, 0)
+        TP, TR, RX = S("TP", 128 * t, 128 * t + 128), S("TR", 64 * t, 64 * t + 64), S("RX", 1024 * (t % 2), 1024 * (t % 2) + 1024)
+        H2 = lambda x, s_, w=64: sub(x, w * s_, w * s_ + w)
+        rows = lambda s_, ha: S("RTH", base[s_] + 64 * ha, base[s_] + 64 * ha + 64)
         for s_ in range(2):
-            pe([(pb(6, 64 * s_, 64 * s_ + 64), C("FN%d" % ha), S("RTH", base[s_] + 64 * ha, base[s_] + 64 * ha + 64)) for ha in range(2)])
-        ts(h0(q0), pb(6, 0, 64), -896.0, AL.add, 0.0, AL.max); tt(h0(q1), h0(q0), A1C, AL.is_gt); tt(h0(TP), h0(q0), h0(q1), AL.mult)
-        ts(h1(q0), pb(6, 64, 128), 0.0, AL.is_equal, 200.0, AL.mult); ts(h1(q1), pb(6, 64, 128), 200.0, AL.min); tt(h1(TP), h1(q0), h1(q1), AL.max)
-        swap(TP, TR, 64, 4 * t)
-        for s_ in range(2):
-            fold(pb(6 + s_, 0, 64), "FE", "RTH", base[s_], 128); ts(sub(SRL, 64 * s_, 64 * s_ + 64), pb(6 + s_, 0, 64), 2063.0, AL.add)
-        for s_ in range(2):
-            rr_, rs_ = (h0(TP), h0(TR)) if s_ == 0 else (h1(TR), h1(TP))
-            bl = lambda s, ha: pb(6 + s_, 128 * s + 64 * ha, 128 * s + 64 * ha + 64)
-            two_ = [[(bl(s, ha), C(("DUP", "DUPE")[ha]), rr_) for s in range(4) for ha in range(2)], [(bl(s, ha), C("NP%d%d" % (s, ha)), rs_) for s in range(4) for ha in range(2)]]
-            pe([(pb(6 + s_), C("ID"), S("ZER", 0, 512))] + two_[s_] +
-               [(bl(s, ha), C("NDUPE" if s_ == 0 else "NQ%d" % s), S("RTH", base[s_] + 64 * ha, base[s_] + 64 * ha + 64)) for s in range(4) for ha in range(2)], True, False)
-            pe(two_[1 - s_], False, True)
-            ts(S("PRS", 512 * s_, 512 * s_ + 512), pb(6 + s_), -0.5, AL.max, 0.5, AL.min)
-        for s_ in range(2):
-            pe([(pb(6, 64 * s_, 64 * s_ + 64), C("SH%d" % ha), S("PRS", 512 * s_ + 128 * s + 64 * ha, 512 * s_ + 128 * s + 64 * ha + 64)) for s in range(4) for ha in range(2)])
-        ts(S("WI", 0, 128), pb(6, 0, 128), 32768.0, AL.add); ts(S("WJ", 0, 128), S("WI", 0, 128), 8191, AL.bitwise_and)
-        ts(S("FLG"), S("WJ", 0, 128), 0.0, AL.is_gt); ts(q3, S("WJ", 0, 128), 1.0 / 8192, AL.mult, -513.5, AL.add)
-        pc = pb(6, 0, 128); pe([(pc, C("BLK"), S("FLG"))])
-        for s_ in range(2): scan(S("INC", 64 * s_, 64 * s_ + 64), S("ONE", 0, 64), sub(pc, 64 * s_, 64 * s_ + 64), 512.0 * s_, AL.mult, AL.add)
-        tt(q0, S("INC"), pc, AL.subtract); ts(q1, pc, 0.0, AL.is_equal); tt(q2, q1, DS, AL.mult); tt(S("TG"), q0, q2, AL.max)
-        pe([(pb(7, 0, 128), C("LS"), S("FLG")), (pb(7, 0, 128), C("ID"), S("INC"))]); tt(S("NUS"), pb(7, 0, 128), q3, AL.add)
-        ext(pb(6, 0, 8), [("c0", S("TG"))], 128); cp(STL, pb(6, 0, 8))
-        iota(S("SW", 0, 1024), [[0, 1024]], 0); cp(IND(S("SW"), STL), S("IOB"))
-        scan(S("SC"), S("SW", 0, 1024), S("SW", 0, 1024), 0.0, AL.max, AL.max)
-        ext(pb(6, 0, 64), [("c0", S("SC"))], 1024); cp(SCL, pb(6, 0, 64))
-        tt(S("NE"), IND(S("NUS"), SCL), S("IO", 0, 1024), AL.subtract); ts(S("NE"), S("NE"), -0.5, AL.max, 0.5, AL.min)
-        ext(pb(7, 0, 64), [("8k", S("NE"))], 1024)
-        w0, w1 = E["w0"], E["w1"]; ts(w0, pb(7, 0, 64), 65536.0, AL.add); ts(w1, w0, 8191, AL.bitwise_and)
-        tt(h0(q2), w1, DX, AL.max); ts(SXL, h0(q2), -1.0, AL.mult, 6159.0, AL.add)
-        mv(sub(SND, 0, 512), IND(XW, sub(SXL, 0, 32)), None, "s"); mv(sub(SND, 512, 1024), IND(XW, sub(SXL, 32, 64)))
-        swap(SND, RX, 512, 4 * t + 2); tag[0] = "cmp"
-        GT, SG, MN, GX = S("EQS"), S("OH"), S("SC"), S("SRG")
+            pe(([] if s_ else [(pb(7, 0, 64), C("ID"), N896)]) + [(pb(7, 64 * s_, 64 * s_ + 64), C("FN%d" % ha), rows(s_, ha)) for ha in range(2)], s_ == 0, s_ == 1)
+        tt(TP, pb(7, 0, 128), A1C, AL.max)
+        send(H2(TP, 0), TR, 3 * t, "nxt", "prv")
 
-        def f(h, a, b):
-            pe([(pb(6 + h), C("ID"), sub(RX, a, b))])
-            tt(sub(GT, a, b), pb(6 + h), sub(SND, a, b), AL.is_lt); tt(sub(MN, a, b), pb(6 + h), sub(SND, a, b), AL.min)
-            pe([(pb(6 + h), C("BLK"), sub(GT, a, b))])
-            if h:
-                act(S("W6"), pb(6 + h), AF.Identity, 8.5, -1.0); put(IND(S("GA"), sub(SXL, 32, 64)), S("W6"))
-                mv(sub(GX, 1024, 2048), IND(S("GA", 0, 2832 + 640 * t), sub(SRL, 64, 128)))
-            act(sub(SG, a, b), pb(6 + h), AF.Sign, 8.5, -1.0)
-            tt(IND(XW, sub(SXL, 32 * h, 32 * h + 32)), sub(MN, a, b), sub(SG, a, b), AL.mult)
-            if not h: mv(sub(GX, 0, 1024), IND(XW, sub(SRL, 0, 64)))
-        halves(f)
+        def number(s_, far, bk):
+            FLG, INC, TG, p = H2(S("FLG"), s_), H2(S("INC"), s_), H2(S("TG"), s_), pb(bk, 0, 64)
+            q0, q1, q2 = [H2(E[k], s_) for k in ("q0", "q1", "q2")]; SW = S("SW", 576 * s_, 576 * s_ + 576); w = sub(SW, 0, 512)
+            tt(FLG, far, H2(A1C, 0), AL.is_gt); pe([(p, C("BLK"), FLG)]); scan(INC, S("ONE", 0, 64), p, 0.0, AL.mult, AL.add)
+            ts(q1, p, 0.0, AL.is_equal); tt(q0, INC, p, AL.subtract); tt(q2, q1, DS, AL.mult); tt(TG, q0, q2, AL.max)
+            ext(pb(bk, 0, 4), [("c0", TG)], 64); cp(H2(STL, s_, 4), pb(bk, 0, 4))
+            iota(w, [[0, 512]], 0); cp(IND(SW, H2(STL, s_, 4)), S("IOB", 0, 64)); scan(H2(S("SC"), s_, 512), w, w, 0.0, AL.max, AL.max)
+            ext(pb(bk, 0, 32), [("c0", H2(S("SC"), s_, 512))], 512); cp(H2(SCL, s_, 32), pb(bk, 0, 32))
+
+        def names(s_, bk):
+            NE, w0, w1, q2 = H2(S("NE"), s_, 512), H2(E["w0"], s_, 32), H2(E["w1"], s_, 32), sub(E["q3"], 64 + 32 * s_, 96 + 32 * s_)
+            tt(NE, IND(H2(S("NUS"), s_), H2(SCL, s_, 32)), S("IO", 0, 512), AL.subtract); ts(NE, NE, -0.5, AL.max, 0.5, AL.min)
+            ext(pb(bk, 0, 32), [("8k", NE)], 512); ts(w0, pb(bk, 0, 32), 65536.0, AL.add); ts(w1, w0, 8191, AL.bitwise_and)
+            if s_:
+                q0 = sub(E["q0"], 0, 32); ts(q0, w1, 2047.0, AL.max, -1.0, AL.mult); ts(S("Lsh"), q0, 6159.0, AL.add)
+            tt(q2, w1, H2(DX, s_, 32), AL.max); ts(H2(SXL, s_, 32), q2, -1.0, AL.mult, 6159.0, AL.add)
+        tag[0] = "own"
+        number(0, H2(TP, 0), 3); p = pb(3, 64, 128)
+        pe([(p, C("NFE%d" % ha), rows(0, ha)) for ha in range(2)] + [(p, C("LS"), H2(S("FLG"), 0)), (p, C("ID"), H2(S("INC"), 0))]); mv(H2(S("NUS"), 0), p, -513.0)
+        names(0, 3); mv(H2(SND, 0, 512), IND(XW, H2(SXL, 0, 32))); send(H2(SND, 0, 512), H2(RX, 1, 512), 3 * t + 1, "nxt", "prv")
         for s_ in range(2):
-            k_, a, p = S("KP", 128 * s_, 128 * s_ + 128), base[s_], pb(6 + s_, 0, 128)
+            fold(pb(3, 0, 64), "FE", "RTH", base[s_], 128); ts(H2(SRL, s_), pb(3, 0, 64), 2063.0, AL.add)
+        tag[0] = "seam"
+        bl = lambda s, ha: pb(7, 128 * s + 64 * ha, 128 * s + 64 * ha + 64)
+        pe([m for s in range(4) for ha in range(2) for m in [(bl(s, ha), C("NP%d%d" % (s, ha)), H2(TP, 1)), (bl(s, ha), C("NQ%d" % s), rows(1, ha))]], True, False)
+        pe([(bl(s, ha), C(("DUP", "DUPE")[ha]), TR) for s in range(4) for ha in range(2)], False, True)
+        ts(S("PRS", 512, 1024), pb(7), -0.5, AL.max, 0.5, AL.min)
+        pe([(pb(7, 0, 64), C("SH%d" % ha), S("PRS", 512 + 128 * s + 64 * ha, 576 + 128 * s + 64 * ha)) for s in range(4) for ha in range(2)])
+        ts(S("WI", 0, 64), pb(7, 0, 64), 32768.0, AL.add); ts(S("WJ", 0, 64), S("WI", 0, 64), 8191, AL.bitwise_and)
+        q3 = sub(E["q3"], 0, 64); ts(q3, S("WJ", 0, 64), 1.0 / 8192, AL.mult, -513.5, AL.add)
+        number(1, TR, 6)
+        pe([(pb(7, 0, 64), C("LS"), H2(S("FLG"), 1)), (pb(7, 0, 64), C("ID"), H2(S("INC"), 1))]); tt(H2(S("NUS"), 1), pb(7, 0, 64), q3, AL.add)
+        names(1, 6)
+        for h in range(2): mv(sub(SND, 512 + 256 * h, 768 + 256 * h), IND(XW, S("Lsh", 16 * h, 16 * h + 16)))
+        send(H2(SND, 1, 512), H2(RX, 0, 512), 3 * t + 2, "prv", "nxt")
+
+    def part_d(t):
+        tag[0] = "cmp"
+        RX = S("RX", 1024 * (t % 2), 1024 * (t % 2) + 1024)
+        GT, SG, MN, GX = S("EQS"), S("OH"), S("SC"), S("SRG")
+        for s_ in (1, 0):
+            a, b, p = 512 * s_, 512 * s_ + 512, pb(7 - s_)
+            if CMP[0][t][s_] == "v":
+                pe([(p, C("ID"), sub(RX, a, b))])
+                tt(sub(GT, a, b), p, sub(SND, a, b), AL.is_lt); tt(sub(MN, a, b), p, sub(SND, a, b), AL.min)
+            else:
+                pe([(p, C("ID"), sub(SND, a, b)), (p, C("NID"), sub(RX, a, b))]); act(sub(MN, a, b), p, AF.Relu); ts(sub(GT, a, b), sub(MN, a, b), 0.0, AL.is_gt)
+                pe([(p, C("ID"), sub(SND, a, b)), (p, C("NID"), sub(MN, a, b))]); mv(sub(MN, a, b), p)
+            pe([(p, C("BLK"), sub(GT, a, b))]); L = sub(SXL, 32 * s_, 32 * s_ + 32)
+            if t < 2:
+                act(sub(SG, a, b), p, AF.Sign, 8.5, -1.0); tt(IND(XW, L), sub(MN, a, b), sub(SG, a, b), AL.mult); signs = XW
+            else:
+                cp(IND(S("G1", 0, 5152), L), sub(MN, a, b)); act(S("W6"), p, AF.Identity, 8.5, -1.0); put(IND(S("GA"), L), S("W6")); signs = S("GA", 0, 4112)
+            for h in range(2): mv(sub(GX, 2 * a + 512 * h, 2 * a + 512 * h + 512), IND(signs, sub(SRL, 64 * s_ + 32 * h, 64 * s_ + 32 * h + 32)))
+            k_, a, p = S("KP", 128 * s_, 128 * s_ + 128), base[s_], pb(7 - s_, 0, 128)
             pe([(p, sub(C("KD"), 15 - l, 143 - l), sub(GX, 1024 * s_ + l, 1024 * s_ + 1024, 8)) for l in range(8)])
-            ts(k_, p, 0.0, AL.is_gt)
-            if t < 2: tt(S("RT", 16 + a, 144 + a), S("RT", 16 + a, 144 + a), k_, AL.mult)
-            tt(S("RTH", a, a + 128), S("RTH", a, a + 128), k_, AL.mult)
-            tt(S("FLS", 128 * s_, 128 * s_ + 128), S("FL", a, a + 128), k_, AL.mult)
+            if t < 2: tt(S("RT", 16 + a, 144 + a), p, S("RT", 16 + a, 144 + a), AL.min)
+            ts(p, p, 0.0, AL.is_gt)
+            tt(S("FLS", 128 * s_, 128 * s_ + 128), p, S("FL", a, a + 128), AL.mult); tt(S("RTH", a, a + 128), p, S("RTH", a, a + 128), AL.mult)
 
     part_a(0)
     for t in range(3):
+        spokes()
         if t == 0: ends()
-        part_b(t)
+        part_b(t); part_c(t)
         if t < 2: part_a(t + 1)
+        middles(t)
         if t == 2:
             cp(S("WI", 256, 512), S("ENC")); ts(S("WJ", 256, 512), S("WI", 256, 512), 2047, AL.bitwise_and); ts(S("GAW"), S("WJ", 256, 512), -1.0, AL.add)
             dma("y", [(T["ymid"][:, :], T["GAW"][:, :])], [S("GAW")], [], 2500)
-        part_c(t)
-    for k in range(4):
-        a, b = 1024 * k, 1024 * k + 1024
-        act(S("G1", a, b), S("X", 16 + a, 16 + b), AF.Abs)
-        dma("y", [(T["ylen"][:, a:b], T["G1"][:, a:b])], [S("G1", a, b)], [], 3500)
-    for h in range(2):
-        a, b = 512 * h, 512 * h + 512
-        pcs = [(0, 128, S("FLS", 128, 256)), (128, 512, S("FL", 128, 512))] if h == 0 else [(0, 384, S("FL", 512, 896)), (384, 512, S("FLS", 0, 128))]
-        pe([(pb(1 + h), C("ID"), S("RTH", a, b))] + [(pb(1 + h, x, y), C("EN2K"), s_) for x, y, s_ in pcs])
-        ts(S("TA", a, b), pb(1 + h), -1.0, AL.add)
-    dma("y", [(T["ynb"][g, :], T["GA"][16 * g:16 * g + 8, 0:1024]) for g in range(8)], [S("TA")], [], 2500)
-    dma("s", [(T["yen"][g, :], T["GA"][16 * g + 8:16 * g + 16, 0:1024]) for g in range(8)], [S("TA")], [], 2500)
+            for a in range(16, 4112, 512): act(S("G1", a, a + 512), S("X", a, a + 512), AF.Abs)
+        part_d(t)
+    dma("y", [(T["ylen"][:, a:a + 1024], T["G1"][:, 16 + a:1040 + a]) for a in range(0, 4096, 1024)], [S("G1", 16, 4112)], [], 5000)
+    ts(BG, DEAD, -8192.0, AL.mult)
+    for bk, a, b, fl_ in ((1, 128, 512, S("FL", 128, 512)), (2, 512, 896, S("FL", 512, 896)), (1, 0, 128, S("FLS", 128, 256)), (2, 896, 1024, S("FLS", 0, 128))):
+        gone = [(pb(bk, x - a, x - a + 64), Al(x // 64), BG) for x in range(a, b, 64)] if b - a > 128 else []
+        pe([(pb(bk, 0, b - a), C("ID"), S("RTH", a, b)), (pb(bk, 0, b - a), C("EN2K"), fl_)] + gone)
+        if gone: ts(S("ZZ", a, b), pb(bk, 0, b - a), -1.0, AL.add, -1.0, AL.max)
+        else: ts(S("ZZ", a, b), pb(bk, 0, b - a), -1.0, AL.add)
+    dma("y", [(T["ynb"][g, :], T["ZZ"][16 * g:16 * g + 8, :]) for g in range(8)], [S("ZZ")], [], 2500)
+    dma("s", [(T["yen"][g, :], T["ZZ"][16 * g + 8:16 * g + 16, :]) for g in range(8)], [S("ZZ")], [], 2500)
 
 
-def polish(ops, fw, res, rng):
+def polish(ops, fw, res, rng, steps):
     n = len(ops); anc = [0] * n; jp = []; js = [[] for _ in ops]
     for i in range(n):
         cover = 0
@@ -691,17 +726,24 @@ def polish(ops, fw, res, rng):
             last[pick[i]] = i
     fin, tail = [0.0] * (n + 1), [0.0] * (n + 1)
 
+    own = lambda i, j, lag: not lag and pick[i] == pick[j]
+    tp = [[j for j, lag in jp[i] if not own(i, j, lag)] for i in range(n)]; tn = [[k for k, lag in js[i] if not own(i, k, lag)] for i in range(n)]
+    gap = [max([lag for _, lag in js[i]] + [0.0]) for i in range(n)]; out_ = [0.0] * n
+    for i in range(n):
+        jp[i] = [(j, 0.0 if own(i, j, lag) else gap[j]) for j, lag in jp[i]]; js[i] = [(k, 0.0 if own(i, k, lag) else gap[i]) for k, lag in js[i]]
+
     def times(a, b):
         for i in topo[a:]:
             s = fin[mp[i]]
-            for j, lag in jp[i]:
-                if fin[j] + lag > s: s = fin[j] + lag
-            fin[i] = s + dur[i]
+            for j in tp[i]:
+                if out_[j] > s: s = out_[j]
+            s += dur[i]; fin[i] = s; out_[i] = s + gap[i]
         for i in topo[b::-1]:
-            s = tail[mn[i]]
-            if late[i] > s: s = late[i]
-            for k, lag in js[i]:
-                if tail[k] + lag > s: s = tail[k] + lag
+            s = 0.0
+            for k in tn[i]:
+                if tail[k] > s: s = tail[k]
+            s = s + gap[i] if s else late[i]
+            if tail[mn[i]] > s: s = tail[mn[i]]
             tail[i] = s + dur[i]
     head = lambda i: max([fin[j] + lag for j, lag in jp[i]] + [0.0])
     rest = lambda i: max([tail[k] + lag for k, lag in js[i]] + [late[i]])
@@ -734,10 +776,9 @@ def polish(ops, fw, res, rng):
         for k, i in enumerate(out): pos[i] = a + k
         times(max(a - 1, 0), min(b + 1, n - 1))
     times(0, n - 1); best = None; tabu = {}
-    for it in range(STEPS[0]):
-        span = max(tail)
-        if best is None or span < best[0] - 1e-6: best = (span, [(fin[i] - dur[i], fin[i], pick[i]) for i in range(n)])
-        i = max(range(n), key=lambda i: (tail[i] > span - 1e-6 and fin[i] - dur[i] < 1e-6, rng.rand())) if it == 0 or tail[path[0]] < span - 1e-6 else path[0]
+    for it in range(steps):
+        i = max(topo[:40], key=lambda i: tail[i]); span = tail[i]
+        if best is None or span < best[0] - 1e-6: best = (span, list(zip([f - d for f, d in zip(fin, dur)], fin, pick)))
         path = [i]
         while True:
             nx = [k for k, lag in js[i] if abs(tail[i] - dur[i] - lag - tail[k]) < 1e-6]
@@ -795,6 +836,7 @@ def emit(ops, g, T):
                     else: hit = bool(m & m2)
                     if hit:
                         (order if (o["q"] == "p" and p["q"] == "p") else deps).add(j)
+                    elif ps: order.add(j)
         for kind, accs in (("r", o["rd"]), ("w", o["wr"])):
             for name, m, bm in accs:
                 l = last.setdefault(name, [])
@@ -802,7 +844,7 @@ def emit(ops, g, T):
                 if name.startswith("pb"): l[:] = [x for x in l if x[0] == i or (o["q"] != "p" and ops[x[0]]["q"] in ("p", o["q"]))]
                 l.append((i, kind, m, bm))
         if "after" in o: order.add([k for k in range(i) if ops[k] is o["after"]][0])
-        o["deps"], o["order"] = deps, order
+        o["deps"], o["order"] = deps, order - deps
     succ = [[] for _ in ops]
     for i, o in enumerate(ops):
         for j in o["deps"] | o["order"]: succ[j].append(i)
@@ -844,7 +886,6 @@ def emit(ops, g, T):
             res = place(sorted(range(n), key=lambda i: (key[i], i)), fw, False)
             rb = place(sorted(range(n), key=lambda i: (-res[i][1], -i)), bw, True)
             return res, place(sorted(range(n), key=lambda i: (-rb[i][1], i)), fw, False)
-        top = None
         hard = [list(o["deps"]) for o in ops]; soft = [list(o["order"]) for o in ops]; late = [o.get("dma", 0.0) for o in ops]
 
         def score(res):
@@ -860,34 +901,43 @@ def emit(ops, g, T):
                     st += (res[i][1] - res[i][0]) * fac[ops[i]["kind"]]; free[q] = st; en_[i] = st + late[i] * fac["x"]
                 tot += wt * max(en_)
             return tot
-        rng = np.random.RandomState(SEED[0]); cur = None; tags = sorted(set(o["tag"] for o in ops)); good = None
-        for it in range(TRIES[0]):
-            bias = dict(good[1]) if good else dict(BIAS)
-            for _ in range(rng.randint(1, 4) if it else 0):
-                k = tags[rng.randint(len(tags))]; bias[k] = bias.get(k, 0.0) + rng.normal(0, rng.choice([1500.0, 6000.0]))
-            for r_ in start(bias):
-                sc_ = score(r_)
-                if good is None or sc_ < good[0]: good = (sc_, bias, r_)
-        res = good[2]
-        for it in range(PASSES[0]):
-            sc_ = score(res)
-            if top is None or sc_ < top[0]: top = (sc_, res, list(pen))
-            if cur is None or sc_ < cur[0] + TEMP[0] * (1.0 - it / PASSES[0]): cur = (sc_, res, list(pen))
-            key = [cur[1][i][0] for i in range(n)]; pen[:] = cur[2]
-            c0 = rng.uniform(0, max(key)); wd = rng.choice([5000.0, 15000.0, 30000.0]); nz = rng.normal(0, rng.choice([300.0, 1000.0, 2500.0]), n)
-            flip = rng.uniform(0, 1, n) < rng.choice([0.0, 0.1])
+        rng = np.random.RandomState(SEED[0])
+
+        def shake():
+            pen[:] = [PEN[0]] * n; res = min(start(BIAS), key=score); top = cur = None
+            for it in range(PASSES[0]):
+                sc_ = score(res)
+                if top is None or sc_ < top[0]: top = (sc_, res)
+                if cur is None or sc_ < cur[0] + TEMP[0] * (1.0 - it / PASSES[0]): cur = (sc_, res, list(pen))
+                key = [cur[1][i][0] for i in range(n)]; pen[:] = cur[2]
+                c0 = rng.uniform(0, max(key)); wd = rng.choice([5000.0, 15000.0, 30000.0]); nz = rng.normal(0, rng.choice([300.0, 1000.0, 2500.0]), n)
+                flip = rng.uniform(0, 1, n) < rng.choice([0.0, 0.1])
+                for i in range(n):
+                    if it and abs(key[i] - c0) < wd:
+                        key[i] += nz[i]
+                        if flip[i]: pen[i] = 3.0 if cur[1][i][2] == "v" else -1.0
+                    for j, _ in fw[i]:
+                        if key[j] >= key[i]: key[i] = key[j] + 0.001
+                res = place(sorted(range(n), key=lambda i: (key[i], i)), fw, False)
+                if it % 2 == 0:
+                    rb = place(sorted(range(n), key=lambda i: (-res[i][1], -i)), bw, True)
+                    res = place(sorted(range(n), key=lambda i: (-rb[i][1], i)), fw, False)
+            return top[1]
+        span = lambda r: max(r[i][1] + late[i] for i in range(n))
+        sends = [i for i in range(n) if ops[i].get("meet")]; pop = [polish(ops, fw, shake(), rng, STEPS[1]) for it in range(POP[0])]
+        cut = [[0.0] + [r[i][0] for i in sends] + [span(r) + 1.0] for r in pop]; key = [None] * n; at = 0.0
+        for s_ in range(len(sends) + 1):
+            p_ = min(range(len(pop)), key=lambda p_: cut[p_][s_ + 1] - cut[p_][s_])
             for i in range(n):
-                if it and abs(key[i] - c0) < wd:
-                    key[i] += nz[i]
-                    if flip[i]: pen[i] = 3.0 if cur[1][i][2] == "v" else -1.0
-                for j, _ in fw[i]:
-                    if key[j] >= key[i]: key[i] = key[j] + 0.001
-            res = place(sorted(range(n), key=lambda i: (key[i], i)), fw, False)
-            if it % 2 == 0:
-                rb = place(sorted(range(n), key=lambda i: (-res[i][1], -i)), bw, True)
-                res = place(sorted(range(n), key=lambda i: (-rb[i][1], i)), fw, False)
-        PLAN[n] = polish(ops, fw, top[1], rng)
-        INFO.append((score(top[1]), score(PLAN[n])))
+                if key[i] is None and pop[p_][i][0] < cut[p_][s_ + 1]:
+                    key[i] = at + max(0.0, pop[p_][i][0] - cut[p_][s_]); pen[i] = -99.0 if pop[p_][i][2] == "v" else 99.0
+            at += cut[p_][s_ + 1] - cut[p_][s_]
+        for i in range(n):
+            for j, _ in fw[i]:
+                if key[j] >= key[i]: key[i] = key[j] + 0.001
+        res = polish(ops, fw, place(sorted(range(n), key=lambda i: (key[i], i)), fw, False), rng, STEPS[0])
+        INFO.append(([round(span(r)) for r in pop], round(at), round(span(res))))
+        PLAN[n] = min(pop + [res], key=span)
     end = [0.0] * n
     for i, o in enumerate(ops):
         o["st"], o["pick"] = PLAN[n][i][0], PLAN[n][i][2]; o["cost"] = PLAN[n][i][1] - o["st"]; end[i] = PLAN[n][i][1] + o.get("dma", 0)
@@ -931,11 +981,9 @@ def rank_program(g, core, T, topo):
         return
     n = len(T.cores)
 
-    def peer(to, half):
-        eng = topo.engines(core, to); back = topo.engines(to, core)
-        eng = eng[:len(eng) // 2] if half == 0 else eng[len(eng) // 2:]
+    def peer(to):
         rid, pid, _ = topo.addr(to)
-        return (rid, pid, sum(1 << x for x in eng), len(eng), len(back) // 2)
+        return (rid, pid, topo.mask(core, to), len(topo.engines(core, to)), len(topo.engines(to, core)))
     ops = []
-    program(ops, T, peer(T.cores[(rank + 1) % n], 0), peer(T.cores[(rank - 1) % n], 1))
+    program(ops, T, peer(T.cores[(rank + 1) % n]), peer(T.cores[(rank - 1) % n]))
     INFO.append((emit(ops, g, T), ops))

@@ -5,44 +5,49 @@ from concourse.mybir import AluOpType as AL, ActivationFunctionType as AF
 F, H, B, I, U = "float32", "float16", "bfloat16", "int32", "uint16"
 SB = {
     "RAW": (2048, I), "X": (5152, B), "RT": (1040, F), "RTH": (1024, H), "TA": (1024, F), "TB": (1024, F), "FL": (1024, B), "FLS": (256, B),
-    "G1": (9216, B), "LN": (512, U), "KT": (1040, B), "CT": (1040, B), "IT": (1040, B), "GR": (1024, H), "HE": (2048, B),
-    "P": (1040, F), "M": (1040, F), "GA": (5392, F), "OV": (9472, B), "EQ": (1024, B), "D2": (1024, H), "GB": (1024, B),
+    "G1": (9216, B), "LN": (512, U), "KT": (1040, B), "CT": (1040, B), "IT": (1040, B), "GR": (1024, F), "HE": (2048, B),
+    "P": (1040, F), "M": (1040, F), "GA": (7584, F), "OV": (9472, B), "EQ": (1024, B), "D2": (1024, H), "GB": (1024, B),
     "GC": (1024, B), "XS": (1024, B), "IDB": (1024, B), "U1J": (1024, F), "LO": (1024, B), "HI": (1024, B), "IO": (1056, F),
-    "IOB": (128, B), "ALL": (2048, B), "Y": (2304, B), "Z": (144 * 14, B), "CM": (128 * 72, B), "ONE": (512, B), "RST": (512, B),
-    "LUT": (2048, B), "EA": (256, U), "EB": (256, U), "ENC": (256, F), "GAW": (256, F), "WN": (3456, B), "ZZ": (1024, F), "ZF": (273, F), "TH": (512, B),
-    "SF": (2624, F), "SI": (1024, I), "SH": (832, B), "SU": (640, U), "S16": (512, H), "W5": (512, F), "W6": (512, F), "WI": (512, I), "WJ": (512, I),
-    "WB": (512, B), "R": (512, B), "PR": (512, B), "SV": (512, B), "INW": (528, H), "NT": (512, F), "WW": (896, F), "CW": (640, H),
-    "YC": (640, H), "GI": (1280, B), "GL": (1280, B), "SRC": (1280, B), "G0": (128, H), "XB": (640, B), "RKW": (64, B), "QS": (64, B), "QR": (256, B),
-    "TP": (384, B), "TR": (384, B), "EQS": (1024, B), "PRS": (1024, H), "FLG": (128, B), "NUS": (128, F), "INC": (128, H), "TG": (128, H),
-    "SW": (1152, B), "SC": (1024, B), "OH": (1024, B), "NE": (1024, H), "SND": (3072, B), "RX": (2048, B), "ONF": (8, F), "EI": (512, I), "OVT": (2048, B), "COL": (16, F), "COI": (16, I), "ZER": (1024, B),
+    "IOB": (128, B), "ALL": (2048, B), "Y": (2304, B), "Z": (144 * 15, B), "CM": (128 * 68, B), "ONE": (1024, B), "RST": (512, B),
+    "LUT": (2048, B), "EA": (256, U), "EB": (256, U), "ENC": (256, F), "GAW": (256, F), "WN": (3456, H), "ZZ": (1024, F), "ZF": (272, F), "TH": (512, B),
+    "SF": (2432, F), "SI": (1024, I), "SH": (960, B), "SU": (400, U), "S16": (512, H), "W5": (512, F), "W6": (512, F), "WI": (512, I), "WJ": (512, I),
+    "WB": (512, B), "R": (512, B), "PR": (512, B), "SV": (512, B), "INW": (272, H), "NT": (512, F), "WW": (1168, F), "CW": (640, H),
+    "YC": (640, H), "GI": (1280, B), "G0": (128, H), "XB": (640, B), "RKW": (64, B), "QS": (64, B), "QR": (256, B),
+    "TP": (384, B), "TR": (384, B), "EQS": (1024, B), "PRS": (1024, H), "FLG": (128, B), "NUS": (128, F), "INC": (144, H), "TG": (144, H),
+    "SW": (1152, B), "SC": (1024, B), "OH": (1024, B), "NE": (1024, H), "SND": (3072, B), "RX": (2048, B), "OVT": (2048, B), "COL": (24, F), "COI": (16, I), "ZER": (1024, B),
 }
 LISTS = {"a": 64, "mk": 64, "sp": 64, "go": 8, "u": 64, "cs": 32, "cw": 40, "i2": 80, "ex": 80, "lu": 80, "ov": 80, "st": 8, "sc": 64, "sx": 64, "sr": 128, "gq": 4, "q": 8}
 SB["Lsh"] = (32, U)
 for _k, _n in LISTS.items():
     SB["L" + _k] = (_n, U)
 SB.update({"SRG": (2048, B), "KP": (256, B), "SM": (3072, B), "SND": (1024, B), "O0": (128, I), "NAM": (640, B), "ZB": (1024, B), "R2": (80, B), "UM": (160, F)})
-ALIAS = {"WI": ("RAW", 1024), "WJ": ("RAW", 1536), "SI": ("RAW", 0), "TA": ("P", 16), "TB": ("ZZ", 0), "GC": ("GB", 0), "EQS": ("SM", 0), "OH": ("SM", 1024),
-         "SC": ("SM", 2048), "NE": ("PRS", 0), "NT": ("W5", 0), "GL": ("G1", 0), "SRC": ("G1", 1280),
+ALIAS = {"WI": ("RAW", 1024), "WJ": ("RAW", 1536), "SI": ("RAW", 0), "TA": ("P", 16), "TB": ("GA", 6560), "ZZ": ("GA", 6560), "WW": ("GA", 5392), "GC": ("GB", 0), "EQS": ("SM", 0), "OH": ("SM", 1024),
+         "SC": ("SM", 2048), "NE": ("PRS", 0), "NT": ("W5", 0),
          "LO": ("EQ", 0), "HI": ("XS", 0), "ZB": ("SRG", 0), "HE": ("G1", 2560), "WB": ("G1", 4752), "R": ("G1", 5264), "PR": ("G1", 5776), "SV": ("G1", 6288)}
 SCRATCH = {k: ("sbuf", [128, n], d) for k, (n, d) in SB.items() if k not in ALIAS}
 for _b in range(8):
     SCRATCH["pb%d" % _b] = ("psum", [128, 512], F)
-ND = 30
+ND = 40
 SEMAPHORES = ["cv", "cs", "cp", "cg"] + ["o%d" % i for i in range(9)] + ["d%d" % i for i in range(ND)] + ["a%d" % i for i in range(9)]
 SIZE = {F: 4, H: 2, B: 2, I: 4, U: 2}
-CYC, PEC, LAT = 0.9, 0.45, 120.0
+CYC, PEC, LAT = 0.9, 0.39, 125.0
 PEN = [1.0, 50.0]
-EDGE = [2, 3, 99]
-EQS, CMP, ABS = ["vv"], [["vs", "vs", "vv"]], [""]
+EDGE = [2, 2, 2]
+SGN = ["ss", "ss", "ss"]
+EQS, CMP, ABS = ["ss", "ss", "ss"], [["vs", "vs", "vv"]], [""]
+DMA, ZOV = [1800.0, 300.0], [1]
 XF, XSE = [1.25, 1.2], [1]
-POP, OVD = [1], [2, 0]
-MBK, STEPS, NEAR, JIT = [4], [10, 16000], [3], [10.0]
-MARK, CUT, HOPW, EDW = [3], [1024], [512], [512]
-HAS = ["mmvv"]
+POP, OVD = [1], [1, 0]
+MBK, STEPS, NEAR, JIT = [4], [6000], [3], [10.0]
+MARK, CUT, HOPW, EDW = [0, 0, 0], [1024], [512], [512]
+SPK = [1, 1, 1]
+WIN = [200, 300]
+NUM = ["pp", "pp", "pp"]
 BLOCKS = [(j, s) for s in range(4) for j in range(2 * s, 8) if j != 2 * s + 1]
 PAIRS = [(0, 8 * j + k, j, k) for j in range(2) for k in range(j + 1, 8)]
 PAIRS += [(1, d, j, k) for d, (j, k) in enumerate((j, k) for j in range(2, 8) for k in range(j + 1, 8))]
-PASSES, PLAN, SEED, TEMP = [400], {}, [5], [1000.0]
+PASSES, PLAN, SEED, TEMP = [60], {}, [5], [1000.0]
+AGAIN, ROOM = [(30, 12000), (0, 12000)], [300.0, 300.0]
 GUESS = [({"o": 1, "g": 1, "s": 1, "p": 1, "x": 1.2}, 130.0, 2.0), ({"o": 1, "g": 0.75, "s": 0.55, "p": 1, "x": 1.2}, 130.0, 1.0),
          ({"o": 1, "g": 1.3, "s": 1.55, "p": 1, "x": 1}, 100.0, 1.0), ({"o": 1, "g": 1.25, "s": 0.7, "p": 1.3, "x": 1.6}, 200.0, 1.0)]
 BIAS = dict([("ends0", 20000.0)] + [(k + str(t), 5000.0) for k in ("pm", "lab", "spk", "edge", "new") for t in range(3)] +
@@ -81,7 +86,8 @@ def program(ops, T, nxt, prv):
     def ap(x):
         if x[0] == "ind":
             return ap(x[1]).indirect(ap(x[2]))
-        return T[x[0]][:, x[1]:x[2]] if x[3] == 1 else T[x[0]][:, x[1]:x[2]:x[3]]
+        t = T[NOW.get(x[0], x[0])]
+        return t[:, x[1]:x[2]] if x[3] == 1 else t[:, x[1]:x[2]:x[3]]
 
     tag = ["", 0]
 
@@ -111,7 +117,7 @@ def program(ops, T, nxt, prv):
         return all(x[0] != "ind" and (x[0].startswith("pb") or SB[x[0]][1] in (F, B)) for x in xs)
 
     def aff_ok(out, a, s1, op0, op1):
-        return fl(out, a) and not (isinstance(s1, tuple) and s1[0].startswith("pb")) and ((op0 == AL.mult and op1 in (None, AL.add)) or (op0 == AL.add and op1 is None))
+        return fl(out, a[1] if a[0] == "ind" else a) and not (isinstance(s1, tuple) and s1[0].startswith("pb")) and ((op0 == AL.mult and op1 in (None, AL.add)) or (op0 == AL.add and op1 is None))
 
     def vcost(out, a, f):
         if out[0] == "ind": return 50 + cols(out) * SCA * CYC
@@ -133,7 +139,7 @@ def program(ops, T, nxt, prv):
                 if op0 == AL.add: return [e["s"].activation(ap(out), ap(a), AF.Identity, bias=sc(s1))]
                 if op1 is None: return [e["s"].activation(ap(out), ap(a), AF.Identity, scale=sc(s1))]
                 return [e["s"].activation(ap(out), ap(a), AF.Identity, bias=sc(s2), scale=sc(s1))]
-            add("vs", fa, [a, s1, s2], [out], vcost(out, a, 0.5 if two(out, a) else 1), cs=vcost(out, a, 1) + 15)
+            add("vs", fa, [a, s1, s2], [out], vcost(out, a, 0.5 if a[0] != "ind" and two(out, a) else 1), cs=vcost(out, a, 1) + 15)
 
         def fn(e):
             if op1 is None: return [e["v"].tensor_scalar(ap(out), ap(a), sc(s1), None, op0)]
@@ -149,7 +155,7 @@ def program(ops, T, nxt, prv):
         add("v", lambda e: [e["v"].memset(ap(out), c)], [], [out], max(64, cols(out) * (0.5 if two(out) else 1)) * CYC)
 
     def scan(out, d0, d1, init, op0, op1):
-        add("v", lambda e: [e["v"].tensor_tensor_scan(ap(out), ap(d0), ap(d1), init, op0, op1)], [d0, d1], [out], max(64, cols(out) * (0.5 if two(out, d0, d1) else 1)) * CYC)
+        add("v", lambda e: [e["v"].tensor_tensor_scan(ap(out), ap(d0), ap(d1), sc(init), op0, op1)], [d0, d1, init], [out], max(64, cols(out) * (0.5 if two(out, d0, d1) else 1)) * CYC)
 
     def act(out, a, func, bias=0.0, scale=1.0):
         add("s", lambda e: [e["s"].activation(ap(out), ap(a), func, bias=sc(bias), scale=sc(scale))], [a, bias, scale], [out], vcost(out, a, 1) + 15)
@@ -175,7 +181,8 @@ def program(ops, T, nxt, prv):
             part.append(i); c += max(64, cols(m[0])) * (4 if SB[m[2][0]][1] == F else 1)
             if c >= CUT[0] or i == n - 1:
                 add("p", lambda e, part=part: [e["p"].matmul(ap(mm[i][0]), ap(mm[i][1]), ap(mm[i][2]), st[i], sp[i]) for i in part],
-                    [mm[i][1] for i in part] + [mm[i][2] for i in part], [mm[i][0] for i in part], c * PEC + (60 if i == n - 1 else 10))
+                    [mm[i][1] for i in part] + [mm[i][2] for i in part], [mm[i][0] for i in part], c * PEC + (60 if i == n - 1 else 10),
+                    cont=[b for b, s in {mm[i][0][0]: st[i] for i in part[::-1]}.items() if not s])
                 part, c = [], 0
 
     def iota(out, pat, base, cm=0):
@@ -185,8 +192,9 @@ def program(ops, T, nxt, prv):
     def asel(out, a, pat, op, fill, base, cm=1):
         add("g", lambda e: [e["g"].affine_select(ap(out), ap(a), pat, op, float(fill), base, cm)], [a], [out], 210 + 2 * cols(out) * CYC)
 
-    def dma(q, pairs, rd, wr, lat):
-        add(q, lambda e: [e[q].dma_start(o, i) for o, i in pairs], rd, wr, 60.0 * len(pairs), dma=lat * XF[1])
+    def dma(q, pairs, rd, wr, kb):
+        c = 60.0 * len(pairs); w = max(c, kb * 1024 / DMA[1])
+        add(q, lambda e: [e[q].dma_start(o, i) for o, i in pairs], rd, wr, w if q == "y" else c, dma=DMA[0] + (0 if q == "y" else w - c))
 
     def pb(b, a=0, e=512, st=1):
         return ("pb%d" % b, a, e, st)
@@ -244,23 +252,23 @@ def program(ops, T, nxt, prv):
     nb, en = T["nb"], T["en"]
     RAW = T["RAW"]
     dma("y", [(RAW[:, 0:512], nb[:, :]), (RAW[:, 512:1024], en[:, :])] +
-        [(RAW[16 * g:16 * g + 16, 1024:1536], nb[16 * (g ^ 1):16 * (g ^ 1) + 16, :]) for g in range(8)], [], [S("RAW", 0, 1536)], 2500)
-    dma("s", [(RAW[16 * g:16 * g + 16, 1536:2048], en[16 * (g ^ 1):16 * (g ^ 1) + 16, :]) for g in range(8)], [], [S("RAW", 1536, 2048)], 2500)
-    dma("y", [(T["X"][:, 16:2192], T["lens"][:, :])], [], [S("X", 16, 2192)], 4000)
+        [(RAW[16 * g:16 * g + 16, 1024:1536], nb[16 * (g ^ 1):16 * (g ^ 1) + 16, :]) for g in range(8)], [], [S("RAW", 0, 1536)], 1024)
+    dma("s", [(RAW[16 * g:16 * g + 16, 1536:2048], en[16 * (g ^ 1):16 * (g ^ 1) + 16, :]) for g in range(8)], [], [S("RAW", 1536, 2048)], 512)
+    dma("y", [(T["X"][:, 16:2192], T["lens"][:, :])], [S("RAW")], [S("X", 16, 2192)], 544)
     RC, HQ, M3, NTB, A64 = [S("COL", i, i + 1) for i in range(5)]
     M8 = [S("COL", 8 + t, 9 + t) for t in range(3)]
     ONE = S("ONE", 0, 128)
-    ms(S("ONE"), 1.0); ms(S("ZER"), 0.0)
+    ms(S("ONE", 0, 512), 1.0); ms(S("ZER"), 0.0); mv(S("ONE", 512, 1024), S("ONE", 0, 512))
     o0 = S("O0", 0, 64); iota(o0, [[2, 32], [1024, 2]], 0, 64)
     iota(S("COI", 0, 1), [[0, 1]], 0, 1)
     blank = ["R1%d" % x for x in (1, 2, 3)] + ["T%d%d" % (b, x) for b in range(2) for x in range(b, 4)] + ["CV", "CV2", "KD", "KD2", "FK"]
     for n in blank: C(n)
     ms(S("Z"), 0.0); ms(S("Y"), 0.0); ms(C("FK"), 0.0); w = 128 * len(blank) - 128
-    dma("y", [(T["CM"][:, a:min(w, a + 1024)], T["ZER"][:, 0:min(w, a + 1024) - a]) for a in range(0, w, 1024)], [S("ZER"), S("RAW"), S("X", 16, 2192)], [S("CM", 0, w)], 4000)
+    dma("y", [(T["CM"][:, a:min(w, a + 1024)], T["ZER"][:, 0:min(w, a + 1024) - a]) for a in range(0, w, 1024)], [S("ZER"), S("RAW")], [S("CM", 0, w)], w // 4)
     ts(S("COI", 1, 2), S("COI", 0, 1), 15, AL.bitwise_and); cp(RC, S("COI", 1, 2))
     ts(S("COI", 2, 3), S("COI", 0, 1), 4, AL.arith_shift_right, 1, AL.bitwise_and); cp(HQ, S("COI", 2, 3))
     ts(S("COI", 3, 4), S("COI", 0, 1), 8, AL.bitwise_and); ts(A64, S("COI", 3, 4), 8.0, AL.mult)
-    ts(M3, RC, 3.0, AL.is_equal); ts(NTB, RC, 64.0, AL.mult, float(1015 - 2 ** 23 - 2048), AL.add)
+    ts(NTB, RC, 64.0, AL.mult, float(1015 - 2 ** 23 - 2048), AL.add)
     for t in range(2): ts(M8[t], RC, 10.0, AL.is_equal, (4.0, 20.0)[t], AL.mult)
     o1 = S("O0", 64, 128); ts(o1, o0, 2047, AL.bitwise_and); o2 = su(64); ts(o2, o1, HQ, AL.add)
 
@@ -275,41 +283,46 @@ def program(ops, T, nxt, prv):
     aff("DUP", 0, 0, 1); aff("ID", 0, 8, 1); aff("FN0", 0, 1000, 1); aff("FN1", 1000, -1000, 1)
     ms(S("XB", 0, 512), 1.0); ms(S("XB", 0, 512, 32), 0.0); ms(S("GB", 0, 512), 0.0); ms(S("GB", 0, 512, 32), 1.0)
     for h in range(2):
-        scan(S("LO", 512 * h, 512 * h + 512), S("XB", 0, 512), S("ONE"), 0.0, AL.mult, AL.add)
-        scan(S("HI", 512 * h, 512 * h + 512), S("ONE"), S("GB", 0, 512), 16.0 * h - 1.0, AL.mult, AL.add)
+        scan(S("LO", 512 * h, 512 * h + 512), S("XB", 0, 512), S("ONE", 0, 512), 0.0, AL.mult, AL.add)
+        scan(S("HI", 512 * h, 512 * h + 512), S("ONE", 0, 512), S("GB", 0, 512), 16.0 * h - 1.0, AL.mult, AL.add)
     M0 = S("COL", 6, 7); ts(M0, RC, 0.0, AL.is_equal)
     asel(S("Y", 15, 2304, 16), S("ONE", 0, 144), [[-1, 16], [-16, 9]], AL.is_equal, 0, 0)
     asel(C("BLK"), ONE, [[-16, 8], [0, 16]], AL.is_ge, 0, 0); asel(C("BLK"), C("BLK"), [[16, 8], [0, 16]], AL.is_ge, 0, 15, -1)
     B8c = sub(C("BLK"), 0, 128, 16)
     asel(Zs("lo8"), B8c, [[16, 8]], AL.is_ge, 0, 7, -1)
     zmake("key", [(0, 2048 * 256), (1, 256), (2, 32 * 256)])
-    V1, VW, DGO, A1C, JK, JG, V256 = sf(64), S("W5"), sf(64), sf(128), sf(64), sf(8), sf(64)
+    V1, VW, DGO, A1C, JG, V256 = sf(64), S("W5"), sf(64), sf(128), sf(8), sf(64)
     iota(V1, [[1, 64]], 1); ts(V1, V1, NTB, AL.add, float(-(1015 - 2 ** 23 - 2048)), AL.add)
-    INEL = sh(64); ts(JK, V1, -8185.0, AL.add); ts(V256, V1, 256.0, AL.mult, -128.0, AL.add)
+    JK = {c: sf(64) for c in set(MARK)}
+    for c, x in JK.items():
+        if c: ts(sub(x, 0, c), sub(V1, 0, c), -9209.0, AL.add)
+        if c < 64: ts(sub(x, c, 64), sub(V1, c, 64), -8185.0, AL.add)
+    INEL = sh(64); ts(V256, V1, 256.0, AL.mult)
+    HLF = S("COL", 10, 11); ts(HLF, RC, 1.0, AL.is_equal, 0.5, AL.mult)
     t0 = sf(64); ts(t0, V1, 128.5, AL.is_lt, 16.0, AL.mult); t1 = sf(64); ts(t1, V1, 896.5, AL.is_gt, 16.0, AL.mult); tt(INEL, t0, t1, AL.add)
     for k in range(8): ms(S("RST", k, 512, 8), -float(2 ** (k - 1)) if k else 1.0e8)
     for n, c in (("KT", 16.0), ("CT", 0.0), ("IT", 0.0), ("RT", 0.0), ("X", 0.0), ("INW", 0.0), ("GA", 0.0)):
         ms(S(n, 0, 16), c)
-    ts(S("KT", 15, 16), M3, -16.0, AL.mult, 16.0, AL.add)
-    ts(S("TA"), IND(S("RAW"), o2), 1.0, AL.add); ts(C("NE2K"), C("FN1"), -2048.0, AL.mult)
-    add("v", lambda e: [e["v"].transpose(ap(S("TB")), ap(S("TA")))], [S("TA")], [S("TB")], 1024 * CYC)
-    act(S("FL"), S("TB"), AF.Sign)
+    ts(S("KT", 15, 16), M0, 16.0, AL.mult, HLF, AL.add); ts(M3, HLF, -1.0, AL.mult)
+    ts(C("NE2K"), C("FN1"), -2048.0, AL.mult)
 
     def f0(h, a, b):
+        ts(S("TA", a, b), IND(S("RAW"), sub(o2, 32 * h, 32 * h + 32)), 1.0, AL.add)
+        add("v", lambda e: [e["v"].transpose(ap(S("TB", a, b)), ap(S("TA", a, b)))], [S("TA", a, b)], [S("TB", a, b)], 512 * CYC)
+        act(S("FL", a, b), S("TB", a, b), AF.Sign)
         pe([(pb(1 + h), C("NE2K"), S("FL", a, b))])
         tt(S("RTH", a, b), pb(1 + h), S("TB", a, b), AL.add)
         pe([(pb(4 + h), Yc(0, 1), S("LO", a, b)), (pb(4 + h), Yc(0, 2), S("HI", a, b))])
-        mv(S("IDB", a, b), pb(4 + h), M3)
+        mv(S("IDB", a, b), pb(4 + h))
     halves(f0)
     iota(S("U1J"), [[1, 64], [64, 16]], 1)
     iota(S("IO"), [[1, 1056]], 0); cp(S("IOB"), S("IO", 0, 128))
     for k in range(4):
-        asel(S("ALL", 512 * k, 512 * k + 512), S("ONE"), [[-1, 4], [-16, 8], [0, 16]], AL.is_equal, 0, -4 * k)
+        asel(S("ALL", 512 * k, 512 * k + 512), S("ONE", 0, 512), [[-1, 4], [-16, 8], [0, 16]], AL.is_equal, 0, -4 * k)
     for k in range(8): ts(sub(C("PW"), k, 128, 8), sub(C("ID"), k, 128, 8), float(2 ** k), AL.mult)
     pe([(pb(7, 0, 8), C("PW"), Zs("lo8"))]); cp(Zs("pow"), pb(7, 0, 8)); zmake("id", [(1, 1), (2, 32)])
-    PWC, PWN, JK2 = S("COL", 14, 15), S("COL", 15, 16), sf(64)
-    pe([(pb(7, 0, 1), C("PW"), S("ONE", 0, 1))]); cp(PWC, pb(7, 0, 1)); ts(PWN, pb(7, 0, 1), -1.0, AL.mult); ts(JK2, V1, -9209.0, AL.add)
-    ts(sub(t0, 16, 17), RC, 1.5, AL.is_gt); ts(sub(t1, 16, 17), RC, 13.5, AL.is_lt, sub(t0, 16, 17), AL.mult); ts(C("INT"), C("ID"), sub(t1, 16, 17), AL.mult)
+    PWN, PWC = S("COL", 15, 16), S("COL", 16, 17)
+    pe([(pb(7, 0, 1), C("PW"), S("ONE", 0, 1))]); ts(PWN, pb(7, 0, 1), -1.0, AL.mult); cp(PWC, pb(7, 0, 1))
 
     ts(C("I8"), C("ID"), 8.0, AL.mult); ts(C("NID"), C("ID"), -1.0, AL.mult); ts(C("IDK"), C("ID"), 1.0 / 1024, AL.mult)
     RC1, WX = S("COL", 7, 8), S("COL", 11, 12)
@@ -318,31 +331,61 @@ def program(ops, T, nxt, prv):
     iota(S("QS"), [[1, 4], [4, 16]], 0); ts(sub(t0, 0, 1), RC, 4.0, AL.mult, 1024.0, AL.add); ts(sub(JG, 0, 4), S("IO", 0, 4), sub(t0, 0, 1), AL.add)
     iota(S("ENC"), [[0, 256]], 2048)
     for c, z in ((0, "lo8"), (4, "lo8"), (5, "pow")): cp(sub(C("FK"), c, 128, 16), Zs(z))
-    ts(sub(t0, 0, 1), RC, 0.5, AL.is_gt); ts(C("KS"), C("ID"), sub(t0, 0, 1), AL.mult); ts(S("CT", 15, 16), M0, 1000.0, AL.mult)
+    ts(sub(t0, 0, 1), RC, 0.5, AL.is_gt); ts(C("KS"), C("ID"), sub(t0, 0, 1), AL.mult)
+    ts(S("CT", 15, 16), M0, 1000.0, AL.mult)
     tag[0] = "ends"
-    ms(S("ZF"), 0.0); VW = pb(5, 0, 256)
-    for h in range(4): ts(sub(VW, 64 * h, 64 * h + 64), S("IO", 0, 1024, 16), RC, AL.add)
-    EO = S("SU", 128, 640)
-    ts(C("I136"), C("ID"), 136.0, AL.mult)
-    for a in range(0, 512, 256):
-        en_, w, x, y, p, q = S("RAW", 512 + a, 768 + a), S("W6", a, a + 256), S("OH", a, a + 256), S("EI", a, a + 256), pb(7, 0, 256), pb(6, 0, 256)
-        tt(x, VW, S("RAW", a, a + 256), AL.is_lt); pe([(q, C("I136"), x)])
-        ts(y, en_, 4, AL.logical_shift_right); ts(w, y, -4351.0, AL.mult, 1040.0, AL.add)
-        ts(p, en_, 272.0, AL.mult, flex=False); tt(w, p, w, AL.add); tt(w, q, w, AL.add); tt(w, VW, w, AL.max); cp(sub(EO, a, a + 256), w)
-    dma("y", [(T["GA"][0:128:16, 1024:5392], T["ZF"][:, :])], [S("ZF")], [S("GA", 1024, 5392)], 2500)
+    ms(S("ZF"), 0.0)
+    for a in range(0, 2176, 272): mv(S("GA", a, a + 272), S("ZF"))
+    dma("y", [(T["GA"][c:128:16, 2176:4352], T["ZF"][:, 0:136]) for c in range(2)], [S("ZF"), S("RAW")], [S("GA", 2176, 4352)], 140)
     tag[0] = ""
-    dma("y", [(T["X"][:, a:b], T["ZER"][:, 0:b - a]) for a, b in ((2192, 3216), (3216, 4240), (4240, 5152))], [S("ZER"), S("RAW"), S("X", 16, 2192)], [S("X", 2192, 5152)], 5000)
+    dma("y", [(T["X"][:, a:b], T["ZER"][:, 0:b - a]) for a, b in ((2192, 3216), (3216, 4240), (4240, 5152))], [S("ZER"), S("RAW")], [S("X", 2192, 5152)], 740)
     ms(S("X", 4112, 4113), 300.0)
-    dma("y", [(T["OV"][:, 1024 * k:1024 * k + 1024], T["ZER"][:, :]) for k in range(8)], [S("ZER"), S("X", 2192, 2200)], [S("OV", 0, 8192)], 12000)
 
-    def zero_ov():
-        dma("y", [(T["OV"][c:128:8, 0:8192], T["ZER"][:, :]) for c in (1, 2)], [S("ZER")], [S("OV", 0, 8192)], 4000)
+    def zero_ov(t, when):
+        if t: dma("y", [(T["OV"][c:128:8, 0:8192], T["ZER"][:, :]) for c in (1, 2)], [S("ZER"), when], [S("OV", 0, 8192)], 512)
+        else: dma("y", [(T["OV"][:, 1024 * k:1024 * k + 1024], T["ZER"][:, :]) for k in range(8)], [S("ZER"), when], [S("OV", 0, 8192)], 2048)
 
     def ends():
         tag[0] = "ends"
-        for k in range(16): put(IND(S("GA"), sub(EO, 32 * k, 32 * k + 32)), S("IO", 32 + 512 * (k % 2), 544 + 512 * (k % 2)))
-        dma("y", [(T["W6"][:, 0:272], T["GA"][0:128:16, 1040:5392])], [S("GA", 1040, 5392)], [S("W6", 0, 272)], 2500)
-        for s_, L in enumerate(("EA", "EB")): ts(S(L, 0, 136), S("W6", 136 * s_, 136 * s_ + 136), -15.8, AL.add, 15.0, AL.max)
+        f, TT, CL, PL, SL = S("SM", 0, 1024), S("ZZ"), S("SU", 64, 200), S("SU", 200, 336), S("SU", 336, 400)
+        cn, em, st, ex, ML, AB = sh(64), sh(64), S("S16", 64, 128), sf(72), sf(136), S("COL", 14, 15)
+        ms(sub(ex, 0, 1), -1088.0); iota(ML, [[16, 136]], 0); ts(ML, ML, RC, AL.add); ts(AB, HLF, 2 * 16416.0, AL.mult)
+        for a in (0, 512): ts(S("M", 16 + a, 528 + a), S("IO", a, a + 512), 1024.0, AL.add)
+        ts(S("W5", 0, 128), S("IO", 0, 128), 2048.0, AL.add)
+        for h in range(2):
+            a, b = 512 * h, 512 * h + 512
+            pe([(pb(14 + h), C("DUP"), S("RTH", a, b))]); tt(sub(f, a, b), pb(14 + h), S("IO", 1 + a, 1 + b), AL.is_gt)
+        p = pb(14, 0, 64)
+        ext(p, [("lo8", f)], 1024); cp(cn, p); ts(em, p, 0.0, AL.is_equal, 8192.0, AL.mult)
+        pe([(p, C("BLK"), cn)]); scan(sub(ex, 1, 65), S("ONE", 0, 64), p, -1088.0, AL.mult, AL.add)
+        pe([(p, C("LT"), cn)]); tt(st, p, sub(ex, 0, 64), AL.add)
+        pe([(p, C("ID"), st), (p, C("ID"), em)]); ts(p, p, 1088.0, AL.add); tt(S("W6", 0, 64), p, DE, AL.min); cp(SL, S("W6", 0, 64))
+        for h in range(2):
+            a, b, p = 512 * h, 512 * h + 512, pb(14 + h)
+            pe([(p, C("LS8"), sub(f, a, b)), (p, C("I4K"), S("RTH", a, b))] + [(sub(p, r, 512, 16), Al(r), sub(st, 32 * h, 32 * h + 32)) for r in range(16)])
+            mv(sub(TT, a, b), p, 576.0)
+            put(IND(S("GA", 0, 5376), sub(SL, 32 * h, 32 * h + 32)), S("IO", 32 + a, 32 + b))
+        for i, a in enumerate(range(0, 2176, 512)):
+            b = min(2176, a + 512); c, d = a // 16, b // 16; p = pb(14, 0, d - c)
+            scan(S("WN", a, b), S("GA", a, b), S("GA", a, b), sub(ex, 66 + i, 67 + i) if a else 0.0, AL.max, AL.max)
+            if b < 2176: cp(sub(ex, 67 + i, 68 + i), S("WN", b - 1, b))
+            ext(p, [("c0", S("WN", a, b))], b - a); ts(sub(CL, c, d), p, -32.0, AL.add, 0.0, AL.max)
+        for lot in ((0, 512), (1024, 1536, 2048)):
+            c, d = lot[0] // 16, min(136, lot[-1] // 16 + 32); p = pb(16, 0, d - c); part = []
+            for a in lot:
+                b = min(2176, a + 512); k = a % 1024; q = pb(15, 0, b - a)
+                y, src = S("PRS", k, k + b - a), S("P", 16 + k, 16 + k + b - a) if a < 2048 else S("W5", 128, 256)
+                tt(y, IND(TT, sub(CL, a // 16, b // 16)), (S("IO", a, b), S("M", a - 1008, b - 1008), S("W5", 0, 128))[a // 1024], AL.subtract); ts(y, y, -0.5, AL.max, 0.5, AL.min)
+                ext(sub(p, a // 16 - c, b // 16 - c), [("e4k", y)], b - a)
+                pe([(q, Zs("l4k", 1), y), (q, Yc(0, 0), S("WN", a, b))]); mv(src, q, AB); part.append((sub(PL, a // 16, b // 16), src))
+            w0, w1, w2, x0, x1 = S("WI", 256, 256 + d - c), S("WI", 336, 336 + d - c), S("WI", 416, 416 + d - c), S("W6", 272, 272 + d - c), S("W6", 400, 400 + d - c)
+            ts(w0, p, 65535.0, AL.add); ts(w1, w0, 4095, AL.bitwise_and); ts(w2, w1, 4, AL.arith_shift_right)
+            ts(x0, w2, 136.0, AL.min, -2175.0, AL.mult); ts(p, w1, 2175.0, AL.min, 136.0, AL.mult); tt(x0, p, x0, AL.add)
+            ts(p, w1, 4000.0, AL.is_lt, 2176.0, AL.mult); tt(x0, p, x0, AL.add); tt(x1, x0, sub(ML, c, d), AL.max); cp(sub(PL, c, d), x1)
+            for l, src in part: put(IND(S("GA", 0, 4352), l), src)
+        dma("y", [(T["W6"][:, 136 * c:136 * c + 136], T["GA"][c:128:16, 2176:4352]) for c in range(2)], [S("GA", 2176, 4352)], [S("W6", 0, 272)], 240)
+        ts(S("EA", 0, 136), S("W6", 0, 136), -15.8, AL.add, 15.0, AL.max)
+        ts(S("WJ", 256, 392), S("W6", 136, 272), -32.0, AL.add); ts(S("WI", 256, 392), S("WJ", 256, 392), 4095, AL.bitwise_and); ts(S("EB", 0, 136), S("WI", 256, 392), -2033.0, AL.add, 1039.0, AL.min)
     for n in ("P", "M"): ms(S(n, 0, 15), 0.0); ms(S(n, 15, 16), 1000.0)
     asel(Zs("en"), B8c, [[-16, 8]], AL.is_ge, 0, -8)
     asel(C("LT"), C("BLK"), [[16, 8], [1, 16]], AL.is_gt, 0, 0, -1)
@@ -364,8 +407,13 @@ def program(ops, T, nxt, prv):
     pe([(pb(7, 0, 1), C("R1%d" % x), sub(x3, x, x + 1)) for x in (1, 2, 3)]); ts(DB[1], pb(7, 0, 1), 1.0 / 1024, AL.mult, -1025.0 - 2057.0 / 8192, AL.add)
     tt(C("LW"), C("LT"), C("BLK"), AL.subtract)
     asel(C("LS"), C("LW"), [[-1, 128]], AL.not_equal, 512, 0); asel(C("LW"), C("LW"), [[-1, 128]], AL.not_equal, 1024, 0)
+    asel(C("LS8"), C("L8"), [[-1, 128]], AL.not_equal, 512, 0); ts(C("L8"), C("L8"), 0.5, AL.mult)
+    pe([(pb(7, 0, 1), C("L8"), S("ONE", 0, 1))]); PRC, RRC = [-7.5, S("COL", 17, 18)], [-7.0 / 8192, S("COL", 18, 19)]
+    ts(PRC[1], pb(7, 0, 1), -1.0, AL.mult, -7.5, AL.add); ts(RRC[1], pb(7, 0, 1), -1.0 / 8192, AL.mult, -7.0 / 8192, AL.add)
+    ts(C("I4K"), C("ID"), 1.0 / 4096, AL.mult)
+    ts(Zs("e4k"), Zs("en"), 4096.0, AL.mult); ts(Zs("l4k"), Zs("lo8"), 4096.0, AL.mult); DE = sf(64); ts(DE, DGO, 4352.0 - 129, AL.add)
     ts(C("EN2K"), C("FN1"), 2048.0, AL.mult)
-    cp(Zs("all"), B8c); ts(Zs("8k"), B8c, 8192.0, AL.mult)
+    cp(Zs("all"), B8c); ts(Zs("nall"), B8c, -1.0, AL.mult); ts(Zs("8k"), B8c, 8192.0, AL.mult)
     zmake("om", [(5, 1)]); ts(Zs("l17"), Zs("lo8"), 1024.0, AL.mult); zmake("l17", [(0, 0)])
     CV, KD = C("CV"), C("KD")
     for ch, w, off in ((1, 1, 15), (2, 32, 15), (9, 1, 23), (10, 32, 23)): poke(sub(CV, off, off + 128, 16), ch, w)
@@ -377,15 +425,16 @@ def program(ops, T, nxt, prv):
         tt(m, m, m2, AL.add)
     for off in (15, 23): poke(sub(KD, off, off + 128, 16), 0, 4096)
     DW, DOV, DX = sf(32), sf(80), sf(64)
-    ts(DW, sub(DGO, 0, 32), 511.0, AL.add); ts(DX, DGO, -1.0, AL.mult, 2175.0, AL.add)
+    ts(DW, sub(DGO, 0, 32), 783.0, AL.add); ts(DX, DGO, 3984.0, AL.add)
     ts(sub(DOV, 0, 64), DGO, 8064.0, AL.add); ts(sub(DOV, 64, 80), sub(DGO, 0, 16), 9088.0, AL.add)
-    DS = sf(64); ts(DS, S("IO", 0, 64), 512.0, AL.add); ts(sub(A1C, 0, 64), S("IO", 0, 64), A64, AL.add, 1.0, AL.add)
+    DS = sf(4); ts(DS, sub(DGO, 0, 4), 383.0, AL.add); ts(sub(A1C, 0, 64), S("IO", 0, 64), A64, AL.add, 1.0, AL.add)
     N896 = sh(64); ms(N896, -896.0); ms(sub(A1C, 64, 128), 0.0)
     asel(C("GE8"), C("B8"), [[-16, 8], [-1, 16]], AL.is_ge, 0, 0)
     pe([(pb(7, 0, 1), C("P2"), S("Y", 15, 16))]); P2C = S("COL", 5, 6); cp(P2C, pb(7, 0, 1))
     ts(S("WI", 0, 256), S("IO", 0, 256), P2C, AL.mult); ts(S("WJ", 0, 256), S("WI", 0, 256), 2048, AL.bitwise_and)
     ts(S("KP"), S("WJ", 0, 256), 0.0, AL.is_equal); pe([(pb(7, 0, 256), C("GE8"), S("KP"))])
-    for n in range(8): ts(S("LUT", 256 * n, 256 * n + 256), pb(7, 0, 256), float(n), AL.is_gt)
+    cp(S("KP"), pb(7, 0, 256))
+    for n in range(8): ts(S("LUT", 256 * n, 256 * n + 256), S("KP"), float(n), AL.is_gt)
     aff("FE0", 8, 1000, 1); aff("FE1", 1008, -1000, 1); aff("DUPE", 8, 0, 1)
     for h in range(2):
         m = 320 * h; pe([(pb(6 + h, 0, 320), Yc(0, 9), S("LO", m, m + 320)), (pb(6 + h, 0, 320), Yc(0, 10), S("HI", m, m + 320))]); mv(S("NAM", m, m + 320), pb(6 + h, 0, 320), M8[0])
@@ -393,33 +442,38 @@ def program(ops, T, nxt, prv):
     for s_ in range(4):
         for ha in range(2): aff("NP%d%d" % (s_, ha), 8 * ha + 2 * s_, 1, 0, C("NEG"))
         tt(C("VB%d" % s_), C("DUP"), C("NP%d0" % s_), AL.subtract)
-    ms(C("N13"), -1.0 / 8192)
+    ms(C("N13"), 1.0 / 8192)
     for ha, (c0, al) in enumerate(((0, 1000), (1000, -1000))):
         aff("SH%d" % ha, c0, al, 1, C("K8")); asel(C("SH%d" % ha), C("SH%d" % ha), [[-16, 8], [-al, 2], [-1, 8]], AL.not_equal, 8192, -c0 - 8)
         aff("NFE%d" % ha, c0 + 8, al, 1, C("N13"))
     for s_ in range(4): aff("NQ%d" % s_, 8 + 2 * s_, 1, 0, C("N13"))
 
-    OK_, M1, CH, NCH, TG1, TG2, TG3, TG4, LB1, LB2, GG, G4 = [sf(64) for _ in range(12)]
+    OK_, CH, NCH, TG1, TG2, TG3, LB1, LB2, GG, G4, TG5 = [sf(64) for _ in range(11)]
     MI, AI, BI = [si(64) for _ in range(3)]
-    SELF, INB, RK1, CB, CON, BB, DGB, BG, SD, DEAD = [sh(64) for _ in range(10)]
-    ms(DEAD, 0.0)
-    E = {"nxt": nxt, "prv": prv, "zero_ov": zero_ov}
+    SELF, RK1, CB, CON, BB, DGB, BG, SD, DEAD = [sh(64) for _ in range(9)]
+    INZ = sh(72); ms(DEAD, 0.0); ms(sub(INZ, 0, 1), 0.0); ms(S("INC", 0, 144, 72), 0.0)
+    E = {"nxt": nxt, "prv": prv, "zero_ov": zero_ov, "won": []}
     for k, w in (("ci", 40), ("c4", 40), ("yi", 40), ("hk", 80), ("vl", 40), ("rr", 80), ("w0", 64), ("w1", 64)): E[k] = si(w)
     for k in ("c2", "i2", "u2", "t2", "t3"): E[k] = sf(80)
-    for k in ("q0", "q1", "q2", "q3"): E[k] = sf(128)
+    for k in ("q0", "q3"): E[k] = sf(128)
     A1H, A1G, LP, LM = [S("S16", 64 * i, 64 * i + 64) for i in range(4)]
     IDR, E2 = S("S16", 256, 384), S("S16", 384, 512)
     AL_, MKL, SPL, GOL, UL, CSL, CWL, I2, EXL, LUL, OVL, STL, SCL, SXL, SRL, GQL, QL = [S("L" + k) for k in LISTS]
     RTW, XW = S("RT"), S("X")
 
-    def hop():
+    def fold(out, f, src, a, n, more=None):
+        pe([(out, C(f + str(h)), S(x, a + h, a + n, 2)) for x in [src] + ([more] if more else []) for h in range(2)])
+
+    def hop(t):
+        tag[:] = ["h", t]
+        for h in range(2):
+            fold(pb(1, 0, 256), "FN", "RTH", 512 * h, 512); ts(S("LN", 256 * h, 256 * h + 256), pb(1, 0, 256), 15.0, AL.add)
+        extc(pb(2, 0, 64), "c0", S("KT", 16, 1040))
+        cp(DGB, pb(2, 0, 64)); ts(pb(2, 0, 64), pb(2, 0, 64), 2048.0 * 256, AL.mult); tt(TG5, pb(2, 0, 64), V256, AL.add); ts(OK_, TG5, float(2 ** 23), AL.min)
         w = HOPW[0]
         for r in range(16):
             for a in range(512 * r, 512 * r + 512, w): mv(S("G1", a, a + w), IND(S("KT"), S("LN", a // 16, (a + w) // 16)))
-            pe([(pb(0), Zs("key", r), S("G1", 512 * r, 512 * r + 512))], r == 0, r == 15)
-
-    def fold(out, f, src, a, n):
-        pe([(out, C(f + "0"), S(src, a, a + n, 2)), (out, C(f + "1"), S(src, a + 1, a + n, 2))])
+            pe([(pb(10), Zs("key", r), S("G1", 512 * r, 512 * r + 512))], r == 0, r == 15)
 
     def part_a(t):
         tag[:] = ["a", t]
@@ -427,43 +481,42 @@ def program(ops, T, nxt, prv):
             a, b, k = 512 * h, 512 * h + 512, 2 * h
             pe([(pb(k), C("ID"), S("IDB", a, b))] + [(pb(k, 64 * r, 64 * r + 64), Yc(8 * h + r, 0), INEL) for r in range(8)], True, False)
             pe([(pb(k), C("FK"), S("FL", a, b))], False, True)
-            mv(S("KT", 16 + a, 16 + b), pb(k))
-            fold(pb(1, 0, 256), "FN", "RTH", a, 512); ts(S("LN", 256 * h, 256 * h + 256), pb(1, 0, 256), 15.0, AL.add)
-        extc(pb(2, 0, 64), "lo8", S("FL"), [(pb(2, 0, 64), C("ID"), INEL)])
-        ts(TG1, pb(2, 0, 64), 2048.0 * 256, AL.mult); tt(OK_, TG1, V256, AL.add)
-        if t >= MARK[0]: cp(DGB, pb(2, 0, 64))
+            mv(S("KT", 16 + a, 16 + b), pb(k), HLF)
+        hop(t); tag[0] = "a"
         for h in range(2): pe([(pb(1 + h), C("DUP"), S("RTH", 512 * h, 512 * h + 512))]); mv(S("RT", 16 + 512 * h, 528 + 512 * h), pb(1 + h))
-        hop()
-        scan(S("W5"), S("RST"), pb(0), 0.0, AL.add, AL.min); ops[-1]["meet"] = True
-        tt(M1, S("W5", 7, 512, 8), OK_, AL.min); ts(MI, M1, 128.0, AL.add, float(2 ** 23), AL.min); ts(AI, MI, 8, AL.arith_shift_right, 2047, AL.bitwise_and)
+        scan(pb(9), S("RST"), pb(10), 0.0, AL.add, AL.min)
+        tt(MI, pb(9, 7, 512, 8), OK_, AL.min); ts(AI, MI, 8, AL.arith_shift_right, 2047, AL.bitwise_and)
         ts(AL_, AI, 15.0, AL.add)
         tt(S("GB"), IND(RTW, AL_), S("U1J"), AL.is_equal)
         cp(A1H, AI); tt(SELF, AI, V1, AL.is_equal); ts(BI, MI, 255, AL.bitwise_and); ts(BB, BI, -1.0, AL.mult)
         for h in range(2):
-            pe([(pb(4 + h), C("KS"), S("KT", 16 + 512 * h, 528 + 512 * h))] + [(blk(4, r), Yc(r, 5), BB) for r in range(8 * h, 8 * h + 8)], True, False)
+            a, b, p = 512 * h, 512 * h + 512, pb(4 + h)
+            pe([(p, C("KS"), S("KT", 16 + a, 16 + b))] + [(blk(4, r), Yc(r, 5), BB) for r in range(8 * h, 8 * h + 8)], True, False)
         ts(LB1, AI, -1000.0, AL.add, flex=False); ts(LB2, AI, -1.0, AL.mult, -1000.0, AL.add, flex=False)
         tt(SD, SELF, DEAD, AL.add)
         pe([(pb(3, 0, 64), C("I8"), A1H)] + [(pb(3, 0, 64), Zs("idx", r), S("GB", r, 1024, 16)) for r in range(16)])
         y, WD = pb(3, 0, 64), S("IT", 16, 528)
-        if t < MARK[0]:
-            tt(TG1, y, JK, AL.min); ts(MKL, TG1, 16376.0, AL.add); cp(IND(S("G1"), MKL), S("ZER"))
-            dma("y", [(T["IT"][:, 16:528], T["G1"][3:128:16, 0:8192])], [S("G1", 0, 8192)], [WD], 2300)
-            pe([(y, C("I8"), SELF)] + [(y, C("NID"), sub(WD, k, 512, 8)) for k in range(8)]); edge = 7.5
-        else:
-            dma("y", [(T["GA"][0:128:16, 0:6144], T["ONF"][:, :])], [S("ONF")], [S("GA", 0, 6144)], 2500)
-            tt(TG1, y, JK2, AL.min); ts(MKL, TG1, 15352.0, AL.add); put(IND(S("GA"), MKL), S("IO", 32, 1056))
-            dma("y", [(T["W6"][16 * g + 2:16 * g + 14, :], T["GA"][16 * g:16 * g + 1, 0:6144]) for g in range(8)], [S("GA", 0, 6144)], [S("W6")], 2300)
-            act(WD, S("W6"), AF.Sign, -2.0)
-            pe([(y, C("I136"), SELF), (y, C("NID"), DGB), (y, C("NID"), DGB)] + [(y, C("INT"), sub(WD, k, 512, 8)) for k in range(8)]); edge = 127.5
+        tt(TG1, y, JK[MARK[t]], AL.min); seen = []; c = MARK[t]; WS = S("IT", 528, 1040)
+        if c < 64:
+            ts(sub(MKL, c, 64), sub(TG1, c, 64), 16376.0, AL.add)
+            cp(IND(S("G1"), sub(MKL, c, 64)), S("ONE", 0, 1024 - 16 * c))
+            dma("y", [(T["IT"][:, 16:528], T["G1"][3:128:16, 0:8192])], [S("G1", 0, 8192)], [WD], 200); seen.append(WD)
+        if c:
+            dma("y", [(T["GA"][0:128:16, a:a + 3072], T["ZF"][:, 0:192]) for a in (16, 3088)], [S("ZF")], [S("GA", 16, 6160)], 200)
+            ts(sub(MKL, 0, c), sub(TG1, 0, c), 15352.0, AL.add)
+            for a in range(0, c, 32): put(IND(S("GA", 16, 7184), sub(MKL, a, a + 32)), S("IO", 32, 544))
+            dma("y", [(T["W6"][16 * g + 2:16 * g + 14, :], T["GA"][16 * g:16 * g + 1, 16:6160]) for g in range(8)], [S("GA", 16, 6160)], [S("W6")], 200)
+            act(WS, S("W6"), AF.Sign); seen.append(WS)
+        pe([(y, C("I8"), SELF), (y, C("I8"), SELF), (y, C("NID"), DGB)] + [(y, C("ID"), sub(x, k, 512, 8)) for x in seen for k in range(8)]); edge = 15.5
         ts(CH, y, edge, AL.is_gt); ts(NCH, y, edge, AL.is_lt, 1000.0, AL.mult)
-        scan(INB, S("ONE", 0, 64), CH, 0.0, AL.mult, AL.add)
+        INB = sub(INZ, 1, 65); scan(INB, S("ONE", 0, 64), CH, 0.0, AL.mult, AL.add)
         off = pb(3, 0, 1); pe([(off, C("LT"), sub(INB, 63, 64))])
         tt(TG2, INB, NCH, AL.add); ts(RK1, TG2, off, AL.add); ts(CON, RK1, 128.5, AL.is_lt)
         for h in range(2):
             pe([(blk(4, r), Yc(r, 0), RK1) for r in range(8 * h, 8 * h + 8)], False, True)
-            mv(S("CT", 16 + 512 * h, 528 + 512 * h), pb(4 + h))
+            mv(S("CT", 16 + 512 * h, 528 + 512 * h), pb(4 + h), M3)
         x0, x1, x2, x3 = [sub(G4, 8 * i, 8 * i + 4) for i in range(4)]
-        tt(x0, sub(INB, 0, 64, 16), sub(CH, 0, 64, 16), AL.subtract); tt(x1, x0, sub(INB, 15, 64, 16), AL.is_equal)
+        x0 = sub(INZ, 0, 64, 16); tt(x1, x0, sub(INB, 15, 64, 16), AL.is_equal)
         tt(x2, x1, sub(JG, 0, 4), AL.mult); tt(x3, x2, x0, AL.add); ts(GQL, x3, off, AL.add)
         QR, E1 = S("QR", 0, 128), S("QR", 128, 256)
         ms(S("G1", 0, 128), 0.0); cp(IND(S("G1", 0, 1920), GQL), S("QS")); scan(QR, S("G1", 0, 128), S("G1", 0, 128), 0.0, AL.max, AL.max)
@@ -473,29 +526,38 @@ def program(ops, T, nxt, prv):
         ext(pb(3, 0, 8), [("all", E2)], 128); ts(GOL, pb(3, 0, 8), 15.0, AL.add)
         cp(S("G0"), IND(RTW, GOL))
         fold(pb(3, 0, 64), "FN", "G0", 0, 128); ts(UL, pb(3, 0, 64), 15.0, AL.add)
-        ts(TG2, CON, 16.0, AL.mult); tt(INEL, INEL, TG2, AL.add)
         tag[0] = "lab"
         for h in range(2): mv(S("GC", 512 * h, 512 * h + 512), IND(S("CT"), sub(AL_, 32 * h, 32 * h + 32)))
         ext(pb(5, 0, 64), [("c0", S("GC"))], 1024)
-        ts(CB, pb(5, 0, 64), 128.5, AL.is_lt); tt(BG, CB, BB, AL.mult); tt(GG, CB, SD, AL.is_gt)
+        ts(CB, pb(5, 0, 64), 128.5, AL.is_lt); tt(GG, CB, SD, AL.is_gt)
+        if not SPK[t]: tt(BG, CB, BB, AL.mult)
         tt(LP, LB1, GG, AL.mult); tt(LM, LB2, GG, AL.mult); tt(DEAD, DEAD, CON, AL.add)
-        w2r(1, [(Al, lambda r: BG)])
+        if t < 2: ts(TG2, CON, 16.0, AL.mult); tt(INEL, INEL, TG2, AL.add)
+        w2r(1, [(Al, lambda r: BB if SPK[t] else BG)])
         for h in range(2):
             p = pb(1 + h)
-            if EQS[0][h] == "v": ts(p, p, PWN, AL.is_equal)
+            if EQS[t][h] == "v": ts(p, p, PWN, AL.is_equal)
             else: act(p, p, AF.Abs, PWC); act(p, p, AF.Relu, 1.0, -1.0)
             tt(S("D2", 512 * h, 512 * h + 512), p, S("RTH", 512 * h, 512 * h + 512), AL.mult)
         extc(pb(1, 0, 64), "en", S("D2")); ts(SPL, pb(1, 0, 64), 2063.0, AL.add)
+        if SPK[t]:
+            if SPK[t] == 2: lengths()
+            w2r(1, [(Al, lambda r: CB)])
+            for h in range(2): tt(S("D2", 512 * h, 512 * h + 512), pb(1 + h), S("D2", 512 * h, 512 * h + 512), AL.mult)
 
-    def spokes():
-        tag[0] = "pm"
+    def lengths():
         for h in range(2): mv(S("XS", 512 * h, 512 * h + 512), IND(XW, sub(SPL, 32 * h, 32 * h + 32)))
+
+    def spokes(t):
+        tag[0] = "pm"
+        if SPK[t] < 2: lengths()
         for b0, tab, lab in ((4, "P", LP), (MBK[0], "M", LM)):
             w2r(b0, [(Al, lambda r, lab=lab: lab), (lambda r: C("IDK"), lambda r: S("XS", r, 1024, 16))])
             halves(lambda h, a, b, b0=b0, tab=tab: mv(S(tab, 16 + a, 16 + b), pb(b0 + h), 1000.0))
 
     def part_b(t):
         tag[:] = ["b", t]
+        zero_ov(t, CH if t or ZOV[0] else OK_)
         for h, a in enumerate((896, 0) if t else ()):
             p = pb(6 + h, 0, 128)
             pe([(p, C("ID"), S("IDB", a, a + 128))] + [(sub(p, 64 * i, 64 * i + 64), Yc(a // 64 + i, 5), BB) for i in range(2)], True, False)
@@ -504,49 +566,49 @@ def program(ops, T, nxt, prv):
         n = 2176 + 640 * t; nch = -(-n // EDW[0]); w = -(-n // (32 * nch)) * 32
         for i, a in enumerate(range(0, n, w)):
             b = min(n, a + w); k = i % 2; ga, zz = S("GA", 16 + a, 16 + b), S("ZZ", 512 * k, 512 * k + b - a)
-            act(ga, IND(S("P"), S("EA", a // 16, b // 16)), AF.Copy)
+            mv(ga, IND(S("P"), S("EA", a // 16, b // 16)))
             tt(zz, IND(S("M"), S("EB", a // 16, b // 16)), ga, AL.add)
             z, x = pb(4 + k, 0, b - a), S("X", 16 + a, 16 + b)
             if i % EDGE[t] == 0:
-                act(z, zz, AF.Abs, 0.0, 1024.0); tt(S("WN", a, b), z, x, AL.is_lt); tt(x, z, x, AL.min)
+                act(z, zz, AF.Abs, 0.25, 1024.0); tt(S("WN", a, b), z, x, AL.min); ts(x, S("WN", a, b), 3.0 * 2 ** 22, AL.add, -3.0 * 2 ** 22, AL.add)
+                E["won"].append((t, a, b))
             else:
                 zb = S("ZB", 512 * k, 512 * k + b - a); act(zb, zz, AF.Abs, 0.0, 1024.0)
                 pe([(z, C("ID"), x), (z, C("NID"), zb)]); act(zb, z, AF.Relu)
-                ts(S("WN", a, b), zb, 0.0, AL.is_gt)
+                ts(S("WN", a, b), zb, 0.0, AL.is_gt, 0.25, AL.mult)
                 pe([(z, C("ID"), x), (z, C("NID"), zb)]); mv(x, z)
         tag[0] = "b"
-        for h in range(2): ts(S("GR", 512 * h, 512 * h + 512), IND(RTW, sub(UL, 32 * h, 32 * h + 32)), -1.0, AL.max)
+        for h in range(2): ts(S("GR", 512 * h, 512 * h + 512), IND(RTW, sub(UL, 32 * h, 32 * h + 32)), -1.0, AL.mult)
         for h in range(2): mv(S("IT", 16 + 512 * h, 528 + 512 * h), IND(S("CT"), sub(UL, 32 * h, 32 * h + 32)))
         J = lambda x, jj: sub(x, 128 * jj, 128 * jj + 128)
         gu = lambda jj, h: S("IT", 16 + 2 * jj + h, 1040, 8)
         FG = S("QR", 0, 128); ts(FG, S("G0"), 0.0, AL.is_gt)
         pe([(pb(0), C("ID"), S("TH"))] + [(J(pb(0), jj), C("VB%d" % jj), FG) for jj in range(4)], True, False)
-        for i in range(4):
-            p, he = pb((3, 1, 2, 6)[i]), S("HE", 512 * i, 512 * i + 512)
-            a, part, K = 64 * (i // 2), list(enumerate(BLOCKS[8 * (i % 2):8 * (i % 2) + 8])), (lambda x, n: sub(x, 64 * n, 64 * n + 64))
-            pe([(K(p, x), C("NP%d0" % s), S("G0", a, a + 64)) for x, (j, s) in part], True, False)
-            pe([(K(p, x), C("ID"), S("GR", 8 * a + j, 8 * a + 512, 8)) for x, (j, s) in part], False, True)
-            if HAS[0][i] == "v": ts(he, p, 0.0, AL.is_equal)
-            elif HAS[0][i] == "s": act(he, p, AF.Abs); act(he, he, AF.Relu, 1.0, -1.0)
-            else: act(he, p, AF.Abs); ts(he, he, 0.0, AL.is_equal)
-            pe([m for x, (j, s) in part for m in [(K(pb(0), 2 * (j // 2) + i // 2), Zs("ha", 8 * (j % 2) + 2 * s), K(he, x)),
-                                                  (K(pb(0), 2 * s + i // 2), Zs("hb", j), K(he, x))]], False, i == 3)
+        pe([(J(pb(1), s), C("NP%d0" % s), S("G0")) for s in range(4)])
+        for x, (j, s) in enumerate(BLOCKS):
+            tt(J(S("HE"), x), J(pb(1), s), S("GR", j, 1024, 8), AL.is_equal)
+            if x % 2: pe([m for y, (j, s) in list(enumerate(BLOCKS))[x - 1:x + 1] for m in [(J(pb(0), j // 2), Zs("ha", 8 * (j % 2) + 2 * s), J(S("HE"), y)),
+                                                                                           (J(pb(0), s), Zs("hb", j), J(S("HE"), y))]], False, x == 15)
         pe([(J(pb(7), jj), C("FB%d" % h), gu(jj, h)) for jj in range(4) for h in range(2)], True, False)
-        ts(S("WB"), pb(0), 0.0, AL.is_gt); ops[-1]["meet"] = True; pe([(pb(7), C("L8"), S("WB"))], False, True)
-        ts(S("PR"), pb(7), -7.5, AL.is_lt); act(S("R"), pb(7), AF.Relu, -7.0 / 8192, -1.0 / 8192)
+        if SGN[t][0] == "v": ts(S("WB"), pb(0), 0.0, AL.is_gt, 2.0, AL.mult); k = 0
+        else: act(S("WB"), pb(0), AF.Sign); k = 1
+        pe([(pb(7), C("L8"), S("WB"))], False, True)
+        if SGN[t][1] == "v": ts(S("PR"), pb(7), PRC[k], AL.is_lt)
+        else: act(S("PR"), pb(7), AF.Sign, PRC[k], -1.0)
+        act(S("R"), pb(7), AF.Relu, RRC[k], -1.0 / 8192)
         tr = lambda n, p, b, src: [(p, C("%s%d%d" % (n, b, x)), J(S(src), x)) for x in sorted(set(q[2 + (n == "T")] // 2 for q in PAIRS if q[0] == b))]
         grp = lambda l: [m + ((1,) if i == 0 else ()) for i, m in enumerate(l)]
         pe([m for b in range(2) for m in grp(tr("R", pb(3, b, 256, 2), b, "PR") + tr("T", pb(3, b, 256, 2), b, "PR"))])
         ts(S("SV", 0, 256), pb(3, 0, 256), 8.5, AL.is_gt)
-        pe([(pb(3, 0, 256), C("BLK"), S("SV", 0, 256))]); scan(S("INW", 16, 272), S("ONE", 0, 256), pb(3, 0, 256), 0.0, AL.mult, AL.add)
-        z0, z1, z2 = sub(TG3, 0, 16), sub(TG3, 16, 32), sub(TG4, 0, 16)
+        pe([(pb(3, 0, 256), C("BLK"), S("SV", 0, 256))]); scan(S("INW", 16, 272), pb(3, 0, 256), S("IO", 656, 912), 0.0, AL.add, AL.min)
+        z2 = sub(TG3, 0, 16)
         ext(pb(2, 0, 16), [("all", S("SV", 0, 256))], 256); ts(S("SV", 256, 272), pb(2, 0, 16), 0.0, AL.is_equal, 4096.0, AL.mult)
         pe([(pb(3, 0, 16), Yc(0, r), S("INW", 15 + r, 271, 16)) for r in range(16)] + [(pb(3, 0, 16), C("ID"), S("SV", 256, 272))])
         for b in range(2):
             p = pb(0, b, 256, 2)
             pe(tr("R", p, b, "R") + tr("T", p, b, "R") + [(p, C("LW"), S("SV", b, 256, 2)), (p, C("ID"), S("INW", 16 + b, 272, 2))])
         for b in range(2): mv(S("NT", b, 256, 2), pb(0, b, 256, 2), DB[b])
-        ts(z0, pb(3, 0, 16), 639.5, AL.is_gt, 1024.0, AL.mult); tt(z1, pb(3, 0, 16), z0, AL.add); tt(z2, z1, sub(DW, 0, 16), AL.min); cp(sub(CSL, 0, 16), z2)
+        tt(z2, pb(3, 0, 16), sub(DW, 0, 16), AL.min); cp(sub(CSL, 0, 16), z2)
         iota(S("WW", 0, 640), [[0, 640]], 0); put(IND(S("WW"), sub(CSL, 0, 16)), S("IO", 32, 288))
         scan(S("CW"), S("WW", 0, 640), S("WW", 0, 640), 0.0, AL.max, AL.max)
         ext(pb(3, 0, 40), [("c0", S("CW"))], 640); ts(CWL, pb(3, 0, 40), -32.0, AL.add)
@@ -560,18 +622,17 @@ def program(ops, T, nxt, prv):
         tt(t2, hk, c2, AL.add); ts(I2, t2, 15.0, AL.add)
         ts(vl, lo(hk), 0.0, AL.is_gt); ts(lo(i2), lo(hk), 0.0, AL.is_equal)
         ts(lo(rr), yi, 3, AL.arith_shift_right, 7, AL.bitwise_and); ts(hi(rr), yi, 7, AL.bitwise_and); ts(S("R2"), rr, 256.0, AL.mult)
-        hs = ((lo, 0, 3), (hi, 640, 0))
+        hs = ((lo, 0, 3), (hi, 640, 0)); GL = {0: "GB", 640: "EQ"}
         for f_, a, b in hs:
             tt(f_(t3), lo(i2), f_(DOV), AL.mult)
             cp(S("GI", a, a + 640), IND(S("IT"), f_(I2)))
             pe([(pb(b, 0, 40), C("ID"), f_(S("R2")))] + [(pb(b, 0, 40), Zs("om", r), S("GI", a + r, a + 640, 16)) for r in range(16)]); cp(f_(LUL), pb(b, 0, 40))
-            mv(S("GL", a, a + 640), IND(S("LUT"), f_(LUL)))
+            mv(S(GL[a], 0, 640), IND(S("LUT"), f_(LUL)))
             pe([(pb(b, 64, 104), Zs("id", r), S("GI", a + r, a + 640, 16)) for r in range(16)], True, False)
         for f_, a, b in hs:
-            pe([(pb(b, 64, 104), Zs("l17", r), S("GL", a + r, a + 640, 16)) for r in range(16)], False, True)
+            pe([(pb(b, 64, 104), Zs("l17", r), S(GL[a], r, 640, 16)) for r in range(16)], False, True)
             tt(f_(t2), pb(b, 64, 104), f_(t3), AL.max); ts(f_(OVL), f_(t2), -1.0, AL.add)
             tt(IND(S("OV"), f_(OVL)), S("GI", 640 - a, 1280 - a), S("NAM"), AL.add)
-        ops[-1]["meet"] = True
         if t < 2: ts(S("NAM"), S("NAM"), M8[1], AL.add)
         tag[0] = "new"
         ext(pb(0, 128, 208), [("id", S("GI"))], 1280)
@@ -584,18 +645,19 @@ def program(ops, T, nxt, prv):
         mv(YY, IND(S("P"), lo(EXL))); tt(S("XB"), IND(S("M"), hi(EXL)), YY, AL.add); ts(S("X", 16 + n, 656 + n), S("XB"), 1024.0, AL.mult, 255.0, AL.min)
         tag[0] = "rows"
         for x in range(2 - OVD[0], 2):
-            dma("ys"[x], [(T["OVT"][64 * c:64 * c + 64, 1024 * x:1024 * x + 1024], T["OV"][c + 1:128:8, 4096 * x:4096 * x + 4096]) for c in range(2)],
-                [S("OV", 4096 * x, 4096 * x + 4096)], [S("OVT", 1024 * x, 1024 * x + 1024)], 2800)
+            dma("y", [(T["OVT"][64 * c:64 * c + 64, 1024 * x:1024 * x + 1024], T["OV"][c + 1:128:8, 4096 * x:4096 * x + 4096]) for c in range(2)],
+                [S("OV", 4096 * x, 4096 * x + 4096)], [S("OVT", 1024 * x, 1024 * x + 1024)], 256)
         for part in (((pb(6, 0, 128), 896, 1024), (pb(6, 128, 256), 0, 128)), ((pb(1, 0, 384), 128, 512),), ((pb(2, 0, 384), 512, 896),)):
             pe([m for p, a, b in part for m in [(p, C("ID"), S("RTH", a, b)), (p, C("NID"), S("D2", a, b))]], True, False)
             far = OVD[0] if len(part) == 1 or OVD[1] else 0
             pe([(p, sub(C("CV"), 15 - l, 143 - l), S("OV", 1024 * l + a, 1024 * l + b)) for p, a, b in part for l in range(8 - 4 * far)] +
                [(p, C("MV%d" % x), S("OVT", 1024 * x + a, 1024 * x + b)) for p, a, b in part for x in range(2 - far, 2)], False, True)
-            for p, a, b in part: cp(S("RTH", a, b), p)
-            for p, a, b in part: act(S("FL", a, b), p, AF.Sign)
-        if t < 2: E["zero_ov"]()
+            for first in (len(part) == 2, len(part) == 1):
+                for p, a, b in part:
+                    if first: cp(S("RTH", a, b), p)
+                    else: act(S("FL", a, b), p, AF.Sign)
         tag[0] = "mid"
-        dma("y", [(T["GAW"][:, :], T["GA"][0:128:16, 16:4112])], [S("GA", 16, 4112)], [S("GAW")], 2500)
+        dma("y", [(T["GAW"][:, :], T["GA"][0:128:16, 16:4112])], [S("GA", 16, 4112)], [S("GAW")], 200)
 
     def middles(t):
         tag[0] = "mid"
@@ -603,9 +665,11 @@ def program(ops, T, nxt, prv):
         for r in range(16):
             a, b, c = 256 * r, min(max(n, 256 * r), 256 * r + 256), min(max(n + 640, 256 * r), 256 * r + 256)
             if b > a: mm.append((pb(0, 0, b - a), Zs("all", r), S("WN", a, b)))
+            for t_, d, f in E["won"]:
+                if t_ == t and min(f, b) > max(d, a): mm.append((pb(0, max(d, a) - a, min(f, b) - a), Zs("nall", r), S("X", 16 + max(d, a), 16 + min(f, b))))
             if c > b: mm.append((pb(0, b - a, c - a), Zs("all", r), S("ONE", 0, c - b)))
         for i in range(0, len(mm), 4): pe(mm[i:i + 4], i == 0, i + 4 >= len(mm))
-        ts(y, y, 8.5, AL.is_gt, 2048.0 * (t + 1), AL.mult); tt(y, y, S("GAW"), AL.add); tt(S("ENC"), y, S("ENC"), AL.max)
+        ts(y, y, 8.5 / 4, AL.is_gt, 2048.0 * (t + 1), AL.mult); tt(y, y, S("GAW"), AL.add); tt(S("ENC"), y, S("ENC"), AL.max)
 
     def send(src, dst, k, to, by):
         o = add("g", lambda e: [e["g"].remote_dma(ap(dst), ap(src), T.sem["a%d" % k], T.sem["o%d" % k], E[to][1], E[to][0], E[to][2])], [src], [], 300.0, send=("o%d" % k, E[to][3]))
@@ -623,25 +687,30 @@ def program(ops, T, nxt, prv):
         tt(TP, pb(7, 0, 128), A1C, AL.max)
         send(H2(TP, 0), TR, 3 * t, "nxt", "prv")
 
+        inc = lambda s_: S("INC", 72 * s_ + 1, 72 * s_ + 65)
+
         def number(s_, far, bk):
-            FLG, INC, TG, p = H2(S("FLG"), s_), H2(S("INC"), s_), H2(S("TG"), s_), pb(bk, 0, 64)
-            q0, q1, q2 = [H2(E[k], s_) for k in ("q0", "q1", "q2")]; SW = S("SW", 576 * s_, 576 * s_ + 576); w = sub(SW, 0, 512)
+            FLG, INC, TG, p, y = H2(S("FLG"), s_), inc(s_), S("TG", 8 * s_, 8 * s_ + 4), pb(bk, 0, 64), pb(bk, 0, 4)
+            q0 = sub(E["q0"], 64 * s_, 64 * s_ + 4); SW = S("SW", 576 * s_, 576 * s_ + 576); w = sub(SW, 0, 512)
             tt(FLG, far, H2(A1C, 0), AL.is_gt); pe([(p, C("BLK"), FLG)]); scan(INC, S("ONE", 0, 64), p, 0.0, AL.mult, AL.add)
-            ts(q1, p, 0.0, AL.is_equal); tt(q0, INC, p, AL.subtract); tt(q2, q1, DS, AL.mult); tt(TG, q0, q2, AL.max)
-            ext(pb(bk, 0, 4), [("c0", TG)], 64); cp(H2(STL, s_, 4), pb(bk, 0, 4))
+            if NUM[t][s_] == "p":
+                ext(pb(13, 0, 4), [("all", FLG)], 64); ts(TG, pb(13, 0, 4), 0.0, AL.is_equal, 1024.0, AL.mult)
+                pe([(y, Yc(0, r), sub(INC, r - 1, 63, 16)) for r in range(16)] + [(y, C("ID"), TG)]); tt(q0, y, DS, AL.min); cp(H2(STL, s_, 4), q0)
+            else:
+                TG = S("TG", 16 + 64 * s_, 80 + 64 * s_); ts(p, p, 0.0, AL.is_equal); tt(p, p, S("IO", 512, 576), AL.mult); tt(TG, p, sub(INC, -1, 63), AL.max)
+                ext(y, [("c0", TG)], 64); cp(H2(STL, s_, 4), y)
             iota(w, [[0, 512]], 0); cp(IND(SW, H2(STL, s_, 4)), S("IOB", 0, 64)); scan(H2(S("SC"), s_, 512), w, w, 0.0, AL.max, AL.max)
             ext(pb(bk, 0, 32), [("c0", H2(S("SC"), s_, 512))], 512); cp(H2(SCL, s_, 32), pb(bk, 0, 32))
 
         def names(s_, bk):
             NE, w0, w1, q2 = H2(S("NE"), s_, 512), H2(E["w0"], s_, 32), H2(E["w1"], s_, 32), sub(E["q3"], 64 + 32 * s_, 96 + 32 * s_)
             tt(NE, IND(H2(S("NUS"), s_), H2(SCL, s_, 32)), S("IO", 0, 512), AL.subtract); ts(NE, NE, -0.5, AL.max, 0.5, AL.min)
-            ext(pb(bk, 0, 32), [("8k", NE)], 512); ts(w0, pb(bk, 0, 32), 65536.0, AL.add); ts(w1, w0, 8191, AL.bitwise_and)
-            if s_:
-                q0 = sub(E["q0"], 0, 32); ts(q0, w1, 2047.0, AL.max, -1.0, AL.mult); ts(S("Lsh"), q0, 6159.0, AL.add)
-            tt(q2, w1, H2(DX, s_, 32), AL.max); ts(H2(SXL, s_, 32), q2, -1.0, AL.mult, 6159.0, AL.add)
+            ext(pb(bk, 0, 32), [("8k", NE)], 512); ts(w0, pb(bk, 0, 32), 65536.0 - 2033, AL.add); ts(w1, w0, 8191, AL.bitwise_and)
+            if s_: ts(S("Lsh"), w1, 4112.0, AL.min)
+            tt(q2, w1, H2(DX, s_, 32), AL.min); cp(H2(SXL, s_, 32), q2)
         tag[0] = "own"
         number(0, H2(TP, 0), 3); p = pb(3, 64, 128)
-        pe([(p, C("NFE%d" % ha), rows(0, ha)) for ha in range(2)] + [(p, C("LS"), H2(S("FLG"), 0)), (p, C("ID"), H2(S("INC"), 0))]); mv(H2(S("NUS"), 0), p, -513.0)
+        pe([(p, C("NFE%d" % ha), rows(0, ha)) for ha in range(2)] + [(p, C("LS"), H2(S("FLG"), 0)), (p, C("ID"), inc(0))]); mv(H2(S("NUS"), 0), p, -513.0)
         names(0, 3); mv(H2(SND, 0, 512), IND(XW, H2(SXL, 0, 32))); send(H2(SND, 0, 512), H2(RX, 1, 512), 3 * t + 1, "nxt", "prv")
         for s_ in range(2):
             fold(pb(3, 0, 64), "FE", "RTH", base[s_], 128); ts(H2(SRL, s_), pb(3, 0, 64), 2063.0, AL.add)
@@ -654,7 +723,7 @@ def program(ops, T, nxt, prv):
         ts(S("WI", 0, 64), pb(7, 0, 64), 32768.0, AL.add); ts(S("WJ", 0, 64), S("WI", 0, 64), 8191, AL.bitwise_and)
         q3 = sub(E["q3"], 0, 64); ts(q3, S("WJ", 0, 64), 1.0 / 8192, AL.mult, -513.5, AL.add)
         number(1, TR, 6)
-        pe([(pb(7, 0, 64), C("LS"), H2(S("FLG"), 1)), (pb(7, 0, 64), C("ID"), H2(S("INC"), 1))]); tt(H2(S("NUS"), 1), pb(7, 0, 64), q3, AL.add)
+        pe([(pb(7, 0, 64), C("LS"), H2(S("FLG"), 1)), (pb(7, 0, 64), C("ID"), inc(1))]); tt(H2(S("NUS"), 1), pb(7, 0, 64), q3, AL.add)
         names(1, 6)
         for h in range(2): mv(sub(SND, 512 + 256 * h, 768 + 256 * h), IND(XW, S("Lsh", 16 * h, 16 * h + 16)))
         send(H2(SND, 1, 512), H2(RX, 0, 512), 3 * t + 2, "prv", "nxt")
@@ -675,7 +744,7 @@ def program(ops, T, nxt, prv):
             if t < 2:
                 act(sub(SG, a, b), p, AF.Sign, 8.5, -1.0); tt(IND(XW, L), sub(MN, a, b), sub(SG, a, b), AL.mult); signs = XW
             else:
-                cp(IND(S("G1", 0, 5152), L), sub(MN, a, b)); act(S("W6"), p, AF.Identity, 8.5, -1.0); put(IND(S("GA"), L), S("W6")); signs = S("GA", 0, 4112)
+                cp(IND(S("G1", 0, 5152), L), sub(MN, a, b)); act(S("W6"), p, AF.Identity, 8.5, -1.0); put(IND(S("GA", 0, 5152), L), S("W6")); signs = S("GA", 0, 4112)
             for h in range(2): mv(sub(GX, 2 * a + 512 * h, 2 * a + 512 * h + 512), IND(signs, sub(SRL, 64 * s_ + 32 * h, 64 * s_ + 32 * h + 32)))
             k_, a, p = S("KP", 128 * s_, 128 * s_ + 128), base[s_], pb(7 - s_, 0, 128)
             pe([(p, sub(C("KD"), 15 - l, 143 - l), sub(GX, 1024 * s_ + l, 1024 * s_ + 1024, 8)) for l in range(8)])
@@ -683,27 +752,26 @@ def program(ops, T, nxt, prv):
             ts(p, p, 0.0, AL.is_gt)
             tt(S("FLS", 128 * s_, 128 * s_ + 128), p, S("FL", a, a + 128), AL.mult); tt(S("RTH", a, a + 128), p, S("RTH", a, a + 128), AL.mult)
 
-    part_a(0)
+    ends(); part_a(0)
     for t in range(3):
-        spokes()
-        if t == 0: ends()
+        spokes(t)
         part_b(t); part_c(t)
         if t < 2: part_a(t + 1)
         middles(t)
         if t == 2:
             cp(S("WI", 256, 512), S("ENC")); ts(S("WJ", 256, 512), S("WI", 256, 512), 2047, AL.bitwise_and); ts(S("GAW"), S("WJ", 256, 512), -1.0, AL.add)
-            dma("y", [(T["ymid"][:, :], T["GAW"][:, :])], [S("GAW")], [], 2500)
+            dma("y", [(T["ymid"][:, :], T["GAW"][:, :])], [S("GAW")], [], 200)
             for a in range(16, 4112, 512): act(S("G1", a, a + 512), S("X", a, a + 512), AF.Abs)
         part_d(t)
-    dma("y", [(T["ylen"][:, a:a + 1024], T["G1"][:, 16 + a:1040 + a]) for a in range(0, 4096, 1024)], [S("G1", 16, 4112)], [], 5000)
+    dma("y", [(T["ylen"][:, a:a + 1024], T["G1"][:, 16 + a:1040 + a]) for a in range(0, 4096, 1024)], [S("G1", 16, 4112)], [], 1024)
     ts(BG, DEAD, -8192.0, AL.mult)
     for bk, a, b, fl_ in ((1, 128, 512, S("FL", 128, 512)), (2, 512, 896, S("FL", 512, 896)), (1, 0, 128, S("FLS", 128, 256)), (2, 896, 1024, S("FLS", 0, 128))):
         gone = [(pb(bk, x - a, x - a + 64), Al(x // 64), BG) for x in range(a, b, 64)] if b - a > 128 else []
         pe([(pb(bk, 0, b - a), C("ID"), S("RTH", a, b)), (pb(bk, 0, b - a), C("EN2K"), fl_)] + gone)
         if gone: ts(S("ZZ", a, b), pb(bk, 0, b - a), -1.0, AL.add, -1.0, AL.max)
         else: ts(S("ZZ", a, b), pb(bk, 0, b - a), -1.0, AL.add)
-    dma("y", [(T["ynb"][g, :], T["ZZ"][16 * g:16 * g + 8, :]) for g in range(8)], [S("ZZ")], [], 2500)
-    dma("s", [(T["yen"][g, :], T["ZZ"][16 * g + 8:16 * g + 16, :]) for g in range(8)], [S("ZZ")], [], 2500)
+    dma("y", [(T["ynb"][g, :], T["GA"][16 * g:16 * g + 8, 6560:7584]) for g in range(8)], [S("ZZ")], [], 512)
+    dma("s", [(T["yen"][g, :], T["GA"][16 * g + 8:16 * g + 16, 6560:7584]) for g in range(8)], [S("ZZ")], [], 512)
 
 
 def polish(ops, fw, res, rng, steps):
@@ -724,7 +792,7 @@ def polish(ops, fw, res, rng, steps):
         if pick[i] != "x":
             if pick[i] in last: mp[i] = last[pick[i]]; mn[last[pick[i]]] = i
             last[pick[i]] = i
-    fin, tail = [0.0] * (n + 1), [0.0] * (n + 1)
+    fin, tail, then = [0.0] * (n + 1), [0.0] * (n + 1), [n] * n
 
     own = lambda i, j, lag: not lag and pick[i] == pick[j]
     tp = [[j for j, lag in jp[i] if not own(i, j, lag)] for i in range(n)]; tn = [[k for k, lag in js[i] if not own(i, k, lag)] for i in range(n)]
@@ -732,19 +800,22 @@ def polish(ops, fw, res, rng, steps):
     for i in range(n):
         jp[i] = [(j, 0.0 if own(i, j, lag) else gap[j]) for j, lag in jp[i]]; js[i] = [(k, 0.0 if own(i, k, lag) else gap[i]) for k, lag in js[i]]
 
+    win = [0, n]
+
     def times(a, b):
-        for i in topo[a:]:
+        for i in topo[a:win[1]]:
             s = fin[mp[i]]
             for j in tp[i]:
                 if out_[j] > s: s = out_[j]
             s += dur[i]; fin[i] = s; out_[i] = s + gap[i]
-        for i in topo[b::-1]:
-            s = 0.0
+        tie = 1e-6 if rng.rand() < 0.5 else -1e-6
+        for i in topo[win[0]:b + 1][::-1]:
+            s = 0.0; w = n
             for k in tn[i]:
-                if tail[k] > s: s = tail[k]
-            s = s + gap[i] if s else late[i]
-            if tail[mn[i]] > s: s = tail[mn[i]]
-            tail[i] = s + dur[i]
+                if tail[k] > s: s = tail[k]; w = k
+            s = s + gap[i] if s else late[i]; k = mn[i]
+            if tail[k] + tie > s and k < n: s = max(s, tail[k]); w = k
+            tail[i] = s + dur[i]; then[i] = w
     head = lambda i: max([fin[j] + lag for j, lag in jp[i]] + [0.0])
     rest = lambda i: max([tail[k] + lag for k, lag in js[i]] + [late[i]])
 
@@ -774,22 +845,36 @@ def polish(ops, fw, res, rng, steps):
         assert len(out) == len(seg)
         topo[a:b + 1] = out
         for k, i in enumerate(out): pos[i] = a + k
-        times(max(a - 1, 0), min(b + 1, n - 1))
+        times(max(a - 1, win[0]), min(b + 1, win[1] - 1))
+
+    def settle(seg, picks):
+        topo[win[0]:win[1]] = seg; last = {}
+        for i, q in zip(seg, picks): pick[i] = q; dur[i] = cost(i, q)
+        for i in topo:
+            if pick[i] != "x": mp[i] = last.get(pick[i], n); mn[mp[i]] = i; mn[i] = n; last[pick[i]] = i
+        mp[n] = mn[n] = n; win[:] = [0, n]; times(0, n - 1)
+        topo.sort(key=lambda i: fin[i] - dur[i])
+        for k, i in enumerate(topo): pos[i] = k
     times(0, n - 1); best = None; tabu = {}
-    for it in range(steps):
-        i = max(topo[:40], key=lambda i: tail[i]); span = tail[i]
-        if best is None or span < best[0] - 1e-6: best = (span, list(zip([f - d for f, d in zip(fin, dur)], fin, pick)))
-        path = [i]
-        while True:
-            nx = [k for k, lag in js[i] if abs(tail[i] - dur[i] - lag - tail[k]) < 1e-6]
-            if mn[i] < n and abs(tail[i] - dur[i] - tail[mn[i]]) < 1e-6: nx.append(mn[i])
-            if not nx: break
-            i = nx[rng.randint(len(nx))] if len(nx) > 1 else nx[0]; path.append(i)
-        blocks = [[path[0]]]
-        for a, b in zip(path, path[1:]):
-            if mn[a] == b: blocks[-1].append(b)
-            else: blocks.append([b])
-        blocks = [b for b in blocks if len(b) > 1]; cand = []
+    for it in range(steps + 1):
+        if it % WIN[1] == 0 or it == steps:
+            if best: settle(*best[1:])
+            lo = (it // WIN[1] * WIN[0] // 2) % n; lo = max(0, min(n - WIN[0], lo - rng.randint(WIN[0] // 2))); hi = min(n, lo + WIN[0]); win[:] = [lo, hi]; best = None
+            if it == steps: break
+        span = 0.0
+        for k in topo[lo:hi]:
+            s = fin[k] - dur[k] + tail[k]
+            if s > span + 1e-6: span = s; i = k
+        if best is None or span < best[0] - 1e-6: best = (span, topo[lo:hi], [pick[k] for k in topo[lo:hi]])
+        blocks = []; run = [i]; cand = []
+        while i < n:
+            k = then[i]
+            if k < n and pos[k] >= hi: k = n
+            if mn[i] == k and k < n: run.append(k)
+            else:
+                if len(run) > 1: blocks.append(run)
+                run = [k]
+            i = k
         for bi in rng.permutation(len(blocks))[:NEAR[0]]:
             b = blocks[bi]; D = lambda l: [(x, dur[x]) for x in l]
             for x in range(len(b) - 1):
@@ -807,7 +892,7 @@ def polish(ops, fw, res, rng, steps):
                     w = topo[k]; h = head(u); r = rest(u); d = cost(u, q)
                     for _ in range(4):
                         cand.append((max(max(h, fin[w]) + d + max(r, tail[mn[w]]), fin[mp[u]] + tail[mn[u]]), u, q, w, mn[w]))
-                        if mp[w] == n or anc[u] >> w & 1 or any(fin[j] > fin[w] - dur[w] for j, _ in jp[u]): break
+                        if mp[w] == n or pos[w] < lo or anc[u] >> w & 1 or any(fin[j] > fin[w] - dur[w] for j, _ in jp[u]): break
                         w = mp[w]
         free = [c for c in cand if tabu.get((c[1], c[3]), -1) < it or c[0] < best[0] - 1.0]
         if not free: continue
@@ -815,11 +900,36 @@ def polish(ops, fw, res, rng, steps):
         tabu[(c[1], mp[c[1]])] = it + 8 + rng.randint(12)
         if c[2] == pick[c[1]] and c[3] < n: tabu[(c[3], mp[c[3]])] = it + 8 + rng.randint(12)
         move(c[1], c[2], c[3], c[4])
-    return best[1] if best else res
+    return list(zip([f - d for f, d in zip(fin, dur)], fin, pick))
 
 
-def emit(ops, g, T):
-    n = len(ops); last = {}; grp = {}
+def tiles(ops):
+    up = {}; own = {}; grp = {}
+
+    def find(a):
+        while up[a] != a: up[a] = up[up[a]]; a = up[a]
+        return a
+    for i, o in enumerate(ops):
+        for kind, accs in (("r", o["rd"]), ("w", o["wr"])):
+            for name, m, _ in accs:
+                if not name.startswith("pb"): continue
+                me = (i, name); up.setdefault(me, me); l = own.setdefault(name, [])
+                if kind == "r":
+                    for m2, w in l:
+                        if m & m2: up[find(w)] = find(me)
+                else:
+                    if name in o.get("cont", ()): up[find(grp[name])] = find(me)
+                    l[:] = [(m2 & ~m, w) for m2, w in l if m2 & ~m] + [(m, me)]
+        if o["q"] == "p":
+            for name, _, _ in o["wr"]: grp[name] = (i, name)
+    num = {}
+    for i, o in enumerate(ops):
+        o["tile"] = {name: "pb%d" % num.setdefault(find((i, name)), len(num)) for name, _, _ in o["rd"] + o["wr"] if name.startswith("pb")}
+        for k in ("rd", "wr"): o[k] = [(o["tile"].get(name, name), m, bm) for name, m, bm in o[k]]
+
+
+def ties(ops):
+    last = {}
     for i, o in enumerate(ops):
         deps, order = set(), set()
         dm = "dma" in o or o["q"] == "x" or "send" in o
@@ -845,7 +955,67 @@ def emit(ops, g, T):
                 l.append((i, kind, m, bm))
         if "after" in o: order.add([k for k in range(i) if ops[k] is o["after"]][0])
         o["deps"], o["order"] = deps, order - deps
+    return {k: sorted(set(x[0] for x in l)) for k, l in last.items() if k.startswith("pb")}
+
+
+def banks(ops, res, rng):
+    n = len(ops); use = {}
+    for i in sorted(range(n), key=lambda i: (res[i][0], i)):
+        for t in set(ops[i]["tile"].values()): use.setdefault(t, []).append(i)
     succ = [[] for _ in ops]
+    for i, o in enumerate(ops):
+        for j in o["deps"] | o["order"]: succ[j].append(i)
+
+    def reaches(src, goal):
+        seen, todo = set(src), list(src); top = max(res[j][0] for j in goal)
+        while todo:
+            i = todo.pop()
+            if i in goal: return True
+            for k in succ[i]:
+                if k not in seen and res[k][0] < top + 20000.0: seen.add(k); todo.append(k)
+        return False
+    rows = [[] for _ in range(8)]; end = [-1e9] * 8
+    for t, l in sorted(use.items(), key=lambda x: res[x[1][0]][0]):
+        a = res[l[0]][0]; other = set(x for i in l for x in ops[i]["tile"].values()) - {t}
+        rank = sorted(range(8), key=lambda b: (0, rng.rand() * ROOM[1] - end[b]) if end[b] + ROOM[0] <= a else (1, end[b]))
+        for b in rank:
+            if rows[b] and (rows[b][-1] in other or reaches(l, set(use[rows[b][-1]]))): continue
+            break
+        if rows[b]:
+            for j in use[rows[b][-1]]: succ[j] += l
+        rows[b].append(t); end[b] = max(end[b], max(res[i][1] for i in l))
+    return rows
+
+
+def seat(ops, rows, res):
+    tail = ties(ops); first = {}
+    for i, o in enumerate(ops):
+        for t in o["tile"].values(): first.setdefault(t, []).append(i)
+    for b, row in enumerate(rows):
+        for t in row:
+            for i in first[t]: ops[i].setdefault("bank", {}).update({k: "pb%d" % b for k, v in ops[i]["tile"].items() if v == t})
+        for t, u in zip(row, row[1:]):
+            for i in first[u]:
+                if i == first[u][0] or not (ops[i]["deps"] | ops[i]["order"]) & set(first[u]):
+                    for j in tail[t]: ops[i]["order" if ops[i]["q"] == "p" == ops[j]["q"] else "deps"].add(j)
+    n = len(ops); succ = [[] for _ in ops]; left = [0] * n
+    for i, o in enumerate(ops):
+        o["order"] = o["order"] - o["deps"]
+        for j in o["deps"] | o["order"]: succ[j].append(i); left[i] += 1
+    key = [r[0] for r in res]; ready = [i for i in range(n) if not left[i]]; out = []
+    while ready:
+        i = min(ready, key=lambda i: (key[i], i)); ready.remove(i); out.append(i)
+        for k in succ[i]:
+            left[k] -= 1
+            if not left[k]: ready.append(k)
+    assert len(out) == n
+    new = {i: k for k, i in enumerate(out)}
+    for o in ops: o["deps"], o["order"] = set(new[j] for j in o["deps"]), set(new[j] for j in o["order"])
+    return out
+
+
+def search(ops, rng, passes, steps, given=None):
+    n = len(ops); succ = [[] for _ in ops]
     for i, o in enumerate(ops):
         for j in o["deps"] | o["order"]: succ[j].append(i)
     pri = [0.0] * n
@@ -877,7 +1047,7 @@ def emit(ops, g, T):
             if q != "x": busy[q].insert(lo, (st, st + c))
             res[i] = (st, st + c, q)
         return res
-    if n not in PLAN:
+    if passes or given:
         def start(bias):
             key = [-pri[i] - bias.get(ops[i]["tag"], 0.0) for i in range(n)]
             for i in range(n - 1, -1, -1):
@@ -901,14 +1071,17 @@ def emit(ops, g, T):
                     st += (res[i][1] - res[i][0]) * fac[ops[i]["kind"]]; free[q] = st; en_[i] = st + late[i] * fac["x"]
                 tot += wt * max(en_)
             return tot
-        rng = np.random.RandomState(SEED[0])
 
         def shake():
-            pen[:] = [PEN[0]] * n; res = min(start(BIAS), key=score); top = cur = None
-            for it in range(PASSES[0]):
+            if given:
+                pen[:] = [-99.0 if r[2] == "v" else 99.0 for r in given]; res = place(range(n), fw, False)
+            else:
+                res = min(start(BIAS), key=score)
+            top = (score(res), res); cur = None
+            for it in range(passes):
                 sc_ = score(res)
-                if top is None or sc_ < top[0]: top = (sc_, res)
-                if cur is None or sc_ < cur[0] + TEMP[0] * (1.0 - it / PASSES[0]): cur = (sc_, res, list(pen))
+                if sc_ < top[0]: top = (sc_, res)
+                if cur is None or sc_ < cur[0] + TEMP[0] * (1.0 - it / passes): cur = (sc_, res, list(pen))
                 key = [cur[1][i][0] for i in range(n)]; pen[:] = cur[2]
                 c0 = rng.uniform(0, max(key)); wd = rng.choice([5000.0, 15000.0, 30000.0]); nz = rng.normal(0, rng.choice([300.0, 1000.0, 2500.0]), n)
                 flip = rng.uniform(0, 1, n) < rng.choice([0.0, 0.1])
@@ -923,24 +1096,27 @@ def emit(ops, g, T):
                     rb = place(sorted(range(n), key=lambda i: (-res[i][1], -i)), bw, True)
                     res = place(sorted(range(n), key=lambda i: (-rb[i][1], i)), fw, False)
             return top[1]
-        span = lambda r: max(r[i][1] + late[i] for i in range(n))
-        sends = [i for i in range(n) if ops[i].get("meet")]; pop = [polish(ops, fw, shake(), rng, STEPS[1]) for it in range(POP[0])]
-        cut = [[0.0] + [r[i][0] for i in sends] + [span(r) + 1.0] for r in pop]; key = [None] * n; at = 0.0
-        for s_ in range(len(sends) + 1):
-            p_ = min(range(len(pop)), key=lambda p_: cut[p_][s_ + 1] - cut[p_][s_])
-            for i in range(n):
-                if key[i] is None and pop[p_][i][0] < cut[p_][s_ + 1]:
-                    key[i] = at + max(0.0, pop[p_][i][0] - cut[p_][s_]); pen[i] = -99.0 if pop[p_][i][2] == "v" else 99.0
-            at += cut[p_][s_ + 1] - cut[p_][s_]
-        for i in range(n):
-            for j, _ in fw[i]:
-                if key[j] >= key[i]: key[i] = key[j] + 0.001
-        res = polish(ops, fw, place(sorted(range(n), key=lambda i: (key[i], i)), fw, False), rng, STEPS[0])
-        INFO.append(([round(span(r)) for r in pop], round(at), round(span(res))))
-        PLAN[n] = min(pop + [res], key=span)
+        res = polish(ops, fw, shake(), rng, steps)
+        return res, score(res)
+
+
+def emit(ops, g, T):
+    n = len(ops); tiles(ops); base = list(ops)
+    if n not in PLAN:
+        rng = np.random.RandomState(SEED[0]); ties(ops); res = search(ops, rng, PASSES[0], STEPS[0])[0]; best = None
+        for passes, steps in AGAIN:
+            ties(base); rows = banks(base, res, rng); out = seat(base, rows, res)
+            new, sc_ = search([base[i] for i in out], rng, passes, steps, [res[i] for i in out])
+            if best is None or sc_ < best[0]: best = (sc_, rows, res, new)
+            INFO.append((round(sc_), round(max(r[1] for r in res)), round(max(r[1] for r in new))))
+            res = [None] * n
+            for i, r in zip(out, new): res[i] = r
+        PLAN[n] = best
+    _, rows, old, res = PLAN[n]
+    ops[:] = [base[i] for i in seat(base, rows, old)]
     end = [0.0] * n
     for i, o in enumerate(ops):
-        o["st"], o["pick"] = PLAN[n][i][0], PLAN[n][i][2]; o["cost"] = PLAN[n][i][1] - o["st"]; end[i] = PLAN[n][i][1] + o.get("dma", 0)
+        o["st"], o["pick"] = res[i][0], res[i][2]; o["cost"] = res[i][1] - o["st"]; end[i] = res[i][1] + o.get("dma", 0)
     seq = sorted(range(n), key=lambda i: (ops[i]["st"], i))
     e = {"v": g.vector, "s": g.scalar, "p": g.tensor, "g": g, "y": g.sync}
     cnt = {}; know = {q: {} for q in e}; nd = [0]
@@ -956,7 +1132,7 @@ def emit(ops, g, T):
             if kn.get(s_, 0) < v:
                 e[q].wait_ge(T.sem[s_], v); kn[s_] = v
                 for a, b in ops[j]["know"].items(): kn[a] = max(kn.get(a, 0), b)
-        o["know"] = dict(kn); e["pick"] = q
+        o["know"] = dict(kn); e["pick"] = q; NOW.clear(); NOW.update(o.get("bank", {}))
         ins = o["fn"](e)
         if "send" in o:
             cnt[o["send"][0]] = o["send"][1]; o["sig"] = o["send"]
@@ -972,7 +1148,7 @@ def emit(ops, g, T):
     return max(end), {q: sum(o["cost"] for o in ops if o["pick"] == q) for q in "vspg"}
 
 
-INFO = []
+INFO, NOW = [], {}
 
 
 def rank_program(g, core, T, topo):

@@ -4,23 +4,23 @@ from concourse.mybir import AluOpType as AL, ActivationFunctionType as AF
 
 F, H, B, I, U = "float32", "float16", "bfloat16", "int32", "uint16"
 SB = {
-    "RAW": (2048, I), "X": (5152, B), "RT": (1040, F), "RTH": (1024, H), "TA": (1024, F), "TB": (1024, F), "FL": (1024, B), "FLS": (256, B),
-    "G1": (9216, B), "LN": (512, U), "KT": (1040, B), "CT": (1040, B), "IT": (1040, B), "GR": (1024, F), "HE": (2048, B),
+    "RAW": (2048, I), "X": (5152, B), "RT": (1056, F), "RTH": (1024, H), "TA": (1024, F), "TB": (1024, F), "FL": (1024, B), "FLS": (256, B),
+    "G1": (6800, B), "LN": (512, U), "KT": (1040, B), "CT": (1040, B), "IT": (1040, B), "GR": (1024, F), "HE": (2048, B),
     "P": (1040, F), "M": (1040, F), "GA": (7584, F), "OV": (9472, B), "EQ": (1024, B), "D2": (1024, H), "GB": (1024, B),
-    "GC": (1024, B), "XS": (1024, B), "IDB": (1024, B), "U1J": (1024, F), "LO": (1024, B), "HI": (1024, B), "IO": (1056, F),
-    "IOB": (128, B), "ALL": (2048, B), "Y": (2304, B), "Z": (144 * 15, B), "CM": (128 * 68, B), "ONE": (1024, B), "RST": (512, B),
-    "LUT": (2048, B), "EA": (256, U), "EB": (256, U), "ENC": (256, F), "GAW": (256, F), "WN": (3456, H), "ZZ": (1024, F), "ZF": (272, F), "TH": (512, B),
+    "GC": (1024, B), "XS": (1024, B), "IDB": (1024, B), "R1": (1024, B), "RA": (1024, B), "RB": (1024, B), "J16": (512, B), "FT": (512, B), "HW": (128, F), "LO": (1024, B), "HI": (1024, B), "IO": (1056, F),
+    "IOB": (128, B), "ALL": (2048, B), "Y": (2304, B), "Z": (144 * 16, B), "CM": (128 * 68, B), "ONE": (1024, B), "RST": (512, B),
+    "LUT": (2048, B), "EA": (256, U), "EB": (256, U), "ENC": (256, F), "GAW": (256, F), "WN": (3456, H), "ZZ": (1024, F), "ZF": (272, F), "WV": (1040, B),
     "SF": (2432, F), "SI": (1024, I), "SH": (960, B), "SU": (400, U), "S16": (512, H), "W5": (512, F), "W6": (512, F), "WI": (512, I), "WJ": (512, I),
     "WB": (512, B), "R": (512, B), "PR": (512, B), "SV": (512, B), "INW": (272, H), "NT": (512, F), "WW": (1168, F), "CW": (640, H),
-    "YC": (640, H), "GI": (1280, B), "G0": (128, H), "XB": (640, B), "RKW": (64, B), "QS": (64, B), "QR": (256, B),
-    "TP": (384, B), "TR": (384, B), "EQS": (1024, B), "PRS": (1024, H), "FLG": (128, B), "NUS": (128, F), "INC": (144, H), "TG": (144, H),
-    "SW": (1152, B), "SC": (1024, B), "OH": (1024, B), "NE": (1024, H), "SND": (3072, B), "RX": (2048, B), "OVT": (2048, B), "COL": (24, F), "COI": (16, I), "ZER": (1024, B),
+    "YC": (640, H), "GI": (1280, B), "G0": (128, H), "XB": (640, B), "RKW": (80, B), "QS": (512, B), "QR": (256, B),
+    "TP": (576, B), "TR": (384, B), "EQS": (1024, B), "PRS": (1024, H), "NUS": (128, F), "INC": (144, H), "TG": (144, H),
+    "SW": (1152, B), "SC": (1024, B), "OH": (1024, B), "NE": (1024, H), "SND": (3072, B), "RX": (2048, B), "OVT": (1024, B), "COL": (24, F), "COI": (16, I), "ZER": (1024, B),
 }
-LISTS = {"a": 64, "mk": 64, "sp": 64, "go": 8, "u": 64, "cs": 32, "cw": 40, "i2": 80, "ex": 80, "lu": 80, "ov": 80, "st": 8, "sc": 64, "sx": 64, "sr": 128, "gq": 4, "q": 8}
+LISTS = {"a": 64, "hx": 4, "sp": 64, "go": 8, "u": 64, "cs": 32, "cw": 40, "i2": 80, "ex": 80, "lu": 80, "ov": 80, "st": 8, "sc": 64, "sx": 64, "sr": 128, "gq": 4, "q": 8}
 SB["Lsh"] = (32, U)
 for _k, _n in LISTS.items():
     SB["L" + _k] = (_n, U)
-SB.update({"SRG": (2048, B), "KP": (256, B), "SM": (3072, B), "SND": (1024, B), "O0": (128, I), "NAM": (640, B), "ZB": (1024, B), "R2": (80, B), "UM": (160, F)})
+SB.update({"SRG": (2048, B), "KP": (256, B), "SM": (3072, B), "SND": (1024, B), "O0": (128, I), "NAM": (640, B), "ZB": (1024, B), "R2": (80, B), "UM": (160, B)})
 ALIAS = {"WI": ("RAW", 1024), "WJ": ("RAW", 1536), "SI": ("RAW", 0), "TA": ("P", 16), "TB": ("GA", 6560), "ZZ": ("GA", 6560), "WW": ("GA", 5392), "GC": ("GB", 0), "EQS": ("SM", 0), "OH": ("SM", 1024),
          "SC": ("SM", 2048), "NE": ("PRS", 0), "NT": ("W5", 0),
          "LO": ("EQ", 0), "HI": ("XS", 0), "ZB": ("SRG", 0), "HE": ("G1", 2560), "WB": ("G1", 4752), "R": ("G1", 5264), "PR": ("G1", 5776), "SV": ("G1", 6288)}
@@ -30,12 +30,13 @@ for _b in range(8):
 ND = 40
 SEMAPHORES = ["cv", "cs", "cp", "cg"] + ["o%d" % i for i in range(9)] + ["d%d" % i for i in range(ND)] + ["a%d" % i for i in range(9)]
 SIZE = {F: 4, H: 2, B: 2, I: 4, U: 2}
-CYC, PEC, LAT = 0.9, 0.39, 125.0
+FIX = [20.0]
+CYC, PEC, LAT = 0.84, 0.39, 170.0
 PEN = [1.0, 50.0]
 EDGE = [2, 2, 2]
 SGN = ["ss", "ss", "ss"]
-EQS, CMP, ABS = ["ss", "ss", "ss"], [["vs", "vs", "vv"]], [""]
-DMA, ZOV = [1800.0, 300.0], [1]
+EQS, CMP, ABS = ["ss", "ss", "ss"], [["vv", "vv", "vv"]], [""]
+DMA, ZOV = [1500.0, 300.0], [1]
 XF, XSE = [1.25, 1.2], [1]
 POP, OVD = [1], [1, 0]
 MBK, STEPS, NEAR, JIT = [4], [6000], [3], [10.0]
@@ -43,16 +44,16 @@ MARK, CUT, HOPW, EDW = [0, 0, 0], [1024], [512], [512]
 SPK = [1, 1, 1]
 WIN = [200, 300]
 NUM = ["pp", "pp", "pp"]
-BLOCKS = [(j, s) for s in range(4) for j in range(2 * s, 8) if j != 2 * s + 1]
-PAIRS = [(0, 8 * j + k, j, k) for j in range(2) for k in range(j + 1, 8)]
-PAIRS += [(1, d, j, k) for d, (j, k) in enumerate((j, k) for j in range(2, 8) for k in range(j + 1, 8))]
-PASSES, PLAN, SEED, TEMP = [60], {}, [5], [1000.0]
-AGAIN, ROOM = [(30, 12000), (0, 12000)], [300.0, 300.0]
-GUESS = [({"o": 1, "g": 1, "s": 1, "p": 1, "x": 1.2}, 130.0, 2.0), ({"o": 1, "g": 0.75, "s": 0.55, "p": 1, "x": 1.2}, 130.0, 1.0),
-         ({"o": 1, "g": 1.3, "s": 1.55, "p": 1, "x": 1}, 100.0, 1.0), ({"o": 1, "g": 1.25, "s": 0.7, "p": 1.3, "x": 1.6}, 200.0, 1.0)]
-BIAS = dict([("ends0", 20000.0)] + [(k + str(t), 5000.0) for k in ("pm", "lab", "spk", "edge", "new") for t in range(3)] +
-                   [(k + str(t), 3000.0) for k in ("seam", "own", "cmp", "rows") for t in range(3)] + [("edge1", 10000.0), ("edge2", 10000.0)])
-GAT, SCA = 1.56, 3.8
+BLOCKS = [(j, s) for s in range(4) for j in range(2 * s + 1)]
+PLACE = {(j, k): 8 * j + k for j in range(2) for k in range(j + 1, 8)}
+LOTS = [1]
+PLACE.update({jk: d + 1 for d, jk in enumerate((j, k) for j in range(2, 8) for k in range(j + 1, 8))})
+PASSES, PLAN, SEED, TEMP, OWN, TRIES = [600, 70, 4000], {}, [11], [250.0], [2.0], [120, 60.0]
+SEATS = [12]
+AGAIN, ROOM = [(0, 90, 6000)], [200.0, 1500.0, 300.0]
+GUESS = [({"o": 1, "g": 0.78, "s": 0.6, "p": 1.05, "x": 0.9}, 200.0, 1.0), ({"o": 1.1, "g": 1.3, "s": 1.6, "p": 1.0, "x": 1.1}, 130.0, 1.0)]
+BIAS = {"ends0": 10000.0}
+GAT, SCA = 1.56, 3.2
 
 
 def S(n, a=0, b=None, st=1):
@@ -106,6 +107,9 @@ def program(ops, T, nxt, prv):
             else:
                 w.append(x)
         kind = q if q in ("p", "x") else "s" if any(x[0] == "ind" for x in wr) else "g" if any(isinstance(x, tuple) and x[0] == "ind" for x in rd) else "o"
+        if kind == "o" and q in ("v", "s", "vs") and "dma" not in kw:
+            cost += FIX[0]
+            if "cs" in kw: kw["cs"] += FIX[0]
         o = dict(q=q, fn=fn, tag=tag[0] + str(tag[1]), kind=kind, rd=[masks(x) for x in r], wr=[masks(x) for x in w], cost=cost)
         o.update(kw); ops.append(o)
         return o
@@ -152,12 +156,16 @@ def program(ops, T, nxt, prv):
         add("v", lambda e: [e["v"].tensor_copy(ap(out), ap(a))], [a], [out], vcost(out, a, 0.5 if a[0] != "ind" and out[0] != "ind" and two(out, a) else 1))
 
     def ms(out, c):
-        add("v", lambda e: [e["v"].memset(ap(out), c)], [], [out], max(64, cols(out) * (0.5 if two(out) else 1)) * CYC)
+        n = cols(out); one = S("ONE", 0, n); cost = max(64, n * (0.5 if two(out) else 1)) * CYC
+        if not fl(out) or n > 512 or out[0] == "ONE": return add("v", lambda e: [e["v"].memset(ap(out), c)], [], [out], cost)
+        fn = lambda e: [e["v"].memset(ap(out), c) if e["pick"] == "v" else e["s"].activation(ap(out), ap(one), AF.Identity, scale=c)]
+        add("vs", fn, [one], [out], cost, cs=max(64, n) * CYC + 15)
 
     def scan(out, d0, d1, init, op0, op1):
         add("v", lambda e: [e["v"].tensor_tensor_scan(ap(out), ap(d0), ap(d1), sc(init), op0, op1)], [d0, d1, init], [out], max(64, cols(out) * (0.5 if two(out, d0, d1) else 1)) * CYC)
 
-    def act(out, a, func, bias=0.0, scale=1.0):
+    def act(out, a, func, bias=0.0, scale=1.0, total=None):
+        if total: return add("s", lambda e: [e["s"].activation(ap(out), ap(a), func, bias=sc(bias), scale=sc(scale), accum_out=ap(total))], [a, bias], [out, total], vcost(out, a, 1) + 35)
         add("s", lambda e: [e["s"].activation(ap(out), ap(a), func, bias=sc(bias), scale=sc(scale))], [a, bias, scale], [out], vcost(out, a, 1) + 15)
 
     def mv(out, a, bias=None, q="vs"):
@@ -169,10 +177,21 @@ def program(ops, T, nxt, prv):
             return [e["v"].tensor_scalar(ap(out), ap(a), sc(bias), None, AL.add)]
         add(q, fn, [a, bias], [out], vcost(out, a, 0.5 if a[0] != "ind" and two(out, a) else 1), cs=vcost(out, a, 1) + 15)
 
+    def relu(out, a, scale, bias, vec):
+        def fn(e):
+            if e["pick"] == "s": return [e["s"].activation(ap(out), ap(a), AF.Relu, bias=sc(bias), scale=scale)]
+            if len(vec) == 2: return [e["v"].tensor_scalar(ap(out), ap(a), vec[0], None, vec[1])]
+            return [e["v"].tensor_scalar(ap(out), ap(a), sc(vec[0]), vec[2], vec[1], vec[3])]
+        add("vs", fn, [a, bias], [out], vcost(out, a, 0.5 if two(out, a) else 1), cs=vcost(out, a, 1) + 15)
+
+    def flags(out, a):
+        fn = lambda e: [e["s"].activation(ap(out), ap(a), AF.Sign) if e["pick"] == "s" else e["v"].tensor_scalar(ap(out), ap(a), 0.0, None, AL.is_gt)]
+        add("vs", fn, [a], [out], vcost(out, a, 1), cs=vcost(out, a, 1) + 15)
+
     def put(out, a):
         add("s", lambda e: [e["s"].activation(ap(out), ap(a), AF.Silu)], [a], [out], vcost(out, a, 1) + 15)
 
-    def pe(mm, first=True, last=True, grp=None):
+    def pe(mm, first=True, last=True, when=None):
         n = len(mm)
         st = [(first if i == 0 else len(m) > 3) for i, m in enumerate(mm)]
         sp = [(last if i == n - 1 else len(mm[i + 1]) > 3) for i in range(n)]
@@ -181,7 +200,7 @@ def program(ops, T, nxt, prv):
             part.append(i); c += max(64, cols(m[0])) * (4 if SB[m[2][0]][1] == F else 1)
             if c >= CUT[0] or i == n - 1:
                 add("p", lambda e, part=part: [e["p"].matmul(ap(mm[i][0]), ap(mm[i][1]), ap(mm[i][2]), st[i], sp[i]) for i in part],
-                    [mm[i][1] for i in part] + [mm[i][2] for i in part], [mm[i][0] for i in part], c * PEC + (60 if i == n - 1 else 10),
+                    [mm[i][1] for i in part] + [mm[i][2] for i in part] + [when], [mm[i][0] for i in part], c * PEC + (60 if i == n - 1 else 10),
                     cont=[b for b, s in {mm[i][0][0]: st[i] for i in part[::-1]}.items() if not s])
                 part, c = [], 0
 
@@ -192,9 +211,9 @@ def program(ops, T, nxt, prv):
     def asel(out, a, pat, op, fill, base, cm=1):
         add("g", lambda e: [e["g"].affine_select(ap(out), ap(a), pat, op, float(fill), base, cm)], [a], [out], 210 + 2 * cols(out) * CYC)
 
-    def dma(q, pairs, rd, wr, kb):
+    def dma(q, pairs, rd, wr, kb, **kw):
         c = 60.0 * len(pairs); w = max(c, kb * 1024 / DMA[1])
-        add(q, lambda e: [e[q].dma_start(o, i) for o, i in pairs], rd, wr, w if q == "y" else c, dma=DMA[0] + (0 if q == "y" else w - c))
+        add(q, lambda e: [e[q].dma_start(o, i, **kw) for o, i in pairs], rd, wr, w if q == "y" else c + (1000.0 if q == "g" else 0.0), dma=DMA[0] + (0 if q == "y" else w - c))
 
     def pb(b, a=0, e=512, st=1):
         return ("pb%d" % b, a, e, st)
@@ -261,10 +280,11 @@ def program(ops, T, nxt, prv):
     ms(S("ONE", 0, 512), 1.0); ms(S("ZER"), 0.0); mv(S("ONE", 512, 1024), S("ONE", 0, 512))
     o0 = S("O0", 0, 64); iota(o0, [[2, 32], [1024, 2]], 0, 64)
     iota(S("COI", 0, 1), [[0, 1]], 0, 1)
-    blank = ["R1%d" % x for x in (1, 2, 3)] + ["T%d%d" % (b, x) for b in range(2) for x in range(b, 4)] + ["CV", "CV2", "KD", "KD2", "FK"]
+    blank = ["CV", "CV2", "KD", "KD2", "FK"]
     for n in blank: C(n)
-    ms(S("Z"), 0.0); ms(S("Y"), 0.0); ms(C("FK"), 0.0); w = 128 * len(blank) - 128
-    dma("y", [(T["CM"][:, a:min(w, a + 1024)], T["ZER"][:, 0:min(w, a + 1024) - a]) for a in range(0, w, 1024)], [S("ZER"), S("RAW")], [S("CM", 0, w)], w // 4)
+    ms(S("Z", 0, 432), 0.0); ms(C("FK"), 0.0); w = 128 * len(blank) - 128
+    for l in ([("Y", 0, 1024), ("Y", 1024, 2048), ("Y", 2048, 2304)], [("Z", 432, 1296), ("Z", 1296, 2304), ("CM", 0, w)]):
+        dma("y", [(T[n][:, a:b], T["ZER"][:, 0:b - a]) for n, a, b in l], [S("ZER"), S("RAW")], [S(*x) for x in l], 576)
     ts(S("COI", 1, 2), S("COI", 0, 1), 15, AL.bitwise_and); cp(RC, S("COI", 1, 2))
     ts(S("COI", 2, 3), S("COI", 0, 1), 4, AL.arith_shift_right, 1, AL.bitwise_and); cp(HQ, S("COI", 2, 3))
     ts(S("COI", 3, 4), S("COI", 0, 1), 8, AL.bitwise_and); ts(A64, S("COI", 3, 4), 8.0, AL.mult)
@@ -281,54 +301,55 @@ def program(ops, T, nxt, prv):
     def zmake(name, ws, off=15):
         for ch, w in ws: poke(Zs(name, None, off), ch, w)
     aff("DUP", 0, 0, 1); aff("ID", 0, 8, 1); aff("FN0", 0, 1000, 1); aff("FN1", 1000, -1000, 1)
-    ms(S("XB", 0, 512), 1.0); ms(S("XB", 0, 512, 32), 0.0); ms(S("GB", 0, 512), 0.0); ms(S("GB", 0, 512, 32), 1.0)
-    for h in range(2):
-        scan(S("LO", 512 * h, 512 * h + 512), S("XB", 0, 512), S("ONE", 0, 512), 0.0, AL.mult, AL.add)
-        scan(S("HI", 512 * h, 512 * h + 512), S("ONE", 0, 512), S("GB", 0, 512), 16.0 * h - 1.0, AL.mult, AL.add)
-    M0 = S("COL", 6, 7); ts(M0, RC, 0.0, AL.is_equal)
+    M0 = S("COL", 6, 7); ts(M0, RC, 0.0, AL.is_equal); x5 = sf(8); m_ = lambda i: sub(x5, i, i + 1)
+    ts(m_(1), RC, 1.0, AL.is_equal); ts(m_(2), RC, 2.0, AL.is_equal); ts(m_(3), M0, 16.0, AL.mult, m_(2), AL.subtract); ts(m_(4), m_(2), 15.0, AL.mult)
+    ms(S("XB", 0, 512), 1.0); ts(S("XB", 0, 512, 32), S("ONE", 0, 16), m_(1), AL.subtract); ts(S("GB", 0, 512), S("ONE", 0, 512), m_(1), AL.mult)
+    ts(S("GB", 0, 512, 32), S("ONE", 0, 16), m_(1), AL.mult, m_(2), AL.add)
+    ts(S("XB", 128, 129), S("XB", 0, 1), M0, AL.subtract); ts(S("GB", 384, 385), M0, 16.0, AL.mult, S("GB", 0, 1), AL.add)
+    scan(S("IDB", 512, 1024), S("XB", 0, 512), S("GB", 0, 512), m_(4), AL.mult, AL.add); mv(S("GB", 384, 385), S("GB", 0, 1))
+    scan(S("IDB", 0, 512), S("XB", 0, 512), S("GB", 0, 512), m_(3), AL.mult, AL.add)
     asel(S("Y", 15, 2304, 16), S("ONE", 0, 144), [[-1, 16], [-16, 9]], AL.is_equal, 0, 0)
     asel(C("BLK"), ONE, [[-16, 8], [0, 16]], AL.is_ge, 0, 0); asel(C("BLK"), C("BLK"), [[16, 8], [0, 16]], AL.is_ge, 0, 15, -1)
     B8c = sub(C("BLK"), 0, 128, 16)
     asel(Zs("lo8"), B8c, [[16, 8]], AL.is_ge, 0, 7, -1)
     zmake("key", [(0, 2048 * 256), (1, 256), (2, 32 * 256)])
-    V1, VW, DGO, A1C, JG, V256 = sf(64), S("W5"), sf(64), sf(128), sf(8), sf(64)
+    V1, VW, DGO, A1C, JG, V256 = sf(64), S("W5"), sf(64), sf(64), sf(8), sf(64)
     iota(V1, [[1, 64]], 1); ts(V1, V1, NTB, AL.add, float(-(1015 - 2 ** 23 - 2048)), AL.add)
-    JK = {c: sf(64) for c in set(MARK)}
-    for c, x in JK.items():
-        if c: ts(sub(x, 0, c), sub(V1, 0, c), -9209.0, AL.add)
-        if c < 64: ts(sub(x, c, 64), sub(V1, c, 64), -8185.0, AL.add)
-    INEL = sh(64); ts(V256, V1, 256.0, AL.mult)
+    INEL = sh(64); ts(V256, V1, 256.0, AL.mult, -256.0, AL.add)
     HLF = S("COL", 10, 11); ts(HLF, RC, 1.0, AL.is_equal, 0.5, AL.mult)
-    t0 = sf(64); ts(t0, V1, 128.5, AL.is_lt, 16.0, AL.mult); t1 = sf(64); ts(t1, V1, 896.5, AL.is_gt, 16.0, AL.mult); tt(INEL, t0, t1, AL.add)
+    t0 = sf(8)
     for k in range(8): ms(S("RST", k, 512, 8), -float(2 ** (k - 1)) if k else 1.0e8)
     for n, c in (("KT", 16.0), ("CT", 0.0), ("IT", 0.0), ("RT", 0.0), ("X", 0.0), ("INW", 0.0), ("GA", 0.0)):
         ms(S(n, 0, 16), c)
-    ts(S("KT", 15, 16), M0, 16.0, AL.mult, HLF, AL.add); ts(M3, HLF, -1.0, AL.mult)
+    ts(S("KT", 15, 16), M0, 31.0, AL.mult); ts(M3, HLF, -1.0, AL.mult)
     ts(C("NE2K"), C("FN1"), -2048.0, AL.mult)
 
     def f0(h, a, b):
         ts(S("TA", a, b), IND(S("RAW"), sub(o2, 32 * h, 32 * h + 32)), 1.0, AL.add)
         add("v", lambda e: [e["v"].transpose(ap(S("TB", a, b)), ap(S("TA", a, b)))], [S("TA", a, b)], [S("TB", a, b)], 512 * CYC)
-        act(S("FL", a, b), S("TB", a, b), AF.Sign)
+        flags(S("FL", a, b), S("TB", a, b))
         pe([(pb(1 + h), C("NE2K"), S("FL", a, b))])
         tt(S("RTH", a, b), pb(1 + h), S("TB", a, b), AL.add)
-        pe([(pb(4 + h), Yc(0, 1), S("LO", a, b)), (pb(4 + h), Yc(0, 2), S("HI", a, b))])
-        mv(S("IDB", a, b), pb(4 + h))
     halves(f0)
-    iota(S("U1J"), [[1, 64], [64, 16]], 1)
     iota(S("IO"), [[1, 1056]], 0); cp(S("IOB"), S("IO", 0, 128))
     for k in range(4):
         asel(S("ALL", 512 * k, 512 * k + 512), S("ONE", 0, 512), [[-1, 4], [-16, 8], [0, 16]], AL.is_equal, 0, -4 * k)
+    halves(lambda h, a, b: (pe([(pb(7), C("DUP"), S("ALL", a, b))]), mv(S("R1", a, b), pb(7))))
+    for j in range(16): ts(S("RA", j, 1024, 16), S("R1", j, 1024, 16), j * j - 1.0, AL.mult); ts(S("RB", j, 1024, 16), S("R1", j, 1024, 16), -2.0 * j, AL.mult)
+    iota(S("J16"), [[0, 32], [1, 16]], 0)
+    MK, MC, DB1, W32, LIM = [S("COL", 19, 20), S("COL", 20, 21)], [S("COL", 21, 22), S("COL", 22, 23)], S("COL", 23, 24), sf(64), sf(64)
+    ts(MK[0], RC, 7.5, AL.is_lt); ts(MK[1], RC, 7.5, AL.is_gt)
+    for h in range(2): ts(MC[h], MK[h], 31.0 / 65536, AL.mult)
+    for d in range(4): ms(sub(W32, 16 * d, 16 * d + 16), 32.0 ** -d)
+    iota(S("COI", 4, 8), [[0, 4]], 0, 1); cp(S("Lhx"), S("COI", 4, 8))
     for k in range(8): ts(sub(C("PW"), k, 128, 8), sub(C("ID"), k, 128, 8), float(2 ** k), AL.mult)
     pe([(pb(7, 0, 8), C("PW"), Zs("lo8"))]); cp(Zs("pow"), pb(7, 0, 8)); zmake("id", [(1, 1), (2, 32)])
     PWN, PWC = S("COL", 15, 16), S("COL", 16, 17)
     pe([(pb(7, 0, 1), C("PW"), S("ONE", 0, 1))]); ts(PWN, pb(7, 0, 1), -1.0, AL.mult); cp(PWC, pb(7, 0, 1))
 
-    ts(C("I8"), C("ID"), 8.0, AL.mult); ts(C("NID"), C("ID"), -1.0, AL.mult); ts(C("IDK"), C("ID"), 1.0 / 1024, AL.mult)
-    RC1, WX = S("COL", 7, 8), S("COL", 11, 12)
-    ts(RC1, RC, 1.0, AL.add); ts(sub(t0, 0, 1), RC, 7.5, AL.is_gt, -16384.0, AL.mult); ts(sub(t1, 0, 1), RC, 7.5, AL.is_lt, RC, AL.mult)
-    tt(WX, sub(t0, 0, 1), sub(t1, 0, 1), AL.add); ts(Zs("idx"), B8c, WX, AL.mult, flex=False)
-    iota(S("QS"), [[1, 4], [4, 16]], 0); ts(sub(t0, 0, 1), RC, 4.0, AL.mult, 1024.0, AL.add); ts(sub(JG, 0, 4), S("IO", 0, 4), sub(t0, 0, 1), AL.add)
+    ts(C("NID"), C("ID"), -1.0, AL.mult); ts(C("IDK"), C("ID"), 1.0 / 1024, AL.mult)
+    RC1 = S("COL", 7, 8); ts(RC1, RC, 1.0, AL.add)
+    ms(S("RKW", 64, 80), 1000.0); ms(S("RT", 1040, 1056), 0.0); ts(Zs("rc"), B8c, RC, AL.mult, flex=False)
     iota(S("ENC"), [[0, 256]], 2048)
     for c, z in ((0, "lo8"), (4, "lo8"), (5, "pow")): cp(sub(C("FK"), c, 128, 16), Zs(z))
     ts(sub(t0, 0, 1), RC, 0.5, AL.is_gt); ts(C("KS"), C("ID"), sub(t0, 0, 1), AL.mult)
@@ -350,8 +371,7 @@ def program(ops, T, nxt, prv):
         f, TT, CL, PL, SL = S("SM", 0, 1024), S("ZZ"), S("SU", 64, 200), S("SU", 200, 336), S("SU", 336, 400)
         cn, em, st, ex, ML, AB = sh(64), sh(64), S("S16", 64, 128), sf(72), sf(136), S("COL", 14, 15)
         ms(sub(ex, 0, 1), -1088.0); iota(ML, [[16, 136]], 0); ts(ML, ML, RC, AL.add); ts(AB, HLF, 2 * 16416.0, AL.mult)
-        for a in (0, 512): ts(S("M", 16 + a, 528 + a), S("IO", a, a + 512), 1024.0, AL.add)
-        ts(S("W5", 0, 128), S("IO", 0, 128), 2048.0, AL.add)
+        iota(S("M", 16, 1040), [[1, 1024]], 1024); iota(S("W5", 0, 128), [[1, 128]], 2048)
         for h in range(2):
             a, b = 512 * h, 512 * h + 512
             pe([(pb(14 + h), C("DUP"), S("RTH", a, b))]); tt(sub(f, a, b), pb(14 + h), S("IO", 1 + a, 1 + b), AL.is_gt)
@@ -391,25 +411,27 @@ def program(ops, T, nxt, prv):
     asel(C("LT"), C("BLK"), [[16, 8], [1, 16]], AL.is_gt, 0, 0, -1)
     iota(DGO, [[16, 64]], 129); ts(DGO, DGO, RC, AL.add)
     for k in range(8): ms(sub(C("P2"), k, 128, 8), float(2 ** (11 - k)))
-    aff("FB0", 4, 1000, 0); aff("FB1", 1004, -1000, 0)
-    for n, off in (("ha", 16), ("hb", 23)): ts(Zs(n), Zs("lo8"), -2.0, AL.mult); ts(Zs(n, None, off), Zs("en"), -2.0, AL.mult)
-    x4 = S("IO", 0, 8, 2); ts(sub(t0, 0, 4), x4, RC, AL.is_equal); ts(sub(t1, 0, 4), x4, 9.0, AL.add, RC, AL.is_equal)
-    tt(sub(t0, 8, 12), sub(t0, 0, 4), sub(t1, 0, 4), AL.add); ts(sub(t1, 8, 12), sub(t0, 8, 12), -8.0, AL.mult, -1.5, AL.add)
-    for jj in range(4): ts(S("TH", 128 * jj, 128 * jj + 128), ONE, sub(t1, 8 + jj, 9 + jj), AL.mult, flex=False)
+    ts(Zs("ha"), Zs("lo8"), -2.0, AL.mult); ts(Zs("ha", None, 16), Zs("en"), -2.0, AL.mult); ts(Zs("hh"), Zs("en"), -2.0, AL.mult)
     asel(C("B8"), ONE, [[-8, 16], [0, 8]], AL.is_ge, 0, 0); asel(C("B8"), C("B8"), [[8, 16], [0, 8]], AL.is_ge, 0, 7, -1)
-    asel(C("L8"), C("B8"), [[16, 8], [1, 16]], AL.is_gt, 0, 0, -1); asel(C("L8"), C("L8"), [[-1, 128]], AL.not_equal, -16, 0)
-    cmn["R00"] = cmn["I8"]
-    for b, d, j, k in PAIRS:
-        poke(sub(C("T%d%d" % (b, k // 2)), d, 128, 16), 8 * (k % 2) + j, 1.0)
-        if b: poke(sub(C("R1%d" % (j // 2)), d, 128, 16), 8 * (j % 2) + k, 8.0)
-    DB = [S("COL", 12, 13), S("COL", 13, 14)]; x3 = sh(8)
-    ts(DB[0], RC, 1.0 / 128, AL.mult, -1025.0 - 2057.0 / 8192, AL.add); ts(sub(x3, 0, 4), S("IO", 0, 64, 16), RC, AL.add)
-    pe([(pb(7, 0, 1), C("R1%d" % x), sub(x3, x, x + 1)) for x in (1, 2, 3)]); ts(DB[1], pb(7, 0, 1), 1.0 / 1024, AL.mult, -1025.0 - 2057.0 / 8192, AL.add)
-    tt(C("LW"), C("LT"), C("BLK"), AL.subtract)
-    asel(C("LS"), C("LW"), [[-1, 128]], AL.not_equal, 512, 0); asel(C("LW"), C("LW"), [[-1, 128]], AL.not_equal, 1024, 0)
-    asel(C("LS8"), C("L8"), [[-1, 128]], AL.not_equal, 512, 0); ts(C("L8"), C("L8"), 0.5, AL.mult)
-    pe([(pb(7, 0, 1), C("L8"), S("ONE", 0, 1))]); PRC, RRC = [-7.5, S("COL", 17, 18)], [-7.0 / 8192, S("COL", 18, 19)]
-    ts(PRC[1], pb(7, 0, 1), -1.0, AL.mult, -7.5, AL.add); ts(RRC[1], pb(7, 0, 1), -1.0 / 8192, AL.mult, -7.0 / 8192, AL.add)
+    asel(C("VM"), ONE, [[0, 8], [-1, 2], [1, 8]], AL.is_gt, 0, 0, 0); aff("EJ0", 0, 1, 0, C("VM")); aff("EK0", 0, 0, 1, C("VM"))
+    x3 = sf(8); c_ = lambda i: sub(x3, i, i + 1); x4 = sh(8)
+    ts(c_(0), RC, -0.5, AL.mult, 7.5, AL.add); ts(c_(1), c_(0), RC, AL.mult, -12.0, AL.add); ts(c_(2), RC, -1.0, AL.mult, 7.0, AL.add); ts(c_(3), c_(2), c_(1), AL.add)
+    ts(c_(4), c_(1), -1.0, AL.mult, RC1, AL.add); ts(C("KL"), C("BLK"), c_(4), AL.mult); ts(C("EK1"), C("BLK"), -100.0, AL.mult, 100.0, AL.add)
+    p = pb(7, 0, 128); pe([(p, C("ID"), C("EK1")), (p, C("ID"), S("J16", 0, 128))]); mv(C("D16"), p); ms(sub(C("D16"), 0, 128, 16), 100.0)
+    ts(C("EK1"), C("D16"), c_(1), AL.is_ge, MK[0], AL.mult); ts(p, C("D16"), c_(3), AL.is_lt); tt(C("EJ1"), p, C("EK1"), AL.mult)
+    pe([(p, C("KL"), C("EJ1")), (p, C("ID"), C("D16"))]); ts(C("EK1"), p, RC, AL.is_equal, MK[0], AL.mult)
+    asel(C("LN"), C("LT"), [[-1, 128]], AL.not_equal, -8.5, 0); ts(C("LN"), C("LN"), -1.0, AL.mult)
+    for b in range(2):
+        pe([(p, C("EJ%d" % b), C("EJ%d" % b)), (p, C("EK%d" % b), C("EJ%d" % b))]); tt(C("LA%d%d" % (b, b)), p, C("LN"), AL.mult)
+        pe([(p, C("EK%d" % b), C("EK%d" % b))]); tt(C("LB%d%d" % (b, b)), p, C("LN"), AL.mult)
+        pe([(p, C("EK0"), C(("EJ1", "EK1")[b]))]); ts(C(("LA01", "LB01")[b]), p, -1.0, AL.mult)
+    DB = [S("COL", 12, 13), S("COL", 13, 14)]; ts(C("I8K"), C("ID"), 1.0 / 8192, AL.mult)
+    ts(c_(7), M0, 1024.0 + 2057.0 / 8192, AL.mult, -1025.0 - 2057.0 / 8192, AL.add)
+    ts(DB[0], RC, 1.0 / 128, AL.mult, c_(7), AL.add); ts(sub(x4, 0, 1), RC, 8.0, AL.mult); mv(sub(x4, 1, 2), RC)
+    pe([(pb(7, 0, 1), C("EJ1"), sub(x4, 0, 1)), (pb(7, 0, 1), C("EK1"), sub(x4, 1, 2))]); ts(DB[1], pb(7, 0, 1), 1.0 / 128, AL.mult, c_(7), AL.add)
+    tt(C("LW"), C("LT"), C("BLK"), AL.subtract); RH = c_(6); ts(RH, M0, -0.5, AL.mult, 0.5, AL.add)
+    asel(C("LS"), C("LW"), [[-1, 128]], AL.not_equal, 512, 0); asel(C("LW"), C("LW"), [[-1, 128]], AL.not_equal, 1024, 0); ms(sub(C("LW"), 0, 128, 16), 0.0)
+    asel(C("LS8"), C("B8"), [[16, 8], [1, 16]], AL.is_gt, 0, 0, -1); asel(C("LS8"), C("LS8"), [[-1, 128]], AL.not_equal, 512, 0)
     ts(C("I4K"), C("ID"), 1.0 / 4096, AL.mult)
     ts(Zs("e4k"), Zs("en"), 4096.0, AL.mult); ts(Zs("l4k"), Zs("lo8"), 4096.0, AL.mult); DE = sf(64); ts(DE, DGO, 4352.0 - 129, AL.add)
     ts(C("EN2K"), C("FN1"), 2048.0, AL.mult)
@@ -426,9 +448,15 @@ def program(ops, T, nxt, prv):
     for off in (15, 23): poke(sub(KD, off, off + 128, 16), 0, 4096)
     DW, DOV, DX = sf(32), sf(80), sf(64)
     ts(DW, sub(DGO, 0, 32), 783.0, AL.add); ts(DX, DGO, 3984.0, AL.add)
-    ts(sub(DOV, 0, 64), DGO, 8064.0, AL.add); ts(sub(DOV, 64, 80), sub(DGO, 0, 16), 9088.0, AL.add)
+    ts(sub(DOV, 0, 64), DGO, -128.0, AL.add); ts(sub(DOV, 64, 80), sub(DGO, 0, 16), 896.0, AL.add)
+    AC, QA, QB, C200 = sf(8), sf(8), sh(8), sh(64); ts(AC, sub(DGO, 0, 8), -128.5, AL.add); ms(C200, 200.0); asel(C("LTK"), C("LT"), [[-1, 128]], AL.not_equal, -1000, 0)
+    MD = sf(80); w = 40 // LOTS[0]; LOB, HIB = S("COL", 18, 19), S("COL", 11, 12)
+    for c in range(2 * LOTS[0]): ts(sub(MD, w * c, w * c + w), sub(DGO, w * (c // 2), w * (c // 2) + w), -129.0, AL.add)
+    ts(LOB, M0, 0.25, AL.mult, -0.25, AL.add); ts(HIB, M0, 15.75, AL.mult, 0.25, AL.add); ts(C("I512"), C("ID"), 512.0, AL.mult); ts(C("I1K"), C("ID"), 1024.0, AL.mult)
+    ts(c_(5), M0, -12288.0, AL.mult, 8192.0, AL.add); ts(Zs("yk"), B8c, c_(5), AL.mult, flex=False)
     DS = sf(4); ts(DS, sub(DGO, 0, 4), 383.0, AL.add); ts(sub(A1C, 0, 64), S("IO", 0, 64), A64, AL.add, 1.0, AL.add)
-    N896 = sh(64); ms(N896, -896.0); ms(sub(A1C, 64, 128), 0.0)
+    N896 = sh(64); ms(N896, -896.0)
+    for h in range(2): ts(C("NFN%d" % h), C("FN%d" % h), -1.0, AL.mult)
     asel(C("GE8"), C("B8"), [[-16, 8], [-1, 16]], AL.is_ge, 0, 0)
     pe([(pb(7, 0, 1), C("P2"), S("Y", 15, 16))]); P2C = S("COL", 5, 6); cp(P2C, pb(7, 0, 1))
     ts(S("WI", 0, 256), S("IO", 0, 256), P2C, AL.mult); ts(S("WJ", 0, 256), S("WI", 0, 256), 2048, AL.bitwise_and)
@@ -437,28 +465,27 @@ def program(ops, T, nxt, prv):
     for n in range(8): ts(S("LUT", 256 * n, 256 * n + 256), S("KP"), float(n), AL.is_gt)
     aff("FE0", 8, 1000, 1); aff("FE1", 1008, -1000, 1); aff("DUPE", 8, 0, 1)
     for h in range(2):
-        m = 320 * h; pe([(pb(6 + h, 0, 320), Yc(0, 9), S("LO", m, m + 320)), (pb(6 + h, 0, 320), Yc(0, 10), S("HI", m, m + 320))]); mv(S("NAM", m, m + 320), pb(6 + h, 0, 320), M8[0])
+        m = 320 * h; pe([(pb(6 + h, 0, 320), Yc(1, 9), S("IDB", m, m + 320)), (pb(6 + h, 0, 320), Yc(2, 10), S("IDB", m, m + 320))]); mv(S("NAM", m, m + 320), pb(6 + h, 0, 320), M8[0])
     ms(C("NEG"), -1.0); ms(C("K8"), 8192.0)
     for s_ in range(4):
         for ha in range(2): aff("NP%d%d" % (s_, ha), 8 * ha + 2 * s_, 1, 0, C("NEG"))
-        tt(C("VB%d" % s_), C("DUP"), C("NP%d0" % s_), AL.subtract)
     ms(C("N13"), 1.0 / 8192)
     for ha, (c0, al) in enumerate(((0, 1000), (1000, -1000))):
         aff("SH%d" % ha, c0, al, 1, C("K8")); asel(C("SH%d" % ha), C("SH%d" % ha), [[-16, 8], [-al, 2], [-1, 8]], AL.not_equal, 8192, -c0 - 8)
         aff("NFE%d" % ha, c0 + 8, al, 1, C("N13"))
     for s_ in range(4): aff("NQ%d" % s_, 8 + 2 * s_, 1, 0, C("N13"))
 
-    OK_, CH, NCH, TG1, TG2, TG3, LB1, LB2, GG, G4, TG5 = [sf(64) for _ in range(11)]
-    MI, AI, BI = [si(64) for _ in range(3)]
-    SELF, RK1, CB, CON, BB, DGB, BG, SD, DEAD = [sh(64) for _ in range(9)]
+    OK_, TG1, TG3, LB1, LB2, GG, TG5 = [sf(64) for _ in range(7)]
+    MI, AI, BI, HI_, LO_, B0, B1 = [si(64) for _ in range(7)]
+    CH, CB, CON, BB, DGB, BG, SD, DEAD = [sh(64) for _ in range(8)]
     INZ = sh(72); ms(DEAD, 0.0); ms(sub(INZ, 0, 1), 0.0); ms(S("INC", 0, 144, 72), 0.0)
     E = {"nxt": nxt, "prv": prv, "zero_ov": zero_ov, "won": []}
-    for k, w in (("ci", 40), ("c4", 40), ("yi", 40), ("hk", 80), ("vl", 40), ("rr", 80), ("w0", 64), ("w1", 64)): E[k] = si(w)
-    for k in ("c2", "i2", "u2", "t2", "t3"): E[k] = sf(80)
+    for k, w in (("ci", 40), ("c4", 40), ("yi", 40), ("hk", 40), ("rr", 80), ("w0", 64), ("w1", 64)): E[k] = si(w)
+    for k in ("c2", "t2"): E[k] = sf(40)
     for k in ("q0", "q3"): E[k] = sf(128)
-    A1H, A1G, LP, LM = [S("S16", 64 * i, 64 * i + 64) for i in range(4)]
+    LP, LM = [S("S16", 64 * i, 64 * i + 64) for i in (2, 3)]
     IDR, E2 = S("S16", 256, 384), S("S16", 384, 512)
-    AL_, MKL, SPL, GOL, UL, CSL, CWL, I2, EXL, LUL, OVL, STL, SCL, SXL, SRL, GQL, QL = [S("L" + k) for k in LISTS]
+    AL_, HXL, SPL, GOL, UL, CSL, CWL, I2, EXL, LUL, OVL, STL, SCL, SXL, SRL, GQL, QL = [S("L" + k) for k in LISTS]
     RTW, XW = S("RT"), S("X")
 
     def fold(out, f, src, a, n, more=None):
@@ -469,70 +496,62 @@ def program(ops, T, nxt, prv):
         for h in range(2):
             fold(pb(1, 0, 256), "FN", "RTH", 512 * h, 512); ts(S("LN", 256 * h, 256 * h + 256), pb(1, 0, 256), 15.0, AL.add)
         extc(pb(2, 0, 64), "c0", S("KT", 16, 1040))
-        cp(DGB, pb(2, 0, 64)); ts(pb(2, 0, 64), pb(2, 0, 64), 2048.0 * 256, AL.mult); tt(TG5, pb(2, 0, 64), V256, AL.add); ts(OK_, TG5, float(2 ** 23), AL.min)
-        w = HOPW[0]
+        ts(pb(2, 0, 64), pb(2, 0, 64), 2048.0 * 256, AL.mult); tt(OK_, pb(2, 0, 64), LIM if t else V256, AL.add)
+        ext(pb(2, 0, 64), [("c0", S("KT", 16, 1040))], 1024); mv(DGB, pb(2, 0, 64), 1.0)
         for r in range(16):
-            for a in range(512 * r, 512 * r + 512, w): mv(S("G1", a, a + w), IND(S("KT"), S("LN", a // 16, (a + w) // 16)))
-            pe([(pb(10), Zs("key", r), S("G1", 512 * r, 512 * r + 512))], r == 0, r == 15)
+            a = 512 * (r % 13); mv(S("G1", a, a + 512), IND(S("KT"), S("LN", 32 * r, 32 * r + 32)))
+            pe([(pb(10), Zs("key", r), S("G1", a, a + 512))], r == 0, r == 15)
 
     def part_a(t):
         tag[:] = ["a", t]
         for h in range(2):
             a, b, k = 512 * h, 512 * h + 512, 2 * h
-            pe([(pb(k), C("ID"), S("IDB", a, b))] + [(pb(k, 64 * r, 64 * r + 64), Yc(8 * h + r, 0), INEL) for r in range(8)], True, False)
+            pe([(pb(k), C("ID"), S("IDB", a, b))] + [(pb(k, 64 * r, 64 * r + 64), Yc(8 * h + r, 0), INEL) for r in range(8) if t], True, False, sub(OVL, 0, 40) if t else None)
             pe([(pb(k), C("FK"), S("FL", a, b))], False, True)
-            mv(S("KT", 16 + a, 16 + b), pb(k), HLF)
+            mv(S("KT", 16 + a, 16 + b), pb(k), M3)
         hop(t); tag[0] = "a"
         for h in range(2): pe([(pb(1 + h), C("DUP"), S("RTH", 512 * h, 512 * h + 512))]); mv(S("RT", 16 + 512 * h, 528 + 512 * h), pb(1 + h))
         scan(pb(9), S("RST"), pb(10), 0.0, AL.add, AL.min)
         tt(MI, pb(9, 7, 512, 8), OK_, AL.min); ts(AI, MI, 8, AL.arith_shift_right, 2047, AL.bitwise_and)
-        ts(AL_, AI, 15.0, AL.add)
-        tt(S("GB"), IND(RTW, AL_), S("U1J"), AL.is_equal)
-        cp(A1H, AI); tt(SELF, AI, V1, AL.is_equal); ts(BI, MI, 255, AL.bitwise_and); ts(BB, BI, -1.0, AL.mult)
+        ft = lambda i, h=None: S("FT", 128 * i, 128 * i + 128) if h is None else S("FT", 128 * i + 64 * h, 128 * i + 64 * h + 64)
+        ts(B0, MI, 65536, AL.bitwise_and); ts(B1, MI, 131072, AL.bitwise_and); ts(LO_, MI, 12, AL.arith_shift_right, 15, AL.bitwise_and); ts(HI_, MI, 8, AL.arith_shift_right, 15, AL.bitwise_and)
+        ts(TG1, B1, 1023.0 / 131072, AL.mult, 1.0, AL.add); lp = pb(11, 128, 192); cp(lp, LO_)
+        for h in range(2): ts(pb(11, 64 * h, 64 * h + 64), B0, MC[h], AL.mult, MK[h], AL.add); ts(ft(0, h), HI_, MK[h], AL.mult)
+        for h in range(2): tt(ft(1, h), pb(11, 64 * h, 64 * h + 64), TG1, AL.mult)
+        for i in (2, 3):
+            for h in range(2): tt(ft(i, h), lp, ft(i - 1, h), AL.mult)
+        for h in range(2):
+            a, b = 512 * h, 512 * h + 512
+            pe([(pb(12), ft(0), S("R1", a, b))]); tt(S("GB", a, b), pb(12), S("J16"), AL.is_equal)
+            for i, n in ((1, "RA"), (2, "RB"), (3, "R1")): pe([(pb(13), ft(i), S(n, a, b))], i == 1, i == 3)
+            relu(S("EQ", a, b), pb(13), -1.0, 0.0, (-1.0, AL.mult, 0.0, AL.max))
+            pe([(pb(3, 0, 128), S("GB", c, c + 128), S("EQ", c, c + 128)) for c in range(a, b, 128)], h == 0, h == 1)
+        mv(S("HW"), pb(3, 0, 128)); tt(B0, IND(S("HW"), HXL), W32, AL.mult); ts(B1, B0, 31, AL.bitwise_and)
+        tt(CH, B1, DGB, AL.is_equal)
+        ts(AL_, AI, 16.0, AL.add); ts(BI, MI, 255, AL.bitwise_and); ts(BB, BI, -1.0, AL.mult); ts(SD, BI, 0.0, AL.is_equal)
         for h in range(2):
             a, b, p = 512 * h, 512 * h + 512, pb(4 + h)
             pe([(p, C("KS"), S("KT", 16 + a, 16 + b))] + [(blk(4, r), Yc(r, 5), BB) for r in range(8 * h, 8 * h + 8)], True, False)
-        ts(LB1, AI, -1000.0, AL.add, flex=False); ts(LB2, AI, -1.0, AL.mult, -1000.0, AL.add, flex=False)
-        tt(SD, SELF, DEAD, AL.add)
-        pe([(pb(3, 0, 64), C("I8"), A1H)] + [(pb(3, 0, 64), Zs("idx", r), S("GB", r, 1024, 16)) for r in range(16)])
-        y, WD = pb(3, 0, 64), S("IT", 16, 528)
-        tt(TG1, y, JK[MARK[t]], AL.min); seen = []; c = MARK[t]; WS = S("IT", 528, 1040)
-        if c < 64:
-            ts(sub(MKL, c, 64), sub(TG1, c, 64), 16376.0, AL.add)
-            cp(IND(S("G1"), sub(MKL, c, 64)), S("ONE", 0, 1024 - 16 * c))
-            dma("y", [(T["IT"][:, 16:528], T["G1"][3:128:16, 0:8192])], [S("G1", 0, 8192)], [WD], 200); seen.append(WD)
-        if c:
-            dma("y", [(T["GA"][0:128:16, a:a + 3072], T["ZF"][:, 0:192]) for a in (16, 3088)], [S("ZF")], [S("GA", 16, 6160)], 200)
-            ts(sub(MKL, 0, c), sub(TG1, 0, c), 15352.0, AL.add)
-            for a in range(0, c, 32): put(IND(S("GA", 16, 7184), sub(MKL, a, a + 32)), S("IO", 32, 544))
-            dma("y", [(T["W6"][16 * g + 2:16 * g + 14, :], T["GA"][16 * g:16 * g + 1, 16:6160]) for g in range(8)], [S("GA", 16, 6160)], [S("W6")], 200)
-            act(WS, S("W6"), AF.Sign); seen.append(WS)
-        pe([(y, C("I8"), SELF), (y, C("I8"), SELF), (y, C("NID"), DGB)] + [(y, C("ID"), sub(x, k, 512, 8)) for x in seen for k in range(8)]); edge = 15.5
-        ts(CH, y, edge, AL.is_gt); ts(NCH, y, edge, AL.is_lt, 1000.0, AL.mult)
-        INB = sub(INZ, 1, 65); scan(INB, S("ONE", 0, 64), CH, 0.0, AL.mult, AL.add)
-        off = pb(3, 0, 1); pe([(off, C("LT"), sub(INB, 63, 64))])
-        tt(TG2, INB, NCH, AL.add); ts(RK1, TG2, off, AL.add); ts(CON, RK1, 128.5, AL.is_lt)
-        for h in range(2):
-            pe([(blk(4, r), Yc(r, 0), RK1) for r in range(8 * h, 8 * h + 8)], False, True)
-            mv(S("CT", 16 + 512 * h, 528 + 512 * h), pb(4 + h), M3)
-        x0, x1, x2, x3 = [sub(G4, 8 * i, 8 * i + 4) for i in range(4)]
-        x0 = sub(INZ, 0, 64, 16); tt(x1, x0, sub(INB, 15, 64, 16), AL.is_equal)
-        tt(x2, x1, sub(JG, 0, 4), AL.mult); tt(x3, x2, x0, AL.add); ts(GQL, x3, off, AL.add)
-        QR, E1 = S("QR", 0, 128), S("QR", 128, 256)
-        ms(S("G1", 0, 128), 0.0); cp(IND(S("G1", 0, 1920), GQL), S("QS")); scan(QR, S("G1", 0, 128), S("G1", 0, 128), 0.0, AL.max, AL.max)
-        ext(pb(3, 0, 8), [("c0", QR)], 128); cp(QL, pb(3, 0, 8)); ts(IDR, QR, 16.0, AL.mult, RC1, AL.add)
-        ext(pb(4, 0, 64), [("c0", S("CT", 16, 1040))], 1024); cp(S("RKW"), pb(4, 0, 64))
-        tt(E1, IND(S("RKW"), QL), S("IO", 1, 129), AL.is_equal); tt(E2, E1, IDR, AL.mult)
-        ext(pb(3, 0, 8), [("all", E2)], 128); ts(GOL, pb(3, 0, 8), 15.0, AL.add)
+        ts(LB1, AI, -999.0, AL.add, flex=False); ts(LB2, AI, -1.0, AL.mult, -1001.0, AL.add, flex=False)
+        INB, p, RK, E1 = sub(INZ, 1, 65), pb(3, 0, 64), S("RKW", 0, 64), S("QR", 128, 256)
+        pe([(p, C("BLK"), CH)]); scan(INB, p, C200, 0.0, AL.add, AL.min)
+        for c in range(8): act(S("QS", 64 * c, 64 * c + 64), INB, AF.Sign, sub(AC, c, c + 1), -1.0, sub(QA, c, c + 1))
+        ts(QL, QA, 0.5, AL.mult, 32.0, AL.add); ts(QB, QA, 8.0, AL.mult, 512.0, AL.add)
+        pe([(p, C("LTK"), CH), (p, C("ID"), sub(INZ, 0, 64))]); mv(RK, p, 1001.0)
+        tt(E1, IND(S("RKW"), QL), S("IO", 1, 129), AL.is_equal)
+        p = pb(3, 0, 8); pe([(p, C("ID"), QB)] + [(p, Zs("rc", r), sub(E1, r, 128, 16)) for r in range(16)]); ts(GOL, p, 16.0, AL.add)
         cp(S("G0"), IND(RTW, GOL))
         fold(pb(3, 0, 64), "FN", "G0", 0, 128); ts(UL, pb(3, 0, 64), 15.0, AL.add)
+        for h in range(2):
+            pe([(pb(4 + h, r, 512, 16), Yc(r, 0), sub(RK, 32 * h, 32 * h + 32)) for r in range(16)], False, True)
+            mv(S("CT", 16 + 512 * h, 528 + 512 * h), pb(4 + h), HLF)
         tag[0] = "lab"
         for h in range(2): mv(S("GC", 512 * h, 512 * h + 512), IND(S("CT"), sub(AL_, 32 * h, 32 * h + 32)))
         ext(pb(5, 0, 64), [("c0", S("GC"))], 1024)
-        ts(CB, pb(5, 0, 64), 128.5, AL.is_lt); tt(GG, CB, SD, AL.is_gt)
+        ts(CB, pb(5, 0, 64), 128.5, AL.is_lt); tt(GG, CB, SD, AL.is_gt); tt(CON, CB, SD, AL.mult)
         if not SPK[t]: tt(BG, CB, BB, AL.mult)
         tt(LP, LB1, GG, AL.mult); tt(LM, LB2, GG, AL.mult); tt(DEAD, DEAD, CON, AL.add)
-        if t < 2: ts(TG2, CON, 16.0, AL.mult); tt(INEL, INEL, TG2, AL.add)
+        if t < 2: ts(INEL, DEAD, 16.0, AL.mult); ts(TG5, DEAD, -2.0 ** 24, AL.mult); tt(LIM, TG5, V256, AL.add)
         w2r(1, [(Al, lambda r: BB if SPK[t] else BG)])
         for h in range(2):
             p = pb(1 + h)
@@ -581,81 +600,77 @@ def program(ops, T, nxt, prv):
         for h in range(2): ts(S("GR", 512 * h, 512 * h + 512), IND(RTW, sub(UL, 32 * h, 32 * h + 32)), -1.0, AL.mult)
         for h in range(2): mv(S("IT", 16 + 512 * h, 528 + 512 * h), IND(S("CT"), sub(UL, 32 * h, 32 * h + 32)))
         J = lambda x, jj: sub(x, 128 * jj, 128 * jj + 128)
-        gu = lambda jj, h: S("IT", 16 + 2 * jj + h, 1040, 8)
-        FG = S("QR", 0, 128); ts(FG, S("G0"), 0.0, AL.is_gt)
-        pe([(pb(0), C("ID"), S("TH"))] + [(J(pb(0), jj), C("VB%d" % jj), FG) for jj in range(4)], True, False)
+        two_ = lambda x, b, a=0: sub(x, a + b, a + 256, 2)
+        FG, DG = S("QR", 0, 128), S("PR", 256, 384); ts(FG, S("G0"), 0.0, AL.is_gt)
+        pe([(two_(pb(0), b), C(m + str(b)), FG) for b in range(2) for m in ("EJ", "EK")], True, False)
         pe([(J(pb(1), s), C("NP%d0" % s), S("G0")) for s in range(4)])
         for x, (j, s) in enumerate(BLOCKS):
             tt(J(S("HE"), x), J(pb(1), s), S("GR", j, 1024, 8), AL.is_equal)
-            if x % 2: pe([m for y, (j, s) in list(enumerate(BLOCKS))[x - 1:x + 1] for m in [(J(pb(0), j // 2), Zs("ha", 8 * (j % 2) + 2 * s), J(S("HE"), y)),
-                                                                                           (J(pb(0), s), Zs("hb", j), J(S("HE"), y))]], False, x == 15)
-        pe([(J(pb(7), jj), C("FB%d" % h), gu(jj, h)) for jj in range(4) for h in range(2)], True, False)
-        if SGN[t][0] == "v": ts(S("WB"), pb(0), 0.0, AL.is_gt, 2.0, AL.mult); k = 0
-        else: act(S("WB"), pb(0), AF.Sign); k = 1
-        pe([(pb(7), C("L8"), S("WB"))], False, True)
-        if SGN[t][1] == "v": ts(S("PR"), pb(7), PRC[k], AL.is_lt)
-        else: act(S("PR"), pb(7), AF.Sign, PRC[k], -1.0)
-        act(S("R"), pb(7), AF.Relu, RRC[k], -1.0 / 8192)
-        tr = lambda n, p, b, src: [(p, C("%s%d%d" % (n, b, x)), J(S(src), x)) for x in sorted(set(q[2 + (n == "T")] // 2 for q in PAIRS if q[0] == b))]
-        grp = lambda l: [m + ((1,) if i == 0 else ()) for i, m in enumerate(l)]
-        pe([m for b in range(2) for m in grp(tr("R", pb(3, b, 256, 2), b, "PR") + tr("T", pb(3, b, 256, 2), b, "PR"))])
-        ts(S("SV", 0, 256), pb(3, 0, 256), 8.5, AL.is_gt)
+            if x % 2 or x > 13: pe([(two_(pb(0), int(j > 1)), Zs("ha", PLACE[j, 2 * s]) if j < 2 * s else Zs("hh", PLACE[j, j + 1]), J(S("HE"), y))
+                                    for y, (j, s) in list(enumerate(BLOCKS))[x - (x < 14):x + 1]], False, x == 15)
+        pe([(pb(2, 0, 128), Yc(4, j), S("IT", 16 + j, 1040, 8)) for j in range(8)]); ts(DG, pb(2, 0, 128), -1.0, AL.mult)
+        pe([(two_(pb(7), b, 256 * e_), C(("EJ%d", "EK%d")[e_] % b), DG) for e_ in range(2) for b in range(2)], True, False)
+        relu(S("WB", 0, 256), pb(0, 0, 256), 1.0, -1.0, (1.5, AL.is_gt))
+        pe([(two_(pb(7), b, 256 * e_), C("L%s%d%d" % ("AB"[e_], c, b)), two_(S("WB"), c)) for e_ in range(2) for c, b in ((0, 0), (0, 1), (1, 1))], False, True)
+        relu(S("PR", 0, 256), pb(7, 0, 256), -200.0, 50.0, (0.25, AL.is_lt, 100.0, AL.mult)); tt(S("SV", 0, 256), pb(7, 256, 512), S("PR", 0, 256), AL.is_gt)
+        relu(S("R"), pb(7), 1.0, RH, (RH, AL.add, 0.0, AL.max))
         pe([(pb(3, 0, 256), C("BLK"), S("SV", 0, 256))]); scan(S("INW", 16, 272), pb(3, 0, 256), S("IO", 656, 912), 0.0, AL.add, AL.min)
         z2 = sub(TG3, 0, 16)
         ext(pb(2, 0, 16), [("all", S("SV", 0, 256))], 256); ts(S("SV", 256, 272), pb(2, 0, 16), 0.0, AL.is_equal, 4096.0, AL.mult)
         pe([(pb(3, 0, 16), Yc(0, r), S("INW", 15 + r, 271, 16)) for r in range(16)] + [(pb(3, 0, 16), C("ID"), S("SV", 256, 272))])
-        for b in range(2):
-            p = pb(0, b, 256, 2)
-            pe(tr("R", p, b, "R") + tr("T", p, b, "R") + [(p, C("LW"), S("SV", b, 256, 2)), (p, C("ID"), S("INW", 16 + b, 272, 2))])
+        p = pb(0, 0, 256)
+        pe([(p, C("IDK"), S("R", 0, 256)), (p, C("I8K"), S("R", 256, 512)), (p, C("LW"), S("SV", 0, 256)), (p, C("ID"), S("INW", 16, 272))])
         for b in range(2): mv(S("NT", b, 256, 2), pb(0, b, 256, 2), DB[b])
         tt(z2, pb(3, 0, 16), sub(DW, 0, 16), AL.min); cp(sub(CSL, 0, 16), z2)
-        iota(S("WW", 0, 640), [[0, 640]], 0); put(IND(S("WW"), sub(CSL, 0, 16)), S("IO", 32, 288))
-        scan(S("CW"), S("WW", 0, 640), S("WW", 0, 640), 0.0, AL.max, AL.max)
+        iota(S("WW", 0, 640), [[0, 640]], 0); iota(S("WV", 0, 640), [[0, 640]], 0)
+        put(IND(S("WW"), sub(CSL, 8, 16)), S("IO", 160, 288)); cp(IND(S("WV"), sub(CSL, 0, 8)), S("IO", 32, 160))
+        scan(S("CW"), S("WV", 0, 640), S("WW", 0, 640), 0.0, AL.max, AL.max)
         ext(pb(3, 0, 40), [("c0", S("CW"))], 640); ts(CWL, pb(3, 0, 40), -32.0, AL.add)
-        tt(S("YC"), IND(S("NT", 0, 256), CWL), S("IO", 0, 640), AL.subtract); ts(S("YC"), S("YC"), -0.5, AL.max, 0.5, AL.min)
-        ci, c4, yi, hk, vl, rr = E["ci"], E["c4"], E["yi"], E["hk"], E["vl"], E["rr"]
-        c2, i2, u2, t2, t3 = E["c2"], E["i2"], E["u2"], E["t2"], E["t3"]
-        lo, hi = (lambda x: sub(x, 0, 40)), (lambda x: sub(x, 40, 80))
-        ts(ci, pb(3, 0, 40), -32.0, AL.add); ts(c4, ci, 254, AL.bitwise_and); ts(lo(c2), c4, 4.0, AL.mult, -3.0, AL.add); ts(hi(c2), c4, 4.0, AL.mult, 1.0, AL.add)
-        ext(pb(3, 64, 104), [("8k", S("YC"))], 640); ts(yi, pb(3, 64, 104), 65536.0, AL.add)
-        ts(lo(hk), yi, 9, AL.arith_shift_right, 15, AL.bitwise_and); ts(hi(hk), yi, 6, AL.arith_shift_right, 7, AL.bitwise_and)
-        tt(t2, hk, c2, AL.add); ts(I2, t2, 15.0, AL.add)
-        ts(vl, lo(hk), 0.0, AL.is_gt); ts(lo(i2), lo(hk), 0.0, AL.is_equal)
-        ts(lo(rr), yi, 3, AL.arith_shift_right, 7, AL.bitwise_and); ts(hi(rr), yi, 7, AL.bitwise_and); ts(S("R2"), rr, 256.0, AL.mult)
-        hs = ((lo, 0, 3), (hi, 640, 0)); GL = {0: "GB", 640: "EQ"}
-        for f_, a, b in hs:
-            tt(f_(t3), lo(i2), f_(DOV), AL.mult)
-            cp(S("GI", a, a + 640), IND(S("IT"), f_(I2)))
-            pe([(pb(b, 0, 40), C("ID"), f_(S("R2")))] + [(pb(b, 0, 40), Zs("om", r), S("GI", a + r, a + 640, 16)) for r in range(16)]); cp(f_(LUL), pb(b, 0, 40))
-            mv(S(GL[a], 0, 640), IND(S("LUT"), f_(LUL)))
-            pe([(pb(b, 64, 104), Zs("id", r), S("GI", a + r, a + 640, 16)) for r in range(16)], True, False)
-        for f_, a, b in hs:
-            pe([(pb(b, 64, 104), Zs("l17", r), S(GL[a], r, 640, 16)) for r in range(16)], False, True)
-            tt(f_(t2), pb(b, 64, 104), f_(t3), AL.max); ts(f_(OVL), f_(t2), -1.0, AL.add)
-            tt(IND(S("OV"), f_(OVL)), S("GI", 640 - a, 1280 - a), S("NAM"), AL.add)
+        ci, c4, yi, hk, rr, c2, t2 = [E[k] for k in ("ci", "c4", "yi", "hk", "rr", "c2", "t2")]
+        vl, i2, t3, cv, tot = S("UM", 0, 80), S("UM", 80, 160), S("S16", 0, 80), S("S16", 80, 120), S("COL", 17, 18); w = 40 // LOTS[0]; c0 = 136 + 40 * t
+        ts(tot, S("INW", 271, 272), 0.0, AL.add); ts(vl, MD, tot, AL.is_lt); ts(i2, MD, tot, AL.is_ge); tt(t3, i2, DOV, AL.mult)
+        ts(ci, pb(3, 0, 40), -32.0, AL.add); ts(c4, ci, 254, AL.bitwise_and); ts(sub(c2, 0, 40), c4, 4.0, AL.mult, 1.0, AL.add)
+        for c in range(LOTS[0]):
+            one = lambda x: sub(x, w * c, w * c + w); end = lambda x, e_, k=1: sub(x, k * w * (2 * c + e_), k * w * (2 * c + e_ + 1)); all_ = lambda x, k=1: sub(x, 2 * k * w * c, 2 * k * w * (c + 1))
+            yc, p, GL = S("YC", 16 * w * c, 16 * w * (c + 1)), pb(3, 64, 64 + w), S(("GB", "EQ")[c % 2], 0, 640)
+            tt(one(cv), one(c2), end(vl, 0), AL.mult)
+            tt(yc, IND(S("NT", 0, 256), one(CWL)), S("IO", 16 * w * c, 16 * w * (c + 1)), AL.subtract); ts(yc, yc, LOB, AL.max, HIB, AL.min)
+            pe([(p, C("I512"), one(cv))] + [(p, Zs("yk", r), sub(yc, r, 16 * w, 16)) for r in range(16)])
+            ts(end(I2, 0), p, 1.0 / 512, AL.mult, 75.0 - 0.499, AL.add); ts(one(yi), p, 30720.0, AL.add)
+            ts(one(hk), one(yi), 6, AL.arith_shift_right, 7, AL.bitwise_and); tt(one(t2), one(hk), one(cv), AL.add); ts(end(I2, 1), one(t2), 15.0, AL.add)
+            ts(end(rr, 0), one(yi), 3, AL.arith_shift_right, 7, AL.bitwise_and); ts(end(rr, 1), one(yi), 7, AL.bitwise_and); ts(all_(S("R2")), all_(rr), 256.0, AL.mult)
+            parts = [(end, 0), (end, 1)] if LOTS[0] == 1 else [(lambda x, e_, k=1: all_(x, k), 0)]
+            for e_ in range(2): cp(end(S("GI"), e_, 16), IND(S("IT"), end(I2, e_)))
+            for f_, e_ in parts:
+                gi, b = f_(S("GI"), e_, 16), 17 + c + e_; m = cols(gi); p, q = pb(b, 0, m // 16), pb(b, 64, 64 + m // 16); gl = GL if LOTS[0] > 1 else S(("GB", "EQ")[e_], 0, 640)
+                pe([(p, C("ID"), f_(S("R2"), e_))] + [(p, Zs("om", r), sub(gi, r, m, 16)) for r in range(16)]); cp(f_(LUL, e_), p)
+                for a in range(0, m, 16 * w): mv(sub(gl, a, a + 16 * w), IND(S("LUT"), sub(f_(LUL, e_), a // 16, a // 16 + w)))
+                pe([(q, C("I1K"), f_(i2, e_)), (q, C("ID"), f_(t3, e_))] + [(q, Zs("id", r), sub(gi, r, m, 16)) for r in range(16)], True, False)
+                pe([(q, Zs("l17", r), sub(gl, r, m, 16)) for r in range(16)], False, True); ts(f_(OVL, e_), q, -1.0, AL.add)
+            for e_ in range(2): tt(IND(S("OV"), end(OVL, e_)), end(S("GI"), 1 - e_, 16), S("NAM", 16 * w * c, 16 * w * (c + 1)), AL.add)
         if t < 2: ts(S("NAM"), S("NAM"), M8[1], AL.add)
         tag[0] = "new"
-        ext(pb(0, 128, 208), [("id", S("GI"))], 1280)
-        c0 = 136 + 40 * t; um = S("UM", 0, 80)
-        for f_, a, b in hs:
-            tt(f_(u2), f_(pb(0, 128, 208)), vl, AL.mult); tt(f_(um), f_(u2), vl, AL.add)
-        ts(EXL, um, 14.0, AL.add)
-        ts(S("EA", c0, c0 + 40), lo(u2), 15.0, AL.add); ts(S("EB", c0, c0 + 40), hi(u2), 15.0, AL.add)
+        p = pb(0, 128, 208); pe([(p, C("ID"), vl)] + [(p, Zs("id", r), S("GI", r, 1280, 16)) for r in range(16)])
+        for c in range(LOTS[0]):
+            for e_ in range(2): ts(S(("EA", "EB")[e_], c0 + w * c, c0 + w * c + w), sub(p, w * (2 * c + e_), w * (2 * c + e_ + 1)), 14.0, AL.add)
         YY = S("GA", 16 + n, 656 + n)
-        mv(YY, IND(S("P"), lo(EXL))); tt(S("XB"), IND(S("M"), hi(EXL)), YY, AL.add); ts(S("X", 16 + n, 656 + n), S("XB"), 1024.0, AL.mult, 255.0, AL.min)
+        mv(YY, IND(S("P"), S("EA", c0, c0 + 40))); tt(S("XB"), IND(S("M"), S("EB", c0, c0 + 40)), YY, AL.add); ts(S("X", 16 + n, 656 + n), S("XB"), 1024.0, AL.mult, 255.0, AL.min)
         tag[0] = "rows"
+        p = pb(19, 0, 64)
+        pe([(p, C("ID"), N896)] + [(p, C(m % h), S(x, 896 + 64 * h, 960 + 64 * h)) for h in range(2) for m, x in (("FN%d", "RTH"), ("NFN%d", "D2"))], True, False, sub(LUL, 0, 40))
+        pe([(p, Zs("id", 8 * h + l), S("OV", 1024 * l + 896 + 64 * h, 1024 * l + 960 + 64 * h)) for l in range(8) for h in range(2)], False, True)
         for x in range(2 - OVD[0], 2):
-            dma("y", [(T["OVT"][64 * c:64 * c + 64, 1024 * x:1024 * x + 1024], T["OV"][c + 1:128:8, 4096 * x:4096 * x + 4096]) for c in range(2)],
-                [S("OV", 4096 * x, 4096 * x + 4096)], [S("OVT", 1024 * x, 1024 * x + 1024)], 256)
+            dma("y", [(T[("WV", "OVT")[x]][64 * c:64 * c + 64, 0:1024], T["OV"][c + 1:128:8, 4096 * x:4096 * x + 4096]) for c in range(2)],
+                [S("OV", 4096 * x, 4096 * x + 4096)], [S(("WV", "OVT")[x], 0, 1024)], 256)
         for part in (((pb(6, 0, 128), 896, 1024), (pb(6, 128, 256), 0, 128)), ((pb(1, 0, 384), 128, 512),), ((pb(2, 0, 384), 512, 896),)):
-            pe([m for p, a, b in part for m in [(p, C("ID"), S("RTH", a, b)), (p, C("NID"), S("D2", a, b))]], True, False)
+            pe([m for p, a, b in part for m in [(p, C("ID"), S("RTH", a, b)), (p, C("NID"), S("D2", a, b))]], True, False, sub(OVL, 0, 40) if t == 2 and len(part) == 1 else sub(LUL, 0, 40))
             far = OVD[0] if len(part) == 1 or OVD[1] else 0
             pe([(p, sub(C("CV"), 15 - l, 143 - l), S("OV", 1024 * l + a, 1024 * l + b)) for p, a, b in part for l in range(8 - 4 * far)] +
-               [(p, C("MV%d" % x), S("OVT", 1024 * x + a, 1024 * x + b)) for p, a, b in part for x in range(2 - far, 2)], False, True)
+               [(p, C("MV%d" % x), S(("WV", "OVT")[x], a, b)) for p, a, b in part for x in range(2 - far, 2)], False, True)
             for first in (len(part) == 2, len(part) == 1):
                 for p, a, b in part:
                     if first: cp(S("RTH", a, b), p)
-                    else: act(S("FL", a, b), p, AF.Sign)
+                    else: flags(S("FL", a, b), p)
         tag[0] = "mid"
         dma("y", [(T["GAW"][:, :], T["GA"][0:128:16, 16:4112])], [S("GA", 16, 4112)], [S("GAW")], 200)
 
@@ -679,20 +694,19 @@ def program(ops, T, nxt, prv):
 
     def part_c(t):
         tag[0] = "seam"
-        TP, TR, RX = S("TP", 128 * t, 128 * t + 128), S("TR", 64 * t, 64 * t + 64), S("RX", 1024 * (t % 2), 1024 * (t % 2) + 1024)
+        TP, TR, RX = S("TP", 192 * t, 192 * t + 192), S("TR", 128 * t, 128 * t + 128), S("RX", 1024 * (t % 2), 1024 * (t % 2) + 1024)
         H2 = lambda x, s_, w=64: sub(x, w * s_, w * s_ + w)
         rows = lambda s_, ha: S("RTH", base[s_] + 64 * ha, base[s_] + 64 * ha + 64)
-        for s_ in range(2):
-            pe(([] if s_ else [(pb(7, 0, 64), C("ID"), N896)]) + [(pb(7, 64 * s_, 64 * s_ + 64), C("FN%d" % ha), rows(s_, ha)) for ha in range(2)], s_ == 0, s_ == 1)
-        tt(TP, pb(7, 0, 128), A1C, AL.max)
-        send(H2(TP, 0), TR, 3 * t, "nxt", "prv")
-
+        tt(H2(TP, 1), pb(19, 0, 64), A1C, AL.is_gt); tt(H2(TP, 0), pb(19, 0, 64), A1C, AL.max)
+        send(sub(TP, 0, 128), TR, 3 * t, "nxt", "prv")
+        pe([(pb(7, 0, 64), C("FN%d" % ha), rows(1, ha)) for ha in range(2)]); mv(H2(TP, 2), pb(7, 0, 64))
+        flg = (H2(TP, 1), H2(TR, 1)); TR = H2(TR, 0)
         inc = lambda s_: S("INC", 72 * s_ + 1, 72 * s_ + 65)
 
-        def number(s_, far, bk):
-            FLG, INC, TG, p, y = H2(S("FLG"), s_), inc(s_), S("TG", 8 * s_, 8 * s_ + 4), pb(bk, 0, 64), pb(bk, 0, 4)
+        def number(s_, bk):
+            FLG, INC, TG, p, y = flg[s_], inc(s_), S("TG", 8 * s_, 8 * s_ + 4), pb(bk, 0, 64), pb(bk, 0, 4)
             q0 = sub(E["q0"], 64 * s_, 64 * s_ + 4); SW = S("SW", 576 * s_, 576 * s_ + 576); w = sub(SW, 0, 512)
-            tt(FLG, far, H2(A1C, 0), AL.is_gt); pe([(p, C("BLK"), FLG)]); scan(INC, S("ONE", 0, 64), p, 0.0, AL.mult, AL.add)
+            pe([(p, C("BLK"), FLG)]); scan(INC, S("ONE", 0, 64), p, 0.0, AL.mult, AL.add)
             if NUM[t][s_] == "p":
                 ext(pb(13, 0, 4), [("all", FLG)], 64); ts(TG, pb(13, 0, 4), 0.0, AL.is_equal, 1024.0, AL.mult)
                 pe([(y, Yc(0, r), sub(INC, r - 1, 63, 16)) for r in range(16)] + [(y, C("ID"), TG)]); tt(q0, y, DS, AL.min); cp(H2(STL, s_, 4), q0)
@@ -709,21 +723,21 @@ def program(ops, T, nxt, prv):
             if s_: ts(S("Lsh"), w1, 4112.0, AL.min)
             tt(q2, w1, H2(DX, s_, 32), AL.min); cp(H2(SXL, s_, 32), q2)
         tag[0] = "own"
-        number(0, H2(TP, 0), 3); p = pb(3, 64, 128)
-        pe([(p, C("NFE%d" % ha), rows(0, ha)) for ha in range(2)] + [(p, C("LS"), H2(S("FLG"), 0)), (p, C("ID"), inc(0))]); mv(H2(S("NUS"), 0), p, -513.0)
+        number(0, 3); p = pb(3, 64, 128)
+        pe([(p, C("NFE%d" % ha), rows(0, ha)) for ha in range(2)] + [(p, C("LS"), flg[0]), (p, C("ID"), inc(0))]); mv(H2(S("NUS"), 0), p, -513.0)
         names(0, 3); mv(H2(SND, 0, 512), IND(XW, H2(SXL, 0, 32))); send(H2(SND, 0, 512), H2(RX, 1, 512), 3 * t + 1, "nxt", "prv")
         for s_ in range(2):
             fold(pb(3, 0, 64), "FE", "RTH", base[s_], 128); ts(H2(SRL, s_), pb(3, 0, 64), 2063.0, AL.add)
         tag[0] = "seam"
         bl = lambda s, ha: pb(7, 128 * s + 64 * ha, 128 * s + 64 * ha + 64)
-        pe([m for s in range(4) for ha in range(2) for m in [(bl(s, ha), C("NP%d%d" % (s, ha)), H2(TP, 1)), (bl(s, ha), C("NQ%d" % s), rows(1, ha))]], True, False)
+        pe([m for s in range(4) for ha in range(2) for m in [(bl(s, ha), C("NP%d%d" % (s, ha)), H2(TP, 2)), (bl(s, ha), C("NQ%d" % s), rows(1, ha))]], True, False)
         pe([(bl(s, ha), C(("DUP", "DUPE")[ha]), TR) for s in range(4) for ha in range(2)], False, True)
         ts(S("PRS", 512, 1024), pb(7), -0.5, AL.max, 0.5, AL.min)
         pe([(pb(7, 0, 64), C("SH%d" % ha), S("PRS", 512 + 128 * s + 64 * ha, 576 + 128 * s + 64 * ha)) for s in range(4) for ha in range(2)])
         ts(S("WI", 0, 64), pb(7, 0, 64), 32768.0, AL.add); ts(S("WJ", 0, 64), S("WI", 0, 64), 8191, AL.bitwise_and)
         q3 = sub(E["q3"], 0, 64); ts(q3, S("WJ", 0, 64), 1.0 / 8192, AL.mult, -513.5, AL.add)
-        number(1, TR, 6)
-        pe([(pb(7, 0, 64), C("LS"), H2(S("FLG"), 1)), (pb(7, 0, 64), C("ID"), inc(1))]); tt(H2(S("NUS"), 1), pb(7, 0, 64), q3, AL.add)
+        number(1, 6)
+        pe([(pb(7, 0, 64), C("LS"), flg[1]), (pb(7, 0, 64), C("ID"), inc(1))]); tt(H2(S("NUS"), 1), pb(7, 0, 64), q3, AL.add)
         names(1, 6)
         for h in range(2): mv(sub(SND, 512 + 256 * h, 768 + 256 * h), IND(XW, S("Lsh", 16 * h, 16 * h + 16)))
         send(H2(SND, 1, 512), H2(RX, 0, 512), 3 * t + 2, "prv", "nxt")
@@ -735,8 +749,8 @@ def program(ops, T, nxt, prv):
         for s_ in (1, 0):
             a, b, p = 512 * s_, 512 * s_ + 512, pb(7 - s_)
             if CMP[0][t][s_] == "v":
-                pe([(p, C("ID"), sub(RX, a, b))])
-                tt(sub(GT, a, b), p, sub(SND, a, b), AL.is_lt); tt(sub(MN, a, b), p, sub(SND, a, b), AL.min)
+                pe([(p, C("ID"), sub(SND, a, b))])
+                tt(sub(GT, a, b), p, sub(RX, a, b), AL.is_gt); tt(sub(MN, a, b), p, sub(RX, a, b), AL.min)
             else:
                 pe([(p, C("ID"), sub(SND, a, b)), (p, C("NID"), sub(RX, a, b))]); act(sub(MN, a, b), p, AF.Relu); ts(sub(GT, a, b), sub(MN, a, b), 0.0, AL.is_gt)
                 pe([(p, C("ID"), sub(SND, a, b)), (p, C("NID"), sub(MN, a, b))]); mv(sub(MN, a, b), p)
@@ -958,6 +972,15 @@ def ties(ops):
     return {k: sorted(set(x[0] for x in l)) for k, l in last.items() if k.startswith("pb")}
 
 
+def later(ops, res):
+    n = len(ops); res = list(res); due = [1e18] * n
+    for i in sorted(range(n), key=lambda i: (-res[i][0], -i)):
+        a, b, q = res[i]
+        if q == "p" and b + ROOM[2] < due[i] < 1e17: res[i] = (a + due[i] - b - ROOM[2], due[i] - ROOM[2], q)
+        for j in ops[i]["deps"] | ops[i]["order"]: due[j] = min(due[j], res[i][0] - LAT)
+    return res
+
+
 def banks(ops, res, rng):
     n = len(ops); use = {}
     for i in sorted(range(n), key=lambda i: (res[i][0], i)):
@@ -977,7 +1000,7 @@ def banks(ops, res, rng):
     rows = [[] for _ in range(8)]; end = [-1e9] * 8
     for t, l in sorted(use.items(), key=lambda x: res[x[1][0]][0]):
         a = res[l[0]][0]; other = set(x for i in l for x in ops[i]["tile"].values()) - {t}
-        rank = sorted(range(8), key=lambda b: (0, rng.rand() * ROOM[1] - end[b]) if end[b] + ROOM[0] <= a else (1, end[b]))
+        rank = sorted(range(8), key=lambda b: rng.rand() * ROOM[1] + end[b])
         for b in rank:
             if rows[b] and (rows[b][-1] in other or reaches(l, set(use[rows[b][-1]]))): continue
             break
@@ -1014,7 +1037,7 @@ def seat(ops, rows, res):
     return out
 
 
-def search(ops, rng, passes, steps, given=None):
+def search(ops, rng, passes, rounds, steps, given=None):
     n = len(ops); succ = [[] for _ in ops]
     for i, o in enumerate(ops):
         for j in o["deps"] | o["order"]: succ[j].append(i)
@@ -1022,91 +1045,181 @@ def search(ops, rng, passes, steps, given=None):
     for i in range(n - 1, -1, -1):
         pri[i] = ops[i]["cost"] + ops[i].get("dma", 0) + LAT + max([pri[k] for k in succ[i]] or [0.0])
     fw = [[(j, LAT + ops[j].get("dma", 0)) for j in o["deps"]] + [(j, ops[j].get("dma", 0)) for j in o["order"]] for o in ops]
-    bw = [[] for _ in ops]; pen = [PEN[0]] * n
+    anc = [0] * n; pre = []; post = [[] for _ in ops]; late = [o.get("dma", 0.0) for o in ops]
     for i in range(n):
-        for j, lag in fw[i]: bw[j].append((i, lag))
+        cover = 0
+        for j, _ in fw[i]: cover |= anc[j]
+        pre.append([(j, lag) for j, lag in fw[i] if late[j] or not cover >> j & 1])
+        for j, _ in fw[i]: anc[i] |= anc[j] | 1 << j
+        for j, lag in pre[i]: post[j].append((i, lag))
+    qs = [o["q"] for o in ops]; cv = [o["cost"] for o in ops]; cs = [o.get("cs", o["cost"]) for o in ops]; kind = [o["kind"] for o in ops]
+    hard = [[j for j, _ in pre[i] if j in ops[i]["deps"]] for i in range(n)]; soft = [[j for j, _ in pre[i] if j not in ops[i]["deps"]] for i in range(n)]
+    flex = [i for i in range(n) if len(qs[i]) == 2]; tags = {}
+    for i, o in enumerate(ops): tags.setdefault(o["tag"], []).append(i)
+    keep = lambda r: [-99.0 if q == "v" else 99.0 for q in r[2]]
+    span = lambda r: max(e + l for e, l in zip(r[1], late))
 
-    def place(order, pre, back):
-        busy = {q: [] for q in "vspgyx"}; res = [None] * n
+    def place(order, need, back, pen):
+        S_ = {q: [] for q in "vspgy"}; E_ = {q: [] for q in "vspgy"}; st_ = [0.0] * n; en = [0.0] * n; pk = [""] * n
         for i in order:
-            o = ops[i]; best = None
-            rdy = max([res[j][1] + lag for j, lag in pre[i]] + [o.get("dma", 0.0) if back else 0.0])
-            for q in o["q"]:
-                c = o.get("cs", o["cost"]) if q == "s" else o["cost"]
-                st, l = rdy, busy[q]
-                lo, hi = 0, len(l)
+            rdy = late[i] if back else 0.0
+            for j, lag in need[i]:
+                if en[j] + lag > rdy: rdy = en[j] + lag
+            best = None
+            for q in qs[i]:
+                if q == "x":
+                    best = (0, q, rdy, cv[i], 0); break
+                c = cs[i] if q == "s" else cv[i]; s, e = S_[q], E_[q]; st = rdy; lo = 0; m = hi = len(s)
+                if m and e[-1] <= st: lo = m
                 while lo < hi:
                     mid = (lo + hi) // 2
-                    if l[mid][1] <= st: lo = mid + 1
+                    if e[mid] <= st: lo = mid + 1
                     else: hi = mid
-                while q != "x" and lo < len(l) and l[lo][0] < st + c:
-                    st = max(st, l[lo][1]); lo += 1
+                while lo < m and s[lo] < st + c:
+                    if e[lo] > st: st = e[lo]
+                    lo += 1
                 key = st + c + (pen[i] * c + PEN[1] if q == "v" else 0.0)
                 if best is None or key < best[0]: best = (key, q, st, c, lo)
             _, q, st, c, lo = best
-            if q != "x": busy[q].insert(lo, (st, st + c))
-            res[i] = (st, st + c, q)
-        return res
-    if passes or given:
-        def start(bias):
-            key = [-pri[i] - bias.get(ops[i]["tag"], 0.0) for i in range(n)]
-            for i in range(n - 1, -1, -1):
-                for j, _ in fw[i]:
-                    if key[j] >= key[i]: key[j] = key[i] - 0.001
-            res = place(sorted(range(n), key=lambda i: (key[i], i)), fw, False)
-            rb = place(sorted(range(n), key=lambda i: (-res[i][1], -i)), bw, True)
-            return res, place(sorted(range(n), key=lambda i: (-rb[i][1], i)), fw, False)
-        hard = [list(o["deps"]) for o in ops]; soft = [list(o["order"]) for o in ops]; late = [o.get("dma", 0.0) for o in ops]
+            if q != "x": S_[q].insert(lo, st); E_[q].insert(lo, st + c)
+            st_[i] = st; en[i] = st + c; pk[i] = q
+        return st_, en, pk
 
-        def score(res):
-            sq = sorted(range(n), key=lambda i: (res[i][0], i)); tot = 0.0
-            for fac, lat, wt in GUESS:
-                free = {}; en_ = [0.0] * n
-                for i in sq:
-                    q = res[i][2]; st = 0.0 if q == "x" else free.get(q, 0.0)
-                    for j in hard[i]:
-                        if en_[j] + lat > st: st = en_[j] + lat
-                    for j in soft[i]:
-                        if en_[j] > st: st = en_[j]
-                    st += (res[i][1] - res[i][0]) * fac[ops[i]["kind"]]; free[q] = st; en_[i] = st + late[i] * fac["x"]
-                tot += wt * max(en_)
-            return tot
+    def both(r, pen):
+        rb = place(sorted(range(n), key=lambda i: (-r[1][i], -i)), post, True, pen)
+        r2 = place(sorted(range(n), key=lambda i: (-rb[1][i], i)), pre, False, pen)
+        return r2 if span(r2) <= span(r) else r
 
-        def shake():
-            if given:
-                pen[:] = [-99.0 if r[2] == "v" else 99.0 for r in given]; res = place(range(n), fw, False)
+    def score(r):
+        sq = sorted(range(n), key=lambda i: (r[0][i], i)); tot = OWN[0] * span(r)
+        for fac, lat, wt in GUESS:
+            free = {q: 0.0 for q in "vspgyx"}; en_ = [0.0] * n; fx = fac["x"]
+            for i in sq:
+                q = r[2][i]; st = free[q]
+                for j in hard[i]:
+                    if en_[j] + lat > st: st = en_[j] + lat
+                for j in soft[i]:
+                    if en_[j] > st: st = en_[j]
+                st += (r[1][i] - r[0][i]) * fac[kind[i]]; en_[i] = st + late[i] * fx
+                if q != "x": free[q] = st
+            tot += wt * max(en_)
+        return tot / (OWN[0] + sum(x[2] for x in GUESS))
+    if given:
+        cur = place(range(n), pre, False, [-99.0 if r[2] == "v" else 99.0 for r in given])
+    else:
+        key = [-pri[i] - BIAS.get(ops[i]["tag"], 0.0) for i in range(n)]; pen = [PEN[0]] * n
+        for i in range(n - 1, -1, -1):
+            for j, _ in pre[i]:
+                if key[j] >= key[i]: key[j] = key[i] - 0.001
+        cur = both(both(place(sorted(range(n), key=lambda i: (key[i], i)), pre, False, pen), pen), pen)
+    sc_ = score(cur); top = (sc_, cur)
+    for it in range(passes):
+        key = np.array(cur[0]); pen = keep(cur); near = np.abs(key - rng.uniform(0, span(cur))) < rng.choice([3000.0, 8000.0, 20000.0])
+        m = rng.randint(4) if near.any() else 0
+        if m == 0: key = key + near * rng.normal(0, rng.choice([200.0, 600.0, 1500.0]), n)
+        elif m == 1:
+            idx = np.array(tags[ops[rng.choice(np.flatnonzero(near))]["tag"]]); key[idx[near[idx]]] += rng.normal(0, 3000.0)
+        else:
+            for i in flex:
+                if near[i] and m == 2: pen[i] = 0.5 * rng.randint(4)
+                elif near[i] and rng.rand() < 0.1: pen[i] = -pen[i]
+        key = key.tolist()
+        for i in range(n):
+            for j, _ in pre[i]:
+                if key[j] >= key[i]: key[i] = key[j] + 0.001
+        r = place(sorted(range(n), key=lambda i: key[i]), pre, False, pen)
+        if it % 3 == 0: r = both(r, keep(r))
+        bar = sc_ - TEMP[0] * (1.0 - it / passes) * np.log(rng.rand() + 1e-12)
+        if span(r) > span(cur) + 3000.0: continue
+        s = score(r)
+        if s < bar:
+            cur, sc_ = r, s
+            if s < top[0]: top = (s, r)
+    res = polish(ops, fw, list(zip(*stretches(ops, pre, post, top[1], rng, rounds))), rng, steps)
+    return res, score(list(zip(*res)))
+
+
+def stretches(ops, pre, post, res, rng, rounds):
+    n = len(ops); late = [o.get("dma", 0.0) for o in ops]; cv = [o["cost"] for o in ops]; cs = [o.get("cs", o["cost"]) for o in ops]
+    st, en, pk = list(res[0]), list(res[1]), list(res[2]); seq = list(range(n)); lo = 0
+    for rd in range(rounds):
+        seq.sort(key=lambda i: (st[i], i))
+        w = (120, 200, 300)[rng.randint(3)]; lo = (lo + w // 3 + rng.randint(w // 3)) % (n - w // 2); hi = min(n, lo + w)
+        tail = [0.0] * n; after = {q: 0.0 for q in "vspgyx"}; free = dict(after)
+        for i in seq[:hi - 1:-1]:
+            t = max([late[i], after[pk[i]] if pk[i] != "x" else 0.0] + [lag + tail[k] for k, lag in post[i]])
+            tail[i] = after[pk[i]] = t + en[i] - st[i]
+        for i in seq[:lo]: free[pk[i]] = en[i]
+        win = seq[lo:hi]; loc = {i: k for k, i in enumerate(win)}; m = len(win)
+        lp = [[(loc[j], lag) for j, lag in pre[i] if j in loc] for i in win]; ls = [[(loc[j], lag) for j, lag in post[i] if j in loc] for i in win]
+        head = [max([0.0] + [en[j] + lag for j, lag in pre[i] if j not in loc]) for i in win]
+        out = [max([late[i]] + [lag + tail[j] for j, lag in post[i] if j not in loc]) for i in win]
+        wq = [ops[i]["q"] for i in win]; wv = [cv[i] for i in win]; ws = [cs[i] for i in win]; flex = [k for k in range(m) if len(wq[k]) == 2]
+
+        def place(order, pen):
+            S_ = {q: [] for q in "vspgy"}; E_ = {q: [] for q in "vspgy"}; a = [0.0] * m; b = [0.0] * m; p = [""] * m; worst = tot = 0.0
+            for k in order:
+                rdy = head[k]
+                for j, lag in lp[k]:
+                    if b[j] + lag > rdy: rdy = b[j] + lag
+                best = None
+                for q in wq[k]:
+                    if q == "x":
+                        best = (0, q, rdy, wv[k], 0); break
+                    c = ws[k] if q == "s" else wv[k]; s, e = S_[q], E_[q]; t = rdy if rdy > free[q] else free[q]; x = y = len(s)
+                    while x and e[x - 1] > t: x -= 1
+                    while x < y and s[x] < t + c:
+                        if e[x] > t: t = e[x]
+                        x += 1
+                    key = t + c + (pen[k] if q == "v" else 0.0)
+                    if best is None or key < best[0]: best = (key, q, t, c, x)
+                _, q, t, c, x = best
+                if q != "x": S_[q].insert(x, t); E_[q].insert(x, t + c)
+                a[k] = t; b[k] = t + c; p[k] = q
+                if t + c + out[k] > worst: worst = t + c + out[k]
+            for q in E_:
+                if E_[q]: tot += E_[q][-1] + after[q]; worst = max(worst, E_[q][-1] + after[q])
+            return worst + 0.01 * tot, a, b, p
+        keep = lambda p: [-1e9 if q == "v" else 1e9 for q in p]
+        top = cur = place(range(m), keep([pk[i] for i in win]))
+        for it in range(TRIES[0]):
+            key = np.array(cur[1]); pen = keep(cur[3]); u = rng.randint(5); near = np.abs(key - key[rng.randint(m)]) < (1000.0, 2500.0, 6000.0)[rng.randint(3)]
+            if u < 2: key = key + near * rng.normal(0, (150.0, 400.0, 1000.0)[rng.randint(3)], m)
+            elif u == 2:
+                pr = [0.0] * m
+                for k in sorted(range(m), key=lambda k: -cur[1][k]): pr[k] = max([out[k]] + [lag + pr[j] for j, lag in ls[k]]) + cur[2][k] - cur[1][k]
+                pr = -np.array(pr); f = rng.rand(); key = np.where(near, key * (1 - f) + f * (pr - np.mean((pr - key)[near])) + rng.normal(0, 100.0, m), key)
             else:
-                res = min(start(BIAS), key=score)
-            top = (score(res), res); cur = None
-            for it in range(passes):
-                sc_ = score(res)
-                if sc_ < top[0]: top = (sc_, res)
-                if cur is None or sc_ < cur[0] + TEMP[0] * (1.0 - it / passes): cur = (sc_, res, list(pen))
-                key = [cur[1][i][0] for i in range(n)]; pen[:] = cur[2]
-                c0 = rng.uniform(0, max(key)); wd = rng.choice([5000.0, 15000.0, 30000.0]); nz = rng.normal(0, rng.choice([300.0, 1000.0, 2500.0]), n)
-                flip = rng.uniform(0, 1, n) < rng.choice([0.0, 0.1])
-                for i in range(n):
-                    if it and abs(key[i] - c0) < wd:
-                        key[i] += nz[i]
-                        if flip[i]: pen[i] = 3.0 if cur[1][i][2] == "v" else -1.0
-                    for j, _ in fw[i]:
-                        if key[j] >= key[i]: key[i] = key[j] + 0.001
-                res = place(sorted(range(n), key=lambda i: (key[i], i)), fw, False)
-                if it % 2 == 0:
-                    rb = place(sorted(range(n), key=lambda i: (-res[i][1], -i)), bw, True)
-                    res = place(sorted(range(n), key=lambda i: (-rb[i][1], i)), fw, False)
-            return top[1]
-        res = polish(ops, fw, shake(), rng, steps)
-        return res, score(res)
+                for k in flex:
+                    if near[k] and u == 3: pen[k] = (0.0, 200.0, 600.0)[rng.randint(3)]
+                    elif near[k] and rng.rand() < 0.2: pen[k] = -pen[k]
+            key = key.tolist()
+            for k in range(m):
+                for j, _ in lp[k]:
+                    if key[j] >= key[k]: key[k] = key[j] + 0.001
+            r = place(sorted(range(m), key=lambda k: key[k]), pen)
+            if r[0] < cur[0] - TRIES[1] * (1 - it / TRIES[0]) * np.log(rng.rand() + 1e-12):
+                cur = r
+                if r[0] < top[0]: top = r
+        for k, i in enumerate(win): st[i], en[i], pk[i] = top[1][k], top[2][k], top[3][k]
+        win.sort(key=lambda i: (st[i], i)); seq[lo:hi] = win; free = {}
+        for i in seq:
+            s = max([free.get(pk[i], 0.0) if pk[i] != "x" else 0.0] + [en[j] + lag for j, lag in pre[i]])
+            st[i] = s; en[i] = free[pk[i]] = s + (cs[i] if pk[i] == "s" else cv[i])
+    return st, en, pk
 
 
 def emit(ops, g, T):
     n = len(ops); tiles(ops); base = list(ops)
     if n not in PLAN:
-        rng = np.random.RandomState(SEED[0]); ties(ops); res = search(ops, rng, PASSES[0], STEPS[0])[0]; best = None
-        for passes, steps in AGAIN:
-            ties(base); rows = banks(base, res, rng); out = seat(base, rows, res)
-            new, sc_ = search([base[i] for i in out], rng, passes, steps, [res[i] for i in out])
+        rng = np.random.RandomState(SEED[0]); ties(ops); res = search(ops, rng, *PASSES)[0]; best = None
+        for how in AGAIN:
+            ties(base); res = later(base, res); tried = []
+            for _ in range(SEATS[0]):
+                ties(base); rows = banks(base, res, rng); out = seat(base, rows, res)
+                tried.append((search([base[i] for i in out], rng, 0, 0, 0, [res[i] for i in out])[1], rows))
+            rows = min(tried, key=lambda x: x[0])[1]; out = seat(base, rows, res)
+            new, sc_ = search([base[i] for i in out], rng, *how, [res[i] for i in out])
             if best is None or sc_ < best[0]: best = (sc_, rows, res, new)
             INFO.append((round(sc_), round(max(r[1] for r in res)), round(max(r[1] for r in new))))
             res = [None] * n

@@ -1,5 +1,4 @@
 import numpy as np
-from concourse.bass import DstId, RemoteDMATransfer
 from concourse.mybir import AluOpType as AL, ActivationFunctionType as AF
 
 F, H, B, I, U = "float32", "float16", "bfloat16", "int32", "uint16"
@@ -7,50 +6,45 @@ SB = {
     "RAW": (2048, I), "X": (5152, B), "RT": (1056, F), "RTH": (1024, H), "TA": (1024, F), "TB": (1024, F), "FL": (1024, B), "FLS": (256, B),
     "G1": (6800, B), "LN": (512, U), "KT": (1040, B), "CT": (1040, B), "IT": (1040, B), "GR": (1024, F), "HE": (2048, B),
     "P": (1040, F), "M": (1040, F), "GA": (7584, F), "OV": (9472, B), "EQ": (1024, B), "D2": (1024, H), "GB": (1024, B),
-    "GC": (1024, B), "XS": (1024, B), "IDB": (1024, B), "R1": (1024, B), "RA": (1024, B), "RB": (1024, B), "J16": (512, B), "FT": (512, B), "HW": (128, F), "LO": (1024, B), "HI": (1024, B), "IO": (1056, F),
+    "GC": (1024, B), "XS": (1024, B), "IDB": (1024, B), "R1": (1024, B), "RA": (1024, B), "RB": (1024, B), "J16": (512, B), "FT": (512, B), "HW": (128, F), "IO": (1056, F),
     "IOB": (128, B), "ALL": (2048, B), "Y": (2304, B), "Z": (144 * 16, B), "CM": (128 * 68, B), "ONE": (1024, B), "RST": (512, B),
     "LUT": (2048, B), "EA": (256, U), "EB": (256, U), "ENC": (256, F), "GAW": (256, F), "WN": (3456, H), "ZZ": (1024, F), "ZF": (272, F), "WV": (1040, B),
     "SF": (2432, F), "SI": (1024, I), "SH": (960, B), "SU": (400, U), "S16": (512, H), "W5": (512, F), "W6": (512, F), "WI": (512, I), "WJ": (512, I),
     "WB": (512, B), "R": (512, B), "PR": (512, B), "SV": (512, B), "INW": (272, H), "NT": (512, F), "WW": (1168, F), "CW": (640, H),
     "YC": (640, H), "GI": (1280, B), "G0": (128, H), "XB": (640, B), "RKW": (80, B), "QS": (512, B), "QR": (256, B),
     "TP": (576, B), "TR": (384, B), "EQS": (1024, B), "PRS": (1024, H), "NUS": (128, F), "INC": (144, H), "TG": (144, H),
-    "SW": (1152, B), "SC": (1024, B), "OH": (1024, B), "NE": (1024, H), "SND": (3072, B), "RX": (2048, B), "OVT": (1024, B), "COL": (24, F), "COI": (16, I), "ZER": (1024, B),
+    "SW": (1152, B), "SC": (1024, B), "OH": (1024, B), "NE": (1024, H), "SND": (3072, B), "RX": (2048, B), "OVT": (1024, B), "COL": (32, F), "COI": (16, I), "ZER": (1024, B),
 }
-LISTS = {"a": 64, "hx": 4, "sp": 64, "go": 8, "u": 64, "cs": 32, "cw": 40, "i2": 80, "ex": 80, "lu": 80, "ov": 80, "st": 8, "sc": 64, "sx": 64, "sr": 128, "gq": 4, "q": 8}
+LISTS = {"a": 64, "hx": 4, "sp": 64, "go": 8, "u": 64, "cs": 32, "cw": 40, "i2": 80, "lu": 80, "ov": 80, "st": 8, "sc": 64, "sx": 64, "sr": 128, "q": 8}
 SB["Lsh"] = (32, U)
 for _k, _n in LISTS.items():
     SB["L" + _k] = (_n, U)
 SB.update({"SRG": (2048, B), "KP": (256, B), "SM": (3072, B), "SND": (1024, B), "O0": (128, I), "NAM": (640, B), "ZB": (1024, B), "R2": (80, B), "UM": (160, B)})
 ALIAS = {"WI": ("RAW", 1024), "WJ": ("RAW", 1536), "SI": ("RAW", 0), "TA": ("P", 16), "TB": ("GA", 6560), "ZZ": ("GA", 6560), "WW": ("GA", 5392), "GC": ("GB", 0), "EQS": ("SM", 0), "OH": ("SM", 1024),
          "SC": ("SM", 2048), "NE": ("PRS", 0), "NT": ("W5", 0),
-         "LO": ("EQ", 0), "HI": ("XS", 0), "ZB": ("SRG", 0), "HE": ("G1", 2560), "WB": ("G1", 4752), "R": ("G1", 5264), "PR": ("G1", 5776), "SV": ("G1", 6288)}
+         "ZB": ("SRG", 0), "HE": ("G1", 2560), "WB": ("G1", 4752), "R": ("G1", 5264), "PR": ("G1", 5776), "SV": ("G1", 6288)}
 SCRATCH = {k: ("sbuf", [128, n], d) for k, (n, d) in SB.items() if k not in ALIAS}
 for _b in range(8):
     SCRATCH["pb%d" % _b] = ("psum", [128, 512], F)
 ND = 40
 SEMAPHORES = ["cv", "cs", "cp", "cg"] + ["o%d" % i for i in range(9)] + ["d%d" % i for i in range(ND)] + ["a%d" % i for i in range(9)]
 SIZE = {F: 4, H: 2, B: 2, I: 4, U: 2}
-FIX = [20.0]
-CYC, PEC, LAT = 0.84, 0.39, 170.0
+CYC, PEC, LAT, FIX = 0.84, 0.39, 180.0, [12.0]
 PEN = [1.0, 50.0]
-EDGE = [2, 2, 2]
-SGN = ["ss", "ss", "ss"]
-EQS, CMP, ABS = ["ss", "ss", "ss"], [["vv", "vv", "vv"]], [""]
-DMA, ZOV = [1500.0, 300.0], [1]
-XF, XSE = [1.25, 1.2], [1]
-POP, OVD = [1], [1, 0]
-MBK, STEPS, NEAR, JIT = [4], [6000], [3], [10.0]
-MARK, CUT, HOPW, EDW = [0, 0, 0], [1024], [512], [512]
-SPK = [1, 1, 1]
+EDGE = [1, 1, 99]
+DMA, XF = [1300.0, 300.0], [1.0]
+OVD = [2, 0]
+NEAR, JIT = [3], [10.0]
+CUT, EDW = [1100], [448]
 WIN = [200, 300]
-NUM = ["pp", "pp", "pp"]
+NUM = "vp"
 BLOCKS = [(j, s) for s in range(4) for j in range(2 * s + 1)]
 PLACE = {(j, k): 8 * j + k for j in range(2) for k in range(j + 1, 8)}
-LOTS = [1]
 PLACE.update({jk: d + 1 for d, jk in enumerate((j, k) for j in range(2, 8) for k in range(j + 1, 8))})
-PASSES, PLAN, SEED, TEMP, OWN, TRIES = [600, 70, 4000], {}, [11], [250.0], [2.0], [120, 60.0]
-SEATS = [12]
-AGAIN, ROOM = [(0, 90, 6000)], [200.0, 1500.0, 300.0]
+LOTS = [1]
+PASSES, AGAIN = [1400, 130, 5000], [(0, 300, 9000)]
+PLAN, SEED, TEMP, OWN, TRIES = {}, [52], [250.0], [2.0], [120, 90.0]
+SEATS, ROOM = [12], [1500.0, 300.0]
 GUESS = [({"o": 1, "g": 0.78, "s": 0.6, "p": 1.05, "x": 0.9}, 200.0, 1.0), ({"o": 1.1, "g": 1.3, "s": 1.6, "p": 1.0, "x": 1.1}, 130.0, 1.0)]
 BIAS = {"ends0": 10000.0}
 GAT, SCA = 1.56, 3.2
@@ -275,7 +269,7 @@ def program(ops, T, nxt, prv):
     dma("s", [(RAW[16 * g:16 * g + 16, 1536:2048], en[16 * (g ^ 1):16 * (g ^ 1) + 16, :]) for g in range(8)], [], [S("RAW", 1536, 2048)], 512)
     dma("y", [(T["X"][:, 16:2192], T["lens"][:, :])], [S("RAW")], [S("X", 16, 2192)], 544)
     RC, HQ, M3, NTB, A64 = [S("COL", i, i + 1) for i in range(5)]
-    M8 = [S("COL", 8 + t, 9 + t) for t in range(3)]
+    M8, M9 = [S("COL", c, c + 1) for c in (3, 8, 9)], [S("COL", 24 + t, 25 + t) for t in range(3)]
     ONE = S("ONE", 0, 128)
     ms(S("ONE", 0, 512), 1.0); ms(S("ZER"), 0.0); mv(S("ONE", 512, 1024), S("ONE", 0, 512))
     o0 = S("O0", 0, 64); iota(o0, [[2, 32], [1024, 2]], 0, 64)
@@ -288,12 +282,14 @@ def program(ops, T, nxt, prv):
     ts(S("COI", 1, 2), S("COI", 0, 1), 15, AL.bitwise_and); cp(RC, S("COI", 1, 2))
     ts(S("COI", 2, 3), S("COI", 0, 1), 4, AL.arith_shift_right, 1, AL.bitwise_and); cp(HQ, S("COI", 2, 3))
     ts(S("COI", 3, 4), S("COI", 0, 1), 8, AL.bitwise_and); ts(A64, S("COI", 3, 4), 8.0, AL.mult)
-    ts(NTB, RC, 64.0, AL.mult, float(1015 - 2 ** 23 - 2048), AL.add)
-    for t in range(2): ts(M8[t], RC, 10.0, AL.is_equal, (4.0, 20.0)[t], AL.mult)
+    for t in range(3): ts(M8[t], RC, 10.0, AL.is_equal, 4.0 + 20.0 * t, AL.mult)
     o1 = S("O0", 64, 128); ts(o1, o0, 2047, AL.bitwise_and); o2 = su(64); ts(o2, o1, HQ, AL.add)
 
     def aff(name, c0, al, be, src=ONE):
         asel(C(name), src, [[-16, 8], [-al, 2], [-be, 8]], AL.is_equal, 0, -c0)
+
+    def affw(name, c0, al, be, w):
+        asel(C(name), S("ZER", 0, 128), [[-16, 8], [-al, 2], [-be, 8]], AL.not_equal, w, -c0)
 
     def poke(x, ch, w):
         asel(x, x, [[-16, 8]], AL.not_equal, w, -ch)
@@ -313,13 +309,12 @@ def program(ops, T, nxt, prv):
     B8c = sub(C("BLK"), 0, 128, 16)
     asel(Zs("lo8"), B8c, [[16, 8]], AL.is_ge, 0, 7, -1)
     zmake("key", [(0, 2048 * 256), (1, 256), (2, 32 * 256)])
-    V1, VW, DGO, A1C, JG, V256 = sf(64), S("W5"), sf(64), sf(64), sf(8), sf(64)
-    iota(V1, [[1, 64]], 1); ts(V1, V1, NTB, AL.add, float(-(1015 - 2 ** 23 - 2048)), AL.add)
-    INEL = sh(64); ts(V256, V1, 256.0, AL.mult, -256.0, AL.add)
+    DGO, A1C, INEL = sf(64), sf(64), sh(64)
     HLF = S("COL", 10, 11); ts(HLF, RC, 1.0, AL.is_equal, 0.5, AL.mult)
     t0 = sf(8)
+    for t in range(3): ts(M9[t], M8[t], HLF, AL.add)
     for k in range(8): ms(S("RST", k, 512, 8), -float(2 ** (k - 1)) if k else 1.0e8)
-    for n, c in (("KT", 16.0), ("CT", 0.0), ("IT", 0.0), ("RT", 0.0), ("X", 0.0), ("INW", 0.0), ("GA", 0.0)):
+    for n, c in (("KT", 16.0), ("CT", 0.0), ("IT", 0.0), ("RT", 0.0), ("X", 0.0), ("INW", 0.0)):
         ms(S(n, 0, 16), c)
     ts(S("KT", 15, 16), M0, 31.0, AL.mult); ts(M3, HLF, -1.0, AL.mult)
     ts(C("NE2K"), C("FN1"), -2048.0, AL.mult)
@@ -356,7 +351,8 @@ def program(ops, T, nxt, prv):
     ts(S("CT", 15, 16), M0, 1000.0, AL.mult)
     tag[0] = "ends"
     ms(S("ZF"), 0.0)
-    for a in range(0, 2176, 272): mv(S("GA", a, a + 272), S("ZF"))
+    mv(S("GR", 0, 272), S("ZF")); mv(S("GR", 272, 544), S("ZF"))
+    dma("y", [(T["GA"][:, a:a + 544], T["GR"][:, 0:544]) for a in range(0, 2176, 544)], [S("GR", 0, 544), S("RAW")], [S("GA", 0, 2176)], 1088)
     dma("y", [(T["GA"][c:128:16, 2176:4352], T["ZF"][:, 0:136]) for c in range(2)], [S("ZF"), S("RAW")], [S("GA", 2176, 4352)], 140)
     tag[0] = ""
     dma("y", [(T["X"][:, a:b], T["ZER"][:, 0:b - a]) for a, b in ((2192, 3216), (3216, 4240), (4240, 5152))], [S("ZER"), S("RAW")], [S("X", 2192, 5152)], 740)
@@ -364,7 +360,7 @@ def program(ops, T, nxt, prv):
 
     def zero_ov(t, when):
         if t: dma("y", [(T["OV"][c:128:8, 0:8192], T["ZER"][:, :]) for c in (1, 2)], [S("ZER"), when], [S("OV", 0, 8192)], 512)
-        else: dma("y", [(T["OV"][:, 1024 * k:1024 * k + 1024], T["ZER"][:, :]) for k in range(8)], [S("ZER"), when], [S("OV", 0, 8192)], 2048)
+        else: dma("y", [(T["OV"][:, a:min(a + 1920, 8192)], T["X"][:, 2192:2192 + min(1920, 8192 - a)]) for a in range(0, 8192, 1920)], [S("X", 2192, 4112), when], [S("OV", 0, 8192)], 2048)
 
     def ends():
         tag[0] = "ends"
@@ -385,8 +381,8 @@ def program(ops, T, nxt, prv):
             pe([(p, C("LS8"), sub(f, a, b)), (p, C("I4K"), S("RTH", a, b))] + [(sub(p, r, 512, 16), Al(r), sub(st, 32 * h, 32 * h + 32)) for r in range(16)])
             mv(sub(TT, a, b), p, 576.0)
             put(IND(S("GA", 0, 5376), sub(SL, 32 * h, 32 * h + 32)), S("IO", 32 + a, 32 + b))
-        for i, a in enumerate(range(0, 2176, 512)):
-            b = min(2176, a + 512); c, d = a // 16, b // 16; p = pb(14, 0, d - c)
+        for i, (a, b) in enumerate(((0, 1024), (1024, 2176))):
+            c, d = a // 16, b // 16; p = pb(14, 0, d - c)
             scan(S("WN", a, b), S("GA", a, b), S("GA", a, b), sub(ex, 66 + i, 67 + i) if a else 0.0, AL.max, AL.max)
             if b < 2176: cp(sub(ex, 67 + i, 68 + i), S("WN", b - 1, b))
             ext(p, [("c0", S("WN", a, b))], b - a); ts(sub(CL, c, d), p, -32.0, AL.add, 0.0, AL.max)
@@ -394,9 +390,10 @@ def program(ops, T, nxt, prv):
             c, d = lot[0] // 16, min(136, lot[-1] // 16 + 32); p = pb(16, 0, d - c); part = []
             for a in lot:
                 b = min(2176, a + 512); k = a % 1024; q = pb(15, 0, b - a)
-                y, src = S("PRS", k, k + b - a), S("P", 16 + k, 16 + k + b - a) if a < 2048 else S("W5", 128, 256)
+                y, src = S("CW" if a == 2048 else "PRS", k, k + b - a), S("P", 16 + k, 16 + k + b - a) if a < 2048 else S("W5", 128, 256)
                 tt(y, IND(TT, sub(CL, a // 16, b // 16)), (S("IO", a, b), S("M", a - 1008, b - 1008), S("W5", 0, 128))[a // 1024], AL.subtract); ts(y, y, -0.5, AL.max, 0.5, AL.min)
-                ext(sub(p, a // 16 - c, b // 16 - c), [("e4k", y)], b - a)
+                if k: ext(sub(p, 0, 64), [("e4k", S("PRS"))], 1024)
+                elif a == 2048: ext(sub(p, 64, 72), [("e4k", y)], 128)
                 pe([(q, Zs("l4k", 1), y), (q, Yc(0, 0), S("WN", a, b))]); mv(src, q, AB); part.append((sub(PL, a // 16, b // 16), src))
             w0, w1, w2, x0, x1 = S("WI", 256, 256 + d - c), S("WI", 336, 336 + d - c), S("WI", 416, 416 + d - c), S("W6", 272, 272 + d - c), S("W6", 400, 400 + d - c)
             ts(w0, p, 65535.0, AL.add); ts(w1, w0, 4095, AL.bitwise_and); ts(w2, w1, 4, AL.arith_shift_right)
@@ -410,7 +407,6 @@ def program(ops, T, nxt, prv):
     asel(Zs("en"), B8c, [[-16, 8]], AL.is_ge, 0, -8)
     asel(C("LT"), C("BLK"), [[16, 8], [1, 16]], AL.is_gt, 0, 0, -1)
     iota(DGO, [[16, 64]], 129); ts(DGO, DGO, RC, AL.add)
-    for k in range(8): ms(sub(C("P2"), k, 128, 8), float(2 ** (11 - k)))
     ts(Zs("ha"), Zs("lo8"), -2.0, AL.mult); ts(Zs("ha", None, 16), Zs("en"), -2.0, AL.mult); ts(Zs("hh"), Zs("en"), -2.0, AL.mult)
     asel(C("B8"), ONE, [[-8, 16], [0, 8]], AL.is_ge, 0, 0); asel(C("B8"), C("B8"), [[8, 16], [0, 8]], AL.is_ge, 0, 7, -1)
     asel(C("VM"), ONE, [[0, 8], [-1, 2], [1, 8]], AL.is_gt, 0, 0, 0); aff("EJ0", 0, 1, 0, C("VM")); aff("EK0", 0, 0, 1, C("VM"))
@@ -425,7 +421,7 @@ def program(ops, T, nxt, prv):
         pe([(p, C("EJ%d" % b), C("EJ%d" % b)), (p, C("EK%d" % b), C("EJ%d" % b))]); tt(C("LA%d%d" % (b, b)), p, C("LN"), AL.mult)
         pe([(p, C("EK%d" % b), C("EK%d" % b))]); tt(C("LB%d%d" % (b, b)), p, C("LN"), AL.mult)
         pe([(p, C("EK0"), C(("EJ1", "EK1")[b]))]); ts(C(("LA01", "LB01")[b]), p, -1.0, AL.mult)
-    DB = [S("COL", 12, 13), S("COL", 13, 14)]; ts(C("I8K"), C("ID"), 1.0 / 8192, AL.mult)
+    DB = [S("COL", 12, 13), S("COL", 13, 14)]
     ts(c_(7), M0, 1024.0 + 2057.0 / 8192, AL.mult, -1025.0 - 2057.0 / 8192, AL.add)
     ts(DB[0], RC, 1.0 / 128, AL.mult, c_(7), AL.add); ts(sub(x4, 0, 1), RC, 8.0, AL.mult); mv(sub(x4, 1, 2), RC)
     pe([(pb(7, 0, 1), C("EJ1"), sub(x4, 0, 1)), (pb(7, 0, 1), C("EK1"), sub(x4, 1, 2))]); ts(DB[1], pb(7, 0, 1), 1.0 / 128, AL.mult, c_(7), AL.add)
@@ -434,58 +430,54 @@ def program(ops, T, nxt, prv):
     asel(C("LS8"), C("B8"), [[16, 8], [1, 16]], AL.is_gt, 0, 0, -1); asel(C("LS8"), C("LS8"), [[-1, 128]], AL.not_equal, 512, 0)
     ts(C("I4K"), C("ID"), 1.0 / 4096, AL.mult)
     ts(Zs("e4k"), Zs("en"), 4096.0, AL.mult); ts(Zs("l4k"), Zs("lo8"), 4096.0, AL.mult); DE = sf(64); ts(DE, DGO, 4352.0 - 129, AL.add)
-    ts(C("EN2K"), C("FN1"), 2048.0, AL.mult)
     cp(Zs("all"), B8c); ts(Zs("nall"), B8c, -1.0, AL.mult); ts(Zs("8k"), B8c, 8192.0, AL.mult)
     zmake("om", [(5, 1)]); ts(Zs("l17"), Zs("lo8"), 1024.0, AL.mult); zmake("l17", [(0, 0)])
     CV, KD = C("CV"), C("KD")
     for ch, w, off in ((1, 1, 15), (2, 32, 15), (9, 1, 23), (10, 32, 23)): poke(sub(CV, off, off + 128, 16), ch, w)
     for x in range(2 - OVD[0], 2):
         m = C("MV%d" % x); ms(m, 0.0)
-        for l in range(4 * x, 4 * x + 4): ms(sub(m, l, 128, 8), 1.0)
-        m2 = S("KP", 128 * x, 128 * x + 128); ts(m2, m, 32.0, AL.mult)
-        for c, y in enumerate((m, m2)): asel(y, y, [[-8, 8], [-4, 2], [-1, 8]], AL.is_equal, 0, 4 * x - 64 * c)
-        tt(m, m, m2, AL.add)
-    for off in (15, 23): poke(sub(KD, off, off + 128, 16), 0, 4096)
+        for l in range(4):
+            y = sub(m, 4 * x + l, 128, 8)
+            for c in range(2): asel(y, y, [[-4, 16]], AL.not_equal, 32 ** c, -l - 64 * c)
+    for off in (15, 23): poke(sub(KD, off, off + 128, 16), 0, 32768)
     DW, DOV, DX = sf(32), sf(80), sf(64)
     ts(DW, sub(DGO, 0, 32), 783.0, AL.add); ts(DX, DGO, 3984.0, AL.add)
-    ts(sub(DOV, 0, 64), DGO, -128.0, AL.add); ts(sub(DOV, 64, 80), sub(DGO, 0, 16), 896.0, AL.add)
+    ts(sub(DOV, 0, 64), DGO, -127.0, AL.add); ts(sub(DOV, 64, 80), sub(DGO, 0, 16), 897.0, AL.add)
     AC, QA, QB, C200 = sf(8), sf(8), sh(8), sh(64); ts(AC, sub(DGO, 0, 8), -128.5, AL.add); ms(C200, 200.0); asel(C("LTK"), C("LT"), [[-1, 128]], AL.not_equal, -1000, 0)
     MD = sf(80); w = 40 // LOTS[0]; LOB, HIB = S("COL", 18, 19), S("COL", 11, 12)
     for c in range(2 * LOTS[0]): ts(sub(MD, w * c, w * c + w), sub(DGO, w * (c // 2), w * (c // 2) + w), -129.0, AL.add)
-    ts(LOB, M0, 0.25, AL.mult, -0.25, AL.add); ts(HIB, M0, 15.75, AL.mult, 0.25, AL.add); ts(C("I512"), C("ID"), 512.0, AL.mult); ts(C("I1K"), C("ID"), 1024.0, AL.mult)
+    ts(LOB, M0, 0.25, AL.mult, -0.25, AL.add); ts(HIB, M0, 15.75, AL.mult, 0.25, AL.add)
     ts(c_(5), M0, -12288.0, AL.mult, 8192.0, AL.add); ts(Zs("yk"), B8c, c_(5), AL.mult, flex=False)
     DS = sf(4); ts(DS, sub(DGO, 0, 4), 383.0, AL.add); ts(sub(A1C, 0, 64), S("IO", 0, 64), A64, AL.add, 1.0, AL.add)
     N896 = sh(64); ms(N896, -896.0)
-    for h in range(2): ts(C("NFN%d" % h), C("FN%d" % h), -1.0, AL.mult)
     asel(C("GE8"), C("B8"), [[-16, 8], [-1, 16]], AL.is_ge, 0, 0)
-    pe([(pb(7, 0, 1), C("P2"), S("Y", 15, 16))]); P2C = S("COL", 5, 6); cp(P2C, pb(7, 0, 1))
-    ts(S("WI", 0, 256), S("IO", 0, 256), P2C, AL.mult); ts(S("WJ", 0, 256), S("WI", 0, 256), 2048, AL.bitwise_and)
+    P2C = S("COL", 5, 6); add("v", lambda e: [e["v"].reciprocal(ap(P2C), ap(PWC))], [PWC], [P2C], 200.0)
+    ts(S("WI", 0, 256), S("IO", 0, 256), P2C, AL.mult, 2048.0, AL.mult); ts(S("WJ", 0, 256), S("WI", 0, 256), 2048, AL.bitwise_and)
     ts(S("KP"), S("WJ", 0, 256), 0.0, AL.is_equal); pe([(pb(7, 0, 256), C("GE8"), S("KP"))])
     cp(S("KP"), pb(7, 0, 256))
     for n in range(8): ts(S("LUT", 256 * n, 256 * n + 256), S("KP"), float(n), AL.is_gt)
     aff("FE0", 8, 1000, 1); aff("FE1", 1008, -1000, 1); aff("DUPE", 8, 0, 1)
     for h in range(2):
-        m = 320 * h; pe([(pb(6 + h, 0, 320), Yc(1, 9), S("IDB", m, m + 320)), (pb(6 + h, 0, 320), Yc(2, 10), S("IDB", m, m + 320))]); mv(S("NAM", m, m + 320), pb(6 + h, 0, 320), M8[0])
-    ms(C("NEG"), -1.0); ms(C("K8"), 8192.0)
+        m = 320 * h; pe([(pb(6 + h, 0, 320), Yc(1, 9), S("IDB", m, m + 320)), (pb(6 + h, 0, 320), Yc(2, 10), S("IDB", m, m + 320))]); mv(S("NAM", m, m + 320), pb(6 + h, 0, 320))
     for s_ in range(4):
-        for ha in range(2): aff("NP%d%d" % (s_, ha), 8 * ha + 2 * s_, 1, 0, C("NEG"))
-    ms(C("N13"), 1.0 / 8192)
+        for ha in range(2): affw("NP%d%d" % (s_, ha), 8 * ha + 2 * s_, 1, 0, -1.0)
     for ha, (c0, al) in enumerate(((0, 1000), (1000, -1000))):
-        aff("SH%d" % ha, c0, al, 1, C("K8")); asel(C("SH%d" % ha), C("SH%d" % ha), [[-16, 8], [-al, 2], [-1, 8]], AL.not_equal, 8192, -c0 - 8)
-        aff("NFE%d" % ha, c0 + 8, al, 1, C("N13"))
-    for s_ in range(4): aff("NQ%d" % s_, 8 + 2 * s_, 1, 0, C("N13"))
+        affw("SH%d" % ha, c0, al, 1, 8192.0); asel(C("SH%d" % ha), C("SH%d" % ha), [[-16, 8], [-al, 2], [-1, 8]], AL.not_equal, 8192, -c0 - 8)
+        affw("NFE%d" % ha, c0 + 8, al, 1, 1.0 / 8192); affw("NFN%d" % ha, c0, al, 1, -1.0)
+    for s_ in range(4): affw("NQ%d" % s_, 8 + 2 * s_, 1, 0, 1.0 / 8192)
+    for n, w in (("I512", 512.0), ("I1K", 1024.0), ("I8K", 1.0 / 8192)): affw(n, 0, 8, 1, w)
+    affw("EN2K", 1000, -1000, 1, 2048.0)
 
     OK_, TG1, TG3, LB1, LB2, GG, TG5 = [sf(64) for _ in range(7)]
     MI, AI, BI, HI_, LO_, B0, B1 = [si(64) for _ in range(7)]
     CH, CB, CON, BB, DGB, BG, SD, DEAD = [sh(64) for _ in range(8)]
     INZ = sh(72); ms(DEAD, 0.0); ms(sub(INZ, 0, 1), 0.0); ms(S("INC", 0, 144, 72), 0.0)
-    E = {"nxt": nxt, "prv": prv, "zero_ov": zero_ov, "won": []}
+    E = {"nxt": nxt, "prv": prv, "zero_ov": zero_ov, "won": [], "sign": []}
     for k, w in (("ci", 40), ("c4", 40), ("yi", 40), ("hk", 40), ("rr", 80), ("w0", 64), ("w1", 64)): E[k] = si(w)
     for k in ("c2", "t2"): E[k] = sf(40)
     for k in ("q0", "q3"): E[k] = sf(128)
     LP, LM = [S("S16", 64 * i, 64 * i + 64) for i in (2, 3)]
-    IDR, E2 = S("S16", 256, 384), S("S16", 384, 512)
-    AL_, HXL, SPL, GOL, UL, CSL, CWL, I2, EXL, LUL, OVL, STL, SCL, SXL, SRL, GQL, QL = [S("L" + k) for k in LISTS]
+    AL_, HXL, SPL, GOL, UL, CSL, CWL, I2, LUL, OVL, STL, SCL, SXL, SRL, QL = [S("L" + k) for k in LISTS]
     RTW, XW = S("RT"), S("X")
 
     def fold(out, f, src, a, n, more=None):
@@ -495,8 +487,9 @@ def program(ops, T, nxt, prv):
         tag[:] = ["h", t]
         for h in range(2):
             fold(pb(1, 0, 256), "FN", "RTH", 512 * h, 512); ts(S("LN", 256 * h, 256 * h + 256), pb(1, 0, 256), 15.0, AL.add)
-        extc(pb(2, 0, 64), "c0", S("KT", 16, 1040))
-        ts(pb(2, 0, 64), pb(2, 0, 64), 2048.0 * 256, AL.mult); tt(OK_, pb(2, 0, 64), LIM if t else V256, AL.add)
+        extc(pb(2, 0, 64), "key", S("KT", 16, 1040))
+        if t: tt(OK_, pb(2, 0, 64), LIM, AL.add)
+        else: mv(OK_, pb(2, 0, 64), -128.0)
         ext(pb(2, 0, 64), [("c0", S("KT", 16, 1040))], 1024); mv(DGB, pb(2, 0, 64), 1.0)
         for r in range(16):
             a = 512 * (r % 13); mv(S("G1", a, a + 512), IND(S("KT"), S("LN", 32 * r, 32 * r + 32)))
@@ -518,8 +511,9 @@ def program(ops, T, nxt, prv):
         ts(TG1, B1, 1023.0 / 131072, AL.mult, 1.0, AL.add); lp = pb(11, 128, 192); cp(lp, LO_)
         for h in range(2): ts(pb(11, 64 * h, 64 * h + 64), B0, MC[h], AL.mult, MK[h], AL.add); ts(ft(0, h), HI_, MK[h], AL.mult)
         for h in range(2): tt(ft(1, h), pb(11, 64 * h, 64 * h + 64), TG1, AL.mult)
-        for i in (2, 3):
-            for h in range(2): tt(ft(i, h), lp, ft(i - 1, h), AL.mult)
+        l2 = pb(11, 192, 256); tt(l2, lp, LO_, AL.mult)
+        for i, x in ((2, lp), (3, l2)):
+            for h in range(2): tt(ft(i, h), x, ft(1, h), AL.mult)
         for h in range(2):
             a, b = 512 * h, 512 * h + 512
             pe([(pb(12), ft(0), S("R1", a, b))]); tt(S("GB", a, b), pb(12), S("J16"), AL.is_equal)
@@ -528,7 +522,7 @@ def program(ops, T, nxt, prv):
             pe([(pb(3, 0, 128), S("GB", c, c + 128), S("EQ", c, c + 128)) for c in range(a, b, 128)], h == 0, h == 1)
         mv(S("HW"), pb(3, 0, 128)); tt(B0, IND(S("HW"), HXL), W32, AL.mult); ts(B1, B0, 31, AL.bitwise_and)
         tt(CH, B1, DGB, AL.is_equal)
-        ts(AL_, AI, 16.0, AL.add); ts(BI, MI, 255, AL.bitwise_and); ts(BB, BI, -1.0, AL.mult); ts(SD, BI, 0.0, AL.is_equal)
+        ts(AL_, AI, 16.0, AL.add); ts(BI, MI, 255, AL.bitwise_and); ts(BB, BI, -1.0, AL.mult); ts(SD, BI, 0.0, AL.is_gt, 129.0, AL.mult)
         for h in range(2):
             a, b, p = 512 * h, 512 * h + 512, pb(4 + h)
             pe([(p, C("KS"), S("KT", 16 + a, 16 + b))] + [(blk(4, r), Yc(r, 5), BB) for r in range(8 * h, 8 * h + 8)], True, False)
@@ -544,43 +538,35 @@ def program(ops, T, nxt, prv):
         fold(pb(3, 0, 64), "FN", "G0", 0, 128); ts(UL, pb(3, 0, 64), 15.0, AL.add)
         for h in range(2):
             pe([(pb(4 + h, r, 512, 16), Yc(r, 0), sub(RK, 32 * h, 32 * h + 32)) for r in range(16)], False, True)
-            mv(S("CT", 16 + 512 * h, 528 + 512 * h), pb(4 + h), HLF)
+            mv(S("CT", 16 + 512 * h, 528 + 512 * h), pb(4 + h), M9[t])
         tag[0] = "lab"
         for h in range(2): mv(S("GC", 512 * h, 512 * h + 512), IND(S("CT"), sub(AL_, 32 * h, 32 * h + 32)))
         ext(pb(5, 0, 64), [("c0", S("GC"))], 1024)
-        ts(CB, pb(5, 0, 64), 128.5, AL.is_lt); tt(GG, CB, SD, AL.is_gt); tt(CON, CB, SD, AL.mult)
-        if not SPK[t]: tt(BG, CB, BB, AL.mult)
+        tt(GG, pb(5, 0, 64), SD, AL.is_lt); ts(CB, pb(5, 0, 64), 128.5, AL.is_lt); tt(CON, CB, GG, AL.subtract)
         tt(LP, LB1, GG, AL.mult); tt(LM, LB2, GG, AL.mult); tt(DEAD, DEAD, CON, AL.add)
-        if t < 2: ts(INEL, DEAD, 16.0, AL.mult); ts(TG5, DEAD, -2.0 ** 24, AL.mult); tt(LIM, TG5, V256, AL.add)
-        w2r(1, [(Al, lambda r: BB if SPK[t] else BG)])
+        if t < 2: ts(INEL, DEAD, 16.0, AL.mult); ts(LIM, DEAD, -2.0 ** 24, AL.mult, -128.0, AL.add)
+        w2r(1, [(Al, lambda r: BB)])
         for h in range(2):
-            p = pb(1 + h)
-            if EQS[t][h] == "v": ts(p, p, PWN, AL.is_equal)
-            else: act(p, p, AF.Abs, PWC); act(p, p, AF.Relu, 1.0, -1.0)
+            p = pb(1 + h); ts(p, p, PWN, AL.is_equal)
             tt(S("D2", 512 * h, 512 * h + 512), p, S("RTH", 512 * h, 512 * h + 512), AL.mult)
         extc(pb(1, 0, 64), "en", S("D2")); ts(SPL, pb(1, 0, 64), 2063.0, AL.add)
-        if SPK[t]:
-            if SPK[t] == 2: lengths()
-            w2r(1, [(Al, lambda r: CB)])
-            for h in range(2): tt(S("D2", 512 * h, 512 * h + 512), pb(1 + h), S("D2", 512 * h, 512 * h + 512), AL.mult)
-
-    def lengths():
-        for h in range(2): mv(S("XS", 512 * h, 512 * h + 512), IND(XW, sub(SPL, 32 * h, 32 * h + 32)))
+        w2r(1, [(Al, lambda r: CB)])
+        for h in range(2): tt(S("D2", 512 * h, 512 * h + 512), pb(1 + h), S("D2", 512 * h, 512 * h + 512), AL.mult)
 
     def spokes(t):
         tag[0] = "pm"
-        if SPK[t] < 2: lengths()
-        for b0, tab, lab in ((4, "P", LP), (MBK[0], "M", LM)):
+        for h in range(2): mv(S("XS", 512 * h, 512 * h + 512), IND(XW, sub(SPL, 32 * h, 32 * h + 32)))
+        for b0, tab, lab in ((4, "P", LP), (4, "M", LM)):
             w2r(b0, [(Al, lambda r, lab=lab: lab), (lambda r: C("IDK"), lambda r: S("XS", r, 1024, 16))])
             halves(lambda h, a, b, b0=b0, tab=tab: mv(S(tab, 16 + a, 16 + b), pb(b0 + h), 1000.0))
 
     def part_b(t):
         tag[:] = ["b", t]
-        zero_ov(t, CH if t or ZOV[0] else OK_)
+        zero_ov(t, CH)
         for h, a in enumerate((896, 0) if t else ()):
             p = pb(6 + h, 0, 128)
             pe([(p, C("ID"), S("IDB", a, a + 128))] + [(sub(p, 64 * i, 64 * i + 64), Yc(a // 64 + i, 5), BB) for i in range(2)], True, False)
-            pe([(p, C("FK"), S("FLS", 128 * h, 128 * h + 128))], False, True); mv(S("CT", 16 + a, 144 + a), p)
+            pe([(p, C("FK"), S("FLS", 128 * h, 128 * h + 128))], False, True); mv(S("CT", 16 + a, 144 + a), p, M8[t])
         tag[0] = "edge"
         n = 2176 + 640 * t; nch = -(-n // EDW[0]); w = -(-n // (32 * nch)) * 32
         for i, a in enumerate(range(0, n, w)):
@@ -591,11 +577,14 @@ def program(ops, T, nxt, prv):
             if i % EDGE[t] == 0:
                 act(z, zz, AF.Abs, 0.25, 1024.0); tt(S("WN", a, b), z, x, AL.min); ts(x, S("WN", a, b), 3.0 * 2 ** 22, AL.add, -3.0 * 2 ** 22, AL.add)
                 E["won"].append((t, a, b))
+                if t == 2: E["sign"].append(x)
             else:
                 zb = S("ZB", 512 * k, 512 * k + b - a); act(zb, zz, AF.Abs, 0.0, 1024.0)
-                pe([(z, C("ID"), x), (z, C("NID"), zb)]); act(zb, z, AF.Relu)
+                pe([(z, C("ID"), x), (z, C("NID"), zb)]); relu(zb, z, 1.0, 0.0, (0.0, AL.max))
                 ts(S("WN", a, b), zb, 0.0, AL.is_gt, 0.25, AL.mult)
-                pe([(z, C("ID"), x), (z, C("NID"), zb)]); mv(x, z)
+                pe([(z, C("ID"), x), (z, C("NID"), zb)])
+                if t < 2: mv(x, z)
+                else: act(x, z, AF.Abs)
         tag[0] = "b"
         for h in range(2): ts(S("GR", 512 * h, 512 * h + 512), IND(RTW, sub(UL, 32 * h, 32 * h + 32)), -1.0, AL.mult)
         for h in range(2): mv(S("IT", 16 + 512 * h, 528 + 512 * h), IND(S("CT"), sub(UL, 32 * h, 32 * h + 32)))
@@ -627,9 +616,9 @@ def program(ops, T, nxt, prv):
         scan(S("CW"), S("WV", 0, 640), S("WW", 0, 640), 0.0, AL.max, AL.max)
         ext(pb(3, 0, 40), [("c0", S("CW"))], 640); ts(CWL, pb(3, 0, 40), -32.0, AL.add)
         ci, c4, yi, hk, rr, c2, t2 = [E[k] for k in ("ci", "c4", "yi", "hk", "rr", "c2", "t2")]
-        vl, i2, t3, cv, tot = S("UM", 0, 80), S("UM", 80, 160), S("S16", 0, 80), S("S16", 80, 120), S("COL", 17, 18); w = 40 // LOTS[0]; c0 = 136 + 40 * t
+        vl, i2, t3, cv, tot = S("UM", 0, 80), S("UM", 80, 160), S("S16", 0, 80), S("S16", 80, 120), S("COL", 17, 18); w = 40 // LOTS[0]; c0 = 136 + 40 * t; ids = S("S16", 256, 336)
         ts(tot, S("INW", 271, 272), 0.0, AL.add); ts(vl, MD, tot, AL.is_lt); ts(i2, MD, tot, AL.is_ge); tt(t3, i2, DOV, AL.mult)
-        ts(ci, pb(3, 0, 40), -32.0, AL.add); ts(c4, ci, 254, AL.bitwise_and); ts(sub(c2, 0, 40), c4, 4.0, AL.mult, 1.0, AL.add)
+        ts(ci, pb(3, 0, 40), 0.5, AL.mult, -16.25, AL.add); ts(sub(c2, 0, 40), ci, 8.0, AL.mult, 1.0, AL.add)
         for c in range(LOTS[0]):
             one = lambda x: sub(x, w * c, w * c + w); end = lambda x, e_, k=1: sub(x, k * w * (2 * c + e_), k * w * (2 * c + e_ + 1)); all_ = lambda x, k=1: sub(x, 2 * k * w * c, 2 * k * w * (c + 1))
             yc, p, GL = S("YC", 16 * w * c, 16 * w * (c + 1)), pb(3, 64, 64 + w), S(("GB", "EQ")[c % 2], 0, 640)
@@ -640,19 +629,18 @@ def program(ops, T, nxt, prv):
             ts(one(hk), one(yi), 6, AL.arith_shift_right, 7, AL.bitwise_and); tt(one(t2), one(hk), one(cv), AL.add); ts(end(I2, 1), one(t2), 15.0, AL.add)
             ts(end(rr, 0), one(yi), 3, AL.arith_shift_right, 7, AL.bitwise_and); ts(end(rr, 1), one(yi), 7, AL.bitwise_and); ts(all_(S("R2")), all_(rr), 256.0, AL.mult)
             parts = [(end, 0), (end, 1)] if LOTS[0] == 1 else [(lambda x, e_, k=1: all_(x, k), 0)]
-            for e_ in range(2): cp(end(S("GI"), e_, 16), IND(S("IT"), end(I2, e_)))
+            for a, b in ((0, w // 2), (w // 2, w), (w, 2 * w)): cp(sub(all_(S("GI"), 16), 16 * a, 16 * b), IND(S("IT"), sub(all_(I2), a, b)))
             for f_, e_ in parts:
                 gi, b = f_(S("GI"), e_, 16), 17 + c + e_; m = cols(gi); p, q = pb(b, 0, m // 16), pb(b, 64, 64 + m // 16); gl = GL if LOTS[0] > 1 else S(("GB", "EQ")[e_], 0, 640)
                 pe([(p, C("ID"), f_(S("R2"), e_))] + [(p, Zs("om", r), sub(gi, r, m, 16)) for r in range(16)]); cp(f_(LUL, e_), p)
-                for a in range(0, m, 16 * w): mv(sub(gl, a, a + 16 * w), IND(S("LUT"), sub(f_(LUL, e_), a // 16, a // 16 + w)))
-                pe([(q, C("I1K"), f_(i2, e_)), (q, C("ID"), f_(t3, e_))] + [(q, Zs("id", r), sub(gi, r, m, 16)) for r in range(16)], True, False)
-                pe([(q, Zs("l17", r), sub(gl, r, m, 16)) for r in range(16)], False, True); ts(f_(OVL, e_), q, -1.0, AL.add)
+                for a in range(0, m, 8 * w * (1 + e_)): mv(sub(gl, a, a + 8 * w * (1 + e_)), IND(S("LUT"), sub(f_(LUL, e_), a // 16, a // 16 + w * (1 + e_) // 2)))
+                if e_ == 0:
+                    y = pb(0, 128, 128 + 2 * w); pe([(y, C("ID"), all_(vl))] + [(y, Zs("id", r), sub(all_(S("GI"), 16), r, 32 * w, 16)) for r in range(16)]); cp(all_(ids), y)
+                    for x in range(2): ts(S(("EA", "EB")[x], c0 + w * c, c0 + w * c + w), sub(y, w * x, w * x + w), 14.0, AL.add)
+                pe([(q, C("I1K"), f_(i2, e_)), (q, C("ID"), f_(t3, e_)), (q, C("ID"), f_(ids, e_))] + [(q, Zs("l17", r), sub(gl, r, m, 16)) for r in range(16)])
+                ts(f_(OVL, e_), q, -2.0, AL.add)
             for e_ in range(2): tt(IND(S("OV"), end(OVL, e_)), end(S("GI"), 1 - e_, 16), S("NAM", 16 * w * c, 16 * w * (c + 1)), AL.add)
-        if t < 2: ts(S("NAM"), S("NAM"), M8[1], AL.add)
         tag[0] = "new"
-        p = pb(0, 128, 208); pe([(p, C("ID"), vl)] + [(p, Zs("id", r), S("GI", r, 1280, 16)) for r in range(16)])
-        for c in range(LOTS[0]):
-            for e_ in range(2): ts(S(("EA", "EB")[e_], c0 + w * c, c0 + w * c + w), sub(p, w * (2 * c + e_), w * (2 * c + e_ + 1)), 14.0, AL.add)
         YY = S("GA", 16 + n, 656 + n)
         mv(YY, IND(S("P"), S("EA", c0, c0 + 40))); tt(S("XB"), IND(S("M"), S("EB", c0, c0 + 40)), YY, AL.add); ts(S("X", 16 + n, 656 + n), S("XB"), 1024.0, AL.mult, 255.0, AL.min)
         tag[0] = "rows"
@@ -707,7 +695,7 @@ def program(ops, T, nxt, prv):
             FLG, INC, TG, p, y = flg[s_], inc(s_), S("TG", 8 * s_, 8 * s_ + 4), pb(bk, 0, 64), pb(bk, 0, 4)
             q0 = sub(E["q0"], 64 * s_, 64 * s_ + 4); SW = S("SW", 576 * s_, 576 * s_ + 576); w = sub(SW, 0, 512)
             pe([(p, C("BLK"), FLG)]); scan(INC, S("ONE", 0, 64), p, 0.0, AL.mult, AL.add)
-            if NUM[t][s_] == "p":
+            if NUM[s_] == "p":
                 ext(pb(13, 0, 4), [("all", FLG)], 64); ts(TG, pb(13, 0, 4), 0.0, AL.is_equal, 1024.0, AL.mult)
                 pe([(y, Yc(0, r), sub(INC, r - 1, 63, 16)) for r in range(16)] + [(y, C("ID"), TG)]); tt(q0, y, DS, AL.min); cp(H2(STL, s_, 4), q0)
             else:
@@ -725,7 +713,9 @@ def program(ops, T, nxt, prv):
         tag[0] = "own"
         number(0, 3); p = pb(3, 64, 128)
         pe([(p, C("NFE%d" % ha), rows(0, ha)) for ha in range(2)] + [(p, C("LS"), flg[0]), (p, C("ID"), inc(0))]); mv(H2(S("NUS"), 0), p, -513.0)
-        names(0, 3); mv(H2(SND, 0, 512), IND(XW, H2(SXL, 0, 32))); send(H2(SND, 0, 512), H2(RX, 1, 512), 3 * t + 1, "nxt", "prv")
+        names(0, 3)
+        for h in range(2): mv(H2(SND, h, 256), IND(XW, H2(SXL, h, 16)))
+        send(H2(SND, 0, 512), H2(RX, 1, 512), 3 * t + 1, "nxt", "prv")
         for s_ in range(2):
             fold(pb(3, 0, 64), "FE", "RTH", base[s_], 128); ts(H2(SRL, s_), pb(3, 0, 64), 2063.0, AL.add)
         tag[0] = "seam"
@@ -746,25 +736,32 @@ def program(ops, T, nxt, prv):
         tag[0] = "cmp"
         RX = S("RX", 1024 * (t % 2), 1024 * (t % 2) + 1024)
         GT, SG, MN, GX = S("EQS"), S("OH"), S("SC"), S("SRG")
+        if t == 2:
+            ts(S("W5"), S("IO", 0, 512), 1100.0, AL.add); put(IND(S("GA", 0, 5152), sub(SXL, 0, 32)), S("W5"))
+            for h in range(2): cp(S("D2", 512 * h, 512 * h + 512), IND(S("GA", 0, 4112), sub(SRL, 32 * h, 32 * h + 32)))
+            ext(pb(5, 0, 64), [("c0", S("D2"))], 1024); ts(sub(SRL, 0, 64), pb(5, 0, 64), -1084.0, AL.add, 15.0, AL.max); ms(S("KT", 15, 16), 1.0)
         for s_ in (1, 0):
             a, b, p = 512 * s_, 512 * s_ + 512, pb(7 - s_)
-            if CMP[0][t][s_] == "v":
-                pe([(p, C("ID"), sub(SND, a, b))])
-                tt(sub(GT, a, b), p, sub(RX, a, b), AL.is_gt); tt(sub(MN, a, b), p, sub(RX, a, b), AL.min)
-            else:
-                pe([(p, C("ID"), sub(SND, a, b)), (p, C("NID"), sub(RX, a, b))]); act(sub(MN, a, b), p, AF.Relu); ts(sub(GT, a, b), sub(MN, a, b), 0.0, AL.is_gt)
-                pe([(p, C("ID"), sub(SND, a, b)), (p, C("NID"), sub(MN, a, b))]); mv(sub(MN, a, b), p)
-            pe([(p, C("BLK"), sub(GT, a, b))]); L = sub(SXL, 32 * s_, 32 * s_ + 32)
+            pe([(p, C("ID"), sub(SND, a, b))])
+            for y, op in ((GT, AL.is_gt), (MN, AL.min))[::-1 if t == 2 else 1]: tt(sub(y, a, b), p, sub(RX, a, b), op)
+            p = pb(20 + s_); pe([(p, C("BLK"), sub(GT, a, b))]); L = sub(SXL, 32 * s_, 32 * s_ + 32)
             if t < 2:
                 act(sub(SG, a, b), p, AF.Sign, 8.5, -1.0); tt(IND(XW, L), sub(MN, a, b), sub(SG, a, b), AL.mult); signs = XW
             else:
-                cp(IND(S("G1", 0, 5152), L), sub(MN, a, b)); act(S("W6"), p, AF.Identity, 8.5, -1.0); put(IND(S("GA", 0, 5152), L), S("W6")); signs = S("GA", 0, 4112)
+                cp(IND(XW, L), sub(MN, a, b)); signs = S("GA", 0, 4112)
+                if s_: act(S("W6"), p, AF.Identity, 8.5, -1.0); put(IND(S("GA", 0, 5152), L), S("W6"))
+                else: signs = S("KT", 0, 528); ts(S("KT", 16, 528), p, -1.0, AL.mult, 8.5, AL.add)
             for h in range(2): mv(sub(GX, 2 * a + 512 * h, 2 * a + 512 * h + 512), IND(signs, sub(SRL, 64 * s_ + 32 * h, 64 * s_ + 32 * h + 32)))
             k_, a, p = S("KP", 128 * s_, 128 * s_ + 128), base[s_], pb(7 - s_, 0, 128)
             pe([(p, sub(C("KD"), 15 - l, 143 - l), sub(GX, 1024 * s_ + l, 1024 * s_ + 1024, 8)) for l in range(8)])
-            if t < 2: tt(S("RT", 16 + a, 144 + a), p, S("RT", 16 + a, 144 + a), AL.min)
-            ts(p, p, 0.0, AL.is_gt)
-            tt(S("FLS", 128 * s_, 128 * s_ + 128), p, S("FL", a, a + 128), AL.mult); tt(S("RTH", a, a + 128), p, S("RTH", a, a + 128), AL.mult)
+            if t == 2:
+                ts(p, p, -1.0, AL.max); tt(S("ZZ", a, a + 128), p, S("ZZ", a, a + 128), AL.min); c, d = (896, 1024) if a else (0, 896)
+                for q, y, o in (("y", "ynb", 0), ("s", "yen", 8)):
+                    dma(q, [(T[y][:, 1024 * k + c:1024 * k + d], T["GA"][k + o:128:16, 6560 + c:6560 + d]) for k in range(8)], [S("ZZ", c, d)], [], (d - c) // 2)
+                continue
+            fls = S("FLS", 128 * s_, 128 * s_ + 128); ts(fls, S("FL", a, a + 128), -2.0 ** 30, AL.mult, 2.0 ** 30, AL.add)
+            tt(S("RT", 16 + a, 144 + a), p, S("RT", 16 + a, 144 + a), AL.min); tt(fls, p, fls, AL.is_gt)
+            ts(p, p, 0.0, AL.is_gt); tt(S("RTH", a, a + 128), p, S("RTH", a, a + 128), AL.mult)
 
     ends(); part_a(0)
     for t in range(3):
@@ -775,17 +772,14 @@ def program(ops, T, nxt, prv):
         if t == 2:
             cp(S("WI", 256, 512), S("ENC")); ts(S("WJ", 256, 512), S("WI", 256, 512), 2047, AL.bitwise_and); ts(S("GAW"), S("WJ", 256, 512), -1.0, AL.add)
             dma("y", [(T["ymid"][:, :], T["GAW"][:, :])], [S("GAW")], [], 200)
-            for a in range(16, 4112, 512): act(S("G1", a, a + 512), S("X", a, a + 512), AF.Abs)
+            for x in E["sign"]: act(x, x, AF.Abs)
+            ts(BG, DEAD, -8192.0, AL.mult)
+            for a in (0, 512):
+                p = pb(1 + a // 512)
+                pe([(p, C("ID"), S("RTH", a, a + 512)), (p, C("EN2K"), S("FL", a, a + 512))] + [(sub(p, x - a, x - a + 64), Al(x // 64), BG) for x in range(max(a, 128), min(a + 512, 896), 64)])
+                ts(S("ZZ", a, a + 512), p, -1.0, AL.add, -1.0, AL.max)
         part_d(t)
-    dma("y", [(T["ylen"][:, a:a + 1024], T["G1"][:, 16 + a:1040 + a]) for a in range(0, 4096, 1024)], [S("G1", 16, 4112)], [], 1024)
-    ts(BG, DEAD, -8192.0, AL.mult)
-    for bk, a, b, fl_ in ((1, 128, 512, S("FL", 128, 512)), (2, 512, 896, S("FL", 512, 896)), (1, 0, 128, S("FLS", 128, 256)), (2, 896, 1024, S("FLS", 0, 128))):
-        gone = [(pb(bk, x - a, x - a + 64), Al(x // 64), BG) for x in range(a, b, 64)] if b - a > 128 else []
-        pe([(pb(bk, 0, b - a), C("ID"), S("RTH", a, b)), (pb(bk, 0, b - a), C("EN2K"), fl_)] + gone)
-        if gone: ts(S("ZZ", a, b), pb(bk, 0, b - a), -1.0, AL.add, -1.0, AL.max)
-        else: ts(S("ZZ", a, b), pb(bk, 0, b - a), -1.0, AL.add)
-    dma("y", [(T["ynb"][g, :], T["GA"][16 * g:16 * g + 8, 6560:7584]) for g in range(8)], [S("ZZ")], [], 512)
-    dma("s", [(T["yen"][g, :], T["GA"][16 * g + 8:16 * g + 16, 6560:7584]) for g in range(8)], [S("ZZ")], [], 512)
+    dma("y", [(T["ylen"][:, :], T["X"][:, 16:4112])], [S("X", 16, 4112)], [], 900)
 
 
 def polish(ops, fw, res, rng, steps):
@@ -976,7 +970,7 @@ def later(ops, res):
     n = len(ops); res = list(res); due = [1e18] * n
     for i in sorted(range(n), key=lambda i: (-res[i][0], -i)):
         a, b, q = res[i]
-        if q == "p" and b + ROOM[2] < due[i] < 1e17: res[i] = (a + due[i] - b - ROOM[2], due[i] - ROOM[2], q)
+        if q == "p" and b + ROOM[1] < due[i] < 1e17: res[i] = (a + due[i] - b - ROOM[1], due[i] - ROOM[1], q)
         for j in ops[i]["deps"] | ops[i]["order"]: due[j] = min(due[j], res[i][0] - LAT)
     return res
 
@@ -1000,7 +994,7 @@ def banks(ops, res, rng):
     rows = [[] for _ in range(8)]; end = [-1e9] * 8
     for t, l in sorted(use.items(), key=lambda x: res[x[1][0]][0]):
         a = res[l[0]][0]; other = set(x for i in l for x in ops[i]["tile"].values()) - {t}
-        rank = sorted(range(8), key=lambda b: rng.rand() * ROOM[1] + end[b])
+        rank = sorted(range(8), key=lambda b: rng.rand() * ROOM[0] + end[b])
         for b in rank:
             if rows[b] and (rows[b][-1] in other or reaches(l, set(use[rows[b][-1]]))): continue
             break

@@ -4,24 +4,24 @@ from concourse.mybir import AluOpType as AL, ActivationFunctionType as AF
 F, H, B, I, U = "float32", "float16", "bfloat16", "int32", "uint16"
 SB = {
     "RAW": (2048, I), "X": (5152, B), "RT": (1056, F), "RTH": (1024, H), "TA": (1024, F), "TB": (1024, F), "FL": (1024, B), "FLS": (256, B),
-    "G1": (6800, B), "LN": (512, U), "KT": (1040, B), "CT": (1040, B), "IT": (1040, B), "GR": (1024, F), "HE": (2048, B),
+    "G1": (6800, B), "LN": (512, U), "KT": (1040, B), "CT": (1040, B), "IT": (1056, B), "GR": (1024, F), "HE": (2048, B),
     "P": (1040, F), "M": (1040, F), "GA": (7584, F), "OV": (9472, B), "EQ": (1024, B), "D2": (1024, H), "GB": (1024, B),
-    "GC": (1024, B), "XS": (1024, B), "IDB": (1024, B), "R1": (1024, B), "RA": (1024, B), "RB": (1024, B), "J16": (512, B), "FT": (512, B), "HW": (128, F), "IO": (1056, F),
-    "IOB": (128, B), "ALL": (2048, B), "Y": (2304, B), "Z": (144 * 16, B), "CM": (128 * 68, B), "ONE": (1024, B), "RST": (512, B),
-    "LUT": (2048, B), "EA": (256, U), "EB": (256, U), "ENC": (256, F), "GAW": (256, F), "WN": (3456, H), "ZZ": (1024, F), "ZF": (272, F), "WV": (1040, B),
-    "SF": (2432, F), "SI": (1024, I), "SH": (960, B), "SU": (400, U), "S16": (512, H), "W5": (512, F), "W6": (512, F), "WI": (512, I), "WJ": (512, I),
-    "WB": (512, B), "R": (512, B), "PR": (512, B), "SV": (512, B), "INW": (272, H), "NT": (512, F), "WW": (1168, F), "CW": (640, H),
+    "GC": (1024, B), "XS": (1024, B), "IDB": (1024, B), "R1": (1024, B), "RA": (512, B), "RB": (1024, B), "J16": (512, B), "FT": (512, B), "HW": (128, F), "IO": (1056, F),
+    "IOB": (128, B), "ALL": (2048, B), "Y": (2304, B), "Z": (144 * 17, B), "CM": (128 * 68, B), "ONE": (512, B), "RST": (512, B),
+    "TS": (1024, B), "DEC": (640, B), "EA": (256, U), "EB": (256, U), "ENC": (256, I), "GAW": (256, F), "WN": (3456, H), "ZZ": (1024, F), "WV": (1040, B),
+    "SF": (1792, F), "SI": (1024, I), "SH": (1024, B), "SU": (400, U), "S16": (512, H), "W5": (512, F), "W6": (512, F), "WI": (512, I), "WJ": (512, I),
+    "WB": (512, B), "R": (512, B), "PR": (512, B), "SV": (512, B), "INW": (288, H), "NT": (272, F), "WW": (2144, F), "CW": (640, H),
     "YC": (640, H), "GI": (1280, B), "G0": (128, H), "XB": (640, B), "RKW": (80, B), "QS": (512, B), "QR": (256, B),
     "TP": (576, B), "TR": (384, B), "EQS": (1024, B), "PRS": (1024, H), "NUS": (128, F), "INC": (144, H), "TG": (144, H),
-    "SW": (1152, B), "SC": (1024, B), "OH": (1024, B), "NE": (1024, H), "SND": (3072, B), "RX": (2048, B), "OVT": (1024, B), "COL": (32, F), "COI": (16, I), "ZER": (1024, B),
+    "SW": (1152, F), "SC": (1024, B), "OH": (1024, B), "NE": (1024, H), "SND": (3072, B), "RX": (2048, B), "OVT": (1024, B), "COL": (32, F), "COI": (16, I), "ZER": (1024, B),
 }
-LISTS = {"a": 64, "hx": 4, "sp": 64, "go": 8, "u": 64, "cs": 32, "cw": 40, "i2": 80, "lu": 80, "ov": 80, "st": 8, "sc": 64, "sx": 64, "sr": 128, "q": 8}
+LISTS = {"a": 64, "hx": 4, "sp": 64, "go": 8, "u": 64, "cs": 18, "i2": 80, "ov": 80, "st": 8, "sx": 64, "sr": 128, "q": 8}
 SB["Lsh"] = (32, U)
 for _k, _n in LISTS.items():
     SB["L" + _k] = (_n, U)
-SB.update({"SRG": (2048, B), "KP": (256, B), "SM": (3072, B), "SND": (1024, B), "O0": (128, I), "NAM": (640, B), "ZB": (1024, B), "R2": (80, B), "UM": (160, B)})
-ALIAS = {"WI": ("RAW", 1024), "WJ": ("RAW", 1536), "SI": ("RAW", 0), "TA": ("P", 16), "TB": ("GA", 6560), "ZZ": ("GA", 6560), "WW": ("GA", 5392), "GC": ("GB", 0), "EQS": ("SM", 0), "OH": ("SM", 1024),
-         "SC": ("SM", 2048), "NE": ("PRS", 0), "NT": ("W5", 0),
+SB.update({"SRG": (2048, B), "SM": (3072, B), "SND": (1024, B), "O0": (128, I), "NAM": (640, B), "ZB": (1024, B), "R2": (80, B), "UM": (160, B)})
+ALIAS = {"WI": ("RAW", 1024), "WJ": ("RAW", 1536), "SI": ("RAW", 0), "TA": ("P", 16), "TB": ("GA", 6560), "ZZ": ("GA", 6560), "WW": ("GA", 4352), "GC": ("GB", 0), "EQS": ("SM", 0), "OH": ("SM", 1024),
+         "SC": ("SM", 2048), "NE": ("PRS", 0),
          "ZB": ("SRG", 0), "HE": ("G1", 2560), "WB": ("G1", 4752), "R": ("G1", 5264), "PR": ("G1", 5776), "SV": ("G1", 6288)}
 SCRATCH = {k: ("sbuf", [128, n], d) for k, (n, d) in SB.items() if k not in ALIAS}
 for _b in range(8):
@@ -36,17 +36,17 @@ DMA, XF = [1300.0, 300.0], [1.0]
 OVD = [2, 0]
 NEAR, JIT = [3], [10.0]
 CUT, EDW = [1100], [448]
-WIN = [200, 300]
+WIN = [150, 200]
+HOP = [1, 1] + [2] * 6 + [1, 1]
+RTG = [0]
 NUM = "vp"
 BLOCKS = [(j, s) for s in range(4) for j in range(2 * s + 1)]
-PLACE = {(j, k): 8 * j + k for j in range(2) for k in range(j + 1, 8)}
-PLACE.update({jk: d + 1 for d, jk in enumerate((j, k) for j in range(2, 8) for k in range(j + 1, 8))})
-LOTS = [1]
-PASSES, AGAIN = [1400, 130, 5000], [(0, 300, 9000)]
-PLAN, SEED, TEMP, OWN, TRIES = {}, [52], [250.0], [2.0], [120, 90.0]
+PLACE = {jk: (d // 14, d % 14 + 1) for d, jk in enumerate((j, k) for j in range(8) for k in range(j + 1, 8))}
+PASSES, AGAIN = [900, 60, 20000], [(0, 120, 30000)]
+PLAN, SEED, TEMP, OWN, TRIES = {}, [7], [250.0], [2.0], [120, 90.0]
 SEATS, ROOM = [12], [1500.0, 300.0]
 GUESS = [({"o": 1, "g": 0.78, "s": 0.6, "p": 1.05, "x": 0.9}, 200.0, 1.0), ({"o": 1.1, "g": 1.3, "s": 1.6, "p": 1.0, "x": 1.1}, 130.0, 1.0)]
-BIAS = {"ends0": 10000.0}
+BIAS = {"ends0": 8000.0}
 GAT, SCA = 1.56, 3.2
 
 
@@ -252,12 +252,7 @@ def program(ops, T, nxt, prv):
         return pb(b0 + r // 8, 64 * (r % 8), 64 * (r % 8) + 64)
 
     def w2r(b0, parts):
-        for half in range(4):
-            mm = []
-            for r in range(4 * half, 4 * half + 4):
-                for i, (lf, rf) in enumerate(parts):
-                    mm.append((blk(b0, r), lf(r), rf(r)) + ((1,) if i == 0 else ()))
-            pe(mm)
+        for h in range(2): pe([(blk(b0, r), lf(r), rf(r)) for r in range(8 * h, 8 * h + 8) for lf, rf in parts])
 
     def halves(fn):
         for h in range(2): fn(h, 512 * h, 512 * h + 512)
@@ -267,22 +262,23 @@ def program(ops, T, nxt, prv):
     dma("y", [(RAW[:, 0:512], nb[:, :]), (RAW[:, 512:1024], en[:, :])] +
         [(RAW[16 * g:16 * g + 16, 1024:1536], nb[16 * (g ^ 1):16 * (g ^ 1) + 16, :]) for g in range(8)], [], [S("RAW", 0, 1536)], 1024)
     dma("s", [(RAW[16 * g:16 * g + 16, 1536:2048], en[16 * (g ^ 1):16 * (g ^ 1) + 16, :]) for g in range(8)], [], [S("RAW", 1536, 2048)], 512)
-    dma("y", [(T["X"][:, 16:2192], T["lens"][:, :])], [S("RAW")], [S("X", 16, 2192)], 544)
     RC, HQ, M3, NTB, A64 = [S("COL", i, i + 1) for i in range(5)]
     M8, M9 = [S("COL", c, c + 1) for c in (3, 8, 9)], [S("COL", 24 + t, 25 + t) for t in range(3)]
     ONE = S("ONE", 0, 128)
-    ms(S("ONE", 0, 512), 1.0); ms(S("ZER"), 0.0); mv(S("ONE", 512, 1024), S("ONE", 0, 512))
+    ms(S("ONE", 0, 512), 1.0); ms(S("ZER"), 0.0)
     o0 = S("O0", 0, 64); iota(o0, [[2, 32], [1024, 2]], 0, 64)
     iota(S("COI", 0, 1), [[0, 1]], 0, 1)
     blank = ["CV", "CV2", "KD", "KD2", "FK"]
     for n in blank: C(n)
     ms(S("Z", 0, 432), 0.0); ms(C("FK"), 0.0); w = 128 * len(blank) - 128
-    for l in ([("Y", 0, 1024), ("Y", 1024, 2048), ("Y", 2048, 2304)], [("Z", 432, 1296), ("Z", 1296, 2304), ("CM", 0, w)]):
+    for l in ([("Y", 0, 1024), ("Y", 1024, 2048), ("Y", 2048, 2304)], [("Z", 432, 1440), ("Z", 1440, 2448), ("CM", 0, w)]):
         dma("y", [(T[n][:, a:b], T["ZER"][:, 0:b - a]) for n, a, b in l], [S("ZER"), S("RAW")], [S(*x) for x in l], 576)
     ts(S("COI", 1, 2), S("COI", 0, 1), 15, AL.bitwise_and); cp(RC, S("COI", 1, 2))
     ts(S("COI", 2, 3), S("COI", 0, 1), 4, AL.arith_shift_right, 1, AL.bitwise_and); cp(HQ, S("COI", 2, 3))
     ts(S("COI", 3, 4), S("COI", 0, 1), 8, AL.bitwise_and); ts(A64, S("COI", 3, 4), 8.0, AL.mult)
-    for t in range(3): ts(M8[t], RC, 10.0, AL.is_equal, 4.0 + 20.0 * t, AL.mult)
+    ODD, NB_, M12 = S("COL", 27, 28), S("COL", 28, 29), S("COL", 29, 30)
+    ts(S("COI", 8, 9), S("COI", 0, 1), 1, AL.bitwise_and); cp(ODD, S("COI", 8, 9)); ts(NB_, RC, 0.5, AL.mult, -9.0, AL.add); ts(NB_, NB_, ODD, AL.mult); ts(M12, RC, 12.0, AL.is_equal)
+    for t in range(3): ts(M8[t], M12, 4.0 + 20.0 * t, AL.mult, NB_, AL.add)
     o1 = S("O0", 64, 128); ts(o1, o0, 2047, AL.bitwise_and); o2 = su(64); ts(o2, o1, HQ, AL.add)
 
     def aff(name, c0, al, be, src=ONE):
@@ -298,75 +294,80 @@ def program(ops, T, nxt, prv):
         for ch, w in ws: poke(Zs(name, None, off), ch, w)
     aff("DUP", 0, 0, 1); aff("ID", 0, 8, 1); aff("FN0", 0, 1000, 1); aff("FN1", 1000, -1000, 1)
     M0 = S("COL", 6, 7); ts(M0, RC, 0.0, AL.is_equal); x5 = sf(8); m_ = lambda i: sub(x5, i, i + 1)
-    ts(m_(1), RC, 1.0, AL.is_equal); ts(m_(2), RC, 2.0, AL.is_equal); ts(m_(3), M0, 16.0, AL.mult, m_(2), AL.subtract); ts(m_(4), m_(2), 15.0, AL.mult)
-    ms(S("XB", 0, 512), 1.0); ts(S("XB", 0, 512, 32), S("ONE", 0, 16), m_(1), AL.subtract); ts(S("GB", 0, 512), S("ONE", 0, 512), m_(1), AL.mult)
-    ts(S("GB", 0, 512, 32), S("ONE", 0, 16), m_(1), AL.mult, m_(2), AL.add)
-    ts(S("XB", 128, 129), S("XB", 0, 1), M0, AL.subtract); ts(S("GB", 384, 385), M0, 16.0, AL.mult, S("GB", 0, 1), AL.add)
-    scan(S("IDB", 512, 1024), S("XB", 0, 512), S("GB", 0, 512), m_(4), AL.mult, AL.add); mv(S("GB", 384, 385), S("GB", 0, 1))
-    scan(S("IDB", 0, 512), S("XB", 0, 512), S("GB", 0, 512), m_(3), AL.mult, AL.add)
+    ts(m_(1), RC, 2.0, AL.is_equal); ts(m_(2), RC, 4.0, AL.is_equal)
+    ts(m_(3), RC, -7.5, AL.add); ts(m_(4), m_(3), m_(3), AL.mult, 36.0, AL.is_gt); ts(S("TP", 0, 64), S("ONE", 0, 64), m_(4), AL.mult, 16.0, AL.mult)
+    iota(S("TP", 64, 128), [[0, 2], [1, 32]], 1); iota(S("TP", 128, 192), [[1, 2], [0, 32]], 0); ts(S("TP", 128, 192), S("TP", 128, 192), RC, AL.add, RC, AL.add)
+    dma("y", [(T["IDB"][2 * c:128:16, :], T["TP"][:, 64 * c:64 * c + 64]) for c in range(3)] + [(T["IDB"][1:128:2, :], T["ZER"][0:64, :])] +
+        [(T["IDB"][c:128:16, :], T["ZER"][0:8, :]) for c in range(6, 16, 2)], [S("TP", 0, 192), S("ZER"), S("RAW")], [S("IDB")], 300)
     asel(S("Y", 15, 2304, 16), S("ONE", 0, 144), [[-1, 16], [-16, 9]], AL.is_equal, 0, 0)
     asel(C("BLK"), ONE, [[-16, 8], [0, 16]], AL.is_ge, 0, 0); asel(C("BLK"), C("BLK"), [[16, 8], [0, 16]], AL.is_ge, 0, 15, -1)
     B8c = sub(C("BLK"), 0, 128, 16)
     asel(Zs("lo8"), B8c, [[16, 8]], AL.is_ge, 0, 7, -1)
-    zmake("key", [(0, 2048 * 256), (1, 256), (2, 32 * 256)])
-    DGO, A1C, INEL = sf(64), sf(64), sh(64)
-    HLF = S("COL", 10, 11); ts(HLF, RC, 1.0, AL.is_equal, 0.5, AL.mult)
+    zmake("key", [(0, 2048 * 256), (2, 256), (4, 32 * 256)])
+    DGO, A1C = sf(64), sf(64)
+    HLF = S("COL", 10, 11); ts(HLF, m_(1), 0.5, AL.mult)
     t0 = sf(8)
-    for t in range(3): ts(M9[t], M8[t], HLF, AL.add)
+    ts(M3, m_(2), 4.0, AL.mult, HLF, AL.subtract)
+    for t in range(3): ts(M9[t], M8[t], M3, AL.subtract)
     for k in range(8): ms(S("RST", k, 512, 8), -float(2 ** (k - 1)) if k else 1.0e8)
     for n, c in (("KT", 16.0), ("CT", 0.0), ("IT", 0.0), ("RT", 0.0), ("X", 0.0), ("INW", 0.0)):
         ms(S(n, 0, 16), c)
-    ts(S("KT", 15, 16), M0, 31.0, AL.mult); ts(M3, HLF, -1.0, AL.mult)
+    ts(S("KT", 15, 16), M0, 31.0, AL.mult)
     ts(C("NE2K"), C("FN1"), -2048.0, AL.mult)
 
     def f0(h, a, b):
-        ts(S("TA", a, b), IND(S("RAW"), sub(o2, 32 * h, 32 * h + 32)), 1.0, AL.add)
-        add("v", lambda e: [e["v"].transpose(ap(S("TB", a, b)), ap(S("TA", a, b)))], [S("TA", a, b)], [S("TB", a, b)], 512 * CYC)
-        flags(S("FL", a, b), S("TB", a, b))
-        pe([(pb(1 + h), C("NE2K"), S("FL", a, b))])
-        tt(S("RTH", a, b), pb(1 + h), S("TB", a, b), AL.add)
+        x, y = S("D2", a, b), S("PRS", a, b)
+        ts(x, IND(S("RAW"), sub(o2, 32 * h, 32 * h + 32)), -999.0, AL.add)
+        add("v", lambda e: [e["v"].transpose(ap(y), ap(x))], [x], [y], 256 * CYC + FIX[0])
+        ts(S("FL", a, b), y, -999.5, AL.is_gt)
+        pe([(pb(1 + h), C("ID"), y), (pb(1 + h), C("NE2K"), S("FL", a, b))])
+        ts(S("RTH", a, b), pb(1 + h), 1000.0, AL.add)
     halves(f0)
     iota(S("IO"), [[1, 1056]], 0); cp(S("IOB"), S("IO", 0, 128))
     for k in range(4):
         asel(S("ALL", 512 * k, 512 * k + 512), S("ONE", 0, 512), [[-1, 4], [-16, 8], [0, 16]], AL.is_equal, 0, -4 * k)
-    halves(lambda h, a, b: (pe([(pb(7), C("DUP"), S("ALL", a, b))]), mv(S("R1", a, b), pb(7))))
-    for j in range(16): ts(S("RA", j, 1024, 16), S("R1", j, 1024, 16), j * j - 1.0, AL.mult); ts(S("RB", j, 1024, 16), S("R1", j, 1024, 16), -2.0 * j, AL.mult)
-    iota(S("J16"), [[0, 32], [1, 16]], 0)
-    MK, MC, DB1, W32, LIM = [S("COL", 19, 20), S("COL", 20, 21)], [S("COL", 21, 22), S("COL", 22, 23)], S("COL", 23, 24), sf(64), sf(64)
+    halves(lambda h, a, b: (pe([(pb(7), C("DUP"), S("ALL", a, b))]), ts(S("R1", a, b), pb(7), -1.0, AL.mult)))
+    for j in range(16): ts(S("RB", j, 1024, 16), S("R1", j, 1024, 16), -131072.0 * j, AL.mult)
+    iota(S("J16"), [[0, 32], [-1, 16]], 0); act(S("RA"), S("J16"), AF.Square, 0.0, 256.0)
+    MK, MC, MD_, W32, LIM = [S("COL", 19, 20), S("COL", 20, 21)], [S("COL", 21, 22), S("COL", 22, 23)], [S("COL", 23, 24), S("COL", 30, 31)], sf(48), sf(64)
     ts(MK[0], RC, 7.5, AL.is_lt); ts(MK[1], RC, 7.5, AL.is_gt)
-    for h in range(2): ts(MC[h], MK[h], 31.0 / 65536, AL.mult)
-    for d in range(4): ms(sub(W32, 16 * d, 16 * d + 16), 32.0 ** -d)
+    for h in range(2): ts(MC[h], MK[h], -992.0 / 65536, AL.mult); ts(MD_[h], MK[h], -1953.0, AL.mult)
+    for d in range(3): ms(sub(W32, 16 * d, 16 * d + 16), 32.0 ** -d)
     iota(S("COI", 4, 8), [[0, 4]], 0, 1); cp(S("Lhx"), S("COI", 4, 8))
-    for k in range(8): ts(sub(C("PW"), k, 128, 8), sub(C("ID"), k, 128, 8), float(2 ** k), AL.mult)
-    pe([(pb(7, 0, 8), C("PW"), Zs("lo8"))]); cp(Zs("pow"), pb(7, 0, 8)); zmake("id", [(1, 1), (2, 32)])
-    PWN, PWC = S("COL", 15, 16), S("COL", 16, 17)
-    pe([(pb(7, 0, 1), C("PW"), S("ONE", 0, 1))]); ts(PWN, pb(7, 0, 1), -1.0, AL.mult); cp(PWC, pb(7, 0, 1))
+    zmake("id", [(2, 1), (4, 32)])
+    x6 = sf(32); TH = sub(x6, 23, 24)
+    ts(sub(x6, 0, 8), S("IO", 1, 17, 2), RC, AL.is_equal, -1.5, AL.mult); tt(sub(x6, 8, 16), sub(x6, 0, 8), S("RST", 0, 8), AL.mult); ts(sub(x6, 24, 25), M0, 1000.0, AL.mult, 0.75, AL.add)
+    scan(sub(x6, 16, 24), sub(x6, 8, 16), sub(x6, 8, 16), sub(x6, 24, 25), AL.max, AL.max)
+    affw("DF", 1, 0, 2, -0.5); asel(C("DF"), C("DF"), [[-16, 8], [0, 2], [-2, 8]], AL.not_equal, 0.5, -3)
+    for w, ch in ((0.0, 17), (0.5, 0)): asel(sub(C("DF"), 7, 128, 8), sub(C("DF"), 7, 128, 8), [[-16, 8], [0, 2]], AL.not_equal, w, -ch)
+    ts(C("TD"), C("ID"), ODD, AL.mult, 0.5, AL.mult)
 
     ts(C("NID"), C("ID"), -1.0, AL.mult); ts(C("IDK"), C("ID"), 1.0 / 1024, AL.mult)
     RC1 = S("COL", 7, 8); ts(RC1, RC, 1.0, AL.add)
     ms(S("RKW", 64, 80), 1000.0); ms(S("RT", 1040, 1056), 0.0); ts(Zs("rc"), B8c, RC, AL.mult, flex=False)
     iota(S("ENC"), [[0, 256]], 2048)
-    for c, z in ((0, "lo8"), (4, "lo8"), (5, "pow")): cp(sub(C("FK"), c, 128, 16), Zs(z))
+    cp(sub(C("FK"), 0, 128, 16), Zs("lo8")); y = sub(C("FK"), 1, 128, 2)
+    asel(y, S("ONE", 0, 64), [[-16, 8], [-1, 8]], AL.is_ge, 0, 0); asel(y, y, [[16, 8], [0, 8]], AL.is_ge, 0, 7, -1)
     ts(sub(t0, 0, 1), RC, 0.5, AL.is_gt); ts(C("KS"), C("ID"), sub(t0, 0, 1), AL.mult)
     ts(S("CT", 15, 16), M0, 1000.0, AL.mult)
     tag[0] = "ends"
-    ms(S("ZF"), 0.0)
-    mv(S("GR", 0, 272), S("ZF")); mv(S("GR", 272, 544), S("ZF"))
+    ms(S("GR", 0, 272), 0.0); ms(S("GR", 272, 544), 0.0)
     dma("y", [(T["GA"][:, a:a + 544], T["GR"][:, 0:544]) for a in range(0, 2176, 544)], [S("GR", 0, 544), S("RAW")], [S("GA", 0, 2176)], 1088)
-    dma("y", [(T["GA"][c:128:16, 2176:4352], T["ZF"][:, 0:136]) for c in range(2)], [S("ZF"), S("RAW")], [S("GA", 2176, 4352)], 140)
+    dma("y", [(T["GA"][c:128:16, 2176:4352], T["GR"][:, 0:136]) for c in range(2)], [S("GR", 0, 136), S("RAW")], [S("GA", 2176, 4352)], 140)
     tag[0] = ""
-    dma("y", [(T["X"][:, a:b], T["ZER"][:, 0:b - a]) for a, b in ((2192, 3216), (3216, 4240), (4240, 5152))], [S("ZER"), S("RAW")], [S("X", 2192, 5152)], 740)
+    dma("y", [(T["X"][:, 16:2192], T["lens"][:, :])] + [(T["X"][:, a:b], T["ZER"][:, 0:b - a]) for a, b in ((2192, 3216), (3216, 4240), (4240, 5152))],
+        [S("ZER"), S("Y", 0, 8), S("Z", 432, 440)], [S("X", 16, 5152)], 1284)
     ms(S("X", 4112, 4113), 300.0)
 
     def zero_ov(t, when):
-        if t: dma("y", [(T["OV"][c:128:8, 0:8192], T["ZER"][:, :]) for c in (1, 2)], [S("ZER"), when], [S("OV", 0, 8192)], 512)
+        if t: dma("y", [(T["OV"][c:128:8, 0:8192], T["ZER"][:, :]) for c in (2, 4)], [S("ZER"), when], [S("OV", 0, 8192)], 512)
         else: dma("y", [(T["OV"][:, a:min(a + 1920, 8192)], T["X"][:, 2192:2192 + min(1920, 8192 - a)]) for a in range(0, 8192, 1920)], [S("X", 2192, 4112), when], [S("OV", 0, 8192)], 2048)
 
     def ends():
         tag[0] = "ends"
         f, TT, CL, PL, SL = S("SM", 0, 1024), S("ZZ"), S("SU", 64, 200), S("SU", 200, 336), S("SU", 336, 400)
         cn, em, st, ex, ML, AB = sh(64), sh(64), S("S16", 64, 128), sf(72), sf(136), S("COL", 14, 15)
-        ms(sub(ex, 0, 1), -1088.0); iota(ML, [[16, 136]], 0); ts(ML, ML, RC, AL.add); ts(AB, HLF, 2 * 16416.0, AL.mult)
+        ms(sub(ex, 0, 1), -1088.0); iota(ML, [[16, 136]], 0); ts(ML, ML, RC, AL.add); ts(AB, RC, 1.0, AL.is_equal, 16416.0, AL.mult)
         iota(S("M", 16, 1040), [[1, 1024]], 1024); iota(S("W5", 0, 128), [[1, 128]], 2048)
         for h in range(2):
             a, b = 512 * h, 512 * h + 512
@@ -403,81 +404,82 @@ def program(ops, T, nxt, prv):
         dma("y", [(T["W6"][:, 136 * c:136 * c + 136], T["GA"][c:128:16, 2176:4352]) for c in range(2)], [S("GA", 2176, 4352)], [S("W6", 0, 272)], 240)
         ts(S("EA", 0, 136), S("W6", 0, 136), -15.8, AL.add, 15.0, AL.max)
         ts(S("WJ", 256, 392), S("W6", 136, 272), -32.0, AL.add); ts(S("WI", 256, 392), S("WJ", 256, 392), 4095, AL.bitwise_and); ts(S("EB", 0, 136), S("WI", 256, 392), -2033.0, AL.add, 1039.0, AL.min)
-    for n in ("P", "M"): ms(S(n, 0, 15), 0.0); ms(S(n, 15, 16), 1000.0)
+    for n in ("P", "M"): iota(S(n, 0, 16), [[0, 16]], 0); iota(S(n, 15, 16), [[0, 1]], 30000)
     asel(Zs("en"), B8c, [[-16, 8]], AL.is_ge, 0, -8)
     asel(C("LT"), C("BLK"), [[16, 8], [1, 16]], AL.is_gt, 0, 0, -1)
     iota(DGO, [[16, 64]], 129); ts(DGO, DGO, RC, AL.add)
     ts(Zs("ha"), Zs("lo8"), -2.0, AL.mult); ts(Zs("ha", None, 16), Zs("en"), -2.0, AL.mult); ts(Zs("hh"), Zs("en"), -2.0, AL.mult)
     asel(C("B8"), ONE, [[-8, 16], [0, 8]], AL.is_ge, 0, 0); asel(C("B8"), C("B8"), [[8, 16], [0, 8]], AL.is_ge, 0, 7, -1)
-    asel(C("VM"), ONE, [[0, 8], [-1, 2], [1, 8]], AL.is_gt, 0, 0, 0); aff("EJ0", 0, 1, 0, C("VM")); aff("EK0", 0, 0, 1, C("VM"))
-    x3 = sf(8); c_ = lambda i: sub(x3, i, i + 1); x4 = sh(8)
-    ts(c_(0), RC, -0.5, AL.mult, 7.5, AL.add); ts(c_(1), c_(0), RC, AL.mult, -12.0, AL.add); ts(c_(2), RC, -1.0, AL.mult, 7.0, AL.add); ts(c_(3), c_(2), c_(1), AL.add)
-    ts(c_(4), c_(1), -1.0, AL.mult, RC1, AL.add); ts(C("KL"), C("BLK"), c_(4), AL.mult); ts(C("EK1"), C("BLK"), -100.0, AL.mult, 100.0, AL.add)
-    p = pb(7, 0, 128); pe([(p, C("ID"), C("EK1")), (p, C("ID"), S("J16", 0, 128))]); mv(C("D16"), p); ms(sub(C("D16"), 0, 128, 16), 100.0)
-    ts(C("EK1"), C("D16"), c_(1), AL.is_ge, MK[0], AL.mult); ts(p, C("D16"), c_(3), AL.is_lt); tt(C("EJ1"), p, C("EK1"), AL.mult)
-    pe([(p, C("KL"), C("EJ1")), (p, C("ID"), C("D16"))]); ts(C("EK1"), p, RC, AL.is_equal, MK[0], AL.mult)
+    x3 = sf(16); c_ = lambda i: sub(x3, i, i + 1); x4 = sh(8)
+    ts(c_(0), RC, -0.5, AL.mult, 7.5, AL.add); ts(c_(2), RC, -1.0, AL.mult, 7.0, AL.add); ts(C("EK1"), C("BLK"), -100.0, AL.mult, 100.0, AL.add)
+    p = pb(7, 0, 128); pe([(p, C("ID"), C("EK1")), (p, C("NID"), S("J16", 0, 128))]); mv(C("D16"), p)
+    for c in (0, 15): iota(sub(C("D16"), c, 128, 16), [[0, 8]], 100)
+    for b in range(2):
+        EJ, EK, c1, c3, c4 = C("EJ%d" % b), C("EK%d" % b), c_(8 + b), c_(10 + b), c_(12 + b)
+        ts(c1, c_(0), RC, AL.mult, 1.0 - 14 * b, AL.add); ts(c3, c_(2), c1, AL.add); ts(c4, c1, -1.0, AL.mult, RC1, AL.add); ts(C("KL"), C("BLK"), c4, AL.mult)
+        ts(EK, C("D16"), c1, AL.is_ge, MK[0], AL.mult); ts(p, C("D16"), c3, AL.is_lt); tt(EJ, p, EK, AL.mult)
+        pe([(p, C("KL"), EJ), (p, C("ID"), C("D16"))]); ts(EK, p, RC, AL.is_equal, MK[0], AL.mult)
     asel(C("LN"), C("LT"), [[-1, 128]], AL.not_equal, -8.5, 0); ts(C("LN"), C("LN"), -1.0, AL.mult)
     for b in range(2):
         pe([(p, C("EJ%d" % b), C("EJ%d" % b)), (p, C("EK%d" % b), C("EJ%d" % b))]); tt(C("LA%d%d" % (b, b)), p, C("LN"), AL.mult)
         pe([(p, C("EK%d" % b), C("EK%d" % b))]); tt(C("LB%d%d" % (b, b)), p, C("LN"), AL.mult)
-        pe([(p, C("EK0"), C(("EJ1", "EK1")[b]))]); ts(C(("LA01", "LB01")[b]), p, -1.0, AL.mult)
-    DB = [S("COL", 12, 13), S("COL", 13, 14)]
-    ts(c_(7), M0, 1024.0 + 2057.0 / 8192, AL.mult, -1025.0 - 2057.0 / 8192, AL.add)
-    ts(DB[0], RC, 1.0 / 128, AL.mult, c_(7), AL.add); ts(sub(x4, 0, 1), RC, 8.0, AL.mult); mv(sub(x4, 1, 2), RC)
-    pe([(pb(7, 0, 1), C("EJ1"), sub(x4, 0, 1)), (pb(7, 0, 1), C("EK1"), sub(x4, 1, 2))]); ts(DB[1], pb(7, 0, 1), 1.0 / 128, AL.mult, c_(7), AL.add)
-    tt(C("LW"), C("LT"), C("BLK"), AL.subtract); RH = c_(6); ts(RH, M0, -0.5, AL.mult, 0.5, AL.add)
-    asel(C("LS"), C("LW"), [[-1, 128]], AL.not_equal, 512, 0); asel(C("LW"), C("LW"), [[-1, 128]], AL.not_equal, 1024, 0); ms(sub(C("LW"), 0, 128, 16), 0.0)
+        pe([(p, C(x), C(("EJ1", "EK1")[b])) for x in ("EK0", "EJ0")[:2 - b]]); ts(C(("LA01", "LB01")[b]), p, -1.0, AL.mult)
+    DB, M15, ME = [S("COL", 12, 13), S("COL", 13, 14)], S("COL", 16, 17), c_(1)
+    ts(M15, RC, 15.0, AL.is_equal); ts(ME, M15, M0, AL.add); ts(c_(3), ME, 1024.0 + 2057.0 / 8192, AL.mult, -1024.0 - 2057.0 / 8192, AL.add); ts(c_(7), c_(3), M0, AL.subtract)
+    ts(sub(x4, 0, 1), RC, 8.0, AL.mult); mv(sub(x4, 1, 2), RC)
+    for b in range(2): pe([(pb(7, 0, 1), C("EJ%d" % b), sub(x4, 0, 1)), (pb(7, 0, 1), C("EK%d" % b), sub(x4, 1, 2))]); ts(DB[b], pb(7, 0, 1), 1.0 / 128, AL.mult, c_(7), AL.add)
+    RH = c_(6); ts(RH, ME, -0.5, AL.mult, 0.5, AL.add)
+    asel(C("LS"), C("LT"), [[-1, 128]], AL.not_equal, 512, 0); asel(C("LW"), C("LT"), [[-1, 128]], AL.not_equal, 1024, 0)
+    asel(sub(C("LW"), 0, 128, 16), B8c, [[0, 8]], AL.is_ge, 0, 0, 0); iota(sub(C("LW"), 15, 128, 16), [[0, 8]], 0)
+    for a in (0, 320): ts(S("DEC", a, a + 320), S("ONE", 0, 320), M15, AL.mult, -1.0, AL.add)
+    ts(S("NT", 256, 272), S("ONE", 0, 16), M15, AL.mult, 1128.0, AL.mult, flex=False); ts(S("NT", 256, 272), S("NT", 256, 272), -1000.0, AL.add)
+    ts(S("INW", 272, 288), S("IO", 0, 16), 2.0, AL.mult, 2100.0, AL.add); ts(S("IT", 1040, 1056), S("ONE", 0, 16), m_(1), AL.mult, -1.0, AL.mult)
     asel(C("LS8"), C("B8"), [[16, 8], [1, 16]], AL.is_gt, 0, 0, -1); asel(C("LS8"), C("LS8"), [[-1, 128]], AL.not_equal, 512, 0)
     ts(C("I4K"), C("ID"), 1.0 / 4096, AL.mult)
     ts(Zs("e4k"), Zs("en"), 4096.0, AL.mult); ts(Zs("l4k"), Zs("lo8"), 4096.0, AL.mult); DE = sf(64); ts(DE, DGO, 4352.0 - 129, AL.add)
-    cp(Zs("all"), B8c); ts(Zs("nall"), B8c, -1.0, AL.mult); ts(Zs("8k"), B8c, 8192.0, AL.mult)
-    zmake("om", [(5, 1)]); ts(Zs("l17"), Zs("lo8"), 1024.0, AL.mult); zmake("l17", [(0, 0)])
+    cp(Zs("all"), B8c); ts(Zs("won"), B8c, 32768.0, AL.mult); ts(Zs("nwon"), B8c, -32768.0, AL.mult); ts(Zs("8k"), B8c, 8192.0, AL.mult)
+    ts(Zs("odd"), B8c, ODD, AL.mult, 1024.0, AL.mult)
     CV, KD = C("CV"), C("KD")
-    for ch, w, off in ((1, 1, 15), (2, 32, 15), (9, 1, 23), (10, 32, 23)): poke(sub(CV, off, off + 128, 16), ch, w)
+    for ch, w, off in ((2, 1, 15), (4, 32, 15), (10, 1, 23), (12, 32, 23)): poke(sub(CV, off, off + 128, 16), ch, w)
     for x in range(2 - OVD[0], 2):
         m = C("MV%d" % x); ms(m, 0.0)
         for l in range(4):
             y = sub(m, 4 * x + l, 128, 8)
             for c in range(2): asel(y, y, [[-4, 16]], AL.not_equal, 32 ** c, -l - 64 * c)
     for off in (15, 23): poke(sub(KD, off, off + 128, 16), 0, 32768)
-    DW, DOV, DX = sf(32), sf(80), sf(64)
-    ts(DW, sub(DGO, 0, 32), 783.0, AL.add); ts(DX, DGO, 3984.0, AL.add)
+    DW, DOV, DX = S("S16", 464, 480), sf(80), sf(64)
+    ts(DW, sub(DGO, 0, 16), 783.0, AL.add); ts(DX, DGO, 3984.0, AL.add)
     ts(sub(DOV, 0, 64), DGO, -127.0, AL.add); ts(sub(DOV, 64, 80), sub(DGO, 0, 16), 897.0, AL.add)
     AC, QA, QB, C200 = sf(8), sf(8), sh(8), sh(64); ts(AC, sub(DGO, 0, 8), -128.5, AL.add); ms(C200, 200.0); asel(C("LTK"), C("LT"), [[-1, 128]], AL.not_equal, -1000, 0)
-    MD = sf(80); w = 40 // LOTS[0]; LOB, HIB = S("COL", 18, 19), S("COL", 11, 12)
-    for c in range(2 * LOTS[0]): ts(sub(MD, w * c, w * c + w), sub(DGO, w * (c // 2), w * (c // 2) + w), -129.0, AL.add)
-    ts(LOB, M0, 0.25, AL.mult, -0.25, AL.add); ts(HIB, M0, 15.75, AL.mult, 0.25, AL.add)
-    ts(c_(5), M0, -12288.0, AL.mult, 8192.0, AL.add); ts(Zs("yk"), B8c, c_(5), AL.mult, flex=False)
+    MD = sf(80); LOB, HIB = S("COL", 18, 19), S("COL", 11, 12)
+    for c in range(2): ts(sub(MD, 40 * c, 40 * c + 40), sub(DGO, 0, 40), -129.0, AL.add)
+    ts(LOB, ME, 0.25, AL.mult, -0.25, AL.add); ts(HIB, ME, 200.0, AL.mult, 0.25, AL.add)
+    ts(c_(4), M0, -12288.0, AL.mult, 8192.0, AL.add); ts(c_(5), M15, -4096.0, AL.mult, c_(4), AL.add); ts(Zs("yk"), B8c, c_(5), AL.mult, flex=False)
     DS = sf(4); ts(DS, sub(DGO, 0, 4), 383.0, AL.add); ts(sub(A1C, 0, 64), S("IO", 0, 64), A64, AL.add, 1.0, AL.add)
     N896 = sh(64); ms(N896, -896.0)
-    asel(C("GE8"), C("B8"), [[-16, 8], [-1, 16]], AL.is_ge, 0, 0)
-    P2C = S("COL", 5, 6); add("v", lambda e: [e["v"].reciprocal(ap(P2C), ap(PWC))], [PWC], [P2C], 200.0)
-    ts(S("WI", 0, 256), S("IO", 0, 256), P2C, AL.mult, 2048.0, AL.mult); ts(S("WJ", 0, 256), S("WI", 0, 256), 2048, AL.bitwise_and)
-    ts(S("KP"), S("WJ", 0, 256), 0.0, AL.is_equal); pe([(pb(7, 0, 256), C("GE8"), S("KP"))])
-    cp(S("KP"), pb(7, 0, 256))
-    for n in range(8): ts(S("LUT", 256 * n, 256 * n + 256), S("KP"), float(n), AL.is_gt)
     aff("FE0", 8, 1000, 1); aff("FE1", 1008, -1000, 1); aff("DUPE", 8, 0, 1)
-    for h in range(2):
-        m = 320 * h; pe([(pb(6 + h, 0, 320), Yc(1, 9), S("IDB", m, m + 320)), (pb(6 + h, 0, 320), Yc(2, 10), S("IDB", m, m + 320))]); mv(S("NAM", m, m + 320), pb(6 + h, 0, 320))
+    dma("y", [(T["NAM"][c:128:16, :], T["IDB"][c - 8:128:16, 0:640]) for c in (10, 12)] + [(T["NAM"][1:128:2, :], T["ZER"][0:64, 0:640])] +
+        [(T["NAM"][c:128:16, :], T["ZER"][0:8, 0:640]) for c in (0, 2, 4, 6, 8, 14)], [S("IDB"), S("ZER")], [S("NAM")], 200)
     for s_ in range(4):
         for ha in range(2): affw("NP%d%d" % (s_, ha), 8 * ha + 2 * s_, 1, 0, -1.0)
     for ha, (c0, al) in enumerate(((0, 1000), (1000, -1000))):
         affw("SH%d" % ha, c0, al, 1, 8192.0); asel(C("SH%d" % ha), C("SH%d" % ha), [[-16, 8], [-al, 2], [-1, 8]], AL.not_equal, 8192, -c0 - 8)
         affw("NFE%d" % ha, c0 + 8, al, 1, 1.0 / 8192); affw("NFN%d" % ha, c0, al, 1, -1.0)
     for s_ in range(4): affw("NQ%d" % s_, 8 + 2 * s_, 1, 0, 1.0 / 8192)
-    for n, w in (("I512", 512.0), ("I1K", 1024.0), ("I8K", 1.0 / 8192)): affw(n, 0, 8, 1, w)
+    for n, w in (("I9K", 9216.0), ("I8K", 1.0 / 8192), ("N64K", -65536.0)): affw(n, 0, 8, 1, w)
     affw("EN2K", 1000, -1000, 1, 2048.0)
 
     OK_, TG1, TG3, LB1, LB2, GG, TG5 = [sf(64) for _ in range(7)]
     MI, AI, BI, HI_, LO_, B0, B1 = [si(64) for _ in range(7)]
-    CH, CB, CON, BB, DGB, BG, SD, DEAD = [sh(64) for _ in range(8)]
-    INZ = sh(72); ms(DEAD, 0.0); ms(sub(INZ, 0, 1), 0.0); ms(S("INC", 0, 144, 72), 0.0)
+    CH, CB, CON, BB, DGB, BG, SD, DEAD, BC = [sh(64) for _ in range(9)]
+    INZ = sh(72); ms(S("INC", 0, 144, 72), 0.0)
+    for x in (CH, DEAD, sub(INZ, 0, 1)): iota(x, [[0, cols(x)]], 0)
     E = {"nxt": nxt, "prv": prv, "zero_ov": zero_ov, "won": [], "sign": []}
-    for k, w in (("ci", 40), ("c4", 40), ("yi", 40), ("hk", 40), ("rr", 80), ("w0", 64), ("w1", 64)): E[k] = si(w)
-    for k in ("c2", "t2"): E[k] = sf(40)
+    for k, w in (("a8", 40), ("yi", 40), ("hk", 40), ("rr", 80), ("w0", 64), ("w1", 64)): E[k] = si(w)
+    E["t2"] = sf(40)
     for k in ("q0", "q3"): E[k] = sf(128)
     LP, LM = [S("S16", 64 * i, 64 * i + 64) for i in (2, 3)]
-    AL_, HXL, SPL, GOL, UL, CSL, CWL, I2, LUL, OVL, STL, SCL, SXL, SRL, QL = [S("L" + k) for k in LISTS]
+    AL_, HXL, SPL, GOL, UL, CSL, I2, OVL, STL, SXL, SRL, QL = [S("L" + k) for k in LISTS]
     RTW, XW = S("RT"), S("X")
 
     def fold(out, f, src, a, n, more=None):
@@ -491,42 +493,47 @@ def program(ops, T, nxt, prv):
         if t: tt(OK_, pb(2, 0, 64), LIM, AL.add)
         else: mv(OK_, pb(2, 0, 64), -128.0)
         ext(pb(2, 0, 64), [("c0", S("KT", 16, 1040))], 1024); mv(DGB, pb(2, 0, 64), 1.0)
-        for r in range(16):
-            a = 512 * (r % 13); mv(S("G1", a, a + 512), IND(S("KT"), S("LN", 32 * r, 32 * r + 32)))
-            pe([(pb(10), Zs("key", r), S("G1", a, a + 512))], r == 0, r == 15)
+        r = a = 0
+        for w in HOP:
+            if a + 512 * w > 6656: a = 0
+            mv(S("G1", a, a + 512 * w), IND(S("KT"), S("LN", 32 * r, 32 * (r + w))))
+            pe([(pb(10), Zs("key", r + i), S("G1", a + 512 * i, a + 512 * i + 512)) for i in range(w)], r == 0, r + w == 16); r += w; a += 512 * w
 
     def part_a(t):
         tag[:] = ["a", t]
         for h in range(2):
             a, b, k = 512 * h, 512 * h + 512, 2 * h
-            pe([(pb(k), C("ID"), S("IDB", a, b))] + [(pb(k, 64 * r, 64 * r + 64), Yc(8 * h + r, 0), INEL) for r in range(8) if t], True, False, sub(OVL, 0, 40) if t else None)
+            pe([(pb(k), C("ID"), S("IDB", a, b))], True, False, sub(OVL, 0, 40) if t else None)
             pe([(pb(k), C("FK"), S("FL", a, b))], False, True)
             mv(S("KT", 16 + a, 16 + b), pb(k), M3)
         hop(t); tag[0] = "a"
-        for h in range(2): pe([(pb(1 + h), C("DUP"), S("RTH", 512 * h, 512 * h + 512))]); mv(S("RT", 16 + 512 * h, 528 + 512 * h), pb(1 + h))
+        if t < RTG[0]:
+            for h in range(2): pe([(pb(1 + h), C("DUP"), S("RTH", 512 * h, 512 * h + 512))]); mv(S("RT", 16 + 512 * h, 528 + 512 * h), pb(1 + h))
+        else:
+            for a in range(0, 1024, 256): asel(S("RT", 16 + a, 272 + a), S("RTH", a, a + 256), [[0, 256]], AL.is_ge, 0, 0, 0)
+            dma("y", [(T["RT"][16 * g + 8:16 * g + 16, 16:1040], T["RT"][16 * g:16 * g + 8, 16:1040]) for g in range(8)], [S("RT", 16, 1040)], [S("RT", 16, 1040)], 256)
         scan(pb(9), S("RST"), pb(10), 0.0, AL.add, AL.min)
         tt(MI, pb(9, 7, 512, 8), OK_, AL.min); ts(AI, MI, 8, AL.arith_shift_right, 2047, AL.bitwise_and)
         ft = lambda i, h=None: S("FT", 128 * i, 128 * i + 128) if h is None else S("FT", 128 * i + 64 * h, 128 * i + 64 * h + 64)
-        ts(B0, MI, 65536, AL.bitwise_and); ts(B1, MI, 131072, AL.bitwise_and); ts(LO_, MI, 12, AL.arith_shift_right, 15, AL.bitwise_and); ts(HI_, MI, 8, AL.arith_shift_right, 15, AL.bitwise_and)
-        ts(TG1, B1, 1023.0 / 131072, AL.mult, 1.0, AL.add); lp = pb(11, 128, 192); cp(lp, LO_)
-        for h in range(2): ts(pb(11, 64 * h, 64 * h + 64), B0, MC[h], AL.mult, MK[h], AL.add); ts(ft(0, h), HI_, MK[h], AL.mult)
-        for h in range(2): tt(ft(1, h), pb(11, 64 * h, 64 * h + 64), TG1, AL.mult)
-        l2 = pb(11, 192, 256); tt(l2, lp, LO_, AL.mult)
-        for i, x in ((2, lp), (3, l2)):
-            for h in range(2): tt(ft(i, h), x, ft(1, h), AL.mult)
+        ts(LO_, MI, 12, AL.arith_shift_right, 2048 + 15, AL.bitwise_and); ts(HI_, MI, 8, AL.arith_shift_right, 15, AL.bitwise_and); ts(B0, MI, 3 * 65536, AL.bitwise_and)
+        for h in range(2): ts(ft(1, h), LO_, MK[h], AL.mult)
+        act(ft(2), ft(1), AF.Square, 0.0, 256.0); fw = S("S16", 336, 464)
+        for h in range(2): ts(ft(0, h), HI_, MK[h], AL.mult); ts(sub(fw, 64 * h, 64 * h + 64), B0, MC[h], AL.mult, MD_[h], AL.min)
         for h in range(2):
             a, b = 512 * h, 512 * h + 512
             pe([(pb(12), ft(0), S("R1", a, b))]); tt(S("GB", a, b), pb(12), S("J16"), AL.is_equal)
-            for i, n in ((1, "RA"), (2, "RB"), (3, "R1")): pe([(pb(13), ft(i), S(n, a, b))], i == 1, i == 3)
-            relu(S("EQ", a, b), pb(13), -1.0, 0.0, (-1.0, AL.mult, 0.0, AL.max))
+            for i, (x, y) in enumerate(((C("NID"), S("RA")), (ft(1), S("RB", a, b)), (ft(2), S("R1", a, b)), (fw, S("R1", a, b)))): pe([(pb(13), x, y)], i == 0, i == 3)
+            relu(S("EQ", a, b), pb(13), 1.0, -1952.0, (-1952.0, AL.add, 0.0, AL.max))
             pe([(pb(3, 0, 128), S("GB", c, c + 128), S("EQ", c, c + 128)) for c in range(a, b, 128)], h == 0, h == 1)
-        mv(S("HW"), pb(3, 0, 128)); tt(B0, IND(S("HW"), HXL), W32, AL.mult); ts(B1, B0, 31, AL.bitwise_and)
-        tt(CH, B1, DGB, AL.is_equal)
-        ts(AL_, AI, 16.0, AL.add); ts(BI, MI, 255, AL.bitwise_and); ts(BB, BI, -1.0, AL.mult); ts(SD, BI, 0.0, AL.is_gt, 129.0, AL.mult)
+        mv(S("HW"), pb(3, 0, 128)); tt(sub(B0, 0, 48), IND(S("HW"), sub(HXL, 0, 3)), W32, AL.mult); ts(sub(B1, 0, 48), sub(B0, 0, 48), 31, AL.bitwise_and)
+        tt(sub(CH, 8, 56), sub(B1, 0, 48), sub(DGB, 8, 56), AL.is_equal)
+        ts(AL_, AI, 16.0 - 128, AL.add); ts(BI, MI, 255, AL.bitwise_and); ts(BB, BI, -1.0, AL.mult); ts(SD, BI, 0.0, AL.is_gt, 129.0, AL.mult)
+        w2r(1, [(Al, lambda r: BB)])
         for h in range(2):
             a, b, p = 512 * h, 512 * h + 512, pb(4 + h)
-            pe([(p, C("KS"), S("KT", 16 + a, 16 + b))] + [(blk(4, r), Yc(r, 5), BB) for r in range(8 * h, 8 * h + 8)], True, False)
-        ts(LB1, AI, -999.0, AL.add, flex=False); ts(LB2, AI, -1.0, AL.mult, -1001.0, AL.add, flex=False)
+            act(S("TS", a, b), pb(1 + h), AF.Sign, TH)
+            pe([(p, C("KS"), S("KT", 16 + a, 16 + b)), (p, C("TD"), S("TS", a, b))], True, False)
+        ts(LB1, AI, -999.0 - 128, AL.add, flex=False); ts(LB2, AI, -1.0, AL.mult, -1001.0 + 128, AL.add, flex=False)
         INB, p, RK, E1 = sub(INZ, 1, 65), pb(3, 0, 64), S("RKW", 0, 64), S("QR", 128, 256)
         pe([(p, C("BLK"), CH)]); scan(INB, p, C200, 0.0, AL.add, AL.min)
         for c in range(8): act(S("QS", 64 * c, 64 * c + 64), INB, AF.Sign, sub(AC, c, c + 1), -1.0, sub(QA, c, c + 1))
@@ -542,12 +549,12 @@ def program(ops, T, nxt, prv):
         tag[0] = "lab"
         for h in range(2): mv(S("GC", 512 * h, 512 * h + 512), IND(S("CT"), sub(AL_, 32 * h, 32 * h + 32)))
         ext(pb(5, 0, 64), [("c0", S("GC"))], 1024)
-        tt(GG, pb(5, 0, 64), SD, AL.is_lt); ts(CB, pb(5, 0, 64), 128.5, AL.is_lt); tt(CON, CB, GG, AL.subtract)
-        tt(LP, LB1, GG, AL.mult); tt(LM, LB2, GG, AL.mult); tt(DEAD, DEAD, CON, AL.add)
-        if t < 2: ts(INEL, DEAD, 16.0, AL.mult); ts(LIM, DEAD, -2.0 ** 24, AL.mult, -128.0, AL.add)
-        w2r(1, [(Al, lambda r: BB)])
+        GG, CON = pb(5, 64, 128), pb(5, 128, 192)
+        tt(GG, pb(5, 0, 64), SD, AL.is_lt); ts(CB, pb(5, 0, 64), 128.5, AL.is_lt)
+        tt(LP, GG, LB1, AL.mult); tt(LM, GG, LB2, AL.mult); tt(CON, CB, GG, AL.subtract); tt(DEAD, CON, DEAD, AL.add)
+        if t < 2: ts(LIM, DEAD, -2.0 ** 23, AL.mult, -128.0, AL.add)
         for h in range(2):
-            p = pb(1 + h); ts(p, p, PWN, AL.is_equal)
+            p = pb(1 + h); pe([(p, C("DF"), S("TS", 512 * h, 512 * h + 512))])
             tt(S("D2", 512 * h, 512 * h + 512), p, S("RTH", 512 * h, 512 * h + 512), AL.mult)
         extc(pb(1, 0, 64), "en", S("D2")); ts(SPL, pb(1, 0, 64), 2063.0, AL.add)
         w2r(1, [(Al, lambda r: CB)])
@@ -556,24 +563,25 @@ def program(ops, T, nxt, prv):
     def spokes(t):
         tag[0] = "pm"
         for h in range(2): mv(S("XS", 512 * h, 512 * h + 512), IND(XW, sub(SPL, 32 * h, 32 * h + 32)))
-        for b0, tab, lab in ((4, "P", LP), (4, "M", LM)):
-            w2r(b0, [(Al, lambda r, lab=lab: lab), (lambda r: C("IDK"), lambda r: S("XS", r, 1024, 16))])
-            halves(lambda h, a, b, b0=b0, tab=tab: mv(S(tab, 16 + a, 16 + b), pb(b0 + h), 1000.0))
+        for tab, lab, off in (("P", LP, 2048.0 * (t + 1)), ("M", LM, -2048.0 * (t + 1))):
+            for h in range(2):
+                rs, a = range(8 * h, 8 * h + 8), 16 + 512 * h
+                pe([(blk(4, r), C("IDK"), S("XS", r, 1024, 16)) for r in rs] + [(blk(4, r), Al(r), lab) for r in rs]); mv(S(tab, a, a + 512), pb(4 + h), 1000.0 + off)
 
     def part_b(t):
         tag[:] = ["b", t]
         zero_ov(t, CH)
         for h, a in enumerate((896, 0) if t else ()):
             p = pb(6 + h, 0, 128)
-            pe([(p, C("ID"), S("IDB", a, a + 128))] + [(sub(p, 64 * i, 64 * i + 64), Yc(a // 64 + i, 5), BB) for i in range(2)], True, False)
+            pe([(p, C("KS"), S("IDB", a, a + 128)), (p, C("TD"), S("TS", a, a + 128))], True, False)
             pe([(p, C("FK"), S("FLS", 128 * h, 128 * h + 128))], False, True); mv(S("CT", 16 + a, 144 + a), p, M8[t])
         tag[0] = "edge"
         n = 2176 + 640 * t; nch = -(-n // EDW[0]); w = -(-n // (32 * nch)) * 32
         for i, a in enumerate(range(0, n, w)):
             b = min(n, a + w); k = i % 2; ga, zz = S("GA", 16 + a, 16 + b), S("ZZ", 512 * k, 512 * k + b - a)
+            z, x = pb(4 + k, 0, b - a), S("X", 16 + a, 16 + b)
             mv(ga, IND(S("P"), S("EA", a // 16, b // 16)))
             tt(zz, IND(S("M"), S("EB", a // 16, b // 16)), ga, AL.add)
-            z, x = pb(4 + k, 0, b - a), S("X", 16 + a, 16 + b)
             if i % EDGE[t] == 0:
                 act(z, zz, AF.Abs, 0.25, 1024.0); tt(S("WN", a, b), z, x, AL.min); ts(x, S("WN", a, b), 3.0 * 2 ** 22, AL.add, -3.0 * 2 ** 22, AL.add)
                 E["won"].append((t, a, b))
@@ -595,63 +603,57 @@ def program(ops, T, nxt, prv):
         pe([(J(pb(1), s), C("NP%d0" % s), S("G0")) for s in range(4)])
         for x, (j, s) in enumerate(BLOCKS):
             tt(J(S("HE"), x), J(pb(1), s), S("GR", j, 1024, 8), AL.is_equal)
-            if x % 2 or x > 13: pe([(two_(pb(0), int(j > 1)), Zs("ha", PLACE[j, 2 * s]) if j < 2 * s else Zs("hh", PLACE[j, j + 1]), J(S("HE"), y))
+            if x % 2 or x > 13: pe([(two_(pb(0), PLACE[j, 2 * s + 1][0]), Zs("ha", PLACE[j, 2 * s][1]) if j < 2 * s else Zs("hh", PLACE[j, j + 1][1]), J(S("HE"), y))
                                     for y, (j, s) in list(enumerate(BLOCKS))[x - (x < 14):x + 1]], False, x == 15)
-        pe([(pb(2, 0, 128), Yc(4, j), S("IT", 16 + j, 1040, 8)) for j in range(8)]); ts(DG, pb(2, 0, 128), -1.0, AL.mult)
+        pe([(pb(2, 0, 128), Yc(1, j), S("IT", 16 + j, 1040, 8)) for j in range(8)]); ts(DG, pb(2, 0, 128), -1.0, AL.mult, -9.0, AL.add)
         pe([(two_(pb(7), b, 256 * e_), C(("EJ%d", "EK%d")[e_] % b), DG) for e_ in range(2) for b in range(2)], True, False)
         relu(S("WB", 0, 256), pb(0, 0, 256), 1.0, -1.0, (1.5, AL.is_gt))
         pe([(two_(pb(7), b, 256 * e_), C("L%s%d%d" % ("AB"[e_], c, b)), two_(S("WB"), c)) for e_ in range(2) for c, b in ((0, 0), (0, 1), (1, 1))], False, True)
         relu(S("PR", 0, 256), pb(7, 0, 256), -200.0, 50.0, (0.25, AL.is_lt, 100.0, AL.mult)); tt(S("SV", 0, 256), pb(7, 256, 512), S("PR", 0, 256), AL.is_gt)
         relu(S("R"), pb(7), 1.0, RH, (RH, AL.add, 0.0, AL.max))
         pe([(pb(3, 0, 256), C("BLK"), S("SV", 0, 256))]); scan(S("INW", 16, 272), pb(3, 0, 256), S("IO", 656, 912), 0.0, AL.add, AL.min)
-        z2 = sub(TG3, 0, 16)
-        ext(pb(2, 0, 16), [("all", S("SV", 0, 256))], 256); ts(S("SV", 256, 272), pb(2, 0, 16), 0.0, AL.is_equal, 4096.0, AL.mult)
-        pe([(pb(3, 0, 16), Yc(0, r), S("INW", 15 + r, 271, 16)) for r in range(16)] + [(pb(3, 0, 16), C("ID"), S("SV", 256, 272))])
+        em = S("S16", 480, 496)
+        pe([(pb(2, 0, 16), C("ID"), DW)] + [(pb(2, 0, 16), Zs("nwon", r), S("SV", r, 256, 16)) for r in range(16)]); ts(em, pb(2, 0, 16), 0.0, AL.max)
+        pe([(pb(3, 0, 17), Yc(0, r), S("INW", 15 + r, 287, 16)) for r in range(16)] + [(pb(3, 0, 16), C("ID"), em)])
         p = pb(0, 0, 256)
-        pe([(p, C("IDK"), S("R", 0, 256)), (p, C("I8K"), S("R", 256, 512)), (p, C("LW"), S("SV", 0, 256)), (p, C("ID"), S("INW", 16, 272))])
+        pe([(two_(p, b), Yc(0, 15), S("IOB")) for b in range(2)] + [(p, C("IDK"), S("R", 0, 256)), (p, C("I8K"), S("R", 256, 512)), (p, C("LW"), S("SV", 0, 256))])
         for b in range(2): mv(S("NT", b, 256, 2), pb(0, b, 256, 2), DB[b])
-        tt(z2, pb(3, 0, 16), sub(DW, 0, 16), AL.min); cp(sub(CSL, 0, 16), z2)
-        iota(S("WW", 0, 640), [[0, 640]], 0); iota(S("WV", 0, 640), [[0, 640]], 0)
-        put(IND(S("WW"), sub(CSL, 8, 16)), S("IO", 160, 288)); cp(IND(S("WV"), sub(CSL, 0, 8)), S("IO", 32, 160))
-        scan(S("CW"), S("WV", 0, 640), S("WW", 0, 640), 0.0, AL.max, AL.max)
-        ext(pb(3, 0, 40), [("c0", S("CW"))], 640); ts(CWL, pb(3, 0, 40), -32.0, AL.add)
-        ci, c4, yi, hk, rr, c2, t2 = [E[k] for k in ("ci", "c4", "yi", "hk", "rr", "c2", "t2")]
-        vl, i2, t3, cv, tot = S("UM", 0, 80), S("UM", 80, 160), S("S16", 0, 80), S("S16", 80, 120), S("COL", 17, 18); w = 40 // LOTS[0]; c0 = 136 + 40 * t; ids = S("S16", 256, 336)
-        ts(tot, S("INW", 271, 272), 0.0, AL.add); ts(vl, MD, tot, AL.is_lt); ts(i2, MD, tot, AL.is_ge); tt(t3, i2, DOV, AL.mult)
-        ts(ci, pb(3, 0, 40), 0.5, AL.mult, -16.25, AL.add); ts(sub(c2, 0, 40), ci, 8.0, AL.mult, 1.0, AL.add)
-        for c in range(LOTS[0]):
-            one = lambda x: sub(x, w * c, w * c + w); end = lambda x, e_, k=1: sub(x, k * w * (2 * c + e_), k * w * (2 * c + e_ + 1)); all_ = lambda x, k=1: sub(x, 2 * k * w * c, 2 * k * w * (c + 1))
-            yc, p, GL = S("YC", 16 * w * c, 16 * w * (c + 1)), pb(3, 64, 64 + w), S(("GB", "EQ")[c % 2], 0, 640)
-            tt(one(cv), one(c2), end(vl, 0), AL.mult)
-            tt(yc, IND(S("NT", 0, 256), one(CWL)), S("IO", 16 * w * c, 16 * w * (c + 1)), AL.subtract); ts(yc, yc, LOB, AL.max, HIB, AL.min)
-            pe([(p, C("I512"), one(cv))] + [(p, Zs("yk", r), sub(yc, r, 16 * w, 16)) for r in range(16)])
-            ts(end(I2, 0), p, 1.0 / 512, AL.mult, 75.0 - 0.499, AL.add); ts(one(yi), p, 30720.0, AL.add)
-            ts(one(hk), one(yi), 6, AL.arith_shift_right, 7, AL.bitwise_and); tt(one(t2), one(hk), one(cv), AL.add); ts(end(I2, 1), one(t2), 15.0, AL.add)
-            ts(end(rr, 0), one(yi), 3, AL.arith_shift_right, 7, AL.bitwise_and); ts(end(rr, 1), one(yi), 7, AL.bitwise_and); ts(all_(S("R2")), all_(rr), 256.0, AL.mult)
-            parts = [(end, 0), (end, 1)] if LOTS[0] == 1 else [(lambda x, e_, k=1: all_(x, k), 0)]
-            for a, b in ((0, w // 2), (w // 2, w), (w, 2 * w)): cp(sub(all_(S("GI"), 16), 16 * a, 16 * b), IND(S("IT"), sub(all_(I2), a, b)))
-            for f_, e_ in parts:
-                gi, b = f_(S("GI"), e_, 16), 17 + c + e_; m = cols(gi); p, q = pb(b, 0, m // 16), pb(b, 64, 64 + m // 16); gl = GL if LOTS[0] > 1 else S(("GB", "EQ")[e_], 0, 640)
-                pe([(p, C("ID"), f_(S("R2"), e_))] + [(p, Zs("om", r), sub(gi, r, m, 16)) for r in range(16)]); cp(f_(LUL, e_), p)
-                for a in range(0, m, 8 * w * (1 + e_)): mv(sub(gl, a, a + 8 * w * (1 + e_)), IND(S("LUT"), sub(f_(LUL, e_), a // 16, a // 16 + w * (1 + e_) // 2)))
-                if e_ == 0:
-                    y = pb(0, 128, 128 + 2 * w); pe([(y, C("ID"), all_(vl))] + [(y, Zs("id", r), sub(all_(S("GI"), 16), r, 32 * w, 16)) for r in range(16)]); cp(all_(ids), y)
-                    for x in range(2): ts(S(("EA", "EB")[x], c0 + w * c, c0 + w * c + w), sub(y, w * x, w * x + w), 14.0, AL.add)
-                pe([(q, C("I1K"), f_(i2, e_)), (q, C("ID"), f_(t3, e_)), (q, C("ID"), f_(ids, e_))] + [(q, Zs("l17", r), sub(gl, r, m, 16)) for r in range(16)])
-                ts(f_(OVL, e_), q, -2.0, AL.add)
-            for e_ in range(2): tt(IND(S("OV"), end(OVL, e_)), end(S("GI"), 1 - e_, 16), S("NAM", 16 * w * c, 16 * w * (c + 1)), AL.add)
+        cp(sub(CSL, 0, 17), pb(3, 0, 17))
+        yc, p = S("YC"), pb(3, 64, 104)
+        iota(S("WW", 0, 640), [[0, 640]], -1000); cp(IND(S("WW"), sub(CSL, 0, 17)), S("NT", 0, 272))
+        scan(yc, S("DEC"), S("WW", 0, 640), -1000.0, AL.add, AL.max); ts(yc, yc, LOB, AL.max, HIB, AL.min)
+        ext(p, [("yk", yc)], 640)
+        a8, yi, hk, rr, t2 = [E[k] for k in ("a8", "yi", "hk", "rr", "t2")]
+        i2, t3, tot, ids, c0 = S("UM", 80, 160), S("S16", 0, 80), S("COL", 17, 18), S("S16", 256, 336), 136 + 40 * t
+        end = lambda x, e_, k=1: sub(x, 40 * k * e_, 40 * k * e_ + 40 * k)
+        ts(tot, S("INW", 271, 272), 0.0, AL.add); ts(i2, MD, tot, AL.is_ge); tt(t3, i2, DOV, AL.mult)
+        ts(yi, p, 28672.0, AL.add); ts(end(I2, 0), p, 1.0 / 512, AL.mult, 72.0 - 0.499, AL.add)
+        ts(end(rr, 0), yi, 3, AL.arith_shift_right, 7, AL.bitwise_and); ts(end(rr, 1), yi, 7, AL.bitwise_and); ts(S("R2"), rr, -1.0, AL.mult, -1.0, AL.add)
+        ts(hk, yi, 6, AL.arith_shift_right, 7, AL.bitwise_and); ts(a8, yi, 9, AL.arith_shift_right, 2040, AL.bitwise_and); tt(t2, hk, a8, AL.add); ts(end(I2, 1), t2, 16.0, AL.add)
+        for a in range(0, 80, 20): cp(S("GI", 16 * a, 16 * a + 320), IND(S("IT"), sub(I2, a, a + 20)))
+        GL = lambda a, b: S("GB", a, b) if b <= 640 else S("EQ", a - 640, b - 640)
+        for k, (a, b) in enumerate(((0, 512), (512, 1024), (1024, 1280))):
+            pe([(pb(22 + k, r, b - a, 16), Al(r), S("R2", a // 16, b // 16)) for r in range(16)])
+            for c, d in ((a, b),) if k != 1 else ((512, 640), (640, 1024)): tt(GL(c, d), pb(22 + k, c - a, d - a), S("GI", c, d), AL.is_ge)
+        y = pb(0, 128, 208); ext(y, [("id", S("GI"))], 1280); cp(ids, y)
+        for x in range(2): ts(S(("EA", "EB")[x], c0, c0 + 40), end(y, x), 15.0, AL.add)
+        for e_ in range(2):
+            q, gl = pb(17 + e_, 0, 40), GL(640 * e_, 640 * e_ + 640)
+            pe([(q, C("I9K"), end(i2, e_)), (q, C("ID"), end(t3, e_))] + [(q, Zs("odd", r), sub(gl, r, 640, 16)) for r in range(16)] + [(q, C("ID"), end(ids, e_))])
+            ts(end(OVL, e_), q, -1025.0, AL.add)
+        for e_ in range(2): tt(IND(S("OV"), end(OVL, e_)), end(S("GI"), 1 - e_, 16), S("NAM"), AL.add)
         tag[0] = "new"
         YY = S("GA", 16 + n, 656 + n)
         mv(YY, IND(S("P"), S("EA", c0, c0 + 40))); tt(S("XB"), IND(S("M"), S("EB", c0, c0 + 40)), YY, AL.add); ts(S("X", 16 + n, 656 + n), S("XB"), 1024.0, AL.mult, 255.0, AL.min)
         tag[0] = "rows"
         p = pb(19, 0, 64)
-        pe([(p, C("ID"), N896)] + [(p, C(m % h), S(x, 896 + 64 * h, 960 + 64 * h)) for h in range(2) for m, x in (("FN%d", "RTH"), ("NFN%d", "D2"))], True, False, sub(LUL, 0, 40))
+        pe([(p, C("ID"), N896)] + [(p, C(m % h), S(x, 896 + 64 * h, 960 + 64 * h)) for h in range(2) for m, x in (("FN%d", "RTH"), ("NFN%d", "D2"))], True, False, ids)
         pe([(p, Zs("id", 8 * h + l), S("OV", 1024 * l + 896 + 64 * h, 1024 * l + 960 + 64 * h)) for l in range(8) for h in range(2)], False, True)
         for x in range(2 - OVD[0], 2):
-            dma("y", [(T[("WV", "OVT")[x]][64 * c:64 * c + 64, 0:1024], T["OV"][c + 1:128:8, 4096 * x:4096 * x + 4096]) for c in range(2)],
+            dma("y", [(T[("WV", "OVT")[x]][64 * c:64 * c + 64, 0:1024], T["OV"][2 * c + 2:128:8, 4096 * x:4096 * x + 4096]) for c in range(2)],
                 [S("OV", 4096 * x, 4096 * x + 4096)], [S(("WV", "OVT")[x], 0, 1024)], 256)
         for part in (((pb(6, 0, 128), 896, 1024), (pb(6, 128, 256), 0, 128)), ((pb(1, 0, 384), 128, 512),), ((pb(2, 0, 384), 512, 896),)):
-            pe([m for p, a, b in part for m in [(p, C("ID"), S("RTH", a, b)), (p, C("NID"), S("D2", a, b))]], True, False, sub(OVL, 0, 40) if t == 2 and len(part) == 1 else sub(LUL, 0, 40))
+            pe([m for p, a, b in part for m in [(p, C("ID"), S("RTH", a, b)), (p, C("NID"), S("D2", a, b))]], True, False, sub(OVL, 0, 40) if t == 2 and len(part) == 1 else ids)
             far = OVD[0] if len(part) == 1 or OVD[1] else 0
             pe([(p, sub(C("CV"), 15 - l, 143 - l), S("OV", 1024 * l + a, 1024 * l + b)) for p, a, b in part for l in range(8 - 4 * far)] +
                [(p, C("MV%d" % x), S(("WV", "OVT")[x], a, b)) for p, a, b in part for x in range(2 - far, 2)], False, True)
@@ -664,15 +666,15 @@ def program(ops, T, nxt, prv):
 
     def middles(t):
         tag[0] = "mid"
-        n = 2176 + 640 * t; y = pb(0, 0, 256); mm = []
+        n = 2176 + 640 * t; y = pb(0, 0, 256); mm = [(y, C("N64K"), S("ONE", 0, 256))]
         for r in range(16):
             a, b, c = 256 * r, min(max(n, 256 * r), 256 * r + 256), min(max(n + 640, 256 * r), 256 * r + 256)
-            if b > a: mm.append((pb(0, 0, b - a), Zs("all", r), S("WN", a, b)))
+            if b > a: mm.append((pb(0, 0, b - a), Zs("won", r), S("WN", a, b)))
             for t_, d, f in E["won"]:
-                if t_ == t and min(f, b) > max(d, a): mm.append((pb(0, max(d, a) - a, min(f, b) - a), Zs("nall", r), S("X", 16 + max(d, a), 16 + min(f, b))))
-            if c > b: mm.append((pb(0, b - a, c - a), Zs("all", r), S("ONE", 0, c - b)))
+                if t_ == t and min(f, b) > max(d, a): mm.append((pb(0, max(d, a) - a, min(f, b) - a), Zs("nwon", r), S("X", 16 + max(d, a), 16 + min(f, b))))
+            if c > b: mm.append((pb(0, b - a, c - a), Zs("won", r), S("ONE", 0, c - b)))
         for i in range(0, len(mm), 4): pe(mm[i:i + 4], i == 0, i + 4 >= len(mm))
-        ts(y, y, 8.5 / 4, AL.is_gt, 2048.0 * (t + 1), AL.mult); tt(y, y, S("GAW"), AL.add); tt(S("ENC"), y, S("ENC"), AL.max)
+        tt(y, y, S("GAW"), AL.min); tt(S("ENC"), y, S("ENC"), AL.max)
 
     def send(src, dst, k, to, by):
         o = add("g", lambda e: [e["g"].remote_dma(ap(dst), ap(src), T.sem["a%d" % k], T.sem["o%d" % k], E[to][1], E[to][0], E[to][2])], [src], [], 300.0, send=("o%d" % k, E[to][3]))
@@ -693,7 +695,7 @@ def program(ops, T, nxt, prv):
 
         def number(s_, bk):
             FLG, INC, TG, p, y = flg[s_], inc(s_), S("TG", 8 * s_, 8 * s_ + 4), pb(bk, 0, 64), pb(bk, 0, 4)
-            q0 = sub(E["q0"], 64 * s_, 64 * s_ + 4); SW = S("SW", 576 * s_, 576 * s_ + 576); w = sub(SW, 0, 512)
+            q0 = sub(E["q0"], 64 * s_, 64 * s_ + 4)
             pe([(p, C("BLK"), FLG)]); scan(INC, S("ONE", 0, 64), p, 0.0, AL.mult, AL.add)
             if NUM[s_] == "p":
                 ext(pb(13, 0, 4), [("all", FLG)], 64); ts(TG, pb(13, 0, 4), 0.0, AL.is_equal, 1024.0, AL.mult)
@@ -701,18 +703,17 @@ def program(ops, T, nxt, prv):
             else:
                 TG = S("TG", 16 + 64 * s_, 80 + 64 * s_); ts(p, p, 0.0, AL.is_equal); tt(p, p, S("IO", 512, 576), AL.mult); tt(TG, p, sub(INC, -1, 63), AL.max)
                 ext(y, [("c0", TG)], 64); cp(H2(STL, s_, 4), y)
-            iota(w, [[0, 512]], 0); cp(IND(SW, H2(STL, s_, 4)), S("IOB", 0, 64)); scan(H2(S("SC"), s_, 512), w, w, 0.0, AL.max, AL.max)
-            ext(pb(bk, 0, 32), [("c0", H2(S("SC"), s_, 512))], 512); cp(H2(SCL, s_, 32), pb(bk, 0, 32))
 
         def names(s_, bk):
             NE, w0, w1, q2 = H2(S("NE"), s_, 512), H2(E["w0"], s_, 32), H2(E["w1"], s_, 32), sub(E["q3"], 64 + 32 * s_, 96 + 32 * s_)
-            tt(NE, IND(H2(S("NUS"), s_), H2(SCL, s_, 32)), S("IO", 0, 512), AL.subtract); ts(NE, NE, -0.5, AL.max, 0.5, AL.min)
-            ext(pb(bk, 0, 32), [("8k", NE)], 512); ts(w0, pb(bk, 0, 32), 65536.0 - 2033, AL.add); ts(w1, w0, 8191, AL.bitwise_and)
+            SW = S("SW", 576 * s_, 576 * s_ + 576); w = sub(SW, 0, 512)
+            iota(w, [[0, 512]], 1000); cp(IND(SW, H2(STL, s_, 4)), H2(S("NUS"), s_)); scan(NE, S("ONE"), w, 1000.0, AL.add, AL.min); ts(NE, NE, -0.5, AL.max, 0.5, AL.min)
+            ext(pb(bk, 0, 32), [("8k", NE)], 512); ts(w0, pb(bk, 0, 32), -1.0, AL.mult, 65536.0 - 2033, AL.add); ts(w1, w0, 8191, AL.bitwise_and)
             if s_: ts(S("Lsh"), w1, 4112.0, AL.min)
             tt(q2, w1, H2(DX, s_, 32), AL.min); cp(H2(SXL, s_, 32), q2)
         tag[0] = "own"
         number(0, 3); p = pb(3, 64, 128)
-        pe([(p, C("NFE%d" % ha), rows(0, ha)) for ha in range(2)] + [(p, C("LS"), flg[0]), (p, C("ID"), inc(0))]); mv(H2(S("NUS"), 0), p, -513.0)
+        pe([(p, C("NFE%d" % ha), rows(0, ha)) for ha in range(2)] + [(p, C("LS"), flg[0])]); ts(H2(S("NUS"), 0), p, -1.0, AL.mult, 512.0, AL.add)
         names(0, 3)
         for h in range(2): mv(H2(SND, h, 256), IND(XW, H2(SXL, h, 16)))
         send(H2(SND, 0, 512), H2(RX, 1, 512), 3 * t + 1, "nxt", "prv")
@@ -725,9 +726,9 @@ def program(ops, T, nxt, prv):
         ts(S("PRS", 512, 1024), pb(7), -0.5, AL.max, 0.5, AL.min)
         pe([(pb(7, 0, 64), C("SH%d" % ha), S("PRS", 512 + 128 * s + 64 * ha, 576 + 128 * s + 64 * ha)) for s in range(4) for ha in range(2)])
         ts(S("WI", 0, 64), pb(7, 0, 64), 32768.0, AL.add); ts(S("WJ", 0, 64), S("WI", 0, 64), 8191, AL.bitwise_and)
-        q3 = sub(E["q3"], 0, 64); ts(q3, S("WJ", 0, 64), 1.0 / 8192, AL.mult, -513.5, AL.add)
+        q3 = sub(E["q3"], 0, 64); ts(q3, S("WJ", 0, 64), -1.0 / 8192, AL.mult, 512.5, AL.add)
         number(1, 6)
-        pe([(pb(7, 0, 64), C("LS"), flg[1]), (pb(7, 0, 64), C("ID"), inc(1))]); tt(H2(S("NUS"), 1), pb(7, 0, 64), q3, AL.add)
+        pe([(pb(8, 0, 64), C("LS"), flg[1])]); tt(H2(S("NUS"), 1), q3, pb(8, 0, 64), AL.subtract)
         names(1, 6)
         for h in range(2): mv(sub(SND, 512 + 256 * h, 768 + 256 * h), IND(XW, S("Lsh", 16 * h, 16 * h + 16)))
         send(H2(SND, 1, 512), H2(RX, 0, 512), 3 * t + 2, "prv", "nxt")
@@ -737,9 +738,9 @@ def program(ops, T, nxt, prv):
         RX = S("RX", 1024 * (t % 2), 1024 * (t % 2) + 1024)
         GT, SG, MN, GX = S("EQS"), S("OH"), S("SC"), S("SRG")
         if t == 2:
-            ts(S("W5"), S("IO", 0, 512), 1100.0, AL.add); put(IND(S("GA", 0, 5152), sub(SXL, 0, 32)), S("W5"))
-            for h in range(2): cp(S("D2", 512 * h, 512 * h + 512), IND(S("GA", 0, 4112), sub(SRL, 32 * h, 32 * h + 32)))
-            ext(pb(5, 0, 64), [("c0", S("D2"))], 1024); ts(sub(SRL, 0, 64), pb(5, 0, 64), -1084.0, AL.add, 15.0, AL.max); ms(S("KT", 15, 16), 1.0)
+            iota(S("W5"), [[1, 512]], 31100); put(IND(S("GA", 0, 5152), sub(SXL, 0, 32)), S("W5"))
+            for h in range(2): ts(S("D2", 512 * h, 512 * h + 512), IND(S("GA", 0, 4112), sub(SRL, 32 * h, 32 * h + 32)), -31000.0, AL.add, 0.0, AL.max)
+            ext(pb(5, 0, 64), [("c0", S("D2"))], 1024); ts(sub(SRL, 0, 64), pb(5, 0, 64), -84.0, AL.add, 15.0, AL.max); ms(S("KT", 15, 16), 1.0)
         for s_ in (1, 0):
             a, b, p = 512 * s_, 512 * s_ + 512, pb(7 - s_)
             pe([(p, C("ID"), sub(SND, a, b))])
@@ -752,7 +753,7 @@ def program(ops, T, nxt, prv):
                 if s_: act(S("W6"), p, AF.Identity, 8.5, -1.0); put(IND(S("GA", 0, 5152), L), S("W6"))
                 else: signs = S("KT", 0, 528); ts(S("KT", 16, 528), p, -1.0, AL.mult, 8.5, AL.add)
             for h in range(2): mv(sub(GX, 2 * a + 512 * h, 2 * a + 512 * h + 512), IND(signs, sub(SRL, 64 * s_ + 32 * h, 64 * s_ + 32 * h + 32)))
-            k_, a, p = S("KP", 128 * s_, 128 * s_ + 128), base[s_], pb(7 - s_, 0, 128)
+            a, p = base[s_], pb(7 - s_, 0, 128)
             pe([(p, sub(C("KD"), 15 - l, 143 - l), sub(GX, 1024 * s_ + l, 1024 * s_ + 1024, 8)) for l in range(8)])
             if t == 2:
                 ts(p, p, -1.0, AL.max); tt(S("ZZ", a, a + 128), p, S("ZZ", a, a + 128), AL.min); c, d = (896, 1024) if a else (0, 896)
@@ -770,7 +771,7 @@ def program(ops, T, nxt, prv):
         if t < 2: part_a(t + 1)
         middles(t)
         if t == 2:
-            cp(S("WI", 256, 512), S("ENC")); ts(S("WJ", 256, 512), S("WI", 256, 512), 2047, AL.bitwise_and); ts(S("GAW"), S("WJ", 256, 512), -1.0, AL.add)
+            ts(S("WJ", 256, 512), S("ENC"), 2047, AL.bitwise_and); ts(S("GAW"), S("WJ", 256, 512), -1.0, AL.add)
             dma("y", [(T["ymid"][:, :], T["GAW"][:, :])], [S("GAW")], [], 200)
             for x in E["sign"]: act(x, x, AF.Abs)
             ts(BG, DEAD, -8192.0, AL.mult)
@@ -937,6 +938,9 @@ def tiles(ops):
 
 
 def ties(ops):
+    if "tails" in ops[0]:
+        for o in ops: o["deps"], o["order"] = set(o["first"][0]), set(o["first"][1])
+        return ops[0]["tails"]
     last = {}
     for i, o in enumerate(ops):
         deps, order = set(), set()
@@ -962,8 +966,9 @@ def ties(ops):
                 if name.startswith("pb"): l[:] = [x for x in l if x[0] == i or (o["q"] != "p" and ops[x[0]]["q"] in ("p", o["q"]))]
                 l.append((i, kind, m, bm))
         if "after" in o: order.add([k for k in range(i) if ops[k] is o["after"]][0])
-        o["deps"], o["order"] = deps, order - deps
-    return {k: sorted(set(x[0] for x in l)) for k, l in last.items() if k.startswith("pb")}
+        o["deps"], o["order"] = deps, order - deps; o["first"] = (set(deps), order - deps)
+    ops[0]["tails"] = {k: sorted(set(x[0] for x in l)) for k, l in last.items() if k.startswith("pb")}
+    return ops[0]["tails"]
 
 
 def later(ops, res):

import numpy as np
from concourse.mybir import AluOpType as AL, ActivationFunctionType as AF

F, H, B, I, U = "float32", "float16", "bfloat16", "int32", "uint16"
SB = {
    "RAW": (2048, I), "X": (5152, B), "RT": (1056, F), "RTH": (1024, H), "TA": (1024, F), "TB": (1024, F), "FL": (1024, B), "FLS": (256, B),
    "G1": (6800, B), "LN": (512, U), "KT": (1040, B), "CT": (1040, B), "IT": (1056, B), "GR": (1024, F), "HE": (2048, B),
    "P": (1040, F), "M": (1040, F), "GA": (7584, F), "OV": (9472, B), "EQ": (1024, B), "D2": (1024, H), "GB": (1024, B),
    "GC": (1024, B), "XS": (1024, B), "IDB": (1024, B), "R1": (1024, B), "RA": (512, B), "RB": (1024, B), "J16": (512, B), "FT": (512, B), "HW": (128, F), "IO": (1056, F),
    "IOB": (128, B), "ALL": (2048, B), "Y": (2304, B), "Z": (144 * 17, B), "CM": (128 * 68, B), "ONE": (512, B), "RST": (512, B),
    "TS": (1024, B), "DEC": (640, B), "EA": (256, U), "EB": (256, U), "ENC": (256, I), "GAW": (256, F), "WN": (3456, H), "ZZ": (1024, F), "WV": (1040, B),
    "SF": (1792, F), "SI": (1024, I), "SH": (1024, B), "SU": (400, U), "S16": (512, H), "W5": (512, F), "W6": (512, F), "WI": (512, I), "WJ": (512, I),
    "WB": (512, B), "R": (512, B), "PR": (512, B), "SV": (512, B), "INW": (288, H), "NT": (272, F), "WW": (2144, F), "CW": (640, H),
    "YC": (640, H), "GI": (1280, B), "G0": (128, H), "XB": (640, B), "RKW": (80, B), "QS": (512, B), "QR": (256, B),
    "TP": (576, B), "TR": (384, B), "EQS": (1024, B), "PRS": (1024, H), "NUS": (128, F), "INC": (144, H), "TG": (144, H),
    "SW": (1152, F), "SC": (1024, B), "OH": (1024, B), "NE": (1024, H), "SND": (3072, B), "RX": (2048, B), "OVT": (1024, B), "COL": (32, F), "COI": (16, I), "ZER": (1024, B),
}
LISTS = {"a": 64, "hx": 4, "sp": 64, "go": 8, "u": 64, "cs": 18, "i2": 80, "ov": 80, "st": 8, "sx": 64, "sr": 128, "q": 8}
SB["Lsh"] = (32, U)
for _k, _n in LISTS.items():
    SB["L" + _k] = (_n, U)
SB.update({"SRG": (2048, B), "SM": (3072, B), "SND": (1024, B), "O0": (128, I), "NAM": (640, B), "ZB": (1024, B), "R2": (80, B), "UM": (160, B)})
ALIAS = {"WI": ("RAW", 1024), "WJ": ("RAW", 1536), "SI": ("RAW", 0), "TA": ("P", 16), "TB": ("GA", 6560), "ZZ": ("GA", 6560), "WW": ("GA", 4352), "GC": ("GB", 0), "EQS": ("SM", 0), "OH": ("SM", 1024),
         "SC": ("SM", 2048), "NE": ("PRS", 0),
         "ZB": ("SRG", 0), "HE": ("G1", 2560), "WB": ("G1", 4752), "R": ("G1", 5264), "PR": ("G1", 5776), "SV": ("G1", 6288)}
SCRATCH = {k: ("sbuf", [128, n], d) for k, (n, d) in SB.items() if k not in ALIAS}
for _b in range(8):
    SCRATCH["pb%d" % _b] = ("psum", [128, 512], F)
ND = 40
SEMAPHORES = ["cv", "cs", "cp", "cg"] + ["o%d" % i for i in range(9)] + ["d%d" % i for i in range(ND)] + ["a%d" % i for i in range(9)]
SIZE = {F: 4, H: 2, B: 2, I: 4, U: 2}
CYC, PEC, LAT, FIX = 0.84, 0.39, 180.0, [12.0]
PEN = [1.0, 50.0]
EDGE = [1, 1, 99]
DMA, XF = [1300.0, 300.0], [1.0]
OVD = [2, 0]
NEAR, JIT = [3], [10.0]
CUT, EDW = [1100], [448]
WIN = [150, 200]
HOP = [1, 1] + [2] * 6 + [1, 1]
RTG = [0]
NUM = "vp"
BLOCKS = [(j, s) for s in range(4) for j in range(2 * s + 1)]
PLACE = {jk: (d // 14, d % 14 + 1) for d, jk in enumerate((j, k) for j in range(8) for k in range(j + 1, 8))}
PASSES, AGAIN = [900, 60, 20000], [(0, 120, 30000)]
PLAN, SEED, TEMP, OWN, TRIES = {}, [7], [250.0], [2.0], [120, 90.0]
SEATS, ROOM = [12], [1500.0, 300.0]
GUESS = [({"o": 1, "g": 0.78, "s": 0.6, "p": 1.05, "x": 0.9}, 200.0, 1.0), ({"o": 1.1, "g": 1.3, "s": 1.6, "p": 1.0, "x": 1.1}, 130.0, 1.0)]
BIAS = {"ends0": 8000.0}
GAT, SCA = 1.56, 3.2


def S(n, a=0, b=None, st=1):
    b = SB[n][0] if b is None else b
    n, o = ALIAS.get(n, (n, 0))
    return (n, a + o, b + o, st)


def IND(w, o):
    return ("ind", w, o)


def cols(x):
    return 16 * cols(x[2]) if x[0] == "ind" else len(range(x[1], x[2], x[3]))


def masks(x):
    n, a, b, st = x
    per = 4 if n.startswith("pb") else 16 // SIZE[SB[n][1]]
    if st == 1:
        m = ((1 << (b - a)) - 1) << a
    else:
        m = 0
        for c in range(a, b, st):
            m |= 1 << c
    lo, hi = a // per, (b - 1) // per
    return n, m, ((1 << (hi - lo + 1)) - 1) << lo


def program(ops, T, nxt, prv):
    def ap(x):
        if x[0] == "ind":
            return ap(x[1]).indirect(ap(x[2]))
        t = T[NOW.get(x[0], x[0])]
        return t[:, x[1]:x[2]] if x[3] == 1 else t[:, x[1]:x[2]:x[3]]

    tag = ["", 0]

    def flat(xs):
        out = []
        for x in xs:
            if isinstance(x, tuple):
                out += [x[1], x[2]] if x[0] == "ind" else [x]
        return out

    def add(q, fn, rd, wr, cost, **kw):
        r, w = flat(rd), []
        for x in wr:
            if x[0] == "ind":
                w.append(x[1]); r.append(x[2])
            else:
                w.append(x)
        kind = q if q in ("p", "x") else "s" if any(x[0] == "ind" for x in wr) else "g" if any(isinstance(x, tuple) and x[0] == "ind" for x in rd) else "o"
        if kind == "o" and q in ("v", "s", "vs") and "dma" not in kw:
            cost += FIX[0]
            if "cs" in kw: kw["cs"] += FIX[0]
        o = dict(q=q, fn=fn, tag=tag[0] + str(tag[1]), kind=kind, rd=[masks(x) for x in r], wr=[masks(x) for x in w], cost=cost)
        o.update(kw); ops.append(o)
        return o

    def two(*xs):
        return all(not x[0].startswith("pb") and SIZE[SB[x[0]][1]] == 2 for x in xs)

    def fl(*xs):
        return all(x[0] != "ind" and (x[0].startswith("pb") or SB[x[0]][1] in (F, B)) for x in xs)

    def aff_ok(out, a, s1, op0, op1):
        return fl(out, a[1] if a[0] == "ind" else a) and not (isinstance(s1, tuple) and s1[0].startswith("pb")) and ((op0 == AL.mult and op1 in (None, AL.add)) or (op0 == AL.add and op1 is None))

    def vcost(out, a, f):
        if out[0] == "ind": return 50 + cols(out) * SCA * CYC
        if a[0] == "ind": return 50 + cols(a) * GAT * CYC
        return max(64, cols(out) * f) * CYC

    def sc(x):
        return ap(x) if isinstance(x, tuple) else x

    def tt(out, a, b, op):
        f = 1 if (a[0].startswith("pb") or b[0].startswith("pb")) else 2
        add("v", lambda e: [e["v"].tensor_tensor(ap(out), ap(a), ap(b), op)], [a, b], [out], vcost(out, a, f))

    def ts(out, a, s1, op0, s2=None, op1=None, flex=True):
        flex = flex and aff_ok(out, a, s1, op0, op1)
        if flex:
            def fa(e):
                if e["pick"] == "v": return fn(e)
                if op0 == AL.add: return [e["s"].activation(ap(out), ap(a), AF.Identity, bias=sc(s1))]
                if op1 is None: return [e["s"].activation(ap(out), ap(a), AF.Identity, scale=sc(s1))]
                return [e["s"].activation(ap(out), ap(a), AF.Identity, bias=sc(s2), scale=sc(s1))]
            add("vs", fa, [a, s1, s2], [out], vcost(out, a, 0.5 if a[0] != "ind" and two(out, a) else 1), cs=vcost(out, a, 1) + 15)

        def fn(e):
            if op1 is None: return [e["v"].tensor_scalar(ap(out), ap(a), sc(s1), None, op0)]
            return [e["v"].tensor_scalar(ap(out), ap(a), sc(s1), sc(s2), op0, op1)]
        if not flex:
            add("v", fn, [a, s1, s2], [out], vcost(out, a, 0.5 if a[0] != "ind" and two(out, a) else 1))

    def cp(out, a):
        if out[0] != "ind" and fl(out, a[1] if a[0] == "ind" else a): return mv(out, a)
        add("v", lambda e: [e["v"].tensor_copy(ap(out), ap(a))], [a], [out], vcost(out, a, 0.5 if a[0] != "ind" and out[0] != "ind" and two(out, a) else 1))

    def ms(out, c):
        n = cols(out); one = S("ONE", 0, n); cost = max(64, n * (0.5 if two(out) else 1)) * CYC
        if not fl(out) or n > 512 or out[0] == "ONE": return add("v", lambda e: [e["v"].memset(ap(out), c)], [], [out], cost)
        fn = lambda e: [e["v"].memset(ap(out), c) if e["pick"] == "v" else e["s"].activation(ap(out), ap(one), AF.Identity, scale=c)]
        add("vs", fn, [one], [out], cost, cs=max(64, n) * CYC + 15)

    def scan(out, d0, d1, init, op0, op1):
        add("v", lambda e: [e["v"].tensor_tensor_scan(ap(out), ap(d0), ap(d1), sc(init), op0, op1)], [d0, d1, init], [out], max(64, cols(out) * (0.5 if two(out, d0, d1) else 1)) * CYC)

    def act(out, a, func, bias=0.0, scale=1.0, total=None):
        if total: return add("s", lambda e: [e["s"].activation(ap(out), ap(a), func, bias=sc(bias), scale=sc(scale), accum_out=ap(total))], [a, bias], [out, total], vcost(out, a, 1) + 35)
        add("s", lambda e: [e["s"].activation(ap(out), ap(a), func, bias=sc(bias), scale=sc(scale))], [a, bias, scale], [out], vcost(out, a, 1) + 15)

    def mv(out, a, bias=None, q="vs"):
        def fn(e):
            if e["pick"] == "s":
                if bias is None: return [e["s"].activation(ap(out), ap(a), AF.Copy)]
                return [e["s"].activation(ap(out), ap(a), AF.Identity, bias=sc(bias))]
            if bias is None: return [e["v"].tensor_copy(ap(out), ap(a))]
            return [e["v"].tensor_scalar(ap(out), ap(a), sc(bias), None, AL.add)]
        add(q, fn, [a, bias], [out], vcost(out, a, 0.5 if a[0] != "ind" and two(out, a) else 1), cs=vcost(out, a, 1) + 15)

    def relu(out, a, scale, bias, vec):
        def fn(e):
            if e["pick"] == "s": return [e["s"].activation(ap(out), ap(a), AF.Relu, bias=sc(bias), scale=scale)]
            if len(vec) == 2: return [e["v"].tensor_scalar(ap(out), ap(a), vec[0], None, vec[1])]
            return [e["v"].tensor_scalar(ap(out), ap(a), sc(vec[0]), vec[2], vec[1], vec[3])]
        add("vs", fn, [a, bias], [out], vcost(out, a, 0.5 if two(out, a) else 1), cs=vcost(out, a, 1) + 15)

    def flags(out, a):
        fn = lambda e: [e["s"].activation(ap(out), ap(a), AF.Sign) if e["pick"] == "s" else e["v"].tensor_scalar(ap(out), ap(a), 0.0, None, AL.is_gt)]
        add("vs", fn, [a], [out], vcost(out, a, 1), cs=vcost(out, a, 1) + 15)

    def put(out, a):
        add("s", lambda e: [e["s"].activation(ap(out), ap(a), AF.Silu)], [a], [out], vcost(out, a, 1) + 15)

    def pe(mm, first=True, last=True, when=None):
        n = len(mm)
        st = [(first if i == 0 else len(m) > 3) for i, m in enumerate(mm)]
        sp = [(last if i == n - 1 else len(mm[i + 1]) > 3) for i in range(n)]
        part, c = [], 0
        for i, m in enumerate(mm):
            part.append(i); c += max(64, cols(m[0])) * (4 if SB[m[2][0]][1] == F else 1)
            if c >= CUT[0] or i == n - 1:
                add("p", lambda e, part=part: [e["p"].matmul(ap(mm[i][0]), ap(mm[i][1]), ap(mm[i][2]), st[i], sp[i]) for i in part],
                    [mm[i][1] for i in part] + [mm[i][2] for i in part] + [when], [mm[i][0] for i in part], c * PEC + (60 if i == n - 1 else 10),
                    cont=[b for b, s in {mm[i][0][0]: st[i] for i in part[::-1]}.items() if not s])
                part, c = [], 0

    def iota(out, pat, base, cm=0):
        kw = {} if SB[out[0]][1] == I else {"allow_small_or_imprecise_dtypes": True}
        add("g", lambda e: [e["g"].iota(ap(out), pat, base, cm, **kw)], [], [out], 160 + 2 * cols(out) * CYC)

    def asel(out, a, pat, op, fill, base, cm=1):
        add("g", lambda e: [e["g"].affine_select(ap(out), ap(a), pat, op, float(fill), base, cm)], [a], [out], 210 + 2 * cols(out) * CYC)

    def dma(q, pairs, rd, wr, kb, **kw):
        c = 60.0 * len(pairs); w = max(c, kb * 1024 / DMA[1])
        add(q, lambda e: [e[q].dma_start(o, i, **kw) for o, i in pairs], rd, wr, w if q == "y" else c + (1000.0 if q == "g" else 0.0), dma=DMA[0] + (0 if q == "y" else w - c))

    def pb(b, a=0, e=512, st=1):
        return ("pb%d" % b, a, e, st)

    def pool(name):
        pos = [0]
        def take(n):
            a = pos[0]; pos[0] += n + (-n) % 8
            assert pos[0] <= SB[name][0], name
            return S(name, a, a + n)
        return take
    sf, si, sh, su = pool("SF"), pool("SI"), pool("SH"), pool("SU")

    def sub(x, a, b, st=1):
        return (x[0], x[1] + a, x[1] + b, st)
    cmn, zn = {}, {}

    def C(n):
        i = cmn.setdefault(n, len(cmn)); return S("CM", 128 * i, 128 * i + 128)

    def Zs(n, c=None, off=15):
        i = zn.setdefault(n, len(zn))
        if c is None: return S("Z", 144 * i + off, 144 * i + off + 128, 16)
        return S("Z", 144 * i + 15 - c, 144 * i + 143 - c)

    def Yc(r, c):
        return S("Y", 144 * r + 15 - c, 144 * r + 143 - c)

    def Al(r):
        return S("ALL", 128 * r, 128 * r + 128)

    def lh(z, r):
        return Yc(0, r) if z == "c0" else S("YF", 15 - r, 143 - r) if z == "f0" else Zs(z, r)

    def ext(out, parts, n):
        pe([(out, lh(z, r), sub(src, r, n, 16)) for z, src in parts for r in range(16)])

    def extc(out, z, src, more=()):
        pe([(out, lh(z, r), sub(src, 64 * r, 64 * r + 64)) for r in range(16)] + list(more))

    def blk(b0, r):
        return pb(b0 + r // 8, 64 * (r % 8), 64 * (r % 8) + 64)

    def w2r(b0, parts):
        for h in range(2): pe([(blk(b0, r), lf(r), rf(r)) for r in range(8 * h, 8 * h + 8) for lf, rf in parts])

    def halves(fn):
        for h in range(2): fn(h, 512 * h, 512 * h + 512)

    nb, en = T["nb"], T["en"]
    RAW = T["RAW"]
    dma("y", [(RAW[:, 0:512], nb[:, :]), (RAW[:, 512:1024], en[:, :])] +
        [(RAW[16 * g:16 * g + 16, 1024:1536], nb[16 * (g ^ 1):16 * (g ^ 1) + 16, :]) for g in range(8)], [], [S("RAW", 0, 1536)], 1024)
    dma("s", [(RAW[16 * g:16 * g + 16, 1536:2048], en[16 * (g ^ 1):16 * (g ^ 1) + 16, :]) for g in range(8)], [], [S("RAW", 1536, 2048)], 512)
    RC, HQ, M3, NTB, A64 = [S("COL", i, i + 1) for i in range(5)]
    M8, M9 = [S("COL", c, c + 1) for c in (3, 8, 9)], [S("COL", 24 + t, 25 + t) for t in range(3)]
    ONE = S("ONE", 0, 128)
    ms(S("ONE", 0, 512), 1.0); ms(S("ZER"), 0.0)
    o0 = S("O0", 0, 64); iota(o0, [[2, 32], [1024, 2]], 0, 64)
    iota(S("COI", 0, 1), [[0, 1]], 0, 1)
    blank = ["CV", "CV2", "KD", "KD2", "FK"]
    for n in blank: C(n)
    ms(S("Z", 0, 432), 0.0); ms(C("FK"), 0.0); w = 128 * len(blank) - 128
    for l in ([("Y", 0, 1024), ("Y", 1024, 2048), ("Y", 2048, 2304)], [("Z", 432, 1440), ("Z", 1440, 2448), ("CM", 0, w)]):
        dma("y", [(T[n][:, a:b], T["ZER"][:, 0:b - a]) for n, a, b in l], [S("ZER"), S("RAW")], [S(*x) for x in l], 576)
    ts(S("COI", 1, 2), S("COI", 0, 1), 15, AL.bitwise_and); cp(RC, S("COI", 1, 2))
    ts(S("COI", 2, 3), S("COI", 0, 1), 4, AL.arith_shift_right, 1, AL.bitwise_and); cp(HQ, S("COI", 2, 3))
    ts(S("COI", 3, 4), S("COI", 0, 1), 8, AL.bitwise_and); ts(A64, S("COI", 3, 4), 8.0, AL.mult)
    ODD, NB_, M12 = S("COL", 27, 28), S("COL", 28, 29), S("COL", 29, 30)
    ts(S("COI", 8, 9), S("COI", 0, 1), 1, AL.bitwise_and); cp(ODD, S("COI", 8, 9)); ts(NB_, RC, 0.5, AL.mult, -9.0, AL.add); ts(NB_, NB_, ODD, AL.mult); ts(M12, RC, 12.0, AL.is_equal)
    for t in range(3): ts(M8[t], M12, 4.0 + 20.0 * t, AL.mult, NB_, AL.add)
    o1 = S("O0", 64, 128); ts(o1, o0, 2047, AL.bitwise_and); o2 = su(64); ts(o2, o1, HQ, AL.add)

    def aff(name, c0, al, be, src=ONE):
        asel(C(name), src, [[-16, 8], [-al, 2], [-be, 8]], AL.is_equal, 0, -c0)

    def affw(name, c0, al, be, w):
        asel(C(name), S("ZER", 0, 128), [[-16, 8], [-al, 2], [-be, 8]], AL.not_equal, w, -c0)

    def poke(x, ch, w):
        asel(x, x, [[-16, 8]], AL.not_equal, w, -ch)

    def zmake(name, ws, off=15):
        for ch, w in ws: poke(Zs(name, None, off), ch, w)
    aff("DUP", 0, 0, 1); aff("ID", 0, 8, 1); aff("FN0", 0, 1000, 1); aff("FN1", 1000, -1000, 1)
    M0 = S("COL", 6, 7); ts(M0, RC, 0.0, AL.is_equal); x5 = sf(8); m_ = lambda i: sub(x5, i, i + 1)
    ts(m_(1), RC, 2.0, AL.is_equal); ts(m_(2), RC, 4.0, AL.is_equal)
    ts(m_(3), RC, -7.5, AL.add); ts(m_(4), m_(3), m_(3), AL.mult, 36.0, AL.is_gt); ts(S("TP", 0, 64), S("ONE", 0, 64), m_(4), AL.mult, 16.0, AL.mult)
    iota(S("TP", 64, 128), [[0, 2], [1, 32]], 1); iota(S("TP", 128, 192), [[1, 2], [0, 32]], 0); ts(S("TP", 128, 192), S("TP", 128, 192), RC, AL.add, RC, AL.add)
    dma("y", [(T["IDB"][2 * c:128:16, :], T["TP"][:, 64 * c:64 * c + 64]) for c in range(3)] + [(T["IDB"][1:128:2, :], T["ZER"][0:64, :])] +
        [(T["IDB"][c:128:16, :], T["ZER"][0:8, :]) for c in range(6, 16, 2)], [S("TP", 0, 192), S("ZER"), S("RAW")], [S("IDB")], 300)
    asel(S("Y", 15, 2304, 16), S("ONE", 0, 144), [[-1, 16], [-16, 9]], AL.is_equal, 0, 0)
    asel(C("BLK"), ONE, [[-16, 8], [0, 16]], AL.is_ge, 0, 0); asel(C("BLK"), C("BLK"), [[16, 8], [0, 16]], AL.is_ge, 0, 15, -1)
    B8c = sub(C("BLK"), 0, 128, 16)
    asel(Zs("lo8"), B8c, [[16, 8]], AL.is_ge, 0, 7, -1)
    zmake("key", [(0, 2048 * 256), (2, 256), (4, 32 * 256)])
    DGO, A1C = sf(64), sf(64)
    HLF = S("COL", 10, 11); ts(HLF, m_(1), 0.5, AL.mult)
    t0 = sf(8)
    ts(M3, m_(2), 4.0, AL.mult, HLF, AL.subtract)
    for t in range(3): ts(M9[t], M8[t], M3, AL.subtract)
    for k in range(8): ms(S("RST", k, 512, 8), -float(2 ** (k - 1)) if k else 1.0e8)
    for n, c in (("KT", 16.0), ("CT", 0.0), ("IT", 0.0), ("RT", 0.0), ("X", 0.0), ("INW", 0.0)):
        ms(S(n, 0, 16), c)
    ts(S("KT", 15, 16), M0, 31.0, AL.mult)
    ts(C("NE2K"), C("FN1"), -2048.0, AL.mult)

    def f0(h, a, b):
        x, y = S("D2", a, b), S("PRS", a, b)
        ts(x, IND(S("RAW"), sub(o2, 32 * h, 32 * h + 32)), -999.0, AL.add)
        add("v", lambda e: [e["v"].transpose(ap(y), ap(x))], [x], [y], 256 * CYC + FIX[0])
        ts(S("FL", a, b), y, -999.5, AL.is_gt)
        pe([(pb(1 + h), C("ID"), y), (pb(1 + h), C("NE2K"), S("FL", a, b))])
        ts(S("RTH", a, b), pb(1 + h), 1000.0, AL.add)
    halves(f0)
    iota(S("IO"), [[1, 1056]], 0); cp(S("IOB"), S("IO", 0, 128))
    for k in range(4):
        asel(S("ALL", 512 * k, 512 * k + 512), S("ONE", 0, 512), [[-1, 4], [-16, 8], [0, 16]], AL.is_equal, 0, -4 * k)
    halves(lambda h, a, b: (pe([(pb(7), C("DUP"), S("ALL", a, b))]), ts(S("R1", a, b), pb(7), -1.0, AL.mult)))
    for j in range(16): ts(S("RB", j, 1024, 16), S("R1", j, 1024, 16), -131072.0 * j, AL.mult)
    iota(S("J16"), [[0, 32], [-1, 16]], 0); act(S("RA"), S("J16"), AF.Square, 0.0, 256.0)
    MK, MC, MD_, W32, LIM = [S("COL", 19, 20), S("COL", 20, 21)], [S("COL", 21, 22), S("COL", 22, 23)], [S("COL", 23, 24), S("COL", 30, 31)], sf(48), sf(64)
    ts(MK[0], RC, 7.5, AL.is_lt); ts(MK[1], RC, 7.5, AL.is_gt)
    for h in range(2): ts(MC[h], MK[h], -992.0 / 65536, AL.mult); ts(MD_[h], MK[h], -1953.0, AL.mult)
    for d in range(3): ms(sub(W32, 16 * d, 16 * d + 16), 32.0 ** -d)
    iota(S("COI", 4, 8), [[0, 4]], 0, 1); cp(S("Lhx"), S("COI", 4, 8))
    zmake("id", [(2, 1), (4, 32)])
    x6 = sf(32); TH = sub(x6, 23, 24)
    ts(sub(x6, 0, 8), S("IO", 1, 17, 2), RC, AL.is_equal, -1.5, AL.mult); tt(sub(x6, 8, 16), sub(x6, 0, 8), S("RST", 0, 8), AL.mult); ts(sub(x6, 24, 25), M0, 1000.0, AL.mult, 0.75, AL.add)
    scan(sub(x6, 16, 24), sub(x6, 8, 16), sub(x6, 8, 16), sub(x6, 24, 25), AL.max, AL.max)
    affw("DF", 1, 0, 2, -0.5); asel(C("DF"), C("DF"), [[-16, 8], [0, 2], [-2, 8]], AL.not_equal, 0.5, -3)
    for w, ch in ((0.0, 17), (0.5, 0)): asel(sub(C("DF"), 7, 128, 8), sub(C("DF"), 7, 128, 8), [[-16, 8], [0, 2]], AL.not_equal, w, -ch)
    ts(C("TD"), C("ID"), ODD, AL.mult, 0.5, AL.mult)

    ts(C("NID"), C("ID"), -1.0, AL.mult); ts(C("IDK"), C("ID"), 1.0 / 1024, AL.mult)
    RC1 = S("COL", 7, 8); ts(RC1, RC, 1.0, AL.add)
    ms(S("RKW", 64, 80), 1000.0); ms(S("RT", 1040, 1056), 0.0); ts(Zs("rc"), B8c, RC, AL.mult, flex=False)
    iota(S("ENC"), [[0, 256]], 2048)
    cp(sub(C("FK"), 0, 128, 16), Zs("lo8")); y = sub(C("FK"), 1, 128, 2)
    asel(y, S("ONE", 0, 64), [[-16, 8], [-1, 8]], AL.is_ge, 0, 0); asel(y, y, [[16, 8], [0, 8]], AL.is_ge, 0, 7, -1)
    ts(sub(t0, 0, 1), RC, 0.5, AL.is_gt); ts(C("KS"), C("ID"), sub(t0, 0, 1), AL.mult)
    ts(S("CT", 15, 16), M0, 1000.0, AL.mult)
    tag[0] = "ends"
    ms(S("GR", 0, 272), 0.0); ms(S("GR", 272, 544), 0.0)
    dma("y", [(T["GA"][:, a:a + 544], T["GR"][:, 0:544]) for a in range(0, 2176, 544)], [S("GR", 0, 544), S("RAW")], [S("GA", 0, 2176)], 1088)
    dma("y", [(T["GA"][c:128:16, 2176:4352], T["GR"][:, 0:136]) for c in range(2)], [S("GR", 0, 136), S("RAW")], [S("GA", 2176, 4352)], 140)
    tag[0] = ""
    dma("y", [(T["X"][:, 16:2192], T["lens"][:, :])] + [(T["X"][:, a:b], T["ZER"][:, 0:b - a]) for a, b in ((2192, 3216), (3216, 4240), (4240, 5152))],
        [S("ZER"), S("Y", 0, 8), S("Z", 432, 440)], [S("X", 16, 5152)], 1284)
    ms(S("X", 4112, 4113), 300.0)

    def zero_ov(t, when):
        if t: dma("y", [(T["OV"][c:128:8, 0:8192], T["ZER"][:, :]) for c in (2, 4)], [S("ZER"), when], [S("OV", 0, 8192)], 512)
        else: dma("y", [(T["OV"][:, a:min(a + 1920, 8192)], T["X"][:, 2192:2192 + min(1920, 8192 - a)]) for a in range(0, 8192, 1920)], [S("X", 2192, 4112), when], [S("OV", 0, 8192)], 2048)

    def ends():
        tag[0] = "ends"
        f, TT, CL, PL, SL = S("SM", 0, 1024), S("ZZ"), S("SU", 64, 200), S("SU", 200, 336), S("SU", 336, 400)
        cn, em, st, ex, ML, AB = sh(64), sh(64), S("S16", 64, 128), sf(72), sf(136), S("COL", 14, 15)
        ms(sub(ex, 0, 1), -1088.0); iota(ML, [[16, 136]], 0); ts(ML, ML, RC, AL.add); ts(AB, RC, 1.0, AL.is_equal, 16416.0, AL.mult)
        iota(S("M", 16, 1040), [[1, 1024]], 1024); iota(S("W5", 0, 128), [[1, 128]], 2048)
        for h in range(2):
            a, b = 512 * h, 512 * h + 512
            pe([(pb(14 + h), C("DUP"), S("RTH", a, b))]); tt(sub(f, a, b), pb(14 + h), S("IO", 1 + a, 1 + b), AL.is_gt)
        p = pb(14, 0, 64)
        ext(p, [("lo8", f)], 1024); cp(cn, p); ts(em, p, 0.0, AL.is_equal, 8192.0, AL.mult)
        pe([(p, C("BLK"), cn)]); scan(sub(ex, 1, 65), S("ONE", 0, 64), p, -1088.0, AL.mult, AL.add)
        pe([(p, C("LT"), cn)]); tt(st, p, sub(ex, 0, 64), AL.add)
        pe([(p, C("ID"), st), (p, C("ID"), em)]); ts(p, p, 1088.0, AL.add); tt(S("W6", 0, 64), p, DE, AL.min); cp(SL, S("W6", 0, 64))
        for h in range(2):
            a, b, p = 512 * h, 512 * h + 512, pb(14 + h)
            pe([(p, C("LS8"), sub(f, a, b)), (p, C("I4K"), S("RTH", a, b))] + [(sub(p, r, 512, 16), Al(r), sub(st, 32 * h, 32 * h + 32)) for r in range(16)])
            mv(sub(TT, a, b), p, 576.0)
            put(IND(S("GA", 0, 5376), sub(SL, 32 * h, 32 * h + 32)), S("IO", 32 + a, 32 + b))
        for i, (a, b) in enumerate(((0, 1024), (1024, 2176))):
            c, d = a // 16, b // 16; p = pb(14, 0, d - c)
            scan(S("WN", a, b), S("GA", a, b), S("GA", a, b), sub(ex, 66 + i, 67 + i) if a else 0.0, AL.max, AL.max)
            if b < 2176: cp(sub(ex, 67 + i, 68 + i), S("WN", b - 1, b))
            ext(p, [("c0", S("WN", a, b))], b - a); ts(sub(CL, c, d), p, -32.0, AL.add, 0.0, AL.max)
        for lot in ((0, 512), (1024, 1536, 2048)):
            c, d = lot[0] // 16, min(136, lot[-1] // 16 + 32); p = pb(16, 0, d - c); part = []
            for a in lot:
                b = min(2176, a + 512); k = a % 1024; q = pb(15, 0, b - a)
                y, src = S("CW" if a == 2048 else "PRS", k, k + b - a), S("P", 16 + k, 16 + k + b - a) if a < 2048 else S("W5", 128, 256)
                tt(y, IND(TT, sub(CL, a // 16, b // 16)), (S("IO", a, b), S("M", a - 1008, b - 1008), S("W5", 0, 128))[a // 1024], AL.subtract); ts(y, y, -0.5, AL.max, 0.5, AL.min)
                if k: ext(sub(p, 0, 64), [("e4k", S("PRS"))], 1024)
                elif a == 2048: ext(sub(p, 64, 72), [("e4k", y)], 128)
                pe([(q, Zs("l4k", 1), y), (q, Yc(0, 0), S("WN", a, b))]); mv(src, q, AB); part.append((sub(PL, a // 16, b // 16), src))
            w0, w1, w2, x0, x1 = S("WI", 256, 256 + d - c), S("WI", 336, 336 + d - c), S("WI", 416, 416 + d - c), S("W6", 272, 272 + d - c), S("W6", 400, 400 + d - c)
            ts(w0, p, 65535.0, AL.add); ts(w1, w0, 4095, AL.bitwise_and); ts(w2, w1, 4, AL.arith_shift_right)
            ts(x0, w2, 136.0, AL.min, -2175.0, AL.mult); ts(p, w1, 2175.0, AL.min, 136.0, AL.mult); tt(x0, p, x0, AL.add)
            ts(p, w1, 4000.0, AL.is_lt, 2176.0, AL.mult); tt(x0, p, x0, AL.add); tt(x1, x0, sub(ML, c, d), AL.max); cp(sub(PL, c, d), x1)
            for l, src in part: put(IND(S("GA", 0, 4352), l), src)
        dma("y", [(T["W6"][:, 136 * c:136 * c + 136], T["GA"][c:128:16, 2176:4352]) for c in range(2)], [S("GA", 2176, 4352)], [S("W6", 0, 272)], 240)
        ts(S("EA", 0, 136), S("W6", 0, 136), -15.8, AL.add, 15.0, AL.max)
        ts(S("WJ", 256, 392), S("W6", 136, 272), -32.0, AL.add); ts(S("WI", 256, 392), S("WJ", 256, 392), 4095, AL.bitwise_and); ts(S("EB", 0, 136), S("WI", 256, 392), -2033.0, AL.add, 1039.0, AL.min)
    for n in ("P", "M"): iota(S(n, 0, 16), [[0, 16]], 0); iota(S(n, 15, 16), [[0, 1]], 30000)
    asel(Zs("en"), B8c, [[-16, 8]], AL.is_ge, 0, -8)
    asel(C("LT"), C("BLK"), [[16, 8], [1, 16]], AL.is_gt, 0, 0, -1)
    iota(DGO, [[16, 64]], 129); ts(DGO, DGO, RC, AL.add)
    ts(Zs("ha"), Zs("lo8"), -2.0, AL.mult); ts(Zs("ha", None, 16), Zs("en"), -2.0, AL.mult); ts(Zs("hh"), Zs("en"), -2.0, AL.mult)
    asel(C("B8"), ONE, [[-8, 16], [0, 8]], AL.is_ge, 0, 0); asel(C("B8"), C("B8"), [[8, 16], [0, 8]], AL.is_ge, 0, 7, -1)
    x3 = sf(16); c_ = lambda i: sub(x3, i, i + 1); x4 = sh(8)
    ts(c_(0), RC, -0.5, AL.mult, 7.5, AL.add); ts(c_(2), RC, -1.0, AL.mult, 7.0, AL.add); ts(C("EK1"), C("BLK"), -100.0, AL.mult, 100.0, AL.add)
    p = pb(7, 0, 128); pe([(p, C("ID"), C("EK1")), (p, C("NID"), S("J16", 0, 128))]); mv(C("D16"), p)
    for c in (0, 15): iota(sub(C("D16"), c, 128, 16), [[0, 8]], 100)
    for b in range(2):
        EJ, EK, c1, c3, c4 = C("EJ%d" % b), C("EK%d" % b), c_(8 + b), c_(10 + b), c_(12 + b)
        ts(c1, c_(0), RC, AL.mult, 1.0 - 14 * b, AL.add); ts(c3, c_(2), c1, AL.add); ts(c4, c1, -1.0, AL.mult, RC1, AL.add); ts(C("KL"), C("BLK"), c4, AL.mult)
        ts(EK, C("D16"), c1, AL.is_ge, MK[0], AL.mult); ts(p, C("D16"), c3, AL.is_lt); tt(EJ, p, EK, AL.mult)
        pe([(p, C("KL"), EJ), (p, C("ID"), C("D16"))]); ts(EK, p, RC, AL.is_equal, MK[0], AL.mult)
    asel(C("LN"), C("LT"), [[-1, 128]], AL.not_equal, -8.5, 0); ts(C("LN"), C("LN"), -1.0, AL.mult)
    for b in range(2):
        pe([(p, C("EJ%d" % b), C("EJ%d" % b)), (p, C("EK%d" % b), C("EJ%d" % b))]); tt(C("LA%d%d" % (b, b)), p, C("LN"), AL.mult)
        pe([(p, C("EK%d" % b), C("EK%d" % b))]); tt(C("LB%d%d" % (b, b)), p, C("LN"), AL.mult)
        pe([(p, C(x), C(("EJ1", "EK1")[b])) for x in ("EK0", "EJ0")[:2 - b]]); ts(C(("LA01", "LB01")[b]), p, -1.0, AL.mult)
    DB, M15, ME = [S("COL", 12, 13), S("COL", 13, 14)], S("COL", 16, 17), c_(1)
    ts(M15, RC, 15.0, AL.is_equal); ts(ME, M15, M0, AL.add); ts(c_(3), ME, 1024.0 + 2057.0 / 8192, AL.mult, -1024.0 - 2057.0 / 8192, AL.add); ts(c_(7), c_(3), M0, AL.subtract)
    ts(sub(x4, 0, 1), RC, 8.0, AL.mult); mv(sub(x4, 1, 2), RC)
    for b in range(2): pe([(pb(7, 0, 1), C("EJ%d" % b), sub(x4, 0, 1)), (pb(7, 0, 1), C("EK%d" % b), sub(x4, 1, 2))]); ts(DB[b], pb(7, 0, 1), 1.0 / 128, AL.mult, c_(7), AL.add)
    RH = c_(6); ts(RH, ME, -0.5, AL.mult, 0.5, AL.add)
    asel(C("LS"), C("LT"), [[-1, 128]], AL.not_equal, 512, 0); asel(C("LW"), C("LT"), [[-1, 128]], AL.not_equal, 1024, 0)
    asel(sub(C("LW"), 0, 128, 16), B8c, [[0, 8]], AL.is_ge, 0, 0, 0); iota(sub(C("LW"), 15, 128, 16), [[0, 8]], 0)
    for a in (0, 320): ts(S("DEC", a, a + 320), S("ONE", 0, 320), M15, AL.mult, -1.0, AL.add)
    ts(S("NT", 256, 272), S("ONE", 0, 16), M15, AL.mult, 1128.0, AL.mult, flex=False); ts(S("NT", 256, 272), S("NT", 256, 272), -1000.0, AL.add)
    ts(S("INW", 272, 288), S("IO", 0, 16), 2.0, AL.mult, 2100.0, AL.add); ts(S("IT", 1040, 1056), S("ONE", 0, 16), m_(1), AL.mult, -1.0, AL.mult)
    asel(C("LS8"), C("B8"), [[16, 8], [1, 16]], AL.is_gt, 0, 0, -1); asel(C("LS8"), C("LS8"), [[-1, 128]], AL.not_equal, 512, 0)
    ts(C("I4K"), C("ID"), 1.0 / 4096, AL.mult)
    ts(Zs("e4k"), Zs("en"), 4096.0, AL.mult); ts(Zs("l4k"), Zs("lo8"), 4096.0, AL.mult); DE = sf(64); ts(DE, DGO, 4352.0 - 129, AL.add)
    cp(Zs("all"), B8c); ts(Zs("won"), B8c, 32768.0, AL.mult); ts(Zs("nwon"), B8c, -32768.0, AL.mult); ts(Zs("8k"), B8c, 8192.0, AL.mult)
    ts(Zs("odd"), B8c, ODD, AL.mult, 1024.0, AL.mult)
    CV, KD = C("CV"), C("KD")
    for ch, w, off in ((2, 1, 15), (4, 32, 15), (10, 1, 23), (12, 32, 23)): poke(sub(CV, off, off + 128, 16), ch, w)
    for x in range(2 - OVD[0], 2):
        m = C("MV%d" % x); ms(m, 0.0)
        for l in range(4):
            y = sub(m, 4 * x + l, 128, 8)
            for c in range(2): asel(y, y, [[-4, 16]], AL.not_equal, 32 ** c, -l - 64 * c)
    for off in (15, 23): poke(sub(KD, off, off + 128, 16), 0, 32768)
    DW, DOV, DX = S("S16", 464, 480), sf(80), sf(64)
    ts(DW, sub(DGO, 0, 16), 783.0, AL.add); ts(DX, DGO, 3984.0, AL.add)
    ts(sub(DOV, 0, 64), DGO, -127.0, AL.add); ts(sub(DOV, 64, 80), sub(DGO, 0, 16), 897.0, AL.add)
    AC, QA, QB, C200 = sf(8), sf(8), sh(8), sh(64); ts(AC, sub(DGO, 0, 8), -128.5, AL.add); ms(C200, 200.0); asel(C("LTK"), C("LT"), [[-1, 128]], AL.not_equal, -1000, 0)
    MD = sf(80); LOB, HIB = S("COL", 18, 19), S("COL", 11, 12)
    for c in range(2): ts(sub(MD, 40 * c, 40 * c + 40), sub(DGO, 0, 40), -129.0, AL.add)
    ts(LOB, ME, 0.25, AL.mult, -0.25, AL.add); ts(HIB, ME, 200.0, AL.mult, 0.25, AL.add)
    ts(c_(4), M0, -12288.0, AL.mult, 8192.0, AL.add); ts(c_(5), M15, -4096.0, AL.mult, c_(4), AL.add); ts(Zs("yk"), B8c, c_(5), AL.mult, flex=False)
    DS = sf(4); ts(DS, sub(DGO, 0, 4), 383.0, AL.add); ts(sub(A1C, 0, 64), S("IO", 0, 64), A64, AL.add, 1.0, AL.add)
    N896 = sh(64); ms(N896, -896.0)
    aff("FE0", 8, 1000, 1); aff("FE1", 1008, -1000, 1); aff("DUPE", 8, 0, 1)
    dma("y", [(T["NAM"][c:128:16, :], T["IDB"][c - 8:128:16, 0:640]) for c in (10, 12)] + [(T["NAM"][1:128:2, :], T["ZER"][0:64, 0:640])] +
        [(T["NAM"][c:128:16, :], T["ZER"][0:8, 0:640]) for c in (0, 2, 4, 6, 8, 14)], [S("IDB"), S("ZER")], [S("NAM")], 200)
    for s_ in range(4):
        for ha in range(2): affw("NP%d%d" % (s_, ha), 8 * ha + 2 * s_, 1, 0, -1.0)
    for ha, (c0, al) in enumerate(((0, 1000), (1000, -1000))):
        affw("SH%d" % ha, c0, al, 1, 8192.0); asel(C("SH%d" % ha), C("SH%d" % ha), [[-16, 8], [-al, 2], [-1, 8]], AL.not_equal, 8192, -c0 - 8)
        affw("NFE%d" % ha, c0 + 8, al, 1, 1.0 / 8192); affw("NFN%d" % ha, c0, al, 1, -1.0)
    for s_ in range(4): affw("NQ%d" % s_, 8 + 2 * s_, 1, 0, 1.0 / 8192)
    for n, w in (("I9K", 9216.0), ("I8K", 1.0 / 8192), ("N64K", -65536.0)): affw(n, 0, 8, 1, w)
    affw("EN2K", 1000, -1000, 1, 2048.0)

    OK_, TG1, TG3, LB1, LB2, GG, TG5 = [sf(64) for _ in range(7)]
    MI, AI, BI, HI_, LO_, B0, B1 = [si(64) for _ in range(7)]
    CH, CB, CON, BB, DGB, BG, SD, DEAD, BC = [sh(64) for _ in range(9)]
    INZ = sh(72); ms(S("INC", 0, 144, 72), 0.0)
    for x in (CH, DEAD, sub(INZ, 0, 1)): iota(x, [[0, cols(x)]], 0)
    E = {"nxt": nxt, "prv": prv, "zero_ov": zero_ov, "won": [], "sign": []}
    for k, w in (("a8", 40), ("yi", 40), ("hk", 40), ("rr", 80), ("w0", 64), ("w1", 64)): E[k] = si(w)
    E["t2"] = sf(40)
    for k in ("q0", "q3"): E[k] = sf(128)
    LP, LM = [S("S16", 64 * i, 64 * i + 64) for i in (2, 3)]
    AL_, HXL, SPL, GOL, UL, CSL, I2, OVL, STL, SXL, SRL, QL = [S("L" + k) for k in LISTS]
    RTW, XW = S("RT"), S("X")

    def fold(out, f, src, a, n, more=None):
        pe([(out, C(f + str(h)), S(x, a + h, a + n, 2)) for x in [src] + ([more] if more else []) for h in range(2)])

    def hop(t):
        tag[:] = ["h", t]
        for h in range(2):
            fold(pb(1, 0, 256), "FN", "RTH", 512 * h, 512); ts(S("LN", 256 * h, 256 * h + 256), pb(1, 0, 256), 15.0, AL.add)
        extc(pb(2, 0, 64), "key", S("KT", 16, 1040))
        if t: tt(OK_, pb(2, 0, 64), LIM, AL.add)
        else: mv(OK_, pb(2, 0, 64), -128.0)
        ext(pb(2, 0, 64), [("c0", S("KT", 16, 1040))], 1024); mv(DGB, pb(2, 0, 64), 1.0)
        r = a = 0
        for w in HOP:
            if a + 512 * w > 6656: a = 0
            mv(S("G1", a, a + 512 * w), IND(S("KT"), S("LN", 32 * r, 32 * (r + w))))
            pe([(pb(10), Zs("key", r + i), S("G1", a + 512 * i, a + 512 * i + 512)) for i in range(w)], r == 0, r + w == 16); r += w; a += 512 * w

    def part_a(t):
        tag[:] = ["a", t]
        for h in range(2):
            a, b, k = 512 * h, 512 * h + 512, 2 * h
            pe([(pb(k), C("ID"), S("IDB", a, b))], True, False, sub(OVL, 0, 40) if t else None)
            pe([(pb(k), C("FK"), S("FL", a, b))], False, True)
            mv(S("KT", 16 + a, 16 + b), pb(k), M3)
        hop(t); tag[0] = "a"
        if t < RTG[0]:
            for h in range(2): pe([(pb(1 + h), C("DUP"), S("RTH", 512 * h, 512 * h + 512))]); mv(S("RT", 16 + 512 * h, 528 + 512 * h), pb(1 + h))
        else:
            for a in range(0, 1024, 256): asel(S("RT", 16 + a, 272 + a), S("RTH", a, a + 256), [[0, 256]], AL.is_ge, 0, 0, 0)
            dma("y", [(T["RT"][16 * g + 8:16 * g + 16, 16:1040], T["RT"][16 * g:16 * g + 8, 16:1040]) for g in range(8)], [S("RT", 16, 1040)], [S("RT", 16, 1040)], 256)
        scan(pb(9), S("RST"), pb(10), 0.0, AL.add, AL.min)
        tt(MI, pb(9, 7, 512, 8), OK_, AL.min); ts(AI, MI, 8, AL.arith_shift_right, 2047, AL.bitwise_and)
        ft = lambda i, h=None: S("FT", 128 * i, 128 * i + 128) if h is None else S("FT", 128 * i + 64 * h, 128 * i + 64 * h + 64)
        ts(LO_, MI, 12, AL.arith_shift_right, 2048 + 15, AL.bitwise_and); ts(HI_, MI, 8, AL.arith_shift_right, 15, AL.bitwise_and); ts(B0, MI, 3 * 65536, AL.bitwise_and)
        for h in range(2): ts(ft(1, h), LO_, MK[h], AL.mult)
        act(ft(2), ft(1), AF.Square, 0.0, 256.0); fw = S("S16", 336, 464)
        for h in range(2): ts(ft(0, h), HI_, MK[h], AL.mult); ts(sub(fw, 64 * h, 64 * h + 64), B0, MC[h], AL.mult, MD_[h], AL.min)
        for h in range(2):
            a, b = 512 * h, 512 * h + 512
            pe([(pb(12), ft(0), S("R1", a, b))]); tt(S("GB", a, b), pb(12), S("J16"), AL.is_equal)
            for i, (x, y) in enumerate(((C("NID"), S("RA")), (ft(1), S("RB", a, b)), (ft(2), S("R1", a, b)), (fw, S("R1", a, b)))): pe([(pb(13), x, y)], i == 0, i == 3)
            relu(S("EQ", a, b), pb(13), 1.0, -1952.0, (-1952.0, AL.add, 0.0, AL.max))
            pe([(pb(3, 0, 128), S("GB", c, c + 128), S("EQ", c, c + 128)) for c in range(a, b, 128)], h == 0, h == 1)
        mv(S("HW"), pb(3, 0, 128)); tt(sub(B0, 0, 48), IND(S("HW"), sub(HXL, 0, 3)), W32, AL.mult); ts(sub(B1, 0, 48), sub(B0, 0, 48), 31, AL.bitwise_and)
        tt(sub(CH, 8, 56), sub(B1, 0, 48), sub(DGB, 8, 56), AL.is_equal)
        ts(AL_, AI, 16.0 - 128, AL.add); ts(BI, MI, 255, AL.bitwise_and); ts(BB, BI, -1.0, AL.mult); ts(SD, BI, 0.0, AL.is_gt, 129.0, AL.mult)
        w2r(1, [(Al, lambda r: BB)])
        for h in range(2):
            a, b, p = 512 * h, 512 * h + 512, pb(4 + h)
            act(S("TS", a, b), pb(1 + h), AF.Sign, TH)
            pe([(p, C("KS"), S("KT", 16 + a, 16 + b)), (p, C("TD"), S("TS", a, b))], True, False)
        ts(LB1, AI, -999.0 - 128, AL.add, flex=False); ts(LB2, AI, -1.0, AL.mult, -1001.0 + 128, AL.add, flex=False)
        INB, p, RK, E1 = sub(INZ, 1, 65), pb(3, 0, 64), S("RKW", 0, 64), S("QR", 128, 256)
        pe([(p, C("BLK"), CH)]); scan(INB, p, C200, 0.0, AL.add, AL.min)
        for c in range(8): act(S("QS", 64 * c, 64 * c + 64), INB, AF.Sign, sub(AC, c, c + 1), -1.0, sub(QA, c, c + 1))
        ts(QL, QA, 0.5, AL.mult, 32.0, AL.add); ts(QB, QA, 8.0, AL.mult, 512.0, AL.add)
        pe([(p, C("LTK"), CH), (p, C("ID"), sub(INZ, 0, 64))]); mv(RK, p, 1001.0)
        tt(E1, IND(S("RKW"), QL), S("IO", 1, 129), AL.is_equal)
        p = pb(3, 0, 8); pe([(p, C("ID"), QB)] + [(p, Zs("rc", r), sub(E1, r, 128, 16)) for r in range(16)]); ts(GOL, p, 16.0, AL.add)
        cp(S("G0"), IND(RTW, GOL))
        fold(pb(3, 0, 64), "FN", "G0", 0, 128); ts(UL, pb(3, 0, 64), 15.0, AL.add)
        for h in range(2):
            pe([(pb(4 + h, r, 512, 16), Yc(r, 0), sub(RK, 32 * h, 32 * h + 32)) for r in range(16)], False, True)
            mv(S("CT", 16 + 512 * h, 528 + 512 * h), pb(4 + h), M9[t])
        tag[0] = "lab"
        for h in range(2): mv(S("GC", 512 * h, 512 * h + 512), IND(S("CT"), sub(AL_, 32 * h, 32 * h + 32)))
        ext(pb(5, 0, 64), [("c0", S("GC"))], 1024)
        GG, CON = pb(5, 64, 128), pb(5, 128, 192)
        tt(GG, pb(5, 0, 64), SD, AL.is_lt); ts(CB, pb(5, 0, 64), 128.5, AL.is_lt)
        tt(LP, GG, LB1, AL.mult); tt(LM, GG, LB2, AL.mult); tt(CON, CB, GG, AL.subtract); tt(DEAD, CON, DEAD, AL.add)
        if t < 2: ts(LIM, DEAD, -2.0 ** 23, AL.mult, -128.0, AL.add)
        for h in range(2):
            p = pb(1 + h); pe([(p, C("DF"), S("TS", 512 * h, 512 * h + 512))])
            tt(S("D2", 512 * h, 512 * h + 512), p, S("RTH", 512 * h, 512 * h + 512), AL.mult)
        extc(pb(1, 0, 64), "en", S("D2")); ts(SPL, pb(1, 0, 64), 2063.0, AL.add)
        w2r(1, [(Al, lambda r: CB)])
        for h in range(2): tt(S("D2", 512 * h, 512 * h + 512), pb(1 + h), S("D2", 512 * h, 512 * h + 512), AL.mult)

    def spokes(t):
        tag[0] = "pm"
        for h in range(2): mv(S("XS", 512 * h, 512 * h + 512), IND(XW, sub(SPL, 32 * h, 32 * h + 32)))
        for tab, lab, off in (("P", LP, 2048.0 * (t + 1)), ("M", LM, -2048.0 * (t + 1))):
            for h in range(2):
                rs, a = range(8 * h, 8 * h + 8), 16 + 512 * h
                pe([(blk(4, r), C("IDK"), S("XS", r, 1024, 16)) for r in rs] + [(blk(4, r), Al(r), lab) for r in rs]); mv(S(tab, a, a + 512), pb(4 + h), 1000.0 + off)

    def part_b(t):
        tag[:] = ["b", t]
        zero_ov(t, CH)
        for h, a in enumerate((896, 0) if t else ()):
            p = pb(6 + h, 0, 128)
            pe([(p, C("KS"), S("IDB", a, a + 128)), (p, C("TD"), S("TS", a, a + 128))], True, False)
            pe([(p, C("FK"), S("FLS", 128 * h, 128 * h + 128))], False, True); mv(S("CT", 16 + a, 144 + a), p, M8[t])
        tag[0] = "edge"
        n = 2176 + 640 * t; nch = -(-n // EDW[0]); w = -(-n // (32 * nch)) * 32
        for i, a in enumerate(range(0, n, w)):
            b = min(n, a + w); k = i % 2; ga, zz = S("GA", 16 + a, 16 + b), S("ZZ", 512 * k, 512 * k + b - a)
            z, x = pb(4 + k, 0, b - a), S("X", 16 + a, 16 + b)
            mv(ga, IND(S("P"), S("EA", a // 16, b // 16)))
            tt(zz, IND(S("M"), S("EB", a // 16, b // 16)), ga, AL.add)
            if i % EDGE[t] == 0:
                act(z, zz, AF.Abs, 0.25, 1024.0); tt(S("WN", a, b), z, x, AL.min); ts(x, S("WN", a, b), 3.0 * 2 ** 22, AL.add, -3.0 * 2 ** 22, AL.add)
                E["won"].append((t, a, b))
                if t == 2: E["sign"].append(x)
            else:
                zb = S("ZB", 512 * k, 512 * k + b - a); act(zb, zz, AF.Abs, 0.0, 1024.0)
                pe([(z, C("ID"), x), (z, C("NID"), zb)]); relu(zb, z, 1.0, 0.0, (0.0, AL.max))
                ts(S("WN", a, b), zb, 0.0, AL.is_gt, 0.25, AL.mult)
                pe([(z, C("ID"), x), (z, C("NID"), zb)])
                if t < 2: mv(x, z)
                else: act(x, z, AF.Abs)
        tag[0] = "b"
        for h in range(2): ts(S("GR", 512 * h, 512 * h + 512), IND(RTW, sub(UL, 32 * h, 32 * h + 32)), -1.0, AL.mult)
        for h in range(2): mv(S("IT", 16 + 512 * h, 528 + 512 * h), IND(S("CT"), sub(UL, 32 * h, 32 * h + 32)))
        J = lambda x, jj: sub(x, 128 * jj, 128 * jj + 128)
        two_ = lambda x, b, a=0: sub(x, a + b, a + 256, 2)
        FG, DG = S("QR", 0, 128), S("PR", 256, 384); ts(FG, S("G0"), 0.0, AL.is_gt)
        pe([(two_(pb(0), b), C(m + str(b)), FG) for b in range(2) for m in ("EJ", "EK")], True, False)
        pe([(J(pb(1), s), C("NP%d0" % s), S("G0")) for s in range(4)])
        for x, (j, s) in enumerate(BLOCKS):
            tt(J(S("HE"), x), J(pb(1), s), S("GR", j, 1024, 8), AL.is_equal)
            if x % 2 or x > 13: pe([(two_(pb(0), PLACE[j, 2 * s + 1][0]), Zs("ha", PLACE[j, 2 * s][1]) if j < 2 * s else Zs("hh", PLACE[j, j + 1][1]), J(S("HE"), y))
                                    for y, (j, s) in list(enumerate(BLOCKS))[x - (x < 14):x + 1]], False, x == 15)
        pe([(pb(2, 0, 128), Yc(1, j), S("IT", 16 + j, 1040, 8)) for j in range(8)]); ts(DG, pb(2, 0, 128), -1.0, AL.mult, -9.0, AL.add)
        pe([(two_(pb(7), b, 256 * e_), C(("EJ%d", "EK%d")[e_] % b), DG) for e_ in range(2) for b in range(2)], True, False)
        relu(S("WB", 0, 256), pb(0, 0, 256), 1.0, -1.0, (1.5, AL.is_gt))
        pe([(two_(pb(7), b, 256 * e_), C("L%s%d%d" % ("AB"[e_], c, b)), two_(S("WB"), c)) for e_ in range(2) for c, b in ((0, 0), (0, 1), (1, 1))], False, True)
        relu(S("PR", 0, 256), pb(7, 0, 256), -200.0, 50.0, (0.25, AL.is_lt, 100.0, AL.mult)); tt(S("SV", 0, 256), pb(7, 256, 512), S("PR", 0, 256), AL.is_gt)
        relu(S("R"), pb(7), 1.0, RH, (RH, AL.add, 0.0, AL.max))
        pe([(pb(3, 0, 256), C("BLK"), S("SV", 0, 256))]); scan(S("INW", 16, 272), pb(3, 0, 256), S("IO", 656, 912), 0.0, AL.add, AL.min)
        em = S("S16", 480, 496)
        pe([(pb(2, 0, 16), C("ID"), DW)] + [(pb(2, 0, 16), Zs("nwon", r), S("SV", r, 256, 16)) for r in range(16)]); ts(em, pb(2, 0, 16), 0.0, AL.max)
        pe([(pb(3, 0, 17), Yc(0, r), S("INW", 15 + r, 287, 16)) for r in range(16)] + [(pb(3, 0, 16), C("ID"), em)])
        p = pb(0, 0, 256)
        pe([(two_(p, b), Yc(0, 15), S("IOB")) for b in range(2)] + [(p, C("IDK"), S("R", 0, 256)), (p, C("I8K"), S("R", 256, 512)), (p, C("LW"), S("SV", 0, 256))])
        for b in range(2): mv(S("NT", b, 256, 2), pb(0, b, 256, 2), DB[b])
        cp(sub(CSL, 0, 17), pb(3, 0, 17))
        yc, p = S("YC"), pb(3, 64, 104)
        iota(S("WW", 0, 640), [[0, 640]], -1000); cp(IND(S("WW"), sub(CSL, 0, 17)), S("NT", 0, 272))
        scan(yc, S("DEC"), S("WW", 0, 640), -1000.0, AL.add, AL.max); ts(yc, yc, LOB, AL.max, HIB, AL.min)
        ext(p, [("yk", yc)], 640)
        a8, yi, hk, rr, t2 = [E[k] for k in ("a8", "yi", "hk", "rr", "t2")]
        i2, t3, tot, ids, c0 = S("UM", 80, 160), S("S16", 0, 80), S("COL", 17, 18), S("S16", 256, 336), 136 + 40 * t
        end = lambda x, e_, k=1: sub(x, 40 * k * e_, 40 * k * e_ + 40 * k)
        ts(tot, S("INW", 271, 272), 0.0, AL.add); ts(i2, MD, tot, AL.is_ge); tt(t3, i2, DOV, AL.mult)
        ts(yi, p, 28672.0, AL.add); ts(end(I2, 0), p, 1.0 / 512, AL.mult, 72.0 - 0.499, AL.add)
        ts(end(rr, 0), yi, 3, AL.arith_shift_right, 7, AL.bitwise_and); ts(end(rr, 1), yi, 7, AL.bitwise_and); ts(S("R2"), rr, -1.0, AL.mult, -1.0, AL.add)
        ts(hk, yi, 6, AL.arith_shift_right, 7, AL.bitwise_and); ts(a8, yi, 9, AL.arith_shift_right, 2040, AL.bitwise_and); tt(t2, hk, a8, AL.add); ts(end(I2, 1), t2, 16.0, AL.add)
        for a in range(0, 80, 20): cp(S("GI", 16 * a, 16 * a + 320), IND(S("IT"), sub(I2, a, a + 20)))
        GL = lambda a, b: S("GB", a, b) if b <= 640 else S("EQ", a - 640, b - 640)
        for k, (a, b) in enumerate(((0, 512), (512, 1024), (1024, 1280))):
            pe([(pb(22 + k, r, b - a, 16), Al(r), S("R2", a // 16, b // 16)) for r in range(16)])
            for c, d in ((a, b),) if k != 1 else ((512, 640), (640, 1024)): tt(GL(c, d), pb(22 + k, c - a, d - a), S("GI", c, d), AL.is_ge)
        y = pb(0, 128, 208); ext(y, [("id", S("GI"))], 1280); cp(ids, y)
        for x in range(2): ts(S(("EA", "EB")[x], c0, c0 + 40), end(y, x), 15.0, AL.add)
        for e_ in range(2):
            q, gl = pb(17 + e_, 0, 40), GL(640 * e_, 640 * e_ + 640)
            pe([(q, C("I9K"), end(i2, e_)), (q, C("ID"), end(t3, e_))] + [(q, Zs("odd", r), sub(gl, r, 640, 16)) for r in range(16)] + [(q, C("ID"), end(ids, e_))])
            ts(end(OVL, e_), q, -1025.0, AL.add)
        for e_ in range(2): tt(IND(S("OV"), end(OVL, e_)), end(S("GI"), 1 - e_, 16), S("NAM"), AL.add)
        tag[0] = "new"
        YY = S("GA", 16 + n, 656 + n)
        mv(YY, IND(S("P"), S("EA", c0, c0 + 40))); tt(S("XB"), IND(S("M"), S("EB", c0, c0 + 40)), YY, AL.add); ts(S("X", 16 + n, 656 + n), S("XB"), 1024.0, AL.mult, 255.0, AL.min)
        tag[0] = "rows"
        p = pb(19, 0, 64)
        pe([(p, C("ID"), N896)] + [(p, C(m % h), S(x, 896 + 64 * h, 960 + 64 * h)) for h in range(2) for m, x in (("FN%d", "RTH"), ("NFN%d", "D2"))], True, False, ids)
        pe([(p, Zs("id", 8 * h + l), S("OV", 1024 * l + 896 + 64 * h, 1024 * l + 960 + 64 * h)) for l in range(8) for h in range(2)], False, True)
        for x in range(2 - OVD[0], 2):
            dma("y", [(T[("WV", "OVT")[x]][64 * c:64 * c + 64, 0:1024], T["OV"][2 * c + 2:128:8, 4096 * x:4096 * x + 4096]) for c in range(2)],
                [S("OV", 4096 * x, 4096 * x + 4096)], [S(("WV", "OVT")[x], 0, 1024)], 256)
        for part in (((pb(6, 0, 128), 896, 1024), (pb(6, 128, 256), 0, 128)), ((pb(1, 0, 384), 128, 512),), ((pb(2, 0, 384), 512, 896),)):
            pe([m for p, a, b in part for m in [(p, C("ID"), S("RTH", a, b)), (p, C("NID"), S("D2", a, b))]], True, False, sub(OVL, 0, 40) if t == 2 and len(part) == 1 else ids)
            far = OVD[0] if len(part) == 1 or OVD[1] else 0
            pe([(p, sub(C("CV"), 15 - l, 143 - l), S("OV", 1024 * l + a, 1024 * l + b)) for p, a, b in part for l in range(8 - 4 * far)] +
               [(p, C("MV%d" % x), S(("WV", "OVT")[x], a, b)) for p, a, b in part for x in range(2 - far, 2)], False, True)
            for first in (len(part) == 2, len(part) == 1):
                for p, a, b in part:
                    if first: cp(S("RTH", a, b), p)
                    else: flags(S("FL", a, b), p)
        tag[0] = "mid"
        dma("y", [(T["GAW"][:, :], T["GA"][0:128:16, 16:4112])], [S("GA", 16, 4112)], [S("GAW")], 200)

    def middles(t):
        tag[0] = "mid"
        n = 2176 + 640 * t; y = pb(0, 0, 256); mm = [(y, C("N64K"), S("ONE", 0, 256))]
        for r in range(16):
            a, b, c = 256 * r, min(max(n, 256 * r), 256 * r + 256), min(max(n + 640, 256 * r), 256 * r + 256)
            if b > a: mm.append((pb(0, 0, b - a), Zs("won", r), S("WN", a, b)))
            for t_, d, f in E["won"]:
                if t_ == t and min(f, b) > max(d, a): mm.append((pb(0, max(d, a) - a, min(f, b) - a), Zs("nwon", r), S("X", 16 + max(d, a), 16 + min(f, b))))
            if c > b: mm.append((pb(0, b - a, c - a), Zs("won", r), S("ONE", 0, c - b)))
        for i in range(0, len(mm), 4): pe(mm[i:i + 4], i == 0, i + 4 >= len(mm))
        tt(y, y, S("GAW"), AL.min); tt(S("ENC"), y, S("ENC"), AL.max)

    def send(src, dst, k, to, by):
        o = add("g", lambda e: [e["g"].remote_dma(ap(dst), ap(src), T.sem["a%d" % k], T.sem["o%d" % k], E[to][1], E[to][0], E[to][2])], [src], [], 300.0, send=("o%d" % k, E[to][3]))
        add("x", None, [], [dst], (3000.0 + 3.5 * cols(src)) * XF[0], after=o, sem=("a%d" % k, E[by][4]))
    base = (896, 0)
    SND = S("SND")

    def part_c(t):
        tag[0] = "seam"
        TP, TR, RX = S("TP", 192 * t, 192 * t + 192), S("TR", 128 * t, 128 * t + 128), S("RX", 1024 * (t % 2), 1024 * (t % 2) + 1024)
        H2 = lambda x, s_, w=64: sub(x, w * s_, w * s_ + w)
        rows = lambda s_, ha: S("RTH", base[s_] + 64 * ha, base[s_] + 64 * ha + 64)
        tt(H2(TP, 1), pb(19, 0, 64), A1C, AL.is_gt); tt(H2(TP, 0), pb(19, 0, 64), A1C, AL.max)
        send(sub(TP, 0, 128), TR, 3 * t, "nxt", "prv")
        pe([(pb(7, 0, 64), C("FN%d" % ha), rows(1, ha)) for ha in range(2)]); mv(H2(TP, 2), pb(7, 0, 64))
        flg = (H2(TP, 1), H2(TR, 1)); TR = H2(TR, 0)
        inc = lambda s_: S("INC", 72 * s_ + 1, 72 * s_ + 65)

        def number(s_, bk):
            FLG, INC, TG, p, y = flg[s_], inc(s_), S("TG", 8 * s_, 8 * s_ + 4), pb(bk, 0, 64), pb(bk, 0, 4)
            q0 = sub(E["q0"], 64 * s_, 64 * s_ + 4)
            pe([(p, C("BLK"), FLG)]); scan(INC, S("ONE", 0, 64), p, 0.0, AL.mult, AL.add)
            if NUM[s_] == "p":
                ext(pb(13, 0, 4), [("all", FLG)], 64); ts(TG, pb(13, 0, 4), 0.0, AL.is_equal, 1024.0, AL.mult)
                pe([(y, Yc(0, r), sub(INC, r - 1, 63, 16)) for r in range(16)] + [(y, C("ID"), TG)]); tt(q0, y, DS, AL.min); cp(H2(STL, s_, 4), q0)
            else:
                TG = S("TG", 16 + 64 * s_, 80 + 64 * s_); ts(p, p, 0.0, AL.is_equal); tt(p, p, S("IO", 512, 576), AL.mult); tt(TG, p, sub(INC, -1, 63), AL.max)
                ext(y, [("c0", TG)], 64); cp(H2(STL, s_, 4), y)

        def names(s_, bk):
            NE, w0, w1, q2 = H2(S("NE"), s_, 512), H2(E["w0"], s_, 32), H2(E["w1"], s_, 32), sub(E["q3"], 64 + 32 * s_, 96 + 32 * s_)
            SW = S("SW", 576 * s_, 576 * s_ + 576); w = sub(SW, 0, 512)
            iota(w, [[0, 512]], 1000); cp(IND(SW, H2(STL, s_, 4)), H2(S("NUS"), s_)); scan(NE, S("ONE"), w, 1000.0, AL.add, AL.min); ts(NE, NE, -0.5, AL.max, 0.5, AL.min)
            ext(pb(bk, 0, 32), [("8k", NE)], 512); ts(w0, pb(bk, 0, 32), -1.0, AL.mult, 65536.0 - 2033, AL.add); ts(w1, w0, 8191, AL.bitwise_and)
            if s_: ts(S("Lsh"), w1, 4112.0, AL.min)
            tt(q2, w1, H2(DX, s_, 32), AL.min); cp(H2(SXL, s_, 32), q2)
        tag[0] = "own"
        number(0, 3); p = pb(3, 64, 128)
        pe([(p, C("NFE%d" % ha), rows(0, ha)) for ha in range(2)] + [(p, C("LS"), flg[0])]); ts(H2(S("NUS"), 0), p, -1.0, AL.mult, 512.0, AL.add)
        names(0, 3)
        for h in range(2): mv(H2(SND, h, 256), IND(XW, H2(SXL, h, 16)))
        send(H2(SND, 0, 512), H2(RX, 1, 512), 3 * t + 1, "nxt", "prv")
        for s_ in range(2):
            fold(pb(3, 0, 64), "FE", "RTH", base[s_], 128); ts(H2(SRL, s_), pb(3, 0, 64), 2063.0, AL.add)
        tag[0] = "seam"
        bl = lambda s, ha: pb(7, 128 * s + 64 * ha, 128 * s + 64 * ha + 64)
        pe([m for s in range(4) for ha in range(2) for m in [(bl(s, ha), C("NP%d%d" % (s, ha)), H2(TP, 2)), (bl(s, ha), C("NQ%d" % s), rows(1, ha))]], True, False)
        pe([(bl(s, ha), C(("DUP", "DUPE")[ha]), TR) for s in range(4) for ha in range(2)], False, True)
        ts(S("PRS", 512, 1024), pb(7), -0.5, AL.max, 0.5, AL.min)
        pe([(pb(7, 0, 64), C("SH%d" % ha), S("PRS", 512 + 128 * s + 64 * ha, 576 + 128 * s + 64 * ha)) for s in range(4) for ha in range(2)])
        ts(S("WI", 0, 64), pb(7, 0, 64), 32768.0, AL.add); ts(S("WJ", 0, 64), S("WI", 0, 64), 8191, AL.bitwise_and)
        q3 = sub(E["q3"], 0, 64); ts(q3, S("WJ", 0, 64), -1.0 / 8192, AL.mult, 512.5, AL.add)
        number(1, 6)
        pe([(pb(8, 0, 64), C("LS"), flg[1])]); tt(H2(S("NUS"), 1), q3, pb(8, 0, 64), AL.subtract)
        names(1, 6)
        for h in range(2): mv(sub(SND, 512 + 256 * h, 768 + 256 * h), IND(XW, S("Lsh", 16 * h, 16 * h + 16)))
        send(H2(SND, 1, 512), H2(RX, 0, 512), 3 * t + 2, "prv", "nxt")

    def part_d(t):
        tag[0] = "cmp"
        RX = S("RX", 1024 * (t % 2), 1024 * (t % 2) + 1024)
        GT, SG, MN, GX = S("EQS"), S("OH"), S("SC"), S("SRG")
        if t == 2:
            iota(S("W5"), [[1, 512]], 31100); put(IND(S("GA", 0, 5152), sub(SXL, 0, 32)), S("W5"))
            for h in range(2): ts(S("D2", 512 * h, 512 * h + 512), IND(S("GA", 0, 4112), sub(SRL, 32 * h, 32 * h + 32)), -31000.0, AL.add, 0.0, AL.max)
            ext(pb(5, 0, 64), [("c0", S("D2"))], 1024); ts(sub(SRL, 0, 64), pb(5, 0, 64), -84.0, AL.add, 15.0, AL.max); ms(S("KT", 15, 16), 1.0)
        for s_ in (1, 0):
            a, b, p = 512 * s_, 512 * s_ + 512, pb(7 - s_)
            pe([(p, C("ID"), sub(SND, a, b))])
            for y, op in ((GT, AL.is_gt), (MN, AL.min))[::-1 if t == 2 else 1]: tt(sub(y, a, b), p, sub(RX, a, b), op)
            p = pb(20 + s_); pe([(p, C("BLK"), sub(GT, a, b))]); L = sub(SXL, 32 * s_, 32 * s_ + 32)
            if t < 2:
                act(sub(SG, a, b), p, AF.Sign, 8.5, -1.0); tt(IND(XW, L), sub(MN, a, b), sub(SG, a, b), AL.mult); signs = XW
            else:
                cp(IND(XW, L), sub(MN, a, b)); signs = S("GA", 0, 4112)
                if s_: act(S("W6"), p, AF.Identity, 8.5, -1.0); put(IND(S("GA", 0, 5152), L), S("W6"))
                else: signs = S("KT", 0, 528); ts(S("KT", 16, 528), p, -1.0, AL.mult, 8.5, AL.add)
            for h in range(2): mv(sub(GX, 2 * a + 512 * h, 2 * a + 512 * h + 512), IND(signs, sub(SRL, 64 * s_ + 32 * h, 64 * s_ + 32 * h + 32)))
            a, p = base[s_], pb(7 - s_, 0, 128)
            pe([(p, sub(C("KD"), 15 - l, 143 - l), sub(GX, 1024 * s_ + l, 1024 * s_ + 1024, 8)) for l in range(8)])
            if t == 2:
                ts(p, p, -1.0, AL.max); tt(S("ZZ", a, a + 128), p, S("ZZ", a, a + 128), AL.min); c, d = (896, 1024) if a else (0, 896)
                for q, y, o in (("y", "ynb", 0), ("s", "yen", 8)):
                    dma(q, [(T[y][:, 1024 * k + c:1024 * k + d], T["GA"][k + o:128:16, 6560 + c:6560 + d]) for k in range(8)], [S("ZZ", c, d)], [], (d - c) // 2)
                continue
            fls = S("FLS", 128 * s_, 128 * s_ + 128); ts(fls, S("FL", a, a + 128), -2.0 ** 30, AL.mult, 2.0 ** 30, AL.add)
            tt(S("RT", 16 + a, 144 + a), p, S("RT", 16 + a, 144 + a), AL.min); tt(fls, p, fls, AL.is_gt)
            ts(p, p, 0.0, AL.is_gt); tt(S("RTH", a, a + 128), p, S("RTH", a, a + 128), AL.mult)

    ends(); part_a(0)
    for t in range(3):
        spokes(t)
        part_b(t); part_c(t)
        if t < 2: part_a(t + 1)
        middles(t)
        if t == 2:
            ts(S("WJ", 256, 512), S("ENC"), 2047, AL.bitwise_and); ts(S("GAW"), S("WJ", 256, 512), -1.0, AL.add)
            dma("y", [(T["ymid"][:, :], T["GAW"][:, :])], [S("GAW")], [], 200)
            for x in E["sign"]: act(x, x, AF.Abs)
            ts(BG, DEAD, -8192.0, AL.mult)
            for a in (0, 512):
                p = pb(1 + a // 512)
                pe([(p, C("ID"), S("RTH", a, a + 512)), (p, C("EN2K"), S("FL", a, a + 512))] + [(sub(p, x - a, x - a + 64), Al(x // 64), BG) for x in range(max(a, 128), min(a + 512, 896), 64)])
                ts(S("ZZ", a, a + 512), p, -1.0, AL.add, -1.0, AL.max)
        part_d(t)
    dma("y", [(T["ylen"][:, :], T["X"][:, 16:4112])], [S("X", 16, 4112)], [], 900)


def polish(ops, fw, res, rng, steps):
    n = len(ops); anc = [0] * n; jp = []; js = [[] for _ in ops]
    for i in range(n):
        cover = 0
        for j, _ in fw[i]: cover |= anc[j]
        jp.append([(j, lag) for j, lag in fw[i] if not cover >> j & 1])
        for j, lag in fw[i]: anc[i] |= anc[j] | 1 << j
        for j, lag in jp[i]: js[j].append((i, lag))
    late = [o.get("dma", 0.0) for o in ops]
    cost = lambda i, q: ops[i].get("cs", ops[i]["cost"]) if q == "s" else ops[i]["cost"]
    pick = [r[2] for r in res]; dur = [cost(i, pick[i]) for i in range(n)] + [0.0]
    topo = sorted(range(n), key=lambda i: (res[i][0], i)); pos = [0] * n
    mp, mn = [n] * (n + 1), [n] * (n + 1); last = {}
    for k, i in enumerate(topo):
        pos[i] = k
        if pick[i] != "x":
            if pick[i] in last: mp[i] = last[pick[i]]; mn[last[pick[i]]] = i
            last[pick[i]] = i
    fin, tail, then = [0.0] * (n + 1), [0.0] * (n + 1), [n] * n

    own = lambda i, j, lag: not lag and pick[i] == pick[j]
    tp = [[j for j, lag in jp[i] if not own(i, j, lag)] for i in range(n)]; tn = [[k for k, lag in js[i] if not own(i, k, lag)] for i in range(n)]
    gap = [max([lag for _, lag in js[i]] + [0.0]) for i in range(n)]; out_ = [0.0] * n
    for i in range(n):
        jp[i] = [(j, 0.0 if own(i, j, lag) else gap[j]) for j, lag in jp[i]]; js[i] = [(k, 0.0 if own(i, k, lag) else gap[i]) for k, lag in js[i]]

    win = [0, n]

    def times(a, b):
        for i in topo[a:win[1]]:
            s = fin[mp[i]]
            for j in tp[i]:
                if out_[j] > s: s = out_[j]
            s += dur[i]; fin[i] = s; out_[i] = s + gap[i]
        tie = 1e-6 if rng.rand() < 0.5 else -1e-6
        for i in topo[win[0]:b + 1][::-1]:
            s = 0.0; w = n
            for k in tn[i]:
                if tail[k] > s: s = tail[k]; w = k
            s = s + gap[i] if s else late[i]; k = mn[i]
            if tail[k] + tie > s and k < n: s = max(s, tail[k]); w = k
            tail[i] = s + dur[i]; then[i] = w
    head = lambda i: max([fin[j] + lag for j, lag in jp[i]] + [0.0])
    rest = lambda i: max([tail[k] + lag for k, lag in js[i]] + [late[i]])

    def guess(seq, before, after):
        s, st = fin[before], []
        for i, d in seq:
            s = max(s, head(i)); st.append(s); s += d
        t, worst = tail[after], 0.0
        for (i, d), s in zip(seq[::-1], st[::-1]):
            t = max(t, rest(i)) + d; worst = max(worst, s + t)
        return worst

    def move(u, q, before, after):
        mn[mp[u]], mp[mn[u]] = mn[u], mp[u]
        mp[u], mn[u] = before, after; mn[before] = u; mp[after] = u; mp[n] = mn[n] = n
        pick[u] = q; dur[u] = cost(u, q)
        a = min([pos[u]] + ([pos[after]] if after < n else [])); b = max([pos[u]] + ([pos[before]] if before < n else []))
        seg = topo[a:b + 1]; inside = set(seg); left = {}
        for i in seg: left[i] = sum(1 for j, _ in jp[i] if j in inside) + (mp[i] in inside)
        ready = [i for i in seg if not left[i]][::-1]; out = []
        while ready:
            i = ready.pop(); out.append(i)
            for k in [k for k, _ in js[i]] + [mn[i]]:
                if k in inside:
                    left[k] -= 1
                    if not left[k]: ready.append(k)
        assert len(out) == len(seg)
        topo[a:b + 1] = out
        for k, i in enumerate(out): pos[i] = a + k
        times(max(a - 1, win[0]), min(b + 1, win[1] - 1))

    def settle(seg, picks):
        topo[win[0]:win[1]] = seg; last = {}
        for i, q in zip(seg, picks): pick[i] = q; dur[i] = cost(i, q)
        for i in topo:
            if pick[i] != "x": mp[i] = last.get(pick[i], n); mn[mp[i]] = i; mn[i] = n; last[pick[i]] = i
        mp[n] = mn[n] = n; win[:] = [0, n]; times(0, n - 1)
        topo.sort(key=lambda i: fin[i] - dur[i])
        for k, i in enumerate(topo): pos[i] = k
    times(0, n - 1); best = None; tabu = {}
    for it in range(steps + 1):
        if it % WIN[1] == 0 or it == steps:
            if best: settle(*best[1:])
            lo = (it // WIN[1] * WIN[0] // 2) % n; lo = max(0, min(n - WIN[0], lo - rng.randint(WIN[0] // 2))); hi = min(n, lo + WIN[0]); win[:] = [lo, hi]; best = None
            if it == steps: break
        span = 0.0
        for k in topo[lo:hi]:
            s = fin[k] - dur[k] + tail[k]
            if s > span + 1e-6: span = s; i = k
        if best is None or span < best[0] - 1e-6: best = (span, topo[lo:hi], [pick[k] for k in topo[lo:hi]])
        blocks = []; run = [i]; cand = []
        while i < n:
            k = then[i]
            if k < n and pos[k] >= hi: k = n
            if mn[i] == k and k < n: run.append(k)
            else:
                if len(run) > 1: blocks.append(run)
                run = [k]
            i = k
        for bi in rng.permutation(len(blocks))[:NEAR[0]]:
            b = blocks[bi]; D = lambda l: [(x, dur[x]) for x in l]
            for x in range(len(b) - 1):
                for y in sorted(set((x + 1, len(b) - 1))):
                    if y - x < 12 and all(tail[k] <= tail[b[y]] and k != b[y] for k, _ in js[b[x]]) and not any(anc[z] >> b[x] & 1 for z in b[x + 1:y + 1]):
                        cand.append((guess(D(b[x + 1:y + 1] + [b[x]]), mp[b[x]], mn[b[y]]), b[x], pick[b[x]], b[y], mn[b[y]]))
            for y in range(2, min(len(b), 12)):
                if all(fin[j] <= fin[b[0]] and j != b[0] for j, _ in jp[b[y]]) and not any(anc[b[y]] >> z & 1 for z in b[:y]):
                    cand.append((guess(D([b[y]] + b[:y]), mp[b[0]], mn[b[y]]), b[y], pick[b[y]], mp[b[0]], b[0]))
            for u in b:
                if len(ops[u]["q"]) == 2:
                    q = "s" if pick[u] == "v" else "v"; k = pos[u] - 1
                    while k >= 0 and pick[topo[k]] != q: k -= 1
                    if k < 0: continue
                    w = topo[k]; h = head(u); r = rest(u); d = cost(u, q)
                    for _ in range(4):
                        cand.append((max(max(h, fin[w]) + d + max(r, tail[mn[w]]), fin[mp[u]] + tail[mn[u]]), u, q, w, mn[w]))
                        if mp[w] == n or pos[w] < lo or anc[u] >> w & 1 or any(fin[j] > fin[w] - dur[w] for j, _ in jp[u]): break
                        w = mp[w]
        free = [c for c in cand if tabu.get((c[1], c[3]), -1) < it or c[0] < best[0] - 1.0]
        if not free: continue
        c = min(free, key=lambda c: c[0] + rng.rand() * JIT[0])
        tabu[(c[1], mp[c[1]])] = it + 8 + rng.randint(12)
        if c[2] == pick[c[1]] and c[3] < n: tabu[(c[3], mp[c[3]])] = it + 8 + rng.randint(12)
        move(c[1], c[2], c[3], c[4])
    return list(zip([f - d for f, d in zip(fin, dur)], fin, pick))


def tiles(ops):
    up = {}; own = {}; grp = {}

    def find(a):
        while up[a] != a: up[a] = up[up[a]]; a = up[a]
        return a
    for i, o in enumerate(ops):
        for kind, accs in (("r", o["rd"]), ("w", o["wr"])):
            for name, m, _ in accs:
                if not name.startswith("pb"): continue
                me = (i, name); up.setdefault(me, me); l = own.setdefault(name, [])
                if kind == "r":
                    for m2, w in l:
                        if m & m2: up[find(w)] = find(me)
                else:
                    if name in o.get("cont", ()): up[find(grp[name])] = find(me)
                    l[:] = [(m2 & ~m, w) for m2, w in l if m2 & ~m] + [(m, me)]
        if o["q"] == "p":
            for name, _, _ in o["wr"]: grp[name] = (i, name)
    num = {}
    for i, o in enumerate(ops):
        o["tile"] = {name: "pb%d" % num.setdefault(find((i, name)), len(num)) for name, _, _ in o["rd"] + o["wr"] if name.startswith("pb")}
        for k in ("rd", "wr"): o[k] = [(o["tile"].get(name, name), m, bm) for name, m, bm in o[k]]


def ties(ops):
    if "tails" in ops[0]:
        for o in ops: o["deps"], o["order"] = set(o["first"][0]), set(o["first"][1])
        return ops[0]["tails"]
    last = {}
    for i, o in enumerate(ops):
        deps, order = set(), set()
        dm = "dma" in o or o["q"] == "x" or "send" in o
        for kind, accs in (("r", o["rd"]), ("w", o["wr"])):
            for name, m, bm in accs:
                ps = name.startswith("pb")
                for j, k2, m2, bm2 in last.get(name, []):
                    if j == i: continue
                    p = ops[j]
                    if ps and (p["q"] != o["q"] or o["q"] == "vs"): hit = True
                    elif kind == "r" and k2 == "r": hit = False
                    elif ps and o["q"] == "p": hit = True
                    elif dm or "dma" in p or p["q"] == "x": hit = bool(bm & bm2)
                    else: hit = bool(m & m2)
                    if hit:
                        (order if (o["q"] == "p" and p["q"] == "p") else deps).add(j)
                    elif ps: order.add(j)
        for kind, accs in (("r", o["rd"]), ("w", o["wr"])):
            for name, m, bm in accs:
                l = last.setdefault(name, [])
                if kind == "w" and not name.startswith("pb"): l[:] = [x for x in l if x[2] & ~m or x[0] == i]
                if name.startswith("pb"): l[:] = [x for x in l if x[0] == i or (o["q"] != "p" and ops[x[0]]["q"] in ("p", o["q"]))]
                l.append((i, kind, m, bm))
        if "after" in o: order.add([k for k in range(i) if ops[k] is o["after"]][0])
        o["deps"], o["order"] = deps, order - deps; o["first"] = (set(deps), order - deps)
    ops[0]["tails"] = {k: sorted(set(x[0] for x in l)) for k, l in last.items() if k.startswith("pb")}
    return ops[0]["tails"]


def later(ops, res):
    n = len(ops); res = list(res); due = [1e18] * n
    for i in sorted(range(n), key=lambda i: (-res[i][0], -i)):
        a, b, q = res[i]
        if q == "p" and b + ROOM[1] < due[i] < 1e17: res[i] = (a + due[i] - b - ROOM[1], due[i] - ROOM[1], q)
        for j in ops[i]["deps"] | ops[i]["order"]: due[j] = min(due[j], res[i][0] - LAT)
    return res


def banks(ops, res, rng):
    n = len(ops); use = {}
    for i in sorted(range(n), key=lambda i: (res[i][0], i)):
        for t in set(ops[i]["tile"].values()): use.setdefault(t, []).append(i)
    succ = [[] for _ in ops]
    for i, o in enumerate(ops):
        for j in o["deps"] | o["order"]: succ[j].append(i)

    def reaches(src, goal):
        seen, todo = set(src), list(src); top = max(res[j][0] for j in goal)
        while todo:
            i = todo.pop()
            if i in goal: return True
            for k in succ[i]:
                if k not in seen and res[k][0] < top + 20000.0: seen.add(k); todo.append(k)
        return False
    rows = [[] for _ in range(8)]; end = [-1e9] * 8
    for t, l in sorted(use.items(), key=lambda x: res[x[1][0]][0]):
        a = res[l[0]][0]; other = set(x for i in l for x in ops[i]["tile"].values()) - {t}
        rank = sorted(range(8), key=lambda b: rng.rand() * ROOM[0] + end[b])
        for b in rank:
            if rows[b] and (rows[b][-1] in other or reaches(l, set(use[rows[b][-1]]))): continue
            break
        if rows[b]:
            for j in use[rows[b][-1]]: succ[j] += l
        rows[b].append(t); end[b] = max(end[b], max(res[i][1] for i in l))
    return rows


def seat(ops, rows, res):
    tail = ties(ops); first = {}
    for i, o in enumerate(ops):
        for t in o["tile"].values(): first.setdefault(t, []).append(i)
    for b, row in enumerate(rows):
        for t in row:
            for i in first[t]: ops[i].setdefault("bank", {}).update({k: "pb%d" % b for k, v in ops[i]["tile"].items() if v == t})
        for t, u in zip(row, row[1:]):
            for i in first[u]:
                if i == first[u][0] or not (ops[i]["deps"] | ops[i]["order"]) & set(first[u]):
                    for j in tail[t]: ops[i]["order" if ops[i]["q"] == "p" == ops[j]["q"] else "deps"].add(j)
    n = len(ops); succ = [[] for _ in ops]; left = [0] * n
    for i, o in enumerate(ops):
        o["order"] = o["order"] - o["deps"]
        for j in o["deps"] | o["order"]: succ[j].append(i); left[i] += 1
    key = [r[0] for r in res]; ready = [i for i in range(n) if not left[i]]; out = []
    while ready:
        i = min(ready, key=lambda i: (key[i], i)); ready.remove(i); out.append(i)
        for k in succ[i]:
            left[k] -= 1
            if not left[k]: ready.append(k)
    assert len(out) == n
    new = {i: k for k, i in enumerate(out)}
    for o in ops: o["deps"], o["order"] = set(new[j] for j in o["deps"]), set(new[j] for j in o["order"])
    return out


def search(ops, rng, passes, rounds, steps, given=None):
    n = len(ops); succ = [[] for _ in ops]
    for i, o in enumerate(ops):
        for j in o["deps"] | o["order"]: succ[j].append(i)
    pri = [0.0] * n
    for i in range(n - 1, -1, -1):
        pri[i] = ops[i]["cost"] + ops[i].get("dma", 0) + LAT + max([pri[k] for k in succ[i]] or [0.0])
    fw = [[(j, LAT + ops[j].get("dma", 0)) for j in o["deps"]] + [(j, ops[j].get("dma", 0)) for j in o["order"]] for o in ops]
    anc = [0] * n; pre = []; post = [[] for _ in ops]; late = [o.get("dma", 0.0) for o in ops]
    for i in range(n):
        cover = 0
        for j, _ in fw[i]: cover |= anc[j]
        pre.append([(j, lag) for j, lag in fw[i] if late[j] or not cover >> j & 1])
        for j, _ in fw[i]: anc[i] |= anc[j] | 1 << j
        for j, lag in pre[i]: post[j].append((i, lag))
    qs = [o["q"] for o in ops]; cv = [o["cost"] for o in ops]; cs = [o.get("cs", o["cost"]) for o in ops]; kind = [o["kind"] for o in ops]
    hard = [[j for j, _ in pre[i] if j in ops[i]["deps"]] for i in range(n)]; soft = [[j for j, _ in pre[i] if j not in ops[i]["deps"]] for i in range(n)]
    flex = [i for i in range(n) if len(qs[i]) == 2]; tags = {}
    for i, o in enumerate(ops): tags.setdefault(o["tag"], []).append(i)
    keep = lambda r: [-99.0 if q == "v" else 99.0 for q in r[2]]
    span = lambda r: max(e + l for e, l in zip(r[1], late))

    def place(order, need, back, pen):
        S_ = {q: [] for q in "vspgy"}; E_ = {q: [] for q in "vspgy"}; st_ = [0.0] * n; en = [0.0] * n; pk = [""] * n
        for i in order:
            rdy = late[i] if back else 0.0
            for j, lag in need[i]:
                if en[j] + lag > rdy: rdy = en[j] + lag
            best = None
            for q in qs[i]:
                if q == "x":
                    best = (0, q, rdy, cv[i], 0); break
                c = cs[i] if q == "s" else cv[i]; s, e = S_[q], E_[q]; st = rdy; lo = 0; m = hi = len(s)
                if m and e[-1] <= st: lo = m
                while lo < hi:
                    mid = (lo + hi) // 2
                    if e[mid] <= st: lo = mid + 1
                    else: hi = mid
                while lo < m and s[lo] < st + c:
                    if e[lo] > st: st = e[lo]
                    lo += 1
                key = st + c + (pen[i] * c + PEN[1] if q == "v" else 0.0)
                if best is None or key < best[0]: best = (key, q, st, c, lo)
            _, q, st, c, lo = best
            if q != "x": S_[q].insert(lo, st); E_[q].insert(lo, st + c)
            st_[i] = st; en[i] = st + c; pk[i] = q
        return st_, en, pk

    def both(r, pen):
        rb = place(sorted(range(n), key=lambda i: (-r[1][i], -i)), post, True, pen)
        r2 = place(sorted(range(n), key=lambda i: (-rb[1][i], i)), pre, False, pen)
        return r2 if span(r2) <= span(r) else r

    def score(r):
        sq = sorted(range(n), key=lambda i: (r[0][i], i)); tot = OWN[0] * span(r)
        for fac, lat, wt in GUESS:
            free = {q: 0.0 for q in "vspgyx"}; en_ = [0.0] * n; fx = fac["x"]
            for i in sq:
                q = r[2][i]; st = free[q]
                for j in hard[i]:
                    if en_[j] + lat > st: st = en_[j] + lat
                for j in soft[i]:
                    if en_[j] > st: st = en_[j]
                st += (r[1][i] - r[0][i]) * fac[kind[i]]; en_[i] = st + late[i] * fx
                if q != "x": free[q] = st
            tot += wt * max(en_)
        return tot / (OWN[0] + sum(x[2] for x in GUESS))
    if given:
        cur = place(range(n), pre, False, [-99.0 if r[2] == "v" else 99.0 for r in given])
    else:
        key = [-pri[i] - BIAS.get(ops[i]["tag"], 0.0) for i in range(n)]; pen = [PEN[0]] * n
        for i in range(n - 1, -1, -1):
            for j, _ in pre[i]:
                if key[j] >= key[i]: key[j] = key[i] - 0.001
        cur = both(both(place(sorted(range(n), key=lambda i: (key[i], i)), pre, False, pen), pen), pen)
    sc_ = score(cur); top = (sc_, cur)
    for it in range(passes):
        key = np.array(cur[0]); pen = keep(cur); near = np.abs(key - rng.uniform(0, span(cur))) < rng.choice([3000.0, 8000.0, 20000.0])
        m = rng.randint(4) if near.any() else 0
        if m == 0: key = key + near * rng.normal(0, rng.choice([200.0, 600.0, 1500.0]), n)
        elif m == 1:
            idx = np.array(tags[ops[rng.choice(np.flatnonzero(near))]["tag"]]); key[idx[near[idx]]] += rng.normal(0, 3000.0)
        else:
            for i in flex:
                if near[i] and m == 2: pen[i] = 0.5 * rng.randint(4)
                elif near[i] and rng.rand() < 0.1: pen[i] = -pen[i]
        key = key.tolist()
        for i in range(n):
            for j, _ in pre[i]:
                if key[j] >= key[i]: key[i] = key[j] + 0.001
        r = place(sorted(range(n), key=lambda i: key[i]), pre, False, pen)
        if it % 3 == 0: r = both(r, keep(r))
        bar = sc_ - TEMP[0] * (1.0 - it / passes) * np.log(rng.rand() + 1e-12)
        if span(r) > span(cur) + 3000.0: continue
        s = score(r)
        if s < bar:
            cur, sc_ = r, s
            if s < top[0]: top = (s, r)
    res = polish(ops, fw, list(zip(*stretches(ops, pre, post, top[1], rng, rounds))), rng, steps)
    return res, score(list(zip(*res)))


def stretches(ops, pre, post, res, rng, rounds):
    n = len(ops); late = [o.get("dma", 0.0) for o in ops]; cv = [o["cost"] for o in ops]; cs = [o.get("cs", o["cost"]) for o in ops]
    st, en, pk = list(res[0]), list(res[1]), list(res[2]); seq = list(range(n)); lo = 0
    for rd in range(rounds):
        seq.sort(key=lambda i: (st[i], i))
        w = (120, 200, 300)[rng.randint(3)]; lo = (lo + w // 3 + rng.randint(w // 3)) % (n - w // 2); hi = min(n, lo + w)
        tail = [0.0] * n; after = {q: 0.0 for q in "vspgyx"}; free = dict(after)
        for i in seq[:hi - 1:-1]:
            t = max([late[i], after[pk[i]] if pk[i] != "x" else 0.0] + [lag + tail[k] for k, lag in post[i]])
            tail[i] = after[pk[i]] = t + en[i] - st[i]
        for i in seq[:lo]: free[pk[i]] = en[i]
        win = seq[lo:hi]; loc = {i: k for k, i in enumerate(win)}; m = len(win)
        lp = [[(loc[j], lag) for j, lag in pre[i] if j in loc] for i in win]; ls = [[(loc[j], lag) for j, lag in post[i] if j in loc] for i in win]
        head = [max([0.0] + [en[j] + lag for j, lag in pre[i] if j not in loc]) for i in win]
        out = [max([late[i]] + [lag + tail[j] for j, lag in post[i] if j not in loc]) for i in win]
        wq = [ops[i]["q"] for i in win]; wv = [cv[i] for i in win]; ws = [cs[i] for i in win]; flex = [k for k in range(m) if len(wq[k]) == 2]

        def place(order, pen):
            S_ = {q: [] for q in "vspgy"}; E_ = {q: [] for q in "vspgy"}; a = [0.0] * m; b = [0.0] * m; p = [""] * m; worst = tot = 0.0
            for k in order:
                rdy = head[k]
                for j, lag in lp[k]:
                    if b[j] + lag > rdy: rdy = b[j] + lag
                best = None
                for q in wq[k]:
                    if q == "x":
                        best = (0, q, rdy, wv[k], 0); break
                    c = ws[k] if q == "s" else wv[k]; s, e = S_[q], E_[q]; t = rdy if rdy > free[q] else free[q]; x = y = len(s)
                    while x and e[x - 1] > t: x -= 1
                    while x < y and s[x] < t + c:
                        if e[x] > t: t = e[x]
                        x += 1
                    key = t + c + (pen[k] if q == "v" else 0.0)
                    if best is None or key < best[0]: best = (key, q, t, c, x)
                _, q, t, c, x = best
                if q != "x": S_[q].insert(x, t); E_[q].insert(x, t + c)
                a[k] = t; b[k] = t + c; p[k] = q
                if t + c + out[k] > worst: worst = t + c + out[k]
            for q in E_:
                if E_[q]: tot += E_[q][-1] + after[q]; worst = max(worst, E_[q][-1] + after[q])
            return worst + 0.01 * tot, a, b, p
        keep = lambda p: [-1e9 if q == "v" else 1e9 for q in p]
        top = cur = place(range(m), keep([pk[i] for i in win]))
        for it in range(TRIES[0]):
            key = np.array(cur[1]); pen = keep(cur[3]); u = rng.randint(5); near = np.abs(key - key[rng.randint(m)]) < (1000.0, 2500.0, 6000.0)[rng.randint(3)]
            if u < 2: key = key + near * rng.normal(0, (150.0, 400.0, 1000.0)[rng.randint(3)], m)
            elif u == 2:
                pr = [0.0] * m
                for k in sorted(range(m), key=lambda k: -cur[1][k]): pr[k] = max([out[k]] + [lag + pr[j] for j, lag in ls[k]]) + cur[2][k] - cur[1][k]
                pr = -np.array(pr); f = rng.rand(); key = np.where(near, key * (1 - f) + f * (pr - np.mean((pr - key)[near])) + rng.normal(0, 100.0, m), key)
            else:
                for k in flex:
                    if near[k] and u == 3: pen[k] = (0.0, 200.0, 600.0)[rng.randint(3)]
                    elif near[k] and rng.rand() < 0.2: pen[k] = -pen[k]
            key = key.tolist()
            for k in range(m):
                for j, _ in lp[k]:
                    if key[j] >= key[k]: key[k] = key[j] + 0.001
            r = place(sorted(range(m), key=lambda k: key[k]), pen)
            if r[0] < cur[0] - TRIES[1] * (1 - it / TRIES[0]) * np.log(rng.rand() + 1e-12):
                cur = r
                if r[0] < top[0]: top = r
        for k, i in enumerate(win): st[i], en[i], pk[i] = top[1][k], top[2][k], top[3][k]
        win.sort(key=lambda i: (st[i], i)); seq[lo:hi] = win; free = {}
        for i in seq:
            s = max([free.get(pk[i], 0.0) if pk[i] != "x" else 0.0] + [en[j] + lag for j, lag in pre[i]])
            st[i] = s; en[i] = free[pk[i]] = s + (cs[i] if pk[i] == "s" else cv[i])
    return st, en, pk


def emit(ops, g, T):
    n = len(ops); tiles(ops); base = list(ops)
    if n not in PLAN:
        rng = np.random.RandomState(SEED[0]); ties(ops); res = search(ops, rng, *PASSES)[0]; best = None
        for how in AGAIN:
            ties(base); res = later(base, res); tried = []
            for _ in range(SEATS[0]):
                ties(base); rows = banks(base, res, rng); out = seat(base, rows, res)
                tried.append((search([base[i] for i in out], rng, 0, 0, 0, [res[i] for i in out])[1], rows))
            rows = min(tried, key=lambda x: x[0])[1]; out = seat(base, rows, res)
            new, sc_ = search([base[i] for i in out], rng, *how, [res[i] for i in out])
            if best is None or sc_ < best[0]: best = (sc_, rows, res, new)
            INFO.append((round(sc_), round(max(r[1] for r in res)), round(max(r[1] for r in new))))
            res = [None] * n
            for i, r in zip(out, new): res[i] = r
        PLAN[n] = best
    _, rows, old, res = PLAN[n]
    ops[:] = [base[i] for i in seat(base, rows, old)]
    end = [0.0] * n
    for i, o in enumerate(ops):
        o["st"], o["pick"] = res[i][0], res[i][2]; o["cost"] = res[i][1] - o["st"]; end[i] = res[i][1] + o.get("dma", 0)
    seq = sorted(range(n), key=lambda i: (ops[i]["st"], i))
    e = {"v": g.vector, "s": g.scalar, "p": g.tensor, "g": g, "y": g.sync}
    cnt = {}; know = {q: {} for q in e}; nd = [0]
    for i in seq:
        o = ops[i]; q = o["pick"]
        if q == "x":
            o["sig"], o["know"] = o["sem"], {}; cnt[o["sem"][0]] = o["sem"][1]
            continue
        kn = know[q]; need = {}
        for j in o["deps"]:
            s_, v = ops[j]["sig"]; need[s_] = max(need.get(s_, (0, j)), (v, j))
        for s_, (v, j) in sorted(need.items(), key=lambda x: -end[x[1][1]]):
            if kn.get(s_, 0) < v:
                e[q].wait_ge(T.sem[s_], v); kn[s_] = v
                for a, b in ops[j]["know"].items(): kn[a] = max(kn.get(a, 0), b)
        o["know"] = dict(kn); e["pick"] = q; NOW.clear(); NOW.update(o.get("bank", {}))
        ins = o["fn"](e)
        if "send" in o:
            cnt[o["send"][0]] = o["send"][1]; o["sig"] = o["send"]
            continue
        if "dma" in o:
            s_, inc = "d%d" % nd[0], 16; nd[0] += 1
        else:
            s_, inc = "c" + q, 1; ins = ins[-1:]
        for x in ins:
            x.then_inc(T.sem[s_], inc); cnt[s_] = cnt.get(s_, 0) + inc
        o["sig"] = (s_, cnt[s_])
    for s_, v in cnt.items(): g.wait_ge(T.sem[s_], v)
    return max(end), {q: sum(o["cost"] for o in ops if o["pick"] == q) for q in "vspg"}


INFO, NOW = [], {}


def rank_program(g, core, T, topo):
    rank = T.rank_of(core)
    if rank is None:
        return
    n = len(T.cores)

    def peer(to):
        rid, pid, _ = topo.addr(to)
        return (rid, pid, topo.mask(core, to), len(topo.engines(core, to)), len(topo.engines(to, core)))
    ops = []
    program(ops, T, peer(T.cores[(rank + 1) % n]), peer(T.cores[(rank - 1) % n]))
    INFO.append((emit(ops, g, T), ops))
